import numpy as np
import ml_dtypes


def mxq(x, axis, fmt="e4m3"):
    dtype, down = {"e4m3": (ml_dtypes.float8_e4m3fn, 7), "e5m2": (ml_dtypes.float8_e5m2, 14)}[fmt]
    v = np.moveaxis(np.asarray(x, np.float32).astype(ml_dtypes.bfloat16).astype(np.float64), axis, -1)
    blocks = v.reshape(v.shape[:-1] + (-1, 32))
    amax = np.abs(blocks).max(-1, keepdims=True)
    byte = np.maximum(np.where(amax > 0, np.frexp(amax)[1] - 1 + 127, 0) - down, 1)
    scale = np.exp2(byte - 127.0)
    codes = (blocks / scale).astype(np.float32).astype(dtype).astype(np.float64)
    return np.moveaxis((codes * scale).reshape(v.shape), -1, axis)


WIDE = False


def mx_kscale(k):
    if not WIDE:
        return np.ones(k)
    levels = np.array([10, -10, 5, -5, 0])
    if k % 512:
        return np.exp2(np.random.permutation(np.resize(levels, k // 32))).repeat(32)
    a = np.empty((k // 512, 16))
    for p in range(k // 512):
        a[p, :8] = np.random.permutation(np.resize(levels, 8))
        for g in range(8):
            far = levels[np.abs(levels - a[p, g]) >= 10]
            a[p, g + 8] = far[np.random.randint(len(far))]
    return np.exp2(a.ravel()).repeat(32)


BF16 = ml_dtypes.bfloat16


def bf(x):
    return np.asarray(x, np.float32).astype(BF16)


def f64(x):
    return np.asarray(x).astype(np.float64)


E2M1 = np.array([0.0, 0.5, 1.0, 1.5, 2.0, 3.0, 4.0, 6.0, -0.0, -0.5, -1.0, -1.5, -2.0, -3.0, -4.0, -6.0])


def pack_weight(w, fmt):
    k, n = w.shape
    w = f64(bf(w)).reshape(k // 32, 32, n)
    amax = np.abs(w).max(1)
    if fmt == "e4m3":
        byte = np.frexp(amax)[1] - 1 + 127 - 7
    else:
        mant, ex = np.frexp(amax / 6.0)
        byte = np.where(mant > 0.5, ex, ex - 1) + 127
    byte = np.clip(np.where(amax > 0, byte, 1), 1, 254)
    scaled = (w * np.exp2(127.0 - byte)[:, None, :]).reshape(k, n).astype(np.float32)
    by_word = np.ascontiguousarray(scaled.reshape(k // 512, 128, 4, n).transpose(0, 1, 3, 2))
    if fmt == "e4m3":
        words = by_word.astype(ml_dtypes.float8_e4m3fn).view(np.uint8)
    else:
        c = by_word.astype(ml_dtypes.float4_e2m1fn).view(np.uint8) & 0xF
        words = c[..., 0::2] | (c[..., 1::2] << 4)
    return np.ascontiguousarray(words), np.ascontiguousarray(byte.astype(np.uint8).reshape(k // 512, 16, n))


def unpack_weight(words, scales, fmt):
    g, p, n, _ = words.shape
    if fmt == "e4m3":
        vals = np.ascontiguousarray(words).view(ml_dtypes.float8_e4m3fn).astype(np.float64)
    else:
        nib = np.empty((g, p, n, 4), np.uint8)
        nib[..., 0::2] = words & 0xF
        nib[..., 1::2] = words >> 4
        vals = E2M1[nib]
    vals = vals * np.repeat(np.exp2(scales.astype(np.float64) - 127.0), 8, axis=1)[..., None]
    return vals.transpose(0, 1, 3, 2).reshape(g * 512, n)
def pack4(w):
    words, scales = pack_weight(w, "e2m1")
    return words.reshape(words.shape[0], 128, -1), scales


def unpack4(words, scales):
    return unpack_weight(words.reshape(words.shape[0], 128, -1, 2), scales, "e2m1")


E4M3FN = np.array([(-1.0 if i & 128 else 1.0) * ((1.0 + (i & 7) / 8.0) * 2.0 ** (((i >> 3) & 15) - 7) if i & 120 else (i & 7) * 2.0 ** -9) for i in range(256)])


def e4m3fn_bytes(y):
    return np.clip(np.asarray(y, np.float64), -448.0, 448.0).astype(np.float32).astype(ml_dtypes.float8_e4m3fn).view(np.uint8)


def e4m3fn_values(b):
    return E4M3FN[b]


L, P, B, D, T = 3, 2, 1024, 1024, 512


def scaled_message(n):
    w = np.exp(n - n.max(-1, keepdims=True))
    return n.shape[-1] * (w / w.sum(-1, keepdims=True))


def log_normalise(q):
    top = q.max(-1, keepdims=True)
    log_z = top + np.log(np.sum(np.exp(q - top), axis=-1, keepdims=True))
    return q - log_z + np.log(q.shape[-1])


def draw0():
    s = mx_kscale(D)
    t = np.stack([mx_kscale(T) for _ in range(P)])
    x = bf(np.random.standard_normal((L, B, D)) * s)
    words, scales = pack4(np.random.standard_normal((D, T)) / np.sqrt(D) / s[:, None])
    return {
        "x": x,
        "we_words": words,
        "we_scales": scales,
        "be": bf(0.3 * np.random.standard_normal(T)),
        "ends": bf(0.5 * np.random.standard_normal((P, T))),
        "gain": bf(np.random.standard_normal((P, T)) * t),
        "trans": bf(np.random.standard_normal((P, T, T)) * 3.5 / np.sqrt(T) / t[:, :, None]),
    }


def core(x, we_words, we_scales, be, ends, gain, trans):
    e = (mxq(f64(x), 2, "e4m3") @ unpack4(we_words, we_scales)) + f64(be)
    en = f64(ends)
    n = np.stack([e[0] + en[0], e[2] + en[1]], axis=0)
    u = scaled_message(n)
    v = u * f64(gain)[:, None, :]
    m = mxq(v, 2, "e4m3") @ mxq(f64(trans), 1, "e4m3")
    c = np.log(np.maximum(1.0 + m / 16.0, 0.1))
    q = e[1] + c[0] + c[1]
    return log_normalise(q)


def setup_inputs():
    drawn = draw0()
    full = np.asarray(drawn['x']).astype(np.float64)
    scale = (np.abs(full).reshape(3, 8, 128, 8, 128).max(axis=(2, 4)) / 448.0).astype(np.float32)
    given = {}
    for key, value in drawn.items():
        if key == 'x':
            given['x_bytes'] = e4m3fn_bytes(full / np.repeat(np.repeat(scale.astype(np.float64), 128, axis=1), 128, axis=2))
            given['x_scale'] = scale
        else:
            given[key] = value
    return given


def reference(x_bytes, x_scale, we_words, we_scales, be, ends, gain, trans):
    return core(e4m3fn_values(x_bytes) * np.repeat(np.repeat(x_scale.astype(np.float64), 128, axis=1), 128, axis=2), we_words, we_scales, be, ends, gain, trans)

@@ -1,0 +1,352 @@
+from contextlib import ExitStack
+
+import concourse.mybir as mybir
+from concourse.masks import make_identity
+
+L, PAIRS, B, D, T = 3, 2, 1024, 1024, 512
+FLOPS = 2 * L * B * D * T + 2 * PAIRS * B * T * T
+
+F32 = mybir.dt.float32
+BF16 = mybir.dt.bfloat16
+I32 = mybir.dt.int32
+U32 = mybir.dt.uint32
+U8 = mybir.dt.uint8
+FP8 = mybir.dt.float8_e4m3fn
+FP8X4 = mybir.dt.float8_e4m3fn_x4
+FP4X4 = mybir.dt.float4_e2m1fn_x4
+ACT = mybir.ActivationFunctionType
+ALU = mybir.AluOpType
+AX = mybir.AxisListType
+
+P = 128
+TILES = B // P
+PASSES = D // 512
+KBLOCKS = D // 128
+FLOOR_M = 14.4
+FLOOR_A = 1.6
+SUM_LAG = 3
+MID_LAG = 1
+NVS = [0, 0, 5, 2, 1, 1, 5, 0, 2, 1, 2, 2, 0, 2, 0, 2, 0, 0, 0, 0, 0, 0, 0, 0, 2, 0, 0, 2, 0, 0, 2, 0, 0, 2]
+PAUSE = [20]
+SORD = 'EWPfLV'
+VORD = '1GafpiFwsxSt0'
+SETUP = [-4, -3, -2, -1, 4, 5, 4]
+L_MSG0 = 2
+L_MSG1 = 3
+L_TV = 4
+L_QV = 5
+L_FL = 6
+L_PR = 7
+L_PS = 7
+LOGS = 1
+XB = 3
+
+
+def tile_chunkflooredmessagemiddlescore_kernel(tc, x_bytes, x_scale, we_words, we_scales, be, ends, gain, trans, out):
+    nc = tc.nc
+
+    units = []
+    for i in range(TILES + MID_LAG):
+        if i < TILES:
+            units += [(i, 0), (i, 2)]
+        if i >= MID_LAG:
+            units += [(i - MID_LAG, 1)]
+    slot_of = {u: s for s, u in enumerate(units)}
+    NU = len(units)
+
+    with ExitStack() as ctx:
+        keep = ctx.enter_context(tc.tile_pool(name="keep", bufs=1))
+        work = ctx.enter_context(tc.tile_pool(name="work", bufs=4))
+        psum = ctx.enter_context(tc.psum_pool(name="psum", bufs=2))
+        ctx.enter_context(tc.manual_schedule())
+
+        rows = keep.tile([P, 2 * T], BF16, name="rows")
+        we_s = keep.tile([P, PASSES, T], U8, name="we_s", align_bytes=64)
+        we_w = keep.tile([P, PASSES, 2 * T], U8, name="we_w", align_bytes=64)
+        xs = keep.tile([P, L * TILES * KBLOCKS], F32, name="xs")
+        ident = keep.tile([P, P], F32, name="ident")
+        coef = keep.tile([P, 10], BF16, name="coef")
+        nc.vector.memset(rows[:].bitcast(I32), 0)
+        nc.vector.memset(we_s[:].rearrange("p g n -> p (g n)").bitcast(I32), 0)
+
+        xb = {}
+
+        def load_x(s):
+            i, l = units[s]
+            xb[s] = keep.tile([P, D], U8, name="xbytes%d" % s)
+            nc.sync.dma_start(out=xb[s][:], in_=x_bytes[l, i * P:(i + 1) * P, :])
+
+        nc.scalar.dma_start(out=xs[:], in_=x_scale.rearrange("l i j -> (l i j)").partition_broadcast(P))
+        load_x(0)
+        load_x(1)
+        nc.sync.dma_start(out=rows[0:1, 0:T], in_=be.rearrange("(o n) -> o n", o=1))
+        nc.sync.dma_start(out=rows[32:65:32, 0:T], in_=ends)
+        nc.sync.dma_start(out=rows[0:33:32, T:2 * T], in_=gain)
+        nc.sync.dma_start(out=we_w[:].bitcast(I32), in_=we_words.rearrange("g p n -> p g n").bitcast(I32))
+        for q in range(4):
+            nc.sync.dma_start(
+                out=we_s[32 * q:32 * q + 4, :, :].bitcast(I32),
+                in_=we_scales[:, 4 * q:4 * q + 4, :].rearrange("g r n -> r g n").bitcast(I32),
+            )
+        load_x(2)
+        load_x(3)
+        tr_raw = {}
+        for p in range(PAIRS):
+            tr_raw[p] = keep.tile([P, 4, T], BF16, name="tr_raw%d" % p)
+            nc.sync.dma_start(out=tr_raw[p][:], in_=trans[p].rearrange("(p j) n -> p j n", j=4))
+            load_x(4 + p)
+        for s in range(6, NU):
+            load_x(s)
+
+        make_identity(nc, ident[:])
+        nc.gpsimd.memset(coef[:], 0.0)
+        nc.gpsimd.memset(coef[0:1, 0:6], -1.0)
+        nc.gpsimd.memset(coef[32:33, 0:2], -1.0)
+        nc.gpsimd.memset(coef[64:65, 4:6], -1.0)
+        nc.gpsimd.memset(coef[0:1, 6:8], float(T))
+        nc.gpsimd.memset(coef[32:33, 8:10], float(T))
+
+        neg_bias = {}
+        gain_t = {}
+
+        def spread(c, half, name):
+            acc = psum.tile([P, T], F32, name="m_ps", tag="m_ps")
+            nc.tensor.matmul(acc[:], lhsT=coef[:, c:c + 1].to_broadcast([P, P]), rhs=rows[:, half * T:(half + 1) * T], start=True, stop=True)
+            wide = keep.tile([P, T], F32, name=name)
+            nc.vector.tensor_copy(out=wide[:], in_=acc[:])
+            return wide
+
+        tr_grouped = {}
+        tr_codes = keep.tile([P, PAIRS, T], U32, name="tr_codes", align_bytes=64)
+        tr_scales = keep.tile([P, PAIRS, T], U8, name="tr_scales", align_bytes=64)
+
+        def interleave_trans(p):
+            tr_grouped[p] = keep.tile([P, T, 4], BF16, name="tr_grouped%d" % p, align_bytes=64)
+            nc.vector.tensor_copy(
+                out=tr_grouped[p][:].rearrange("p (c i) t -> p c t i", i=4),
+                in_=tr_raw[p][:].rearrange("p t (c i) -> p c t i", i=4),
+            )
+
+        def quantize_trans(p):
+            nc.vector.quantize_mx(out=tr_codes[:, p, :].bitcast(FP8X4), scales=tr_scales[:, p, :], in_=tr_grouped[p][:].rearrange("p n t -> p (n t)"))
+
+        xw, xt, xg, xq, xqs, e_ps, neg_n, neg_max, ex = {}, {}, {}, {}, {}, {}, {}, {}, {}
+        sums = [keep.tile([P, 3], F32, name="sums%d" % i) for i in range(TILES + SUM_LAG)]
+        inv = [keep.tile([P, 3], F32, name="inv%d" % i) for i in range(TILES + SUM_LAG)]
+
+        def widen(s, blocks, on_vector):
+            i, l = units[s]
+            if s not in xw:
+                xw[s] = work.tile([P, D], BF16, name="xw", tag="xw", bufs=4)
+            for j in blocks:
+                cols = slice(j * 128, (j + 1) * 128)
+                c = (l * TILES + i) * KBLOCKS + j
+                if on_vector:
+                    nc.vector.tensor_scalar(out=xw[s][:, cols], in0=xb[s][:, cols].bitcast(FP8), scalar1=xs[:, c:c + 1], scalar2=None, op0=ALU.mult)
+                else:
+                    nc.scalar.activation(out=xw[s][:, cols], in_=xb[s][:, cols].bitcast(FP8), func=ACT.Copy, scale=xs[:, c:c + 1])
+
+        def turn_x(s):
+            words = xw[s][:].bitcast(F32)
+            xt[s] = psum.tile([P, PASSES, 2, P], F32, name="xt", tag="xt", bufs=3)
+            for g in range(PASSES):
+                for u in range(2):
+                    nc.tensor.transpose(xt[s][:, g, u, :], words[:, 256 * g + u:256 * (g + 1):2], ident[:])
+
+        def empty_x(s):
+            xg[s] = work.tile([P, PASSES, P, 2], F32, name="xg", tag="xg", align_bytes=64)
+            nc.scalar.copy(out=xg[s][:], in_=xt[s][:].rearrange("p g u r -> p g r u"))
+
+        def quantize_x(s):
+            xq[s] = work.tile([P, PASSES * P], U32, name="xq", tag="xq", align_bytes=64)
+            xqs[s] = work.tile([P, PASSES * P], U8, name="xqs", tag="xqs", align_bytes=64)
+            nc.vector.quantize_mx(out=xq[s][:].bitcast(FP8X4), scales=xqs[s][:], in_=xg[s][:].rearrange("p g r u -> p (g r u)").bitcast(BF16))
+
+        def emit(s):
+            e_ps[s] = psum.tile([P, T], F32, name="e_ps", tag="e_ps")
+            for g in range(PASSES):
+                cols = slice(g * P, (g + 1) * P)
+                nc.tensor.matmul_mx(
+                    out=e_ps[s][:], lhsT=xq[s][:, cols].bitcast(FP8X4), lhsT_scale=xqs[s][:, cols],
+                    rhs=we_w[:, g, :].bitcast(FP4X4), rhs_scale=we_s[:, g, :], start=(g == 0), stop=(g == PASSES - 1),
+                )
+
+        def add_bias(s):
+            i, l = units[s]
+            if l == 1:
+                neg_n[s] = keep.tile([P, T], F32, name="neg_mid%d" % i)
+            else:
+                neg_n[s] = work.tile([P, T], F32, name="neg_n", tag="neg_n")
+            nc.vector.tensor_tensor(out=neg_n[s][:], in0=neg_bias[l][:], in1=e_ps[s][:], op=ALU.subtract)
+
+        def find_max(s):
+            neg_max[s] = keep.tile([P, 1], F32, name="neg_max%d" % s)
+            nc.vector.tensor_reduce(out=neg_max[s][:], in_=neg_n[s][:], axis=AX.X, op=ALU.min)
+
+        def exponent(s):
+            i, l = units[s]
+            if l == 1:
+                ex[s] = work.tile([P, T], F32, name="ex_mid", tag="ex_mid", bufs=6)
+                nc.scalar.activation(out=ex[s][:], in_=neg_n[s][:], func=ACT.Exp, bias=neg_max[s][:], scale=-1.0)
+            else:
+                ex[s] = work.tile([P, T], F32, name="ex", tag="ex", bufs=6)
+                nc.scalar.activation(out=ex[s][:], in_=neg_n[s][:], func=ACT.Exp, bias=neg_max[s][:], scale=-1.0, accum_out=sums[i][:, l // 2:l // 2 + 1])
+
+        v, vt, vg, vq, vqs, m_ps, fl0, fl1, prod, logp = {}, {}, {}, {}, {}, {}, {}, {}, {}, {}
+
+        def invert(i, cols):
+            nc.vector.reciprocal(out=inv[i][:, cols], in_=sums[i][:, cols])
+
+        def message(i, p):
+            s = slot_of[i, 2 * p]
+            if p == 0:
+                v[i] = work.tile([P, PAIRS, T], BF16, name="v", tag="v")
+            nc.vector.scalar_tensor_tensor(out=v[i][:, p, :], in0=ex[s][:], scalar=inv[i][:, p:p + 1], in1=gain_t[p][:], op0=ALU.mult, op1=ALU.mult)
+
+        def turn_v(i):
+            vt[i] = psum.tile([P, PAIRS, 2, P], F32, name="vt", tag="vt", bufs=1)
+            words = v[i][:].rearrange("p a n -> p (a n)").bitcast(F32)
+            for p in range(PAIRS):
+                for u in range(2):
+                    nc.tensor.transpose(vt[i][:, p, u, :], words[:, 256 * p + u:256 * (p + 1):2], ident[:])
+
+        def empty_v(i):
+            vg[i] = work.tile([P, PAIRS, P, 2], F32, name="vg", tag="vg", align_bytes=64)
+            nc.scalar.copy(out=vg[i][:], in_=vt[i][:].rearrange("p g u r -> p g r u"))
+
+        def quantize_v(i):
+            vq[i] = work.tile([P, PAIRS * P], U32, name="vq", tag="vq", align_bytes=64)
+            vqs[i] = work.tile([P, PAIRS * P], U8, name="vqs", tag="vqs", align_bytes=64)
+            nc.vector.quantize_mx(out=vq[i][:].bitcast(FP8X4), scales=vqs[i][:], in_=vg[i][:].rearrange("p g r u -> p (g r u)").bitcast(BF16))
+
+        def pass_on(i):
+            for p in range(PAIRS):
+                cols = slice(p * P, (p + 1) * P)
+                m_ps[i, p] = psum.tile([P, T], F32, name="m_ps", tag="m_ps")
+                nc.tensor.matmul_mx(
+                    out=m_ps[i, p][:], lhsT=vq[i][:, cols].bitcast(FP8X4), lhsT_scale=vqs[i][:, cols],
+                    rhs=tr_codes[:, p, :].bitcast(FP8X4), rhs_scale=tr_scales[:, p, :], start=True, stop=True,
+                )
+
+        def floor_first(i):
+            fl0[i] = work.tile([P, T], F32, name="fl0", tag="fl0")
+            nc.scalar.activation(out=fl0[i][:], in_=m_ps[i, 0][:], func=ACT.Relu, bias=FLOOR_M, scale=1.0)
+
+        def floor_second(i):
+            fl1[i] = work.tile([P, T], F32, name="fl1", tag="fl1")
+            nc.vector.tensor_scalar(out=fl1[i][:], in0=m_ps[i, 1][:], scalar1=-FLOOR_M, scalar2=16.0, op0=ALU.max, op1=ALU.add)
+
+        def multiply(i):
+            prod[i] = keep.tile([P, T], F32, name="prod%d" % i)
+            nc.vector.scalar_tensor_tensor(out=prod[i][:], in0=fl0[i][:], scalar=FLOOR_A, in1=fl1[i][:], op0=ALU.add, op1=ALU.mult)
+
+        def partition_sum(i):
+            s = slot_of[i, 1]
+            weighted = work.tile([P, T], F32, name="weighted", tag="weighted", bufs=1)
+            nc.vector.scalar_tensor_tensor(out=weighted[:], in0=ex[s][:], scalar=1.0 / T, in1=prod[i][:], op0=ALU.mult, op1=ALU.mult, accum_out=sums[i + SUM_LAG][:, 2:3])
+
+        def take_log(i):
+            logp[i] = work.tile([P, T], F32, name="logp", tag="logp", bufs=8)
+            nc.scalar.activation(out=logp[i][:], in_=prod[i][:], func=ACT.Ln, scale=inv[i + SUM_LAG][:, 2:3])
+
+        def finish(i):
+            s = slot_of[i, 1]
+            res = work.tile([P, T], F32, name="res", tag="res", bufs=8)
+            nc.vector.scalar_tensor_tensor(out=res[:], in0=logp[i][:], scalar=neg_max[s][:], in1=neg_n[s][:], op0=ALU.add, op1=ALU.subtract)
+            nc.sync.dma_start(out=out[i * P:(i + 1) * P, :], in_=res[:])
+
+        def live(s):
+            return 0 <= s < NU
+
+        def tile_at(s, lag):
+            u = s - lag
+            return units[u][0] if live(u) and units[u][1] == 2 else None
+
+        def vector_blocks(s):
+            return NVS[s + 4] if s < NU else 0
+
+        def at(s, lag, stage, *more):
+            if tile_at(s, lag) is not None:
+                stage(tile_at(s, lag), *more)
+
+        ready, logged = [], []
+
+        def invert_sums(i):
+            invert(i, slice(0, 3 if i >= SUM_LAG else 2))
+            if i >= SUM_LAG:
+                ready.append(i - SUM_LAG)
+
+        def invert_last(i):
+            if i + SUM_LAG >= TILES:
+                invert(i + SUM_LAG, slice(2, 3))
+                ready.append(i)
+
+        s = -4
+        done = 0
+        clock = -4
+        while done < TILES:
+            nv = vector_blocks(s)
+            z = -99 if s in PAUSE else clock
+            clock += 0 if s in PAUSE else 1
+            if s == SETUP[0]:
+                neg_bias[0] = spread(0, 0, "neg_bias0")
+                neg_bias[2] = spread(4, 0, "neg_bias2")
+            if live(s + 3):
+                turn_x(s + 3)
+            at(z, L_TV, turn_v)
+            if live(s + 1):
+                quantize_x(s + 1)
+            at(z, L_QV, quantize_v)
+            if live(s + 1):
+                emit(s + 1)
+            at(z, L_QV, pass_on)
+            finishing = list(logged)
+            logged.clear()
+            def logs():
+                if s >= NU:
+                    for i in ready[:LOGS]:
+                        take_log(i)
+                        logged.append(i)
+                        ready.remove(i)
+            ssteps = {
+                "P": lambda: exponent(s - 1) if live(s - 1) else None,
+                "f": lambda: at(z, L_FL, floor_first),
+                "E": lambda: empty_x(s + 2) if live(s + 2) else None,
+                "V": lambda: at(z, L_TV, empty_v),
+                "W": lambda: widen(s + 4, range(nv, KBLOCKS), False) if live(s + 4) else None,
+                "L": logs,
+            }
+            for c in SORD:
+                ssteps[c]()
+            def setup_work():
+                if s == SETUP[1]:
+                    gain_t[0] = spread(6, 1, "gain0")
+                    gain_t[1] = spread(8, 1, "gain1")
+                if s == SETUP[2]:
+                    neg_bias[1] = spread(2, 0, "neg_bias1")
+                for p in range(2):
+                    if s == SETUP[3 + p]:
+                        interleave_trans(p)
+            def setup2():
+                for p in range(2):
+                    if s == SETUP[5 + p]:
+                        quantize_trans(p)
+            steps = {
+                "w": lambda: widen(s + 4, range(nv), True) if live(s + 4) else None,
+                "i": lambda: (at(z, L_MSG0, invert_sums), at(z, L_PS + 1, invert_last)),
+                "a": lambda: add_bias(s) if live(s) else None,
+                "p": lambda: at(z, L_PR, multiply),
+                "1": lambda: at(z, L_MSG1, message, 1),
+                "0": lambda: at(z, L_MSG0, message, 0),
+                "s": setup_work,
+                "x": lambda: find_max(s) if live(s) else None,
+                "t": setup2,
+                "f": lambda: at(z, L_FL, floor_second),
+                "F": lambda: [finish(i) for i in finishing[:1]],
+                "S": lambda: at(z, L_PS, partition_sum),
+                "G": lambda: [finish(i) for i in finishing[1:]],
+            }
+            for c in VORD:
+                steps[c]()
+            done += len(finishing)
+            s += 1

@@ -26,11 +26,11 @@ FLOOR_M = 14.4
 FLOOR_A = 1.6
 SUM_LAG = 3
 MID_LAG = 1
-NVS = [0, 0, 5, 2, 1, 1, 5, 0, 2, 1, 2, 2, 0, 2, 0, 2, 0, 0, 0, 0, 0, 0, 0, 0, 2, 0, 0, 2, 0, 0, 2, 0, 0, 2]
-PAUSE = [20]
-SORD = 'EWPfLV'
-VORD = '1GafpiFwsxSt0'
-SETUP = [-4, -3, -2, -1, 4, 5, 4]
+NVS = [0, 2, 5, 3, 2, 2, 2, 2, 2, 2, 2, 2, 1, 1, 1, 1, 1, 1, 1, 0, 0, 0, 0, 0]
+PAUSE = []
+SORD = "PfEVWLR"
+VORD = "wiap10sxtfFSG"
+SETUP = [-3, -2, -1, 0, 1, 1, 2]
 L_MSG0 = 2
 L_MSG1 = 3
 L_TV = 4
@@ -38,8 +38,12 @@ L_QV = 5
 L_FL = 6
 L_PR = 7
 L_PS = 7
-LOGS = 1
-XB = 3
+LOGS = 3
+WARM = 2
+FLS = 8
+FPE = 0
+GP = 0
+ORDER = [('spr', 0), ('Wv', 0), ('Wv', 1), ('Ws', 0), ('spr', 2), ('Ws', 1), ('T', 0), ('E', 0), ('Ws', 2), ('T', 1), ('it', 0), ('Wv', 2), ('Q', 0), ('Wv', 3), ('E', 1), ('Ws', 3), ('Q', 1), ('Ws', 4), ('qt', 0), ('T', 2), ('M', 0), ('M', 1), ('A', 0), ('T', 3), ('E', 2), ('Wv', 4), ('X', 0), ('A', 1), ('T', 4), ('Wv', 5), ('P', 0), ('Ws', 5), ('Q', 2), ('X', 1), ('M', 2), ('it', 1), ('sg', 0), ('E', 3), ('qt', 1), ('T', 5), ('Q', 3), ('M', 3), ('E', 4), ('Ws', 6), ('P', 1), ('A', 2), ('Wv', 6), ('X', 2), ('T', 6), ('Q', 4), ('M', 4), ('E', 5), ('Ws', 7), ('P', 2), ('A', 3), ('Wv', 7), ('inv', 0), ('X', 3), ('m0', 0), ('T', 7), ('Q', 5), ('M', 5), ('E', 6), ('Ws', 8), ('P', 3), ('A', 4), ('Wv', 8), ('m1', 0), ('X', 4), ('T', 8), ('TV', 0), ('Q', 6), ('M', 6), ('E', 7), ('Ws', 9), ('P', 4), ('EV', 0), ('A', 5), ('Wv', 9), ('inv', 1), ('X', 5), ('m0', 1), ('T', 9), ('Q', 7), ('QV', 0), ('M', 7), ('MM', 0), ('E', 8), ('Ws', 10), ('P', 5), ('A', 6), ('Wv', 10), ('m1', 1), ('X', 6), ('T', 10), ('TV', 1), ('Q', 8), ('M', 8), ('E', 9), ('Ws', 11), ('P', 6), ('f0', 0), ('EV', 1), ('f1', 0), ('A', 7), ('Wv', 11), ('X', 7), ('T', 11), ('Q', 9), ('QV', 1), ('M', 9), ('MM', 1), ('E', 10), ('Ws', 12), ('P', 7), ('A', 8), ('pr', 0), ('Wv', 12), ('inv', 2), ('X', 8), ('ps', 0), ('m0', 2), ('T', 12), ('Q', 10), ('M', 10), ('E', 11), ('Ws', 13), ('P', 8), ('f0', 1), ('f1', 1), ('A', 9), ('Wv', 13), ('m1', 2), ('X', 9), ('T', 13), ('TV', 2), ('Q', 11), ('M', 11), ('E', 12), ('Ws', 14), ('P', 9), ('EV', 2), ('A', 10), ('pr', 1), ('Wv', 14), ('X', 10), ('ps', 1), ('T', 14), ('Q', 12), ('QV', 2), ('M', 12), ('MM', 2), ('E', 13), ('Ws', 15), ('P', 10), ('A', 11), ('Wv', 15), ('inv', 3), ('X', 11), ('m0', 3), ('T', 15), ('Q', 13), ('M', 13), ('E', 14), ('Ws', 16), ('P', 11), ('f0', 2), ('f1', 2), ('A', 12), ('Wv', 16), ('m1', 3), ('X', 12), ('T', 16), ('TV', 3), ('Q', 14), ('M', 14), ('E', 15), ('Ws', 17), ('P', 12), ('EV', 3), ('A', 13), ('pr', 2), ('Wv', 17), ('X', 13), ('ps', 2), ('T', 17), ('Q', 15), ('QV', 3), ('M', 15), ('MM', 3), ('E', 16), ('Ws', 18), ('P', 13), ('A', 14), ('Wv', 18), ('inv', 4), ('X', 14), ('m0', 4), ('T', 18), ('Q', 16), ('M', 16), ('E', 17), ('Ws', 19), ('P', 14), ('f0', 3), ('f1', 3), ('A', 15), ('Wv', 19), ('m1', 4), ('X', 15), ('T', 19), ('TV', 4), ('Q', 17), ('M', 17), ('E', 18), ('Ws', 20), ('P', 15), ('EV', 4), ('A', 16), ('pr', 3), ('Wv', 20), ('X', 16), ('ps', 3), ('T', 20), ('Q', 18), ('QV', 4), ('M', 18), ('MM', 4), ('E', 19), ('Ws', 21), ('P', 16), ('A', 17), ('Wv', 21), ('inv', 5), ('X', 17), ('m0', 5), ('T', 21), ('Q', 19), ('M', 19), ('E', 20), ('Ws', 22), ('P', 17), ('f0', 4), ('f1', 4), ('A', 18), ('Wv', 22), ('m1', 5), ('X', 18), ('Q', 20), ('E', 21), ('A', 19), ('T', 22), ('P', 18), ('pr', 4), ('M', 20), ('A', 20), ('Q', 21), ('inv', 6), ('Ws', 23), ('TV', 5), ('X', 19), ('EV', 5), ('M', 21), ('Wv', 23), ('m0', 6), ('E', 22), ('m1', 6), ('QV', 5), ('T', 23), ('X', 20), ('MM', 5), ('P', 19), ('TV', 6), ('E', 23), ('op', 1), ('Q', 22), ('f0', 5), ('A', 21), ('P', 20), ('M', 22), ('ps', 4), ('X', 21), ('EV', 6), ('Q', 23), ('f1s', 5), ('P', 21), ('QV', 6), ('A', 22), ('M', 23), ('A', 23), ('X', 22), ('inv', 7), ('MM', 6), ('X', 23), ('f0', 6), ('m0', 7), ('m1', 7), ('f1', 6), ('pr', 5), ('pr', 6), ('P', 22), ('op', 2), ('P', 23), ('op', 0), ('TV', 7), ('ps', 6), ('ln', 4), ('EV', 7), ('ln', 0), ('ln', 2), ('QV', 7), ('MM', 7), ('ps', 5), ('cl', 0), ('ln', 1), ('fin', 4), ('ln', 3), ('invl', 5), ('f1', 7), ('invl', 6), ('ln', 5), ('f0', 7), ('fin', 3), ('fin', 5), ('cl', 1), ('pr', 7), ('ps', 7), ('fs', 0), ('fs', 1), ('ln', 6), ('invl', 7), ('ln', 7), ('fin', 6), ('cl', 2), ('fs', 2), ('fin', 7)]
 
 
 def tile_chunkflooredmessagemiddlescore_kernel(tc, x_bytes, x_scale, we_words, we_scales, be, ends, gain, trans, out):
@@ -60,12 +64,15 @@ def tile_chunkflooredmessagemiddlescore_kernel(tc, x_bytes, x_scale, we_words, w
         psum = ctx.enter_context(tc.psum_pool(name="psum", bufs=2))
         ctx.enter_context(tc.manual_schedule())
 
-        rows = keep.tile([P, 2 * T], BF16, name="rows")
+        rows = keep.tile([P, T], BF16, name="rows")
+        be_wide = keep.tile([P, T], BF16, name="be_wide")
+        gain_raw = keep.tile([P, PAIRS * T], BF16, name="gain_raw")
+        gain_wide = keep.tile([P, PAIRS * T], BF16, name="gain_wide")
         we_s = keep.tile([P, PASSES, T], U8, name="we_s", align_bytes=64)
         we_w = keep.tile([P, PASSES, 2 * T], U8, name="we_w", align_bytes=64)
         xs = keep.tile([P, L * TILES * KBLOCKS], F32, name="xs")
         ident = keep.tile([P, P], F32, name="ident")
-        coef = keep.tile([P, 10], BF16, name="coef")
+        coef = keep.tile([P, 4], BF16, name="coef")
         nc.vector.memset(rows[:].bitcast(I32), 0)
         nc.vector.memset(we_s[:].rearrange("p g n -> p (g n)").bitcast(I32), 0)
 
@@ -77,11 +84,17 @@ def tile_chunkflooredmessagemiddlescore_kernel(tc, x_bytes, x_scale, we_words, w
             nc.sync.dma_start(out=xb[s][:], in_=x_bytes[l, i * P:(i + 1) * P, :])
 
         nc.scalar.dma_start(out=xs[:], in_=x_scale.rearrange("l i j -> (l i j)").partition_broadcast(P))
+        tr_raw = {}
+
+        def load_trans(p):
+            tr_raw[p] = keep.tile([P, 4, T], BF16, name="tr_raw%d" % p)
+            nc.sync.dma_start(out=tr_raw[p][:], in_=trans[p].rearrange("(p j) n -> p j n", j=4))
+
         load_x(0)
+        nc.sync.dma_start(out=rows[0:1, :], in_=be.rearrange("(o n) -> o n", o=1))
+        nc.sync.dma_start(out=rows[32:65:32, :], in_=ends)
         load_x(1)
-        nc.sync.dma_start(out=rows[0:1, 0:T], in_=be.rearrange("(o n) -> o n", o=1))
-        nc.sync.dma_start(out=rows[32:65:32, 0:T], in_=ends)
-        nc.sync.dma_start(out=rows[0:33:32, T:2 * T], in_=gain)
+        load_trans(0)
         nc.sync.dma_start(out=we_w[:].bitcast(I32), in_=we_words.rearrange("g p n -> p g n").bitcast(I32))
         for q in range(4):
             nc.sync.dma_start(
@@ -90,28 +103,27 @@ def tile_chunkflooredmessagemiddlescore_kernel(tc, x_bytes, x_scale, we_words, w
             )
         load_x(2)
         load_x(3)
-        tr_raw = {}
-        for p in range(PAIRS):
-            tr_raw[p] = keep.tile([P, 4, T], BF16, name="tr_raw%d" % p)
-            nc.sync.dma_start(out=tr_raw[p][:], in_=trans[p].rearrange("(p j) n -> p j n", j=4))
-            load_x(4 + p)
+        nc.sync.dma_start(out=gain_raw[:], in_=gain.rearrange("a n -> (a n)").partition_broadcast(P))
+        load_x(4)
+        load_trans(1)
+        load_x(5)
+        nc.sync.dma_start(out=be_wide[:], in_=be.partition_broadcast(P))
         for s in range(6, NU):
             load_x(s)
 
-        make_identity(nc, ident[:])
         nc.gpsimd.memset(coef[:], 0.0)
-        nc.gpsimd.memset(coef[0:1, 0:6], -1.0)
+        nc.gpsimd.memset(coef[0:1, :], -1.0)
         nc.gpsimd.memset(coef[32:33, 0:2], -1.0)
-        nc.gpsimd.memset(coef[64:65, 4:6], -1.0)
-        nc.gpsimd.memset(coef[0:1, 6:8], float(T))
-        nc.gpsimd.memset(coef[32:33, 8:10], float(T))
+        nc.gpsimd.memset(coef[64:65, 2:4], -1.0)
+        make_identity(nc, ident[:])
+        neg_ident = keep.tile([P, P], F32, name="neg_ident")
+        nc.gpsimd.tensor_scalar(out=neg_ident[:], in0=ident[:], scalar1=-1.0, scalar2=0.0, op0=ALU.mult, op1=ALU.add)
 
         neg_bias = {}
-        gain_t = {}
 
-        def spread(c, half, name):
+        def spread(c, name):
             acc = psum.tile([P, T], F32, name="m_ps", tag="m_ps")
-            nc.tensor.matmul(acc[:], lhsT=coef[:, c:c + 1].to_broadcast([P, P]), rhs=rows[:, half * T:(half + 1) * T], start=True, stop=True)
+            nc.tensor.matmul(acc[:], lhsT=coef[:, c:c + 1].to_broadcast([P, P]), rhs=rows[:], start=True, stop=True)
             wide = keep.tile([P, T], F32, name=name)
             nc.vector.tensor_copy(out=wide[:], in_=acc[:])
             return wide
@@ -149,6 +161,8 @@ def tile_chunkflooredmessagemiddlescore_kernel(tc, x_bytes, x_scale, we_words, w
         def turn_x(s):
             words = xw[s][:].bitcast(F32)
             xt[s] = psum.tile([P, PASSES, 2, P], F32, name="xt", tag="xt", bufs=3)
+            for w in range(WARM):
+                nc.tensor.matmul(xt[s][:, 0, w, :], lhsT=ident[:], rhs=ident[:], start=True, stop=True)
             for g in range(PASSES):
                 for u in range(2):
                     nc.tensor.transpose(xt[s][:, g, u, :], words[:, 256 * g + u:256 * (g + 1):2], ident[:])
@@ -175,9 +189,10 @@ def tile_chunkflooredmessagemiddlescore_kernel(tc, x_bytes, x_scale, we_words, w
             i, l = units[s]
             if l == 1:
                 neg_n[s] = keep.tile([P, T], F32, name="neg_mid%d" % i)
+                nc.vector.scalar_tensor_tensor(out=neg_n[s][:], in0=e_ps[s][:], scalar=-1.0, in1=be_wide[:], op0=ALU.mult, op1=ALU.subtract)
             else:
                 neg_n[s] = work.tile([P, T], F32, name="neg_n", tag="neg_n")
-            nc.vector.tensor_tensor(out=neg_n[s][:], in0=neg_bias[l][:], in1=e_ps[s][:], op=ALU.subtract)
+                nc.vector.tensor_tensor(out=neg_n[s][:], in0=neg_bias[l][:], in1=e_ps[s][:], op=ALU.subtract)
 
         def find_max(s):
             neg_max[s] = keep.tile([P, 1], F32, name="neg_max%d" % s)
@@ -201,7 +216,7 @@ def tile_chunkflooredmessagemiddlescore_kernel(tc, x_bytes, x_scale, we_words, w
             s = slot_of[i, 2 * p]
             if p == 0:
                 v[i] = work.tile([P, PAIRS, T], BF16, name="v", tag="v")
-            nc.vector.scalar_tensor_tensor(out=v[i][:, p, :], in0=ex[s][:], scalar=inv[i][:, p:p + 1], in1=gain_t[p][:], op0=ALU.mult, op1=ALU.mult)
+            nc.vector.scalar_tensor_tensor(out=v[i][:, p, :], in0=ex[s][:], scalar=inv[i][:, p:p + 1], in1=gain_wide[:, p * T:(p + 1) * T], op0=ALU.mult, op1=ALU.mult)
 
         def turn_v(i):
             vt[i] = psum.tile([P, PAIRS, 2, P], F32, name="vt", tag="vt", bufs=1)
@@ -230,13 +245,21 @@ def tile_chunkflooredmessagemiddlescore_kernel(tc, x_bytes, x_scale, we_words, w
 
         def floor_first(i):
             fl0[i] = work.tile([P, T], F32, name="fl0", tag="fl0")
+            if i < GP:
+                return
             nc.scalar.activation(out=fl0[i][:], in_=m_ps[i, 0][:], func=ACT.Relu, bias=FLOOR_M, scale=1.0)
 
         def floor_second(i):
             fl1[i] = work.tile([P, T], F32, name="fl1", tag="fl1")
             nc.vector.tensor_scalar(out=fl1[i][:], in0=m_ps[i, 1][:], scalar1=-FLOOR_M, scalar2=16.0, op0=ALU.max, op1=ALU.add)
+            if i < GP:
+                nc.vector.tensor_scalar(out=fl0[i][:], in0=m_ps[i, 0][:], scalar1=-FLOOR_M, scalar2=16.0, op0=ALU.max, op1=ALU.add)
+                prod[i] = keep.tile([P, T], F32, name="prod%d" % i)
+                nc.gpsimd.tensor_tensor(out=prod[i][:], in0=fl0[i][:], in1=fl1[i][:], op=ALU.mult)
 
         def multiply(i):
+            if i < GP:
+                return
             prod[i] = keep.tile([P, T], F32, name="prod%d" % i)
             nc.vector.scalar_tensor_tensor(out=prod[i][:], in0=fl0[i][:], scalar=FLOOR_A, in1=fl1[i][:], op0=ALU.add, op1=ALU.mult)
 
@@ -249,104 +272,44 @@ def tile_chunkflooredmessagemiddlescore_kernel(tc, x_bytes, x_scale, we_words, w
             logp[i] = work.tile([P, T], F32, name="logp", tag="logp", bufs=8)
             nc.scalar.activation(out=logp[i][:], in_=prod[i][:], func=ACT.Ln, scale=inv[i + SUM_LAG][:, 2:3])
 
+        def open_total(i):
+            s = slot_of[i, 1]
+            total[i] = psum.tile([P, T], F32, name="xt", tag="xt", bufs=3)
+            nc.tensor.matmul(total[i][:], lhsT=neg_ident[:], rhs=neg_n[s][:], start=True, stop=False)
+
+        def close_total(i):
+            nc.tensor.matmul(total[i][:], lhsT=ident[:], rhs=logp[i][:], start=False, stop=True)
+
+        def floor_second_scalar(i):
+            cut = work.tile([P, T], F32, name="cut", tag="cut")
+            fl1[i] = work.tile([P, T], F32, name="fl1", tag="fl1")
+            nc.scalar.activation(out=cut[:], in_=m_ps[i, 1][:], func=ACT.Relu, bias=FLOOR_M, scale=1.0)
+            nc.scalar.activation(out=fl1[i][:], in_=cut[:], func=ACT.Identity, bias=FLOOR_A, scale=1.0)
+
+        def finish_scalar(i):
+            s = slot_of[i, 1]
+            res = work.tile([P, T], F32, name="res", tag="res", bufs=8)
+            nc.scalar.activation(out=res[:], in_=total[i][:], func=ACT.Identity, bias=neg_max[s][:], scale=1.0)
+            nc.sync.dma_start(out=out[i * P:(i + 1) * P, :], in_=res[:])
+
+        total = {}
+
         def finish(i):
             s = slot_of[i, 1]
             res = work.tile([P, T], F32, name="res", tag="res", bufs=8)
             nc.vector.scalar_tensor_tensor(out=res[:], in0=logp[i][:], scalar=neg_max[s][:], in1=neg_n[s][:], op0=ALU.add, op1=ALU.subtract)
             nc.sync.dma_start(out=out[i * P:(i + 1) * P, :], in_=res[:])
 
-        def live(s):
-            return 0 <= s < NU
-
-        def tile_at(s, lag):
-            u = s - lag
-            return units[u][0] if live(u) and units[u][1] == 2 else None
-
-        def vector_blocks(s):
-            return NVS[s + 4] if s < NU else 0
-
-        def at(s, lag, stage, *more):
-            if tile_at(s, lag) is not None:
-                stage(tile_at(s, lag), *more)
-
-        ready, logged = [], []
-
-        def invert_sums(i):
-            invert(i, slice(0, 3 if i >= SUM_LAG else 2))
-            if i >= SUM_LAG:
-                ready.append(i - SUM_LAG)
-
-        def invert_last(i):
-            if i + SUM_LAG >= TILES:
-                invert(i + SUM_LAG, slice(2, 3))
-                ready.append(i)
-
-        s = -4
-        done = 0
-        clock = -4
-        while done < TILES:
-            nv = vector_blocks(s)
-            z = -99 if s in PAUSE else clock
-            clock += 0 if s in PAUSE else 1
-            if s == SETUP[0]:
-                neg_bias[0] = spread(0, 0, "neg_bias0")
-                neg_bias[2] = spread(4, 0, "neg_bias2")
-            if live(s + 3):
-                turn_x(s + 3)
-            at(z, L_TV, turn_v)
-            if live(s + 1):
-                quantize_x(s + 1)
-            at(z, L_QV, quantize_v)
-            if live(s + 1):
-                emit(s + 1)
-            at(z, L_QV, pass_on)
-            finishing = list(logged)
-            logged.clear()
-            def logs():
-                if s >= NU:
-                    for i in ready[:LOGS]:
-                        take_log(i)
-                        logged.append(i)
-                        ready.remove(i)
-            ssteps = {
-                "P": lambda: exponent(s - 1) if live(s - 1) else None,
-                "f": lambda: at(z, L_FL, floor_first),
-                "E": lambda: empty_x(s + 2) if live(s + 2) else None,
-                "V": lambda: at(z, L_TV, empty_v),
-                "W": lambda: widen(s + 4, range(nv, KBLOCKS), False) if live(s + 4) else None,
-                "L": logs,
-            }
-            for c in SORD:
-                ssteps[c]()
-            def setup_work():
-                if s == SETUP[1]:
-                    gain_t[0] = spread(6, 1, "gain0")
-                    gain_t[1] = spread(8, 1, "gain1")
-                if s == SETUP[2]:
-                    neg_bias[1] = spread(2, 0, "neg_bias1")
-                for p in range(2):
-                    if s == SETUP[3 + p]:
-                        interleave_trans(p)
-            def setup2():
-                for p in range(2):
-                    if s == SETUP[5 + p]:
-                        quantize_trans(p)
-            steps = {
-                "w": lambda: widen(s + 4, range(nv), True) if live(s + 4) else None,
-                "i": lambda: (at(z, L_MSG0, invert_sums), at(z, L_PS + 1, invert_last)),
-                "a": lambda: add_bias(s) if live(s) else None,
-                "p": lambda: at(z, L_PR, multiply),
-                "1": lambda: at(z, L_MSG1, message, 1),
-                "0": lambda: at(z, L_MSG0, message, 0),
-                "s": setup_work,
-                "x": lambda: find_max(s) if live(s) else None,
-                "t": setup2,
-                "f": lambda: at(z, L_FL, floor_second),
-                "F": lambda: [finish(i) for i in finishing[:1]],
-                "S": lambda: at(z, L_PS, partition_sum),
-                "G": lambda: [finish(i) for i in finishing[1:]],
-            }
-            for c in VORD:
-                steps[c]()
-            done += len(finishing)
-            s += 1
+        def scale_gain(unused):
+            nc.vector.tensor_scalar(out=gain_wide[:], in0=gain_raw[:], scalar1=float(T), scalar2=None, op0=ALU.mult)
+        def spr(l):
+            neg_bias[l] = spread(l, "neg_bias%d" % l)
+        ST = {"T": turn_x, "E": empty_x, "Q": quantize_x, "M": emit, "A": add_bias, "X": find_max, "P": exponent,
+              "m0": lambda i: message(i, 0), "m1": lambda i: message(i, 1), "TV": turn_v, "EV": empty_v, "QV": quantize_v, "MM": pass_on,
+              "f0": floor_first, "f1": floor_second, "f1s": floor_second_scalar, "pr": multiply, "ps": partition_sum,
+              "inv": lambda i: invert(i, slice(0, 3 if i >= SUM_LAG else 2)), "invl": lambda i: invert(i + SUM_LAG, slice(2, 3)),
+              "ln": take_log, "fin": finish, "op": open_total, "cl": close_total, "fs": finish_scalar,
+              "spr": spr, "sg": scale_gain, "it": interleave_trans, "qt": quantize_trans,
+              "Ws": lambda s: widen(s, range(NVS[s], KBLOCKS), False), "Wv": lambda s: widen(s, range(NVS[s]), True)}
+        for name, a in ORDER:
+            ST[name](a)

@@ -26,7 +26,7 @@ FLOOR_M = 14.4
 FLOOR_A = 1.6
 SUM_LAG = 3
 MID_LAG = 1
-NVS = [0, 2, 5, 3, 2, 2, 2, 2, 2, 2, 2, 2, 1, 1, 1, 1, 1, 1, 1, 0, 0, 0, 0, 0]
+NVS = [2, 1, 3, 2, 3, 3, 3, 3, 3, 3, 2, 2, 2, 2, 2, 2, 2, 2, 2, 2, 2, 1, 0, 0]
 PAUSE = []
 SORD = "PfEVWLR"
 VORD = "wiap10sxtfFSG"
@@ -39,11 +39,11 @@ L_FL = 6
 L_PR = 7
 L_PS = 7
 LOGS = 3
-WARM = 2
+WARM = 0
 FLS = 8
 FPE = 0
 GP = 0
-ORDER = [('spr', 0), ('Wv', 0), ('Wv', 1), ('Ws', 0), ('spr', 2), ('Ws', 1), ('T', 0), ('E', 0), ('Ws', 2), ('T', 1), ('it', 0), ('Wv', 2), ('Q', 0), ('Wv', 3), ('E', 1), ('Ws', 3), ('Q', 1), ('Ws', 4), ('qt', 0), ('T', 2), ('M', 0), ('M', 1), ('A', 0), ('T', 3), ('E', 2), ('Wv', 4), ('X', 0), ('A', 1), ('T', 4), ('Wv', 5), ('P', 0), ('Ws', 5), ('Q', 2), ('X', 1), ('M', 2), ('it', 1), ('sg', 0), ('E', 3), ('qt', 1), ('T', 5), ('Q', 3), ('M', 3), ('E', 4), ('Ws', 6), ('P', 1), ('A', 2), ('Wv', 6), ('X', 2), ('T', 6), ('Q', 4), ('M', 4), ('E', 5), ('Ws', 7), ('P', 2), ('A', 3), ('Wv', 7), ('inv', 0), ('X', 3), ('m0', 0), ('T', 7), ('Q', 5), ('M', 5), ('E', 6), ('Ws', 8), ('P', 3), ('A', 4), ('Wv', 8), ('m1', 0), ('X', 4), ('T', 8), ('TV', 0), ('Q', 6), ('M', 6), ('E', 7), ('Ws', 9), ('P', 4), ('EV', 0), ('A', 5), ('Wv', 9), ('inv', 1), ('X', 5), ('m0', 1), ('T', 9), ('Q', 7), ('QV', 0), ('M', 7), ('MM', 0), ('E', 8), ('Ws', 10), ('P', 5), ('A', 6), ('Wv', 10), ('m1', 1), ('X', 6), ('T', 10), ('TV', 1), ('Q', 8), ('M', 8), ('E', 9), ('Ws', 11), ('P', 6), ('f0', 0), ('EV', 1), ('f1', 0), ('A', 7), ('Wv', 11), ('X', 7), ('T', 11), ('Q', 9), ('QV', 1), ('M', 9), ('MM', 1), ('E', 10), ('Ws', 12), ('P', 7), ('A', 8), ('pr', 0), ('Wv', 12), ('inv', 2), ('X', 8), ('ps', 0), ('m0', 2), ('T', 12), ('Q', 10), ('M', 10), ('E', 11), ('Ws', 13), ('P', 8), ('f0', 1), ('f1', 1), ('A', 9), ('Wv', 13), ('m1', 2), ('X', 9), ('T', 13), ('TV', 2), ('Q', 11), ('M', 11), ('E', 12), ('Ws', 14), ('P', 9), ('EV', 2), ('A', 10), ('pr', 1), ('Wv', 14), ('X', 10), ('ps', 1), ('T', 14), ('Q', 12), ('QV', 2), ('M', 12), ('MM', 2), ('E', 13), ('Ws', 15), ('P', 10), ('A', 11), ('Wv', 15), ('inv', 3), ('X', 11), ('m0', 3), ('T', 15), ('Q', 13), ('M', 13), ('E', 14), ('Ws', 16), ('P', 11), ('f0', 2), ('f1', 2), ('A', 12), ('Wv', 16), ('m1', 3), ('X', 12), ('T', 16), ('TV', 3), ('Q', 14), ('M', 14), ('E', 15), ('Ws', 17), ('P', 12), ('EV', 3), ('A', 13), ('pr', 2), ('Wv', 17), ('X', 13), ('ps', 2), ('T', 17), ('Q', 15), ('QV', 3), ('M', 15), ('MM', 3), ('E', 16), ('Ws', 18), ('P', 13), ('A', 14), ('Wv', 18), ('inv', 4), ('X', 14), ('m0', 4), ('T', 18), ('Q', 16), ('M', 16), ('E', 17), ('Ws', 19), ('P', 14), ('f0', 3), ('f1', 3), ('A', 15), ('Wv', 19), ('m1', 4), ('X', 15), ('T', 19), ('TV', 4), ('Q', 17), ('M', 17), ('E', 18), ('Ws', 20), ('P', 15), ('EV', 4), ('A', 16), ('pr', 3), ('Wv', 20), ('X', 16), ('ps', 3), ('T', 20), ('Q', 18), ('QV', 4), ('M', 18), ('MM', 4), ('E', 19), ('Ws', 21), ('P', 16), ('A', 17), ('Wv', 21), ('inv', 5), ('X', 17), ('m0', 5), ('T', 21), ('Q', 19), ('M', 19), ('E', 20), ('Ws', 22), ('P', 17), ('f0', 4), ('f1', 4), ('A', 18), ('Wv', 22), ('m1', 5), ('X', 18), ('Q', 20), ('E', 21), ('A', 19), ('T', 22), ('P', 18), ('pr', 4), ('M', 20), ('A', 20), ('Q', 21), ('inv', 6), ('Ws', 23), ('TV', 5), ('X', 19), ('EV', 5), ('M', 21), ('Wv', 23), ('m0', 6), ('E', 22), ('m1', 6), ('QV', 5), ('T', 23), ('X', 20), ('MM', 5), ('P', 19), ('TV', 6), ('E', 23), ('op', 1), ('Q', 22), ('f0', 5), ('A', 21), ('P', 20), ('M', 22), ('ps', 4), ('X', 21), ('EV', 6), ('Q', 23), ('f1s', 5), ('P', 21), ('QV', 6), ('A', 22), ('M', 23), ('A', 23), ('X', 22), ('inv', 7), ('MM', 6), ('X', 23), ('f0', 6), ('m0', 7), ('m1', 7), ('f1', 6), ('pr', 5), ('pr', 6), ('P', 22), ('op', 2), ('P', 23), ('op', 0), ('TV', 7), ('ps', 6), ('ln', 4), ('EV', 7), ('ln', 0), ('ln', 2), ('QV', 7), ('MM', 7), ('ps', 5), ('cl', 0), ('ln', 1), ('fin', 4), ('ln', 3), ('invl', 5), ('f1', 7), ('invl', 6), ('ln', 5), ('f0', 7), ('fin', 3), ('fin', 5), ('cl', 1), ('pr', 7), ('ps', 7), ('fs', 0), ('fs', 1), ('ln', 6), ('invl', 7), ('ln', 7), ('fin', 6), ('cl', 2), ('fs', 2), ('fin', 7)]
+ORDER = [('Wv', 0), ('Wv', 1), ('Ws', 0), ('spr', 0), ('Ws', 1), ('spr', 2), ('T', 0), ('it', 0), ('T', 1), ('E', 0), ('Ws', 2), ('Q', 0), ('M', 0), ('Wv', 2), ('qt', 0), ('Wv', 3), ('A', 0), ('E', 1), ('T', 2), ('Q', 1), ('X', 0), ('Wv', 4), ('Ws', 3), ('T', 3), ('E', 2), ('Q', 2), ('P', 0), ('Ws', 4), ('M', 1), ('it', 1), ('Ws', 5), ('Wv', 5), ('A', 1), ('sg', 0), ('E', 3), ('T', 4), ('X', 1), ('M', 2), ('qt', 1), ('T', 5), ('Q', 3), ('M', 3), ('E', 4), ('Ws', 6), ('P', 1), ('A', 2), ('Wv', 6), ('X', 2), ('T', 6), ('Q', 4), ('M', 4), ('E', 5), ('Ws', 7), ('P', 2), ('A', 3), ('Wv', 7), ('inv', 0), ('X', 3), ('m0', 0), ('T', 7), ('Q', 5), ('M', 5), ('E', 6), ('Ws', 8), ('P', 3), ('A', 4), ('Wv', 8), ('m1', 0), ('X', 4), ('T', 8), ('TV', 0), ('Q', 6), ('M', 6), ('E', 7), ('Ws', 9), ('P', 4), ('EV', 0), ('A', 5), ('Wv', 9), ('inv', 1), ('X', 5), ('m0', 1), ('T', 9), ('Q', 7), ('QV', 0), ('M', 7), ('MM', 0), ('E', 8), ('Ws', 10), ('P', 5), ('A', 6), ('Wv', 10), ('m1', 1), ('X', 6), ('T', 10), ('TV', 1), ('Q', 8), ('M', 8), ('E', 9), ('Ws', 11), ('P', 6), ('f0', 0), ('EV', 1), ('f1', 0), ('A', 7), ('Wv', 11), ('X', 7), ('T', 11), ('Q', 9), ('QV', 1), ('M', 9), ('MM', 1), ('E', 10), ('Ws', 12), ('P', 7), ('A', 8), ('pr', 0), ('Wv', 12), ('inv', 2), ('X', 8), ('ps', 0), ('m0', 2), ('T', 12), ('Q', 10), ('M', 10), ('E', 11), ('Ws', 13), ('P', 8), ('f0', 1), ('f1', 1), ('A', 9), ('Wv', 13), ('m1', 2), ('X', 9), ('T', 13), ('TV', 2), ('Q', 11), ('M', 11), ('E', 12), ('Ws', 14), ('P', 9), ('EV', 2), ('A', 10), ('pr', 1), ('Wv', 14), ('X', 10), ('ps', 1), ('T', 14), ('Q', 12), ('QV', 2), ('M', 12), ('MM', 2), ('E', 13), ('Ws', 15), ('P', 10), ('A', 11), ('Wv', 15), ('inv', 3), ('X', 11), ('m0', 3), ('T', 15), ('Q', 13), ('M', 13), ('E', 14), ('Ws', 16), ('P', 11), ('f0', 2), ('f1', 2), ('A', 12), ('Wv', 16), ('m1', 3), ('X', 12), ('T', 16), ('TV', 3), ('Q', 14), ('M', 14), ('E', 15), ('Ws', 17), ('P', 12), ('EV', 3), ('A', 13), ('pr', 2), ('Wv', 17), ('X', 13), ('ps', 2), ('T', 17), ('Q', 15), ('QV', 3), ('M', 15), ('MM', 3), ('E', 16), ('Ws', 18), ('P', 13), ('A', 14), ('Wv', 18), ('inv', 4), ('X', 14), ('m0', 4), ('T', 18), ('Q', 16), ('M', 16), ('E', 17), ('Ws', 19), ('P', 14), ('f0', 3), ('f1', 3), ('A', 15), ('Wv', 19), ('m1', 4), ('X', 15), ('T', 19), ('TV', 4), ('Q', 17), ('M', 17), ('E', 18), ('Ws', 20), ('P', 15), ('EV', 4), ('A', 16), ('pr', 3), ('Wv', 20), ('X', 16), ('ps', 3), ('T', 20), ('Q', 18), ('QV', 4), ('M', 18), ('MM', 4), ('E', 19), ('Ws', 21), ('P', 16), ('A', 17), ('Wv', 21), ('inv', 5), ('X', 17), ('m0', 5), ('T', 21), ('Q', 19), ('M', 19), ('E', 20), ('Ws', 22), ('P', 17), ('f0', 4), ('f1', 4), ('A', 18), ('Wv', 22), ('m1', 5), ('X', 18), ('E', 21), ('TV', 5), ('A', 19), ('pr', 4), ('P', 18), ('EV', 5), ('Q', 21), ('T', 22), ('Q', 20), ('Wv', 23), ('inv', 6), ('Ws', 23), ('X', 19), ('M', 21), ('QV', 5), ('E', 22), ('M', 20), ('m0', 6), ('A', 21), ('m1', 6), ('T', 23), ('A', 20), ('MM', 5), ('Q', 22), ('TV', 6), ('X', 21), ('P', 19), ('E', 23), ('f0', 5), ('Q', 23), ('M', 22), ('EV', 6), ('X', 20), ('M', 23), ('A', 22), ('QV', 6), ('f1s', 5), ('P', 20), ('A', 23), ('X', 22), ('ps', 4), ('P', 21), ('MM', 6), ('f0', 6), ('P', 22), ('X', 23), ('inv', 7), ('f1', 6), ('op', 0), ('m0', 7), ('op', 1), ('P', 23), ('ln', 4), ('m1', 7), ('pr', 6), ('ps', 6), ('pr', 5), ('TV', 7), ('EV', 7), ('QV', 7), ('op', 2), ('ln', 3), ('MM', 7), ('ln', 0), ('ps', 5), ('fin', 4), ('f0', 7), ('invl', 5), ('ln', 1), ('cl', 0), ('cl', 1), ('invl', 6), ('fin', 3), ('f1', 7), ('ln', 5), ('fin', 5), ('pr', 7), ('ps', 7), ('fs', 0), ('ln', 2), ('fs', 1), ('invl', 7), ('ln', 6), ('ln', 7), ('cl', 2), ('fin', 6), ('fin', 7), ('fs', 2)]
 
 
 def tile_chunkflooredmessagemiddlescore_kernel(tc, x_bytes, x_scale, we_words, we_scales, be, ends, gain, trans, out):

@@ -26,7 +26,7 @@ FLOOR_M = 14.4
 FLOOR_A = 1.6
 SUM_LAG = 3
 MID_LAG = 1
-NVS = [2, 1, 3, 2, 3, 3, 3, 3, 3, 3, 2, 2, 2, 2, 2, 2, 2, 2, 2, 2, 2, 1, 0, 0]
+NVS = [3, 4, 3, 2, 2, 2, 2, 2, 1, 1, 1, 1, 1, 1, 1, 1, 0, 0, 0, 0, 0, 0, 0, 0]
 PAUSE = []
 SORD = "PfEVWLR"
 VORD = "wiap10sxtfFSG"
@@ -39,11 +39,14 @@ L_FL = 6
 L_PR = 7
 L_PS = 7
 LOGS = 3
-WARM = 0
+WARM = 1
 FLS = 8
 FPE = 0
 GP = 0
-ORDER = [('Wv', 0), ('Wv', 1), ('Ws', 0), ('spr', 0), ('Ws', 1), ('spr', 2), ('T', 0), ('it', 0), ('T', 1), ('E', 0), ('Ws', 2), ('Q', 0), ('M', 0), ('Wv', 2), ('qt', 0), ('Wv', 3), ('A', 0), ('E', 1), ('T', 2), ('Q', 1), ('X', 0), ('Wv', 4), ('Ws', 3), ('T', 3), ('E', 2), ('Q', 2), ('P', 0), ('Ws', 4), ('M', 1), ('it', 1), ('Ws', 5), ('Wv', 5), ('A', 1), ('sg', 0), ('E', 3), ('T', 4), ('X', 1), ('M', 2), ('qt', 1), ('T', 5), ('Q', 3), ('M', 3), ('E', 4), ('Ws', 6), ('P', 1), ('A', 2), ('Wv', 6), ('X', 2), ('T', 6), ('Q', 4), ('M', 4), ('E', 5), ('Ws', 7), ('P', 2), ('A', 3), ('Wv', 7), ('inv', 0), ('X', 3), ('m0', 0), ('T', 7), ('Q', 5), ('M', 5), ('E', 6), ('Ws', 8), ('P', 3), ('A', 4), ('Wv', 8), ('m1', 0), ('X', 4), ('T', 8), ('TV', 0), ('Q', 6), ('M', 6), ('E', 7), ('Ws', 9), ('P', 4), ('EV', 0), ('A', 5), ('Wv', 9), ('inv', 1), ('X', 5), ('m0', 1), ('T', 9), ('Q', 7), ('QV', 0), ('M', 7), ('MM', 0), ('E', 8), ('Ws', 10), ('P', 5), ('A', 6), ('Wv', 10), ('m1', 1), ('X', 6), ('T', 10), ('TV', 1), ('Q', 8), ('M', 8), ('E', 9), ('Ws', 11), ('P', 6), ('f0', 0), ('EV', 1), ('f1', 0), ('A', 7), ('Wv', 11), ('X', 7), ('T', 11), ('Q', 9), ('QV', 1), ('M', 9), ('MM', 1), ('E', 10), ('Ws', 12), ('P', 7), ('A', 8), ('pr', 0), ('Wv', 12), ('inv', 2), ('X', 8), ('ps', 0), ('m0', 2), ('T', 12), ('Q', 10), ('M', 10), ('E', 11), ('Ws', 13), ('P', 8), ('f0', 1), ('f1', 1), ('A', 9), ('Wv', 13), ('m1', 2), ('X', 9), ('T', 13), ('TV', 2), ('Q', 11), ('M', 11), ('E', 12), ('Ws', 14), ('P', 9), ('EV', 2), ('A', 10), ('pr', 1), ('Wv', 14), ('X', 10), ('ps', 1), ('T', 14), ('Q', 12), ('QV', 2), ('M', 12), ('MM', 2), ('E', 13), ('Ws', 15), ('P', 10), ('A', 11), ('Wv', 15), ('inv', 3), ('X', 11), ('m0', 3), ('T', 15), ('Q', 13), ('M', 13), ('E', 14), ('Ws', 16), ('P', 11), ('f0', 2), ('f1', 2), ('A', 12), ('Wv', 16), ('m1', 3), ('X', 12), ('T', 16), ('TV', 3), ('Q', 14), ('M', 14), ('E', 15), ('Ws', 17), ('P', 12), ('EV', 3), ('A', 13), ('pr', 2), ('Wv', 17), ('X', 13), ('ps', 2), ('T', 17), ('Q', 15), ('QV', 3), ('M', 15), ('MM', 3), ('E', 16), ('Ws', 18), ('P', 13), ('A', 14), ('Wv', 18), ('inv', 4), ('X', 14), ('m0', 4), ('T', 18), ('Q', 16), ('M', 16), ('E', 17), ('Ws', 19), ('P', 14), ('f0', 3), ('f1', 3), ('A', 15), ('Wv', 19), ('m1', 4), ('X', 15), ('T', 19), ('TV', 4), ('Q', 17), ('M', 17), ('E', 18), ('Ws', 20), ('P', 15), ('EV', 4), ('A', 16), ('pr', 3), ('Wv', 20), ('X', 16), ('ps', 3), ('T', 20), ('Q', 18), ('QV', 4), ('M', 18), ('MM', 4), ('E', 19), ('Ws', 21), ('P', 16), ('A', 17), ('Wv', 21), ('inv', 5), ('X', 17), ('m0', 5), ('T', 21), ('Q', 19), ('M', 19), ('E', 20), ('Ws', 22), ('P', 17), ('f0', 4), ('f1', 4), ('A', 18), ('Wv', 22), ('m1', 5), ('X', 18), ('E', 21), ('TV', 5), ('A', 19), ('pr', 4), ('P', 18), ('EV', 5), ('Q', 21), ('T', 22), ('Q', 20), ('Wv', 23), ('inv', 6), ('Ws', 23), ('X', 19), ('M', 21), ('QV', 5), ('E', 22), ('M', 20), ('m0', 6), ('A', 21), ('m1', 6), ('T', 23), ('A', 20), ('MM', 5), ('Q', 22), ('TV', 6), ('X', 21), ('P', 19), ('E', 23), ('f0', 5), ('Q', 23), ('M', 22), ('EV', 6), ('X', 20), ('M', 23), ('A', 22), ('QV', 6), ('f1s', 5), ('P', 20), ('A', 23), ('X', 22), ('ps', 4), ('P', 21), ('MM', 6), ('f0', 6), ('P', 22), ('X', 23), ('inv', 7), ('f1', 6), ('op', 0), ('m0', 7), ('op', 1), ('P', 23), ('ln', 4), ('m1', 7), ('pr', 6), ('ps', 6), ('pr', 5), ('TV', 7), ('EV', 7), ('QV', 7), ('op', 2), ('ln', 3), ('MM', 7), ('ln', 0), ('ps', 5), ('fin', 4), ('f0', 7), ('invl', 5), ('ln', 1), ('cl', 0), ('cl', 1), ('invl', 6), ('fin', 3), ('f1', 7), ('ln', 5), ('fin', 5), ('pr', 7), ('ps', 7), ('fs', 0), ('ln', 2), ('fs', 1), ('invl', 7), ('ln', 6), ('ln', 7), ('cl', 2), ('fin', 6), ('fin', 7), ('fs', 2)]
+SPS = 1
+RIDE = 6
+XM = 1
+ORDER = [('Wv', 0), ('Wv', 1), ('Ws', 0), ('spr', 0), ('Ws', 1), ('T', 0), ('E', 0), ('spr', 2), ('T', 1), ('Ws', 2), ('it', 0), ('E', 1), ('Q', 0), ('Ws', 3), ('Wv', 2), ('M', 0), ('qt', 0), ('Wv', 3), ('T', 2), ('A', 0), ('Q', 1), ('sg', 0), ('Ws', 4), ('M', 1), ('X', 0), ('Wv', 4), ('E', 2), ('A', 1), ('T', 3), ('Ws', 5), ('Q', 2), ('it', 1), ('P', 0), ('T', 4), ('M', 2), ('E', 3), ('Wv', 5), ('X', 1), ('qt', 1), ('T', 5), ('Q', 3), ('M', 3), ('Ws', 6), ('E', 4), ('P', 1), ('A', 2), ('Wv', 6), ('X', 2), ('T', 6), ('Q', 4), ('M', 4), ('Ws', 7), ('E', 5), ('inv', 0), ('A', 3), ('m0', 0), ('Wv', 7), ('X', 3), ('T', 7), ('Q', 5), ('M', 5), ('Ws', 8), ('E', 6), ('P', 2), ('P', 3), ('m1', 0), ('A', 4), ('Wv', 8), ('X', 4), ('T', 8), ('TV', 0), ('Q', 6), ('M', 6), ('Ws', 9), ('E', 7), ('P', 4), ('EV', 0), ('inv', 1), ('A', 5), ('m0', 1), ('Wv', 9), ('X', 5), ('T', 9), ('Q', 7), ('QV', 0), ('M', 7), ('MM', 0), ('Ws', 10), ('E', 8), ('m1', 1), ('A', 6), ('Wv', 10), ('X', 6), ('T', 10), ('TV', 1), ('Q', 8), ('M', 8), ('Ws', 11), ('E', 9), ('P', 5), ('P', 6), ('EV', 1), ('f0', 0), ('A', 7), ('f1', 0), ('Wv', 11), ('X', 7), ('T', 11), ('Q', 9), ('QV', 1), ('M', 9), ('MM', 1), ('Ws', 12), ('E', 10), ('P', 7), ('pr', 0), ('inv', 2), ('A', 8), ('m0', 2), ('ps', 0), ('Wv', 12), ('X', 8), ('T', 12), ('Q', 10), ('M', 10), ('Ws', 13), ('E', 11), ('f0', 1), ('m1', 2), ('A', 9), ('f1', 1), ('Wv', 13), ('X', 9), ('T', 13), ('TV', 2), ('Q', 11), ('M', 11), ('Ws', 14), ('E', 12), ('P', 8), ('P', 9), ('EV', 2), ('pr', 1), ('A', 10), ('ps', 1), ('Wv', 14), ('X', 10), ('T', 14), ('Q', 12), ('QV', 2), ('M', 12), ('MM', 2), ('Ws', 15), ('E', 13), ('P', 10), ('inv', 3), ('A', 11), ('m0', 3), ('Wv', 15), ('X', 11), ('T', 15), ('Q', 13), ('M', 13), ('Ws', 16), ('E', 14), ('f0', 2), ('m1', 3), ('A', 12), ('f1', 2), ('Wv', 16), ('X', 12), ('T', 16), ('TV', 3), ('Q', 14), ('M', 14), ('Ws', 17), ('E', 15), ('P', 11), ('P', 12), ('EV', 3), ('pr', 2), ('A', 13), ('ps', 2), ('Wv', 17), ('X', 13), ('T', 17), ('Q', 15), ('QV', 3), ('M', 15), ('MM', 3), ('Ws', 18), ('E', 16), ('P', 13), ('inv', 4), ('A', 14), ('m0', 4), ('Wv', 18), ('X', 14), ('T', 18), ('Q', 16), ('M', 16), ('Ws', 19), ('E', 17), ('f0', 3), ('m1', 4), ('A', 15), ('f1', 3), ('Wv', 19), ('X', 15), ('T', 19), ('TV', 4), ('Q', 17), ('M', 17), ('Ws', 20), ('E', 18), ('P', 14), ('P', 15), ('EV', 4), ('pr', 3), ('A', 16), ('ps', 3), ('Wv', 20), ('X', 16), ('T', 20), ('Q', 18), ('QV', 4), ('M', 18), ('MM', 4), ('Ws', 21), ('E', 19), ('P', 16), ('inv', 5), ('A', 17), ('m0', 5), ('Wv', 21), ('X', 17), ('T', 21), ('Q', 19), ('M', 19), ('Ws', 22), ('E', 20), ('f0', 4), ('m1', 5), ('A', 18), ('f1', 4), ('Wv', 22), ('X', 18), ('Ws', 23), ('A', 19), ('TV', 5), ('Wv', 23), ('T', 22), ('Q', 20), ('EV', 5), ('pr', 4), ('E', 21), ('X', 19), ('Q', 21), ('E', 22), ('M', 20), ('Q', 22), ('P', 18), ('T', 23), ('P', 17), ('A', 20), ('MM', 5), ('E', 23), ('M', 21), ('inv', 6), ('m0', 6), ('Q', 23), ('M', 22), ('f0', 5), ('A', 21), ('m1', 6), ('P', 19), ('X', 20), ('M', 23), ('f1s', 5), ('X', 21), ('A', 23), ('A', 22), ('P', 20), ('X', 23), ('X', 22), ('TV', 6), ('ps', 4), ('P', 21), ('EV', 6), ('op', 1), ('op', 0), ('inv', 7), ('P', 23), ('QV', 6), ('P', 22), ('m0', 7), ('m1', 7), ('ln', 2), ('MM', 6), ('TV', 7), ('pr', 5), ('fin', 2), ('ln', 4), ('EV', 7), ('f1', 6), ('QV', 7), ('f0', 6), ('ps', 5), ('fin', 4), ('ln', 3), ('invl', 5), ('ln', 1), ('MM', 7), ('pr', 6), ('f0', 7), ('fin', 3), ('ln', 0), ('ps', 6), ('ln', 5), ('invl', 6), ('cl', 1), ('f1s', 7), ('fin', 5), ('pr', 7), ('fs', 1), ('ps', 7), ('invl', 7), ('cl', 0), ('fs', 0), ('ln', 6), ('fin', 6), ('ln', 7), ('QV', 5), ('fin', 7)]
 
 
 def tile_chunkflooredmessagemiddlescore_kernel(tc, x_bytes, x_scale, we_words, we_scales, be, ends, gain, trans, out):
@@ -91,17 +94,17 @@ def tile_chunkflooredmessagemiddlescore_kernel(tc, x_bytes, x_scale, we_words, w
             nc.sync.dma_start(out=tr_raw[p][:], in_=trans[p].rearrange("(p j) n -> p j n", j=4))
 
         load_x(0)
+        load_x(1)
         nc.sync.dma_start(out=rows[0:1, :], in_=be.rearrange("(o n) -> o n", o=1))
         nc.sync.dma_start(out=rows[32:65:32, :], in_=ends)
-        load_x(1)
         load_trans(0)
+        load_x(2)
         nc.sync.dma_start(out=we_w[:].bitcast(I32), in_=we_words.rearrange("g p n -> p g n").bitcast(I32))
         for q in range(4):
             nc.sync.dma_start(
                 out=we_s[32 * q:32 * q + 4, :, :].bitcast(I32),
                 in_=we_scales[:, 4 * q:4 * q + 4, :].rearrange("g r n -> r g n").bitcast(I32),
             )
-        load_x(2)
         load_x(3)
         nc.sync.dma_start(out=gain_raw[:], in_=gain.rearrange("a n -> (a n)").partition_broadcast(P))
         load_x(4)
@@ -125,7 +128,10 @@ def tile_chunkflooredmessagemiddlescore_kernel(tc, x_bytes, x_scale, we_words, w
             acc = psum.tile([P, T], F32, name="m_ps", tag="m_ps")
             nc.tensor.matmul(acc[:], lhsT=coef[:, c:c + 1].to_broadcast([P, P]), rhs=rows[:], start=True, stop=True)
             wide = keep.tile([P, T], F32, name=name)
-            nc.vector.tensor_copy(out=wide[:], in_=acc[:])
+            if SPS:
+                nc.scalar.copy(out=wide[:], in_=acc[:])
+            else:
+                nc.vector.tensor_copy(out=wide[:], in_=acc[:])
             return wide
 
         tr_grouped = {}
@@ -167,14 +173,25 @@ def tile_chunkflooredmessagemiddlescore_kernel(tc, x_bytes, x_scale, we_words, w
                 for u in range(2):
                     nc.tensor.transpose(xt[s][:, g, u, :], words[:, 256 * g + u:256 * (g + 1):2], ident[:])
 
+        rider = {slot_of[i, 2] + RIDE: i for i in range(TILES) if slot_of[i, 2] + RIDE < NU}
+        host = {i: s for s, i in rider.items()}
+
+        def grouped(s):
+            if s not in xg:
+                xg[s] = work.tile([P, 4 if s in rider else 2, P, 2], F32, name="xg", tag="xg", align_bytes=64)
+            return xg[s]
+
         def empty_x(s):
-            xg[s] = work.tile([P, PASSES, P, 2], F32, name="xg", tag="xg", align_bytes=64)
-            nc.scalar.copy(out=xg[s][:], in_=xt[s][:].rearrange("p g u r -> p g r u"))
+            nc.scalar.copy(out=grouped(s)[:, 0:2], in_=xt[s][:].rearrange("p g u r -> p g r u"))
 
         def quantize_x(s):
-            xq[s] = work.tile([P, PASSES * P], U32, name="xq", tag="xq", align_bytes=64)
-            xqs[s] = work.tile([P, PASSES * P], U8, name="xqs", tag="xqs", align_bytes=64)
+            width = (4 if s in rider else 2) * P
+            xq[s] = work.tile([P, width], U32, name="xq", tag="xq", align_bytes=64)
+            xqs[s] = work.tile([P, width], U8, name="xqs", tag="xqs", align_bytes=64)
             nc.vector.quantize_mx(out=xq[s][:].bitcast(FP8X4), scales=xqs[s][:], in_=xg[s][:].rearrange("p g r u -> p (g r u)").bitcast(BF16))
+            if s in rider:
+                vq[rider[s]] = xq[s][:, 2 * P:]
+                vqs[rider[s]] = xqs[s][:, 2 * P:]
 
         def emit(s):
             e_ps[s] = psum.tile([P, T], F32, name="e_ps", tag="e_ps")
@@ -185,23 +202,36 @@ def tile_chunkflooredmessagemiddlescore_kernel(tc, x_bytes, x_scale, we_words, w
                     rhs=we_w[:, g, :].bitcast(FP4X4), rhs_scale=we_s[:, g, :], start=(g == 0), stop=(g == PASSES - 1),
                 )
 
+        neg_pair = {}
+
         def add_bias(s):
             i, l = units[s]
             if l == 1:
                 neg_n[s] = keep.tile([P, T], F32, name="neg_mid%d" % i)
                 nc.vector.scalar_tensor_tensor(out=neg_n[s][:], in0=e_ps[s][:], scalar=-1.0, in1=be_wide[:], op0=ALU.mult, op1=ALU.subtract)
             else:
-                neg_n[s] = work.tile([P, T], F32, name="neg_n", tag="neg_n")
+                if l == 0:
+                    neg_pair[i] = work.tile([P, PAIRS, T], F32, name="neg_pair", tag="neg_pair", bufs=3)
+                neg_n[s] = neg_pair[i][:, l // 2, :]
                 nc.vector.tensor_tensor(out=neg_n[s][:], in0=neg_bias[l][:], in1=e_ps[s][:], op=ALU.subtract)
 
         def find_max(s):
+            i, l = units[s]
+            if l == 0 and i >= XM:
+                return
+            if l == 2 and i >= XM:
+                both = keep.tile([P, 2], F32, name="neg_max%d" % s)
+                nc.vector.tensor_reduce(out=both[:], in_=neg_pair[i][:], axis=AX.X, op=ALU.min)
+                neg_max[s - 1] = both[:, 0:1]
+                neg_max[s] = both[:, 1:2]
+                return
             neg_max[s] = keep.tile([P, 1], F32, name="neg_max%d" % s)
             nc.vector.tensor_reduce(out=neg_max[s][:], in_=neg_n[s][:], axis=AX.X, op=ALU.min)
 
         def exponent(s):
             i, l = units[s]
             if l == 1:
-                ex[s] = work.tile([P, T], F32, name="ex_mid", tag="ex_mid", bufs=6)
+                ex[s] = work.tile([P, T], F32, name="ex_mid", tag="ex_mid", bufs=4)
                 nc.scalar.activation(out=ex[s][:], in_=neg_n[s][:], func=ACT.Exp, bias=neg_max[s][:], scale=-1.0)
             else:
                 ex[s] = work.tile([P, T], F32, name="ex", tag="ex", bufs=6)
@@ -226,10 +256,15 @@ def tile_chunkflooredmessagemiddlescore_kernel(tc, x_bytes, x_scale, we_words, w
                     nc.tensor.transpose(vt[i][:, p, u, :], words[:, 256 * p + u:256 * (p + 1):2], ident[:])
 
         def empty_v(i):
-            vg[i] = work.tile([P, PAIRS, P, 2], F32, name="vg", tag="vg", align_bytes=64)
+            if i in host:
+                nc.scalar.copy(out=grouped(host[i])[:, 2:4], in_=vt[i][:].rearrange("p g u r -> p g r u"))
+                return
+            vg[i] = work.tile([P, PAIRS, P, 2], F32, name="vg", tag="vg", bufs=2, align_bytes=64)
             nc.scalar.copy(out=vg[i][:], in_=vt[i][:].rearrange("p g u r -> p g r u"))
 
         def quantize_v(i):
+            if i in host:
+                return
             vq[i] = work.tile([P, PAIRS * P], U32, name="vq", tag="vq", align_bytes=64)
             vqs[i] = work.tile([P, PAIRS * P], U8, name="vqs", tag="vqs", align_bytes=64)
             nc.vector.quantize_mx(out=vq[i][:].bitcast(FP8X4), scales=vqs[i][:], in_=vg[i][:].rearrange("p g r u -> p (g r u)").bitcast(BF16))
@@ -274,21 +309,21 @@ def tile_chunkflooredmessagemiddlescore_kernel(tc, x_bytes, x_scale, we_words, w
 
         def open_total(i):
             s = slot_of[i, 1]
-            total[i] = psum.tile([P, T], F32, name="xt", tag="xt", bufs=3)
+            total[i] = psum.tile([P, T], F32, name="xt", tag="xt", bufs=3) if i < 3 else psum.tile([P, T], F32, name="e_ps", tag="e_ps")
             nc.tensor.matmul(total[i][:], lhsT=neg_ident[:], rhs=neg_n[s][:], start=True, stop=False)
 
         def close_total(i):
             nc.tensor.matmul(total[i][:], lhsT=ident[:], rhs=logp[i][:], start=False, stop=True)
 
         def floor_second_scalar(i):
-            cut = work.tile([P, T], F32, name="cut", tag="cut")
+            cut = work.tile([P, T], F32, name="cut", tag="cut", bufs=1)
             fl1[i] = work.tile([P, T], F32, name="fl1", tag="fl1")
             nc.scalar.activation(out=cut[:], in_=m_ps[i, 1][:], func=ACT.Relu, bias=FLOOR_M, scale=1.0)
             nc.scalar.activation(out=fl1[i][:], in_=cut[:], func=ACT.Identity, bias=FLOOR_A, scale=1.0)
 
         def finish_scalar(i):
             s = slot_of[i, 1]
-            res = work.tile([P, T], F32, name="res", tag="res", bufs=8)
+            res = work.tile([P, T], F32, name="res", tag="res", bufs=6)
             nc.scalar.activation(out=res[:], in_=total[i][:], func=ACT.Identity, bias=neg_max[s][:], scale=1.0)
             nc.sync.dma_start(out=out[i * P:(i + 1) * P, :], in_=res[:])
 
@@ -296,7 +331,7 @@ def tile_chunkflooredmessagemiddlescore_kernel(tc, x_bytes, x_scale, we_words, w
 
         def finish(i):
             s = slot_of[i, 1]
-            res = work.tile([P, T], F32, name="res", tag="res", bufs=8)
+            res = work.tile([P, T], F32, name="res", tag="res", bufs=6)
             nc.vector.scalar_tensor_tensor(out=res[:], in0=logp[i][:], scalar=neg_max[s][:], in1=neg_n[s][:], op0=ALU.add, op1=ALU.subtract)
             nc.sync.dma_start(out=out[i * P:(i + 1) * P, :], in_=res[:])
 

@@ -20,46 +20,33 @@ AX = mybir.AxisListType
 
 P = 128
 TILES = B // P
+LAST_TILE = TILES - 1
 PASSES = D // 512
-KBLOCKS = D // 128
-FLOOR_M = 14.4
-FLOOR_A = 1.6
+SCALE_BLOCKS = D // 128
+PASS_WORDS = 256
+HALF = T // 2
+
+FLOOR_SHIFT = 14.4
+FLOOR_VALUE = 1.6
+
+VECTOR_BLOCKS = [3, 4, 3, 3] + [2] * 12 + [1] * 4 + [0] * 4
+
 SUM_LAG = 3
-MID_LAG = 1
-NVS = [3, 4, 3, 2, 2, 2, 2, 2, 1, 1, 1, 1, 1, 1, 1, 1, 0, 0, 0, 0, 0, 0, 0, 0]
-PAUSE = []
-SORD = "PfEVWLR"
-VORD = "wiap10sxtfFSG"
-SETUP = [-3, -2, -1, 0, 1, 1, 2]
-L_MSG0 = 2
-L_MSG1 = 3
-L_TV = 4
-L_QV = 5
-L_FL = 6
-L_PR = 7
-L_PS = 7
-LOGS = 3
-WARM = 1
-FLS = 8
-FPE = 0
-GP = 0
-SPS = 1
 RIDE = 6
-XM = 1
-ORDER = [('Wv', 0), ('Wv', 1), ('Ws', 0), ('spr', 0), ('Ws', 1), ('T', 0), ('E', 0), ('spr', 2), ('T', 1), ('Ws', 2), ('it', 0), ('E', 1), ('Q', 0), ('Ws', 3), ('Wv', 2), ('M', 0), ('qt', 0), ('Wv', 3), ('T', 2), ('A', 0), ('Q', 1), ('sg', 0), ('Ws', 4), ('M', 1), ('X', 0), ('Wv', 4), ('E', 2), ('A', 1), ('T', 3), ('Ws', 5), ('Q', 2), ('it', 1), ('P', 0), ('T', 4), ('M', 2), ('E', 3), ('Wv', 5), ('X', 1), ('qt', 1), ('T', 5), ('Q', 3), ('M', 3), ('Ws', 6), ('E', 4), ('P', 1), ('A', 2), ('Wv', 6), ('X', 2), ('T', 6), ('Q', 4), ('M', 4), ('Ws', 7), ('E', 5), ('inv', 0), ('A', 3), ('m0', 0), ('Wv', 7), ('X', 3), ('T', 7), ('Q', 5), ('M', 5), ('Ws', 8), ('E', 6), ('P', 2), ('P', 3), ('m1', 0), ('A', 4), ('Wv', 8), ('X', 4), ('T', 8), ('TV', 0), ('Q', 6), ('M', 6), ('Ws', 9), ('E', 7), ('P', 4), ('EV', 0), ('inv', 1), ('A', 5), ('m0', 1), ('Wv', 9), ('X', 5), ('T', 9), ('Q', 7), ('QV', 0), ('M', 7), ('MM', 0), ('Ws', 10), ('E', 8), ('m1', 1), ('A', 6), ('Wv', 10), ('X', 6), ('T', 10), ('TV', 1), ('Q', 8), ('M', 8), ('Ws', 11), ('E', 9), ('P', 5), ('P', 6), ('EV', 1), ('f0', 0), ('A', 7), ('f1', 0), ('Wv', 11), ('X', 7), ('T', 11), ('Q', 9), ('QV', 1), ('M', 9), ('MM', 1), ('Ws', 12), ('E', 10), ('P', 7), ('pr', 0), ('inv', 2), ('A', 8), ('m0', 2), ('ps', 0), ('Wv', 12), ('X', 8), ('T', 12), ('Q', 10), ('M', 10), ('Ws', 13), ('E', 11), ('f0', 1), ('m1', 2), ('A', 9), ('f1', 1), ('Wv', 13), ('X', 9), ('T', 13), ('TV', 2), ('Q', 11), ('M', 11), ('Ws', 14), ('E', 12), ('P', 8), ('P', 9), ('EV', 2), ('pr', 1), ('A', 10), ('ps', 1), ('Wv', 14), ('X', 10), ('T', 14), ('Q', 12), ('QV', 2), ('M', 12), ('MM', 2), ('Ws', 15), ('E', 13), ('P', 10), ('inv', 3), ('A', 11), ('m0', 3), ('Wv', 15), ('X', 11), ('T', 15), ('Q', 13), ('M', 13), ('Ws', 16), ('E', 14), ('f0', 2), ('m1', 3), ('A', 12), ('f1', 2), ('Wv', 16), ('X', 12), ('T', 16), ('TV', 3), ('Q', 14), ('M', 14), ('Ws', 17), ('E', 15), ('P', 11), ('P', 12), ('EV', 3), ('pr', 2), ('A', 13), ('ps', 2), ('Wv', 17), ('X', 13), ('T', 17), ('Q', 15), ('QV', 3), ('M', 15), ('MM', 3), ('Ws', 18), ('E', 16), ('P', 13), ('inv', 4), ('A', 14), ('m0', 4), ('Wv', 18), ('X', 14), ('T', 18), ('Q', 16), ('M', 16), ('Ws', 19), ('E', 17), ('f0', 3), ('m1', 4), ('A', 15), ('f1', 3), ('Wv', 19), ('X', 15), ('T', 19), ('TV', 4), ('Q', 17), ('M', 17), ('Ws', 20), ('E', 18), ('P', 14), ('P', 15), ('EV', 4), ('pr', 3), ('A', 16), ('ps', 3), ('Wv', 20), ('X', 16), ('T', 20), ('Q', 18), ('QV', 4), ('M', 18), ('MM', 4), ('Ws', 21), ('E', 19), ('P', 16), ('inv', 5), ('A', 17), ('m0', 5), ('Wv', 21), ('X', 17), ('T', 21), ('Q', 19), ('M', 19), ('Ws', 22), ('E', 20), ('f0', 4), ('m1', 5), ('A', 18), ('f1', 4), ('Wv', 22), ('X', 18), ('Ws', 23), ('A', 19), ('TV', 5), ('Wv', 23), ('T', 22), ('Q', 20), ('EV', 5), ('pr', 4), ('E', 21), ('X', 19), ('Q', 21), ('E', 22), ('M', 20), ('Q', 22), ('P', 18), ('T', 23), ('P', 17), ('A', 20), ('MM', 5), ('E', 23), ('M', 21), ('inv', 6), ('m0', 6), ('Q', 23), ('M', 22), ('f0', 5), ('A', 21), ('m1', 6), ('P', 19), ('X', 20), ('M', 23), ('f1s', 5), ('X', 21), ('A', 23), ('A', 22), ('P', 20), ('X', 23), ('X', 22), ('TV', 6), ('ps', 4), ('P', 21), ('EV', 6), ('op', 1), ('op', 0), ('inv', 7), ('P', 23), ('QV', 6), ('P', 22), ('m0', 7), ('m1', 7), ('ln', 2), ('MM', 6), ('TV', 7), ('pr', 5), ('fin', 2), ('ln', 4), ('EV', 7), ('f1', 6), ('QV', 7), ('f0', 6), ('ps', 5), ('fin', 4), ('ln', 3), ('invl', 5), ('ln', 1), ('MM', 7), ('pr', 6), ('f0', 7), ('fin', 3), ('ln', 0), ('ps', 6), ('ln', 5), ('invl', 6), ('cl', 1), ('f1s', 7), ('fin', 5), ('pr', 7), ('fs', 1), ('ps', 7), ('invl', 7), ('cl', 0), ('fs', 0), ('ln', 6), ('fin', 6), ('ln', 7), ('QV', 5), ('fin', 7)]
+FIRST_SLOT, END_SLOT = 2, 19
 
 
 def tile_chunkflooredmessagemiddlescore_kernel(tc, x_bytes, x_scale, we_words, we_scales, be, ends, gain, trans, out):
     nc = tc.nc
 
     units = []
-    for i in range(TILES + MID_LAG):
+    for i in range(TILES + 1):
         if i < TILES:
             units += [(i, 0), (i, 2)]
-        if i >= MID_LAG:
-            units += [(i - MID_LAG, 1)]
-    slot_of = {u: s for s, u in enumerate(units)}
-    NU = len(units)
+        if i >= 1:
+            units += [(i - 1, 1)]
+    unit_of = {u: s for s, u in enumerate(units)}
+    n_units = len(units)
 
     with ExitStack() as ctx:
         keep = ctx.enter_context(tc.tile_pool(name="keep", bufs=1))
@@ -73,26 +60,24 @@ def tile_chunkflooredmessagemiddlescore_kernel(tc, x_bytes, x_scale, we_words, w
         gain_wide = keep.tile([P, PAIRS * T], BF16, name="gain_wide")
         we_s = keep.tile([P, PASSES, T], U8, name="we_s", align_bytes=64)
         we_w = keep.tile([P, PASSES, 2 * T], U8, name="we_w", align_bytes=64)
-        xs = keep.tile([P, L * TILES * KBLOCKS], F32, name="xs")
+        xs = keep.tile([P, L * TILES * SCALE_BLOCKS], F32, name="xs")
         ident = keep.tile([P, P], F32, name="ident")
-        coef = keep.tile([P, 4], BF16, name="coef")
+        pick = keep.tile([P, 4], BF16, name="pick")
         nc.vector.memset(rows[:].bitcast(I32), 0)
         nc.vector.memset(we_s[:].rearrange("p g n -> p (g n)").bitcast(I32), 0)
 
-        xb = {}
+        x_raw, trans_raw = {}, {}
 
         def load_x(s):
             i, l = units[s]
-            xb[s] = keep.tile([P, D], U8, name="xbytes%d" % s)
-            nc.sync.dma_start(out=xb[s][:], in_=x_bytes[l, i * P:(i + 1) * P, :])
-
-        nc.scalar.dma_start(out=xs[:], in_=x_scale.rearrange("l i j -> (l i j)").partition_broadcast(P))
-        tr_raw = {}
+            x_raw[s] = keep.tile([P, D], U8, name="xbytes%d" % s)
+            nc.sync.dma_start(out=x_raw[s][:], in_=x_bytes[l, i * P:(i + 1) * P, :])
 
         def load_trans(p):
-            tr_raw[p] = keep.tile([P, 4, T], BF16, name="tr_raw%d" % p)
-            nc.sync.dma_start(out=tr_raw[p][:], in_=trans[p].rearrange("(p j) n -> p j n", j=4))
+            trans_raw[p] = keep.tile([P, 4, T], BF16, name="tr_raw%d" % p)
+            nc.sync.dma_start(out=trans_raw[p][:], in_=trans[p].rearrange("(p j) n -> p j n", j=4))
 
+        nc.scalar.dma_start(out=xs[:], in_=x_scale.rearrange("l i j -> (l i j)").partition_broadcast(P))
         load_x(0)
         load_x(1)
         nc.sync.dma_start(out=rows[0:1, :], in_=be.rearrange("(o n) -> o n", o=1))
@@ -111,240 +96,321 @@ def tile_chunkflooredmessagemiddlescore_kernel(tc, x_bytes, x_scale, we_words, w
         load_trans(1)
         load_x(5)
         nc.sync.dma_start(out=be_wide[:], in_=be.partition_broadcast(P))
-        for s in range(6, NU):
+        for s in range(6, n_units):
             load_x(s)
 
-        nc.gpsimd.memset(coef[:], 0.0)
-        nc.gpsimd.memset(coef[0:1, :], -1.0)
-        nc.gpsimd.memset(coef[32:33, 0:2], -1.0)
-        nc.gpsimd.memset(coef[64:65, 2:4], -1.0)
+        nc.gpsimd.memset(pick[:], 0.0)
+        nc.gpsimd.memset(pick[0:1, :], -1.0)
+        nc.gpsimd.memset(pick[32:33, 0:2], -1.0)
+        nc.gpsimd.memset(pick[64:65, 2:4], -1.0)
         make_identity(nc, ident[:])
         neg_ident = keep.tile([P, P], F32, name="neg_ident")
         nc.gpsimd.tensor_scalar(out=neg_ident[:], in0=ident[:], scalar1=-1.0, scalar2=0.0, op0=ALU.mult, op1=ALU.add)
 
         neg_bias = {}
 
-        def spread(c, name):
+        def spread_bias(l):
             acc = psum.tile([P, T], F32, name="m_ps", tag="m_ps")
-            nc.tensor.matmul(acc[:], lhsT=coef[:, c:c + 1].to_broadcast([P, P]), rhs=rows[:], start=True, stop=True)
-            wide = keep.tile([P, T], F32, name=name)
-            if SPS:
-                nc.scalar.copy(out=wide[:], in_=acc[:])
-            else:
-                nc.vector.tensor_copy(out=wide[:], in_=acc[:])
-            return wide
+            nc.tensor.matmul(acc[:], lhsT=pick[:, l:l + 1].to_broadcast([P, P]), rhs=rows[:], start=True, stop=True)
+            neg_bias[l] = keep.tile([P, T], F32, name="neg_bias%d" % l)
+            nc.scalar.copy(out=neg_bias[l][:], in_=acc[:])
 
-        tr_grouped = {}
-        tr_codes = keep.tile([P, PAIRS, T], U32, name="tr_codes", align_bytes=64)
-        tr_scales = keep.tile([P, PAIRS, T], U8, name="tr_scales", align_bytes=64)
+        def scale_gain(p):
+            nc.vector.tensor_scalar(out=gain_wide[:, p * T:], in0=gain_raw[:, p * T:], scalar1=float(T), scalar2=None, op0=ALU.mult)
+
+        trans_grouped = {}
+        trans_codes = keep.tile([P, PAIRS, T], U32, name="tr_codes", align_bytes=64)
+        trans_scales = keep.tile([P, PAIRS, T], U8, name="tr_scales", align_bytes=64)
 
         def interleave_trans(p):
-            tr_grouped[p] = keep.tile([P, T, 4], BF16, name="tr_grouped%d" % p, align_bytes=64)
+            trans_grouped[p] = keep.tile([P, T, 4], BF16, name="tr_grouped%d" % p, align_bytes=64)
             nc.vector.tensor_copy(
-                out=tr_grouped[p][:].rearrange("p (c i) t -> p c t i", i=4),
-                in_=tr_raw[p][:].rearrange("p t (c i) -> p c t i", i=4),
+                out=trans_grouped[p][:].rearrange("p (c i) t -> p c t i", i=4),
+                in_=trans_raw[p][:].rearrange("p t (c i) -> p c t i", i=4),
             )
 
         def quantize_trans(p):
-            nc.vector.quantize_mx(out=tr_codes[:, p, :].bitcast(FP8X4), scales=tr_scales[:, p, :], in_=tr_grouped[p][:].rearrange("p n t -> p (n t)"))
+            nc.vector.quantize_mx(
+                out=trans_codes[:, p, :].bitcast(FP8X4), scales=trans_scales[:, p, :],
+                in_=trans_grouped[p][:].rearrange("p n t -> p (n t)"),
+            )
 
-        xw, xt, xg, xq, xqs, e_ps, neg_n, neg_max, ex = {}, {}, {}, {}, {}, {}, {}, {}, {}
+        x_wide, x_turned, grouped, x_codes, x_scales, e_ps = {}, {}, {}, {}, {}, {}
+        neg_pair, neg_n, neg_max, expo = {}, {}, {}, {}
         sums = [keep.tile([P, 3], F32, name="sums%d" % i) for i in range(TILES + SUM_LAG)]
-        inv = [keep.tile([P, 3], F32, name="inv%d" % i) for i in range(TILES + SUM_LAG)]
+        inverse = [keep.tile([P, 3], F32, name="inv%d" % i) for i in range(TILES + SUM_LAG)]
+        rider = {unit_of[i, 2] + RIDE: i for i in range(TILES) if unit_of[i, 2] + RIDE < n_units}
+        carrier = {i: s for s, i in rider.items()}
+        v_codes, v_scales = {}, {}
 
-        def widen(s, blocks, on_vector):
+        def wide_blocks(s, blocks):
             i, l = units[s]
-            if s not in xw:
-                xw[s] = work.tile([P, D], BF16, name="xw", tag="xw", bufs=4)
+            if s not in x_wide:
+                x_wide[s] = work.tile([P, D], BF16, name="xw", tag="xw")
+            found = []
             for j in blocks:
                 cols = slice(j * 128, (j + 1) * 128)
-                c = (l * TILES + i) * KBLOCKS + j
-                if on_vector:
-                    nc.vector.tensor_scalar(out=xw[s][:, cols], in0=xb[s][:, cols].bitcast(FP8), scalar1=xs[:, c:c + 1], scalar2=None, op0=ALU.mult)
-                else:
-                    nc.scalar.activation(out=xw[s][:, cols], in_=xb[s][:, cols].bitcast(FP8), func=ACT.Copy, scale=xs[:, c:c + 1])
+                c = (l * TILES + i) * SCALE_BLOCKS + j
+                found.append((x_raw[s][:, cols].bitcast(FP8), x_wide[s][:, cols], xs[:, c:c + 1]))
+            return found
+
+        def widen_vector(s):
+            for src, dst, scale in wide_blocks(s, range(VECTOR_BLOCKS[s])):
+                nc.vector.tensor_scalar(out=dst, in0=src, scalar1=scale, scalar2=None, op0=ALU.mult)
+
+        def widen_scalar(s):
+            for src, dst, scale in wide_blocks(s, range(VECTOR_BLOCKS[s], SCALE_BLOCKS)):
+                nc.scalar.activation(out=dst, in_=src, func=ACT.Copy, scale=scale)
+
+        def turn(bank, values):
+            words = values.bitcast(F32)
+            for g in range(2):
+                for u in range(2):
+                    nc.tensor.transpose(bank[:, g, u, :], words[:, PASS_WORDS * g + u:PASS_WORDS * (g + 1):2], ident[:])
 
         def turn_x(s):
-            words = xw[s][:].bitcast(F32)
-            xt[s] = psum.tile([P, PASSES, 2, P], F32, name="xt", tag="xt", bufs=3)
-            for w in range(WARM):
-                nc.tensor.matmul(xt[s][:, 0, w, :], lhsT=ident[:], rhs=ident[:], start=True, stop=True)
-            for g in range(PASSES):
-                for u in range(2):
-                    nc.tensor.transpose(xt[s][:, g, u, :], words[:, 256 * g + u:256 * (g + 1):2], ident[:])
+            x_turned[s] = psum.tile([P, PASSES, 2, P], F32, name="xt", tag="xt", bufs=3)
+            turn(x_turned[s], x_wide[s][:])
 
-        rider = {slot_of[i, 2] + RIDE: i for i in range(TILES) if slot_of[i, 2] + RIDE < NU}
-        host = {i: s for s, i in rider.items()}
-
-        def grouped(s):
-            if s not in xg:
-                xg[s] = work.tile([P, 4 if s in rider else 2, P, 2], F32, name="xg", tag="xg", align_bytes=64)
-            return xg[s]
+        def grouped_of(s):
+            if s not in grouped:
+                grouped[s] = work.tile([P, 4 if s in rider else 2, P, 2], F32, name="xg", tag="xg", align_bytes=64)
+            return grouped[s]
 
         def empty_x(s):
-            nc.scalar.copy(out=grouped(s)[:, 0:2], in_=xt[s][:].rearrange("p g u r -> p g r u"))
+            nc.scalar.copy(out=grouped_of(s)[:, 0:2], in_=x_turned[s][:].rearrange("p g u r -> p g r u"))
 
         def quantize_x(s):
             width = (4 if s in rider else 2) * P
-            xq[s] = work.tile([P, width], U32, name="xq", tag="xq", align_bytes=64)
-            xqs[s] = work.tile([P, width], U8, name="xqs", tag="xqs", align_bytes=64)
-            nc.vector.quantize_mx(out=xq[s][:].bitcast(FP8X4), scales=xqs[s][:], in_=xg[s][:].rearrange("p g r u -> p (g r u)").bitcast(BF16))
+            x_codes[s] = work.tile([P, width], U32, name="xq", tag="xq", align_bytes=64)
+            x_scales[s] = work.tile([P, width], U8, name="xqs", tag="xqs", align_bytes=64)
+            nc.vector.quantize_mx(
+                out=x_codes[s][:].bitcast(FP8X4), scales=x_scales[s][:],
+                in_=grouped[s][:].rearrange("p g r u -> p (g r u)").bitcast(BF16),
+            )
             if s in rider:
-                vq[rider[s]] = xq[s][:, 2 * P:]
-                vqs[rider[s]] = xqs[s][:, 2 * P:]
+                v_codes[rider[s]] = x_codes[s][:, 2 * P:]
+                v_scales[rider[s]] = x_scales[s][:, 2 * P:]
 
         def emit(s):
             e_ps[s] = psum.tile([P, T], F32, name="e_ps", tag="e_ps")
             for g in range(PASSES):
                 cols = slice(g * P, (g + 1) * P)
                 nc.tensor.matmul_mx(
-                    out=e_ps[s][:], lhsT=xq[s][:, cols].bitcast(FP8X4), lhsT_scale=xqs[s][:, cols],
+                    out=e_ps[s][:], lhsT=x_codes[s][:, cols].bitcast(FP8X4), lhsT_scale=x_scales[s][:, cols],
                     rhs=we_w[:, g, :].bitcast(FP4X4), rhs_scale=we_s[:, g, :], start=(g == 0), stop=(g == PASSES - 1),
                 )
-
-        neg_pair = {}
 
         def add_bias(s):
             i, l = units[s]
             if l == 1:
                 neg_n[s] = keep.tile([P, T], F32, name="neg_mid%d" % i)
-                nc.vector.scalar_tensor_tensor(out=neg_n[s][:], in0=e_ps[s][:], scalar=-1.0, in1=be_wide[:], op0=ALU.mult, op1=ALU.subtract)
+                nc.vector.scalar_tensor_tensor(
+                    out=neg_n[s][:], in0=e_ps[s][:], scalar=-1.0, in1=be_wide[:], op0=ALU.mult, op1=ALU.subtract,
+                )
             else:
                 if l == 0:
                     neg_pair[i] = work.tile([P, PAIRS, T], F32, name="neg_pair", tag="neg_pair", bufs=3)
                 neg_n[s] = neg_pair[i][:, l // 2, :]
                 nc.vector.tensor_tensor(out=neg_n[s][:], in0=neg_bias[l][:], in1=e_ps[s][:], op=ALU.subtract)
 
-        def find_max(s):
+        def paired(s):
             i, l = units[s]
-            if l == 0 and i >= XM:
-                return
-            if l == 2 and i >= XM:
+            return l != 1 and i >= 1
+
+        def find_max(s):
+            if paired(s):
                 both = keep.tile([P, 2], F32, name="neg_max%d" % s)
-                nc.vector.tensor_reduce(out=both[:], in_=neg_pair[i][:], axis=AX.X, op=ALU.min)
+                nc.vector.tensor_reduce(out=both[:], in_=neg_pair[units[s][0]][:], axis=AX.X, op=ALU.min)
                 neg_max[s - 1] = both[:, 0:1]
                 neg_max[s] = both[:, 1:2]
-                return
-            neg_max[s] = keep.tile([P, 1], F32, name="neg_max%d" % s)
-            nc.vector.tensor_reduce(out=neg_max[s][:], in_=neg_n[s][:], axis=AX.X, op=ALU.min)
+            else:
+                neg_max[s] = keep.tile([P, 1], F32, name="neg_max%d" % s)
+                nc.vector.tensor_reduce(out=neg_max[s][:], in_=neg_n[s][:], axis=AX.X, op=ALU.min)
 
         def exponent(s):
             i, l = units[s]
             if l == 1:
-                ex[s] = work.tile([P, T], F32, name="ex_mid", tag="ex_mid", bufs=4)
-                nc.scalar.activation(out=ex[s][:], in_=neg_n[s][:], func=ACT.Exp, bias=neg_max[s][:], scale=-1.0)
+                expo[s] = work.tile([P, T], F32, name="ex_mid", tag="ex_mid")
+                nc.scalar.activation(out=expo[s][:], in_=neg_n[s][:], func=ACT.Exp, bias=neg_max[s][:], scale=-1.0)
             else:
-                ex[s] = work.tile([P, T], F32, name="ex", tag="ex", bufs=6)
-                nc.scalar.activation(out=ex[s][:], in_=neg_n[s][:], func=ACT.Exp, bias=neg_max[s][:], scale=-1.0, accum_out=sums[i][:, l // 2:l // 2 + 1])
+                expo[s] = work.tile([P, T], F32, name="ex", tag="ex", bufs=6)
+                nc.scalar.activation(
+                    out=expo[s][:], in_=neg_n[s][:], func=ACT.Exp, bias=neg_max[s][:], scale=-1.0,
+                    accum_out=sums[i][:, l // 2:l // 2 + 1],
+                )
 
-        v, vt, vg, vq, vqs, m_ps, fl0, fl1, prod, logp = {}, {}, {}, {}, {}, {}, {}, {}, {}, {}
+        v, v_turned, v_grouped, m_ps, cut0, floored1, product, log_a, total = {}, {}, {}, {}, {}, {}, {}, {}, {}
 
-        def invert(i, cols):
-            nc.vector.reciprocal(out=inv[i][:, cols], in_=sums[i][:, cols])
+        def invert_sums(i):
+            cols = slice(0, 3 if i >= SUM_LAG else 2)
+            nc.vector.reciprocal(out=inverse[i][:, cols], in_=sums[i][:, cols])
+
+        def invert_weight(i):
+            nc.vector.reciprocal(out=inverse[i + SUM_LAG][:, 2:3], in_=sums[i + SUM_LAG][:, 2:3])
 
         def message(i, p):
-            s = slot_of[i, 2 * p]
-            if p == 0:
-                v[i] = work.tile([P, PAIRS, T], BF16, name="v", tag="v")
-            nc.vector.scalar_tensor_tensor(out=v[i][:, p, :], in0=ex[s][:], scalar=inv[i][:, p:p + 1], in1=gain_wide[:, p * T:(p + 1) * T], op0=ALU.mult, op1=ALU.mult)
+            nc.vector.scalar_tensor_tensor(
+                out=v[i][:, p, :], in0=expo[unit_of[i, 2 * p]][:], scalar=inverse[i][:, p:p + 1],
+                in1=gain_wide[:, p * T:(p + 1) * T], op0=ALU.mult, op1=ALU.mult,
+            )
+
+        def message_first(i):
+            v[i] = work.tile([P, PAIRS, T], BF16, name="v", tag="v")
+            message(i, 0)
+
+        def message_second(i):
+            message(i, 1)
 
         def turn_v(i):
-            vt[i] = psum.tile([P, PAIRS, 2, P], F32, name="vt", tag="vt", bufs=1)
-            words = v[i][:].rearrange("p a n -> p (a n)").bitcast(F32)
-            for p in range(PAIRS):
-                for u in range(2):
-                    nc.tensor.transpose(vt[i][:, p, u, :], words[:, 256 * p + u:256 * (p + 1):2], ident[:])
+            v_turned[i] = psum.tile([P, PAIRS, 2, P], F32, name="vt", tag="vt", bufs=1)
+            turn(v_turned[i], v[i][:].rearrange("p a n -> p (a n)"))
 
         def empty_v(i):
-            if i in host:
-                nc.scalar.copy(out=grouped(host[i])[:, 2:4], in_=vt[i][:].rearrange("p g u r -> p g r u"))
-                return
-            vg[i] = work.tile([P, PAIRS, P, 2], F32, name="vg", tag="vg", bufs=2, align_bytes=64)
-            nc.scalar.copy(out=vg[i][:], in_=vt[i][:].rearrange("p g u r -> p g r u"))
+            if i in carrier:
+                dst = grouped_of(carrier[i])[:, 2:4]
+            else:
+                v_grouped[i] = work.tile([P, PAIRS, P, 2], F32, name="vg", tag="vg", bufs=2, align_bytes=64)
+                dst = v_grouped[i][:]
+            nc.scalar.copy(out=dst, in_=v_turned[i][:].rearrange("p g u r -> p g r u"))
 
         def quantize_v(i):
-            if i in host:
-                return
-            vq[i] = work.tile([P, PAIRS * P], U32, name="vq", tag="vq", align_bytes=64)
-            vqs[i] = work.tile([P, PAIRS * P], U8, name="vqs", tag="vqs", align_bytes=64)
-            nc.vector.quantize_mx(out=vq[i][:].bitcast(FP8X4), scales=vqs[i][:], in_=vg[i][:].rearrange("p g r u -> p (g r u)").bitcast(BF16))
+            v_codes[i] = work.tile([P, PAIRS * P], U32, name="vq", tag="vq", align_bytes=64)
+            v_scales[i] = work.tile([P, PAIRS * P], U8, name="vqs", tag="vqs", align_bytes=64)
+            nc.vector.quantize_mx(
+                out=v_codes[i][:].bitcast(FP8X4), scales=v_scales[i][:],
+                in_=v_grouped[i][:].rearrange("p g r u -> p (g r u)").bitcast(BF16),
+            )
 
         def pass_on(i):
             for p in range(PAIRS):
                 cols = slice(p * P, (p + 1) * P)
                 m_ps[i, p] = psum.tile([P, T], F32, name="m_ps", tag="m_ps")
                 nc.tensor.matmul_mx(
-                    out=m_ps[i, p][:], lhsT=vq[i][:, cols].bitcast(FP8X4), lhsT_scale=vqs[i][:, cols],
-                    rhs=tr_codes[:, p, :].bitcast(FP8X4), rhs_scale=tr_scales[:, p, :], start=True, stop=True,
+                    out=m_ps[i, p][:], lhsT=v_codes[i][:, cols].bitcast(FP8X4), lhsT_scale=v_scales[i][:, cols],
+                    rhs=trans_codes[:, p, :].bitcast(FP8X4), rhs_scale=trans_scales[:, p, :], start=True, stop=True,
                 )
 
         def floor_first(i):
-            fl0[i] = work.tile([P, T], F32, name="fl0", tag="fl0")
-            if i < GP:
-                return
-            nc.scalar.activation(out=fl0[i][:], in_=m_ps[i, 0][:], func=ACT.Relu, bias=FLOOR_M, scale=1.0)
+            cut0[i] = work.tile([P, T], F32, name="fl0", tag="fl0")
+            nc.scalar.activation(out=cut0[i][:], in_=m_ps[i, 0][:], func=ACT.Relu, bias=FLOOR_SHIFT, scale=1.0)
 
         def floor_second(i):
-            fl1[i] = work.tile([P, T], F32, name="fl1", tag="fl1")
-            nc.vector.tensor_scalar(out=fl1[i][:], in0=m_ps[i, 1][:], scalar1=-FLOOR_M, scalar2=16.0, op0=ALU.max, op1=ALU.add)
-            if i < GP:
-                nc.vector.tensor_scalar(out=fl0[i][:], in0=m_ps[i, 0][:], scalar1=-FLOOR_M, scalar2=16.0, op0=ALU.max, op1=ALU.add)
-                prod[i] = keep.tile([P, T], F32, name="prod%d" % i)
-                nc.gpsimd.tensor_tensor(out=prod[i][:], in0=fl0[i][:], in1=fl1[i][:], op=ALU.mult)
-
-        def multiply(i):
-            if i < GP:
-                return
-            prod[i] = keep.tile([P, T], F32, name="prod%d" % i)
-            nc.vector.scalar_tensor_tensor(out=prod[i][:], in0=fl0[i][:], scalar=FLOOR_A, in1=fl1[i][:], op0=ALU.add, op1=ALU.mult)
-
-        def partition_sum(i):
-            s = slot_of[i, 1]
-            weighted = work.tile([P, T], F32, name="weighted", tag="weighted", bufs=1)
-            nc.vector.scalar_tensor_tensor(out=weighted[:], in0=ex[s][:], scalar=1.0 / T, in1=prod[i][:], op0=ALU.mult, op1=ALU.mult, accum_out=sums[i + SUM_LAG][:, 2:3])
-
-        def take_log(i):
-            logp[i] = work.tile([P, T], F32, name="logp", tag="logp", bufs=8)
-            nc.scalar.activation(out=logp[i][:], in_=prod[i][:], func=ACT.Ln, scale=inv[i + SUM_LAG][:, 2:3])
-
-        def open_total(i):
-            s = slot_of[i, 1]
-            total[i] = psum.tile([P, T], F32, name="xt", tag="xt", bufs=3) if i < 3 else psum.tile([P, T], F32, name="e_ps", tag="e_ps")
-            nc.tensor.matmul(total[i][:], lhsT=neg_ident[:], rhs=neg_n[s][:], start=True, stop=False)
-
-        def close_total(i):
-            nc.tensor.matmul(total[i][:], lhsT=ident[:], rhs=logp[i][:], start=False, stop=True)
+            floored1[i] = work.tile([P, T], F32, name="fl1", tag="fl1")
+            nc.vector.tensor_scalar(
+                out=floored1[i][:], in0=m_ps[i, 1][:], scalar1=-FLOOR_SHIFT, scalar2=16.0, op0=ALU.max, op1=ALU.add,
+            )
 
         def floor_second_scalar(i):
-            cut = work.tile([P, T], F32, name="cut", tag="cut", bufs=1)
-            fl1[i] = work.tile([P, T], F32, name="fl1", tag="fl1")
-            nc.scalar.activation(out=cut[:], in_=m_ps[i, 1][:], func=ACT.Relu, bias=FLOOR_M, scale=1.0)
-            nc.scalar.activation(out=fl1[i][:], in_=cut[:], func=ACT.Identity, bias=FLOOR_A, scale=1.0)
+            cut1 = work.tile([P, T], F32, name="cut", tag="cut", bufs=1)
+            floored1[i] = work.tile([P, T], F32, name="fl1", tag="fl1")
+            nc.scalar.activation(out=cut1[:], in_=m_ps[i, 1][:], func=ACT.Relu, bias=FLOOR_SHIFT, scale=1.0)
+            nc.scalar.activation(out=floored1[i][:], in_=cut1[:], func=ACT.Identity, bias=FLOOR_VALUE, scale=1.0)
 
-        def finish_scalar(i):
-            s = slot_of[i, 1]
-            res = work.tile([P, T], F32, name="res", tag="res", bufs=6)
-            nc.scalar.activation(out=res[:], in_=total[i][:], func=ACT.Identity, bias=neg_max[s][:], scale=1.0)
-            nc.sync.dma_start(out=out[i * P:(i + 1) * P, :], in_=res[:])
+        def multiply(i):
+            product[i] = keep.tile([P, T], F32, name="prod%d" % i)
+            nc.vector.scalar_tensor_tensor(
+                out=product[i][:], in0=cut0[i][:], scalar=FLOOR_VALUE, in1=floored1[i][:], op0=ALU.add, op1=ALU.mult,
+            )
 
-        total = {}
+        def weigh(i):
+            terms = work.tile([P, T], F32, name="weighted", tag="weighted", bufs=1)
+            nc.vector.scalar_tensor_tensor(
+                out=terms[:], in0=expo[unit_of[i, 1]][:], scalar=1.0 / T, in1=product[i][:], op0=ALU.mult, op1=ALU.mult,
+                accum_out=sums[i + SUM_LAG][:, 2:3],
+            )
+
+        def pieces(i):
+            return [slice(0, HALF), slice(HALF, T)] if i == LAST_TILE else [slice(0, T)]
+
+        def take_log(i):
+            for h, cols in enumerate(pieces(i)):
+                log_a[i, h] = work.tile([P, cols.stop - cols.start], F32, name="logp", tag="logp", bufs=TILES + 1)
+                nc.scalar.activation(out=log_a[i, h][:], in_=product[i][:, cols], func=ACT.Ln, scale=inverse[i + SUM_LAG][:, 2:3])
 
         def finish(i):
-            s = slot_of[i, 1]
+            s = unit_of[i, 1]
+            for h, cols in enumerate(pieces(i)):
+                res = work.tile([P, cols.stop - cols.start], F32, name="res", tag="res", bufs=6)
+                nc.vector.scalar_tensor_tensor(
+                    out=res[:], in0=log_a[i, h][:], scalar=neg_max[s][:], in1=neg_n[s][:, cols], op0=ALU.add, op1=ALU.subtract,
+                )
+                nc.sync.dma_start(out=out[i * P:(i + 1) * P, cols], in_=res[:])
+
+        def open_total(i):
+            total[i] = psum.tile([P, T], F32, name="xt", tag="xt", bufs=3)
+            nc.tensor.matmul(total[i][:], lhsT=neg_ident[:], rhs=neg_n[unit_of[i, 1]][:], start=True, stop=False)
+
+        def close_total(i):
+            nc.tensor.matmul(total[i][:], lhsT=ident[:], rhs=log_a[i, 0][:], start=False, stop=True)
+
+        def finish_total(i):
             res = work.tile([P, T], F32, name="res", tag="res", bufs=6)
-            nc.vector.scalar_tensor_tensor(out=res[:], in0=logp[i][:], scalar=neg_max[s][:], in1=neg_n[s][:], op0=ALU.add, op1=ALU.subtract)
+            nc.scalar.activation(out=res[:], in_=total[i][:], func=ACT.Identity, bias=neg_max[unit_of[i, 1]][:], scale=1.0)
             nc.sync.dma_start(out=out[i * P:(i + 1) * P, :], in_=res[:])
 
-        def scale_gain(unused):
-            nc.vector.tensor_scalar(out=gain_wide[:], in0=gain_raw[:], scalar1=float(T), scalar2=None, op0=ALU.mult)
-        def spr(l):
-            neg_bias[l] = spread(l, "neg_bias%d" % l)
-        ST = {"T": turn_x, "E": empty_x, "Q": quantize_x, "M": emit, "A": add_bias, "X": find_max, "P": exponent,
-              "m0": lambda i: message(i, 0), "m1": lambda i: message(i, 1), "TV": turn_v, "EV": empty_v, "QV": quantize_v, "MM": pass_on,
-              "f0": floor_first, "f1": floor_second, "f1s": floor_second_scalar, "pr": multiply, "ps": partition_sum,
-              "inv": lambda i: invert(i, slice(0, 3 if i >= SUM_LAG else 2)), "invl": lambda i: invert(i + SUM_LAG, slice(2, 3)),
-              "ln": take_log, "fin": finish, "op": open_total, "cl": close_total, "fs": finish_scalar,
-              "spr": spr, "sg": scale_gain, "it": interleave_trans, "qt": quantize_trans,
-              "Ws": lambda s: widen(s, range(NVS[s], KBLOCKS), False), "Wv": lambda s: widen(s, range(NVS[s]), True)}
-        for name, a in ORDER:
-            ST[name](a)
+        head = [
+            (widen_scalar, 0), (widen_vector, 0), (widen_vector, 1), (widen_scalar, 1), (spread_bias, 0), (turn_x, 0),
+            (interleave_trans, 0), (empty_x, 0), (quantize_x, 0), (widen_vector, 2), (widen_scalar, 2), (turn_x, 1),
+            (empty_x, 1), (quantize_trans, 0), (quantize_x, 1), (spread_bias, 2), (widen_scalar, 3), (emit, 0),
+            (add_bias, 0), (emit, 1), (widen_scalar, 4), (turn_x, 2), (widen_vector, 3), (find_max, 0),
+            (widen_vector, 4), (empty_x, 2), (add_bias, 1), (turn_x, 3), (interleave_trans, 1), (widen_vector, 5),
+            (quantize_x, 2), (exponent, 0), (scale_gain, 0), (empty_x, 3), (widen_scalar, 5), (turn_x, 4), (emit, 2),
+            (find_max, 1),
+        ]
+        for step, index in head:
+            step(index)
+
+        def for_tile(s, lag, step):
+            if s - lag >= 0 and units[s - lag][1] == 2:
+                step(units[s - lag][0])
+
+        quantize_trans(1)
+        for s in range(FIRST_SLOT, END_SLOT):
+            turn_x(s + 3)
+            for_tile(s, 4, turn_v)
+            quantize_x(s + 1)
+            emit(s + 1)
+            for_tile(s, 5, pass_on)
+
+            widen_scalar(s + 4)
+            empty_x(s + 2)
+            for_tile(s, 4, empty_v)
+            if paired(s - 1):
+                if units[s - 1][1] == 2:
+                    exponent(s - 2)
+                    exponent(s - 1)
+            else:
+                exponent(s - 1)
+            for_tile(s, 6, floor_first)
+
+            if VECTOR_BLOCKS[s + 4] > 0:
+                widen_vector(s + 4)
+            for_tile(s, 2, invert_sums)
+            add_bias(s)
+            for_tile(s, 6, floor_second)
+            for_tile(s, 7, multiply)
+            for_tile(s, 3, message_second)
+            for_tile(s, 2, message_first)
+            if not (paired(s) and units[s][1] == 0):
+                find_max(s)
+            for_tile(s, 7, weigh)
+
+        tail = [
+            (turn_x, 22), (empty_x, 21), (add_bias, 19), (turn_v, 5), (quantize_x, 20), (widen_scalar, 23),
+            (emit, 20), (multiply, 4), (empty_v, 5), (exponent, 17), (find_max, 19), (turn_x, 23), (quantize_x, 21),
+            (add_bias, 20), (pass_on, 5), (emit, 21), (exponent, 18), (empty_x, 23), (invert_sums, 6),
+            (message_first, 6), (message_second, 6), (exponent, 19), (empty_x, 22), (turn_v, 6), (quantize_x, 23),
+            (add_bias, 21), (quantize_x, 22), (find_max, 21), (emit, 23), (add_bias, 23), (emit, 22), (add_bias, 22),
+            (floor_second_scalar, 5), (empty_v, 6), (floor_first, 5), (open_total, 1), (exponent, 21), (exponent, 20),
+            (find_max, 23), (find_max, 22), (weigh, 4), (multiply, 5), (invert_sums, 7), (exponent, 23),
+            (quantize_v, 6), (open_total, 0), (exponent, 22), (pass_on, 6), (take_log, 0), (weigh, 5),
+            (message_first, 7), (floor_first, 6), (take_log, 2), (message_second, 7), (turn_v, 7), (floor_second, 6),
+            (close_total, 0), (invert_weight, 5), (take_log, 1), (multiply, 6), (finish, 2), (empty_v, 7),
+            (quantize_v, 7), (weigh, 6), (take_log, 5), (take_log, 4), (finish, 5), (pass_on, 7), (floor_first, 7),
+            (floor_second, 7), (close_total, 1), (finish_total, 0), (invert_weight, 6), (finish_total, 1),
+            (multiply, 7), (finish, 4), (take_log, 6), (weigh, 7), (finish, 6), (take_log, 3), (invert_weight, 7),
+            (finish, 3), (take_log, 7), (finish, 7),
+        ]
+        for step, index in tail:
+            step(index)

@@ -22,31 +22,22 @@ P = 128
 TILES = B // P
 LAST_TILE = TILES - 1
 PASSES = D // 512
-SCALE_BLOCKS = D // 128
+QUADS = 4
 PASS_WORDS = 256
 HALF = T // 2
 
 FLOOR_SHIFT = 14.4
 FLOOR_VALUE = 1.6
 
-VECTOR_BLOCKS = [3, 4, 3, 3] + [2] * 12 + [1] * 4 + [0] * 4
-
-SUM_LAG = 3
-RIDE = 6
-FIRST_SLOT, END_SLOT = 2, 19
+VECTOR_EMPTIES = 1
+VECTOR_HALVES = (2, 4)
 
 
 def tile_chunkflooredmessagemiddlescore_kernel(tc, x_bytes, x_scale, we_words, we_scales, be, ends, gain, trans, out):
     nc = tc.nc
 
-    units = []
-    for i in range(TILES + 1):
-        if i < TILES:
-            units += [(i, 0), (i, 2)]
-        if i >= 1:
-            units += [(i - 1, 1)]
+    units = [(i, l) for i in range(TILES) for l in (0, 2, 1)]
     unit_of = {u: s for s, u in enumerate(units)}
-    n_units = len(units)
 
     with ExitStack() as ctx:
         keep = ctx.enter_context(tc.tile_pool(name="keep", bufs=1))
@@ -56,67 +47,71 @@ def tile_chunkflooredmessagemiddlescore_kernel(tc, x_bytes, x_scale, we_words, w
 
         rows = keep.tile([P, T], BF16, name="rows")
         be_wide = keep.tile([P, T], BF16, name="be_wide")
+        pick = keep.tile([P, 2 * L], BF16, name="pick")
         gain_raw = keep.tile([P, PAIRS * T], BF16, name="gain_raw")
         gain_wide = keep.tile([P, PAIRS * T], BF16, name="gain_wide")
         we_s = keep.tile([P, PASSES, T], U8, name="we_s", align_bytes=64)
         we_w = keep.tile([P, PASSES, 2 * T], U8, name="we_w", align_bytes=64)
-        xs = keep.tile([P, L * TILES * SCALE_BLOCKS], F32, name="xs")
+        xs_all = keep.tile([P, L * TILES * PASSES, QUADS], F32, name="xs_all")
+        xs = keep.tile([P, L * TILES * PASSES], F32, name="xs")
         ident = keep.tile([P, P], F32, name="ident")
-        pick = keep.tile([P, 4], BF16, name="pick")
         nc.vector.memset(rows[:].bitcast(I32), 0)
         nc.vector.memset(we_s[:].rearrange("p g n -> p (g n)").bitcast(I32), 0)
 
         x_raw, trans_raw = {}, {}
 
-        def load_x(s):
-            i, l = units[s]
-            x_raw[s] = keep.tile([P, D], U8, name="xbytes%d" % s)
-            nc.sync.dma_start(out=x_raw[s][:], in_=x_bytes[l, i * P:(i + 1) * P, :])
+        def load_x(i, positions):
+            found = list(range(L))[positions]
+            raw = keep.tile([P, len(found), D], U8, name="xbytes%d_%d" % (i, found[0]))
+            nc.sync.dma_start(out=raw[:], in_=x_bytes[positions, i * P:(i + 1) * P, :].rearrange("l r k -> r l k"))
+            for j, l in enumerate(found):
+                x_raw[unit_of[i, l]] = raw[:, j, :]
 
         def load_trans(p):
             trans_raw[p] = keep.tile([P, 4, T], BF16, name="tr_raw%d" % p)
             nc.sync.dma_start(out=trans_raw[p][:], in_=trans[p].rearrange("(p j) n -> p j n", j=4))
 
-        nc.scalar.dma_start(out=xs[:], in_=x_scale.rearrange("l i j -> (l i j)").partition_broadcast(P))
-        load_x(0)
-        load_x(1)
+        nc.scalar.dma_start(out=xs_all[:].rearrange("p c q -> p (c q)"), in_=x_scale.rearrange("l i j -> (l i j)").partition_broadcast(P))
+        load_x(0, slice(0, 1))
         nc.sync.dma_start(out=rows[0:1, :], in_=be.rearrange("(o n) -> o n", o=1))
         nc.sync.dma_start(out=rows[32:65:32, :], in_=ends)
-        load_trans(0)
-        load_x(2)
+        load_x(0, slice(2, 3))
+        load_x(1, slice(0, 3, 2))
         nc.sync.dma_start(out=we_w[:].bitcast(I32), in_=we_words.rearrange("g p n -> p g n").bitcast(I32))
+        load_trans(0)
         for q in range(4):
             nc.sync.dma_start(
                 out=we_s[32 * q:32 * q + 4, :, :].bitcast(I32),
                 in_=we_scales[:, 4 * q:4 * q + 4, :].rearrange("g r n -> r g n").bitcast(I32),
             )
-        load_x(3)
+        load_x(0, slice(1, 2))
         nc.sync.dma_start(out=gain_raw[:], in_=gain.rearrange("a n -> (a n)").partition_broadcast(P))
-        load_x(4)
         load_trans(1)
-        load_x(5)
+        load_x(2, slice(0, 3))
         nc.sync.dma_start(out=be_wide[:], in_=be.partition_broadcast(P))
-        for s in range(6, n_units):
-            load_x(s)
+        load_x(1, slice(1, 2))
+        for i in range(3, TILES):
+            load_x(i, slice(0, 3))
 
         nc.gpsimd.memset(pick[:], 0.0)
         nc.gpsimd.memset(pick[0:1, :], -1.0)
         nc.gpsimd.memset(pick[32:33, 0:2], -1.0)
-        nc.gpsimd.memset(pick[64:65, 2:4], -1.0)
+        nc.gpsimd.memset(pick[64:65, 4:6], -1.0)
         make_identity(nc, ident[:])
-        neg_ident = keep.tile([P, P], F32, name="neg_ident")
-        nc.gpsimd.tensor_scalar(out=neg_ident[:], in0=ident[:], scalar1=-1.0, scalar2=0.0, op0=ALU.mult, op1=ALU.add)
+
+        for q in range(QUADS):
+            nc.vector.tensor_copy(out=xs[32 * q:32 * q + 32, :], in_=xs_all[32 * q:32 * q + 32, :, q])
 
         neg_bias = {}
 
         def spread_bias(l):
-            acc = psum.tile([P, T], F32, name="m_ps", tag="m_ps")
-            nc.tensor.matmul(acc[:], lhsT=pick[:, l:l + 1].to_broadcast([P, P]), rhs=rows[:], start=True, stop=True)
+            acc = psum.tile([P, T], F32, name="sum_ps", tag="sum_ps", bufs=5)
+            nc.tensor.matmul(acc[:], lhsT=pick[:, 2 * l:2 * l + 1].to_broadcast([P, P]), rhs=rows[:], start=True, stop=True)
             neg_bias[l] = keep.tile([P, T], F32, name="neg_bias%d" % l)
-            nc.scalar.copy(out=neg_bias[l][:], in_=acc[:])
+            nc.vector.tensor_copy(out=neg_bias[l][:], in_=acc[:])
 
-        def scale_gain(p):
-            nc.vector.tensor_scalar(out=gain_wide[:, p * T:], in0=gain_raw[:, p * T:], scalar1=float(T), scalar2=None, op0=ALU.mult)
+        def scale_gain():
+            nc.vector.tensor_scalar(out=gain_wide[:], in0=gain_raw[:], scalar1=float(T), scalar2=None, op0=ALU.mult)
 
         trans_grouped = {}
         trans_codes = keep.tile([P, PAIRS, T], U32, name="tr_codes", align_bytes=64)
@@ -136,31 +131,15 @@ def tile_chunkflooredmessagemiddlescore_kernel(tc, x_bytes, x_scale, we_words, w
             )
 
         x_wide, x_turned, grouped, x_codes, x_scales, e_ps = {}, {}, {}, {}, {}, {}
-        neg_pair, neg_n, neg_max, expo = {}, {}, {}, {}
-        sums = [keep.tile([P, 3], F32, name="sums%d" % i) for i in range(TILES + SUM_LAG)]
-        inverse = [keep.tile([P, 3], F32, name="inv%d" % i) for i in range(TILES + SUM_LAG)]
-        rider = {unit_of[i, 2] + RIDE: i for i in range(TILES) if unit_of[i, 2] + RIDE < n_units}
-        carrier = {i: s for s, i in rider.items()}
-        v_codes, v_scales = {}, {}
+        neg_n, neg_max, expo = {}, {}, {}
+        sums = [keep.tile([P, PAIRS], F32, name="sums%d" % i) for i in range(TILES)]
+        inverse = [keep.tile([P, PAIRS], F32, name="inv%d" % i) for i in range(TILES)]
+        weight = keep.tile([P, TILES], F32, name="weight")
+        inv_weight = keep.tile([P, TILES], F32, name="inv_weight")
 
-        def wide_blocks(s, blocks):
-            i, l = units[s]
-            if s not in x_wide:
-                x_wide[s] = work.tile([P, D], BF16, name="xw", tag="xw")
-            found = []
-            for j in blocks:
-                cols = slice(j * 128, (j + 1) * 128)
-                c = (l * TILES + i) * SCALE_BLOCKS + j
-                found.append((x_raw[s][:, cols].bitcast(FP8), x_wide[s][:, cols], xs[:, c:c + 1]))
-            return found
-
-        def widen_vector(s):
-            for src, dst, scale in wide_blocks(s, range(VECTOR_BLOCKS[s])):
-                nc.vector.tensor_scalar(out=dst, in0=src, scalar1=scale, scalar2=None, op0=ALU.mult)
-
-        def widen_scalar(s):
-            for src, dst, scale in wide_blocks(s, range(VECTOR_BLOCKS[s], SCALE_BLOCKS)):
-                nc.scalar.activation(out=dst, in_=src, func=ACT.Copy, scale=scale)
+        def widen(s):
+            x_wide[s] = work.tile([P, D], BF16, name="xw", tag="xw")
+            nc.scalar.copy(out=x_wide[s][:], in_=x_raw[s].bitcast(FP8))
 
         def turn(bank, values):
             words = values.bitcast(F32)
@@ -172,28 +151,39 @@ def tile_chunkflooredmessagemiddlescore_kernel(tc, x_bytes, x_scale, we_words, w
             x_turned[s] = psum.tile([P, PASSES, 2, P], F32, name="xt", tag="xt", bufs=3)
             turn(x_turned[s], x_wide[s][:])
 
-        def grouped_of(s):
-            if s not in grouped:
-                grouped[s] = work.tile([P, 4 if s in rider else 2, P, 2], F32, name="xg", tag="xg", align_bytes=64)
-            return grouped[s]
+        def vector_passes(s):
+            return PASSES if s < VECTOR_EMPTIES else (1 if units[s][1] == 1 and units[s][0] in VECTOR_HALVES else 0)
 
-        def empty_x(s):
-            nc.scalar.copy(out=grouped_of(s)[:, 0:2], in_=x_turned[s][:].rearrange("p g u r -> p g r u"))
+        def scaled_passes(s, passes):
+            i, l = units[s]
+            if s not in grouped:
+                grouped[s] = work.tile([P, PASSES, P, 4], BF16, name="xg", tag="xg", align_bytes=64)
+            found = []
+            for g in passes:
+                src = x_turned[s][:, g].rearrange("p u r -> p (u r)").bitcast(BF16).rearrange("p (u r e) -> p r u e", u=2, e=2)
+                dst = grouped[s][:, g].rearrange("p r (u e) -> p r u e", u=2)
+                c = (l * TILES + i) * PASSES + g
+                found.append((src, dst, xs[:, c:c + 1]))
+            return found
+
+        def empty_vector(s):
+            for src, dst, scale in scaled_passes(s, range(PASSES - vector_passes(s), PASSES)):
+                nc.vector.tensor_scalar(out=dst, in0=src, scalar1=scale, scalar2=None, op0=ALU.mult)
+
+        def empty_scalar(s):
+            for src, dst, scale in scaled_passes(s, range(PASSES - vector_passes(s))):
+                nc.scalar.activation(out=dst, in_=src, func=ACT.Copy, scale=scale)
 
         def quantize_x(s):
-            width = (4 if s in rider else 2) * P
-            x_codes[s] = work.tile([P, width], U32, name="xq", tag="xq", align_bytes=64)
-            x_scales[s] = work.tile([P, width], U8, name="xqs", tag="xqs", align_bytes=64)
+            x_codes[s] = work.tile([P, PASSES * P], U32, name="xq", tag="xq", align_bytes=64)
+            x_scales[s] = work.tile([P, PASSES * P], U8, name="xqs", tag="xqs", align_bytes=64)
             nc.vector.quantize_mx(
                 out=x_codes[s][:].bitcast(FP8X4), scales=x_scales[s][:],
-                in_=grouped[s][:].rearrange("p g r u -> p (g r u)").bitcast(BF16),
+                in_=grouped[s][:].rearrange("p g r t -> p (g r t)"),
             )
-            if s in rider:
-                v_codes[rider[s]] = x_codes[s][:, 2 * P:]
-                v_scales[rider[s]] = x_scales[s][:, 2 * P:]
 
         def emit(s):
-            e_ps[s] = psum.tile([P, T], F32, name="e_ps", tag="e_ps")
+            e_ps[s] = psum.tile([P, T], F32, name="sum_ps", tag="sum_ps", bufs=5)
             for g in range(PASSES):
                 cols = slice(g * P, (g + 1) * P)
                 nc.tensor.matmul_mx(
@@ -205,49 +195,35 @@ def tile_chunkflooredmessagemiddlescore_kernel(tc, x_bytes, x_scale, we_words, w
             i, l = units[s]
             if l == 1:
                 neg_n[s] = keep.tile([P, T], F32, name="neg_mid%d" % i)
+            else:
+                neg_n[s] = work.tile([P, T], F32, name="neg_end", tag="neg_end")
+            if l == 1:
                 nc.vector.scalar_tensor_tensor(
                     out=neg_n[s][:], in0=e_ps[s][:], scalar=-1.0, in1=be_wide[:], op0=ALU.mult, op1=ALU.subtract,
                 )
             else:
-                if l == 0:
-                    neg_pair[i] = work.tile([P, PAIRS, T], F32, name="neg_pair", tag="neg_pair", bufs=3)
-                neg_n[s] = neg_pair[i][:, l // 2, :]
                 nc.vector.tensor_tensor(out=neg_n[s][:], in0=neg_bias[l][:], in1=e_ps[s][:], op=ALU.subtract)
 
-        def paired(s):
-            i, l = units[s]
-            return l != 1 and i >= 1
-
         def find_max(s):
-            if paired(s):
-                both = keep.tile([P, 2], F32, name="neg_max%d" % s)
-                nc.vector.tensor_reduce(out=both[:], in_=neg_pair[units[s][0]][:], axis=AX.X, op=ALU.min)
-                neg_max[s - 1] = both[:, 0:1]
-                neg_max[s] = both[:, 1:2]
-            else:
-                neg_max[s] = keep.tile([P, 1], F32, name="neg_max%d" % s)
-                nc.vector.tensor_reduce(out=neg_max[s][:], in_=neg_n[s][:], axis=AX.X, op=ALU.min)
+            neg_max[s] = keep.tile([P, 1], F32, name="neg_max%d" % s)
+            nc.vector.tensor_reduce(out=neg_max[s][:], in_=neg_n[s][:], axis=AX.X, op=ALU.min)
 
         def exponent(s):
             i, l = units[s]
             if l == 1:
-                expo[s] = work.tile([P, T], F32, name="ex_mid", tag="ex_mid")
+                expo[s] = work.tile([P, T], F32, name="ex_mid", tag="ex_mid", bufs=4)
                 nc.scalar.activation(out=expo[s][:], in_=neg_n[s][:], func=ACT.Exp, bias=neg_max[s][:], scale=-1.0)
             else:
-                expo[s] = work.tile([P, T], F32, name="ex", tag="ex", bufs=6)
+                expo[s] = work.tile([P, T], F32, name="ex", tag="ex", bufs=8)
                 nc.scalar.activation(
                     out=expo[s][:], in_=neg_n[s][:], func=ACT.Exp, bias=neg_max[s][:], scale=-1.0,
                     accum_out=sums[i][:, l // 2:l // 2 + 1],
                 )
 
-        v, v_turned, v_grouped, m_ps, cut0, floored1, product, log_a, total = {}, {}, {}, {}, {}, {}, {}, {}, {}
+        v, v_turned, v_grouped, v_codes, v_scales, m_ps, cut0, floored1, product, log_a = {}, {}, {}, {}, {}, {}, {}, {}, {}, {}
 
         def invert_sums(i):
-            cols = slice(0, 3 if i >= SUM_LAG else 2)
-            nc.vector.reciprocal(out=inverse[i][:, cols], in_=sums[i][:, cols])
-
-        def invert_weight(i):
-            nc.vector.reciprocal(out=inverse[i + SUM_LAG][:, 2:3], in_=sums[i + SUM_LAG][:, 2:3])
+            nc.vector.reciprocal(out=inverse[i][:], in_=sums[i][:])
 
         def message(i, p):
             nc.vector.scalar_tensor_tensor(
@@ -256,27 +232,23 @@ def tile_chunkflooredmessagemiddlescore_kernel(tc, x_bytes, x_scale, we_words, w
             )
 
         def message_first(i):
-            v[i] = work.tile([P, PAIRS, T], BF16, name="v", tag="v")
+            v[i] = work.tile([P, PAIRS, T], BF16, name="v", tag="v", bufs=2)
             message(i, 0)
 
         def message_second(i):
             message(i, 1)
 
         def turn_v(i):
-            v_turned[i] = psum.tile([P, PAIRS, 2, P], F32, name="vt", tag="vt", bufs=1)
+            v_turned[i] = psum.tile([P, PAIRS, 2, P], F32, name="xt", tag="xt", bufs=3)
             turn(v_turned[i], v[i][:].rearrange("p a n -> p (a n)"))
 
         def empty_v(i):
-            if i in carrier:
-                dst = grouped_of(carrier[i])[:, 2:4]
-            else:
-                v_grouped[i] = work.tile([P, PAIRS, P, 2], F32, name="vg", tag="vg", bufs=2, align_bytes=64)
-                dst = v_grouped[i][:]
-            nc.scalar.copy(out=dst, in_=v_turned[i][:].rearrange("p g u r -> p g r u"))
+            v_grouped[i] = work.tile([P, PAIRS, P, 2], F32, name="vg", tag="vg", bufs=2, align_bytes=64)
+            nc.scalar.copy(out=v_grouped[i][:], in_=v_turned[i][:].rearrange("p g u r -> p g r u"))
 
         def quantize_v(i):
-            v_codes[i] = work.tile([P, PAIRS * P], U32, name="vq", tag="vq", align_bytes=64)
-            v_scales[i] = work.tile([P, PAIRS * P], U8, name="vqs", tag="vqs", align_bytes=64)
+            v_codes[i] = work.tile([P, PAIRS * P], U32, name="vq", tag="vq", bufs=2, align_bytes=64)
+            v_scales[i] = work.tile([P, PAIRS * P], U8, name="vqs", tag="vqs", bufs=2, align_bytes=64)
             nc.vector.quantize_mx(
                 out=v_codes[i][:].bitcast(FP8X4), scales=v_scales[i][:],
                 in_=v_grouped[i][:].rearrange("p g r u -> p (g r u)").bitcast(BF16),
@@ -285,27 +257,21 @@ def tile_chunkflooredmessagemiddlescore_kernel(tc, x_bytes, x_scale, we_words, w
         def pass_on(i):
             for p in range(PAIRS):
                 cols = slice(p * P, (p + 1) * P)
-                m_ps[i, p] = psum.tile([P, T], F32, name="m_ps", tag="m_ps")
+                m_ps[i, p] = psum.tile([P, T], F32, name="sum_ps", tag="sum_ps", bufs=5)
                 nc.tensor.matmul_mx(
                     out=m_ps[i, p][:], lhsT=v_codes[i][:, cols].bitcast(FP8X4), lhsT_scale=v_scales[i][:, cols],
                     rhs=trans_codes[:, p, :].bitcast(FP8X4), rhs_scale=trans_scales[:, p, :], start=True, stop=True,
                 )
 
         def floor_first(i):
-            cut0[i] = work.tile([P, T], F32, name="fl0", tag="fl0")
+            cut0[i] = work.tile([P, T], F32, name="fl0", tag="fl0", bufs=2)
             nc.scalar.activation(out=cut0[i][:], in_=m_ps[i, 0][:], func=ACT.Relu, bias=FLOOR_SHIFT, scale=1.0)
 
         def floor_second(i):
-            floored1[i] = work.tile([P, T], F32, name="fl1", tag="fl1")
+            floored1[i] = work.tile([P, T], F32, name="fl1", tag="fl1", bufs=2)
             nc.vector.tensor_scalar(
                 out=floored1[i][:], in0=m_ps[i, 1][:], scalar1=-FLOOR_SHIFT, scalar2=16.0, op0=ALU.max, op1=ALU.add,
             )
-
-        def floor_second_scalar(i):
-            cut1 = work.tile([P, T], F32, name="cut", tag="cut", bufs=1)
-            floored1[i] = work.tile([P, T], F32, name="fl1", tag="fl1")
-            nc.scalar.activation(out=cut1[:], in_=m_ps[i, 1][:], func=ACT.Relu, bias=FLOOR_SHIFT, scale=1.0)
-            nc.scalar.activation(out=floored1[i][:], in_=cut1[:], func=ACT.Identity, bias=FLOOR_VALUE, scale=1.0)
 
         def multiply(i):
             product[i] = keep.tile([P, T], F32, name="prod%d" % i)
@@ -317,8 +283,11 @@ def tile_chunkflooredmessagemiddlescore_kernel(tc, x_bytes, x_scale, we_words, w
             terms = work.tile([P, T], F32, name="weighted", tag="weighted", bufs=1)
             nc.vector.scalar_tensor_tensor(
                 out=terms[:], in0=expo[unit_of[i, 1]][:], scalar=1.0 / T, in1=product[i][:], op0=ALU.mult, op1=ALU.mult,
-                accum_out=sums[i + SUM_LAG][:, 2:3],
+                accum_out=weight[:, i:i + 1],
             )
+
+        def invert_weights(first, end):
+            nc.vector.reciprocal(out=inv_weight[:, first:end], in_=weight[:, first:end])
 
         def pieces(i):
             return [slice(0, HALF), slice(HALF, T)] if i == LAST_TILE else [slice(0, T)]
@@ -326,91 +295,140 @@ def tile_chunkflooredmessagemiddlescore_kernel(tc, x_bytes, x_scale, we_words, w
         def take_log(i):
             for h, cols in enumerate(pieces(i)):
                 log_a[i, h] = work.tile([P, cols.stop - cols.start], F32, name="logp", tag="logp", bufs=TILES + 1)
-                nc.scalar.activation(out=log_a[i, h][:], in_=product[i][:, cols], func=ACT.Ln, scale=inverse[i + SUM_LAG][:, 2:3])
+                nc.scalar.activation(out=log_a[i, h][:], in_=product[i][:, cols], func=ACT.Ln, scale=inv_weight[:, i:i + 1])
 
         def finish(i):
             s = unit_of[i, 1]
             for h, cols in enumerate(pieces(i)):
-                res = work.tile([P, cols.stop - cols.start], F32, name="res", tag="res", bufs=6)
+                res = work.tile([P, cols.stop - cols.start], F32, name="res", tag="res", bufs=TILES + 1)
                 nc.vector.scalar_tensor_tensor(
                     out=res[:], in0=log_a[i, h][:], scalar=neg_max[s][:], in1=neg_n[s][:, cols], op0=ALU.add, op1=ALU.subtract,
                 )
                 nc.sync.dma_start(out=out[i * P:(i + 1) * P, cols], in_=res[:])
 
-        def open_total(i):
-            total[i] = psum.tile([P, T], F32, name="xt", tag="xt", bufs=3)
-            nc.tensor.matmul(total[i][:], lhsT=neg_ident[:], rhs=neg_n[unit_of[i, 1]][:], start=True, stop=False)
+        def on_unit(step, i, l):
+            if 0 <= i < TILES:
+                step(unit_of[i, l])
 
-        def close_total(i):
-            nc.tensor.matmul(total[i][:], lhsT=ident[:], rhs=log_a[i, 0][:], start=False, stop=True)
+        def on_tile(step, i, otherwise=None):
+            if 0 <= i < TILES:
+                step(i)
+            elif i < 0 and otherwise is not None and i in otherwise:
+                otherwise[i]()
 
-        def finish_total(i):
-            res = work.tile([P, T], F32, name="res", tag="res", bufs=6)
-            nc.scalar.activation(out=res[:], in_=total[i][:], func=ACT.Identity, bias=neg_max[unit_of[i, 1]][:], scale=1.0)
-            nc.sync.dma_start(out=out[i * P:(i + 1) * P, :], in_=res[:])
+        def quantize_and_emit(s):
+            quantize_x(s)
+            emit(s)
 
-        head = [
-            (widen_scalar, 0), (widen_vector, 0), (widen_vector, 1), (widen_scalar, 1), (spread_bias, 0), (turn_x, 0),
-            (interleave_trans, 0), (empty_x, 0), (quantize_x, 0), (widen_vector, 2), (widen_scalar, 2), (turn_x, 1),
-            (empty_x, 1), (quantize_trans, 0), (quantize_x, 1), (spread_bias, 2), (widen_scalar, 3), (emit, 0),
-            (add_bias, 0), (emit, 1), (widen_scalar, 4), (turn_x, 2), (widen_vector, 3), (find_max, 0),
-            (widen_vector, 4), (empty_x, 2), (add_bias, 1), (turn_x, 3), (interleave_trans, 1), (widen_vector, 5),
-            (quantize_x, 2), (exponent, 0), (scale_gain, 0), (empty_x, 3), (widen_scalar, 5), (turn_x, 4), (emit, 2),
-            (find_max, 1),
-        ]
-        for step, index in head:
-            step(index)
+        def quantize_and_pass_on(i):
+            quantize_v(i)
+            pass_on(i)
 
-        def for_tile(s, lag, step):
-            if s - lag >= 0 and units[s - lag][1] == 2:
-                step(units[s - lag][0])
+        spread_bias(0)
+        spread_bias(2)
+        for k in range(-2, LAST_TILE):
+            on_unit(empty_scalar, k, 2)
+            on_unit(quantize_and_emit, k, 0)
+            on_tile(invert_sums, k - 1)
+            on_unit(find_max, k - 2, 1)
+            on_tile(floor_first, k - 2)
+            on_tile(message_first, k - 1, {-1: lambda: interleave_trans(0)})
+            on_tile(message_second, k - 1)
+            on_unit(exponent, k - 2, 1)
+            on_tile(turn_v, k - 1)
 
-        quantize_trans(1)
-        for s in range(FIRST_SLOT, END_SLOT):
-            turn_x(s + 3)
-            for_tile(s, 4, turn_v)
-            quantize_x(s + 1)
-            emit(s + 1)
-            for_tile(s, 5, pass_on)
+            on_unit(quantize_and_emit, k, 2)
+            on_unit(empty_scalar, k - 1, 1)
+            on_unit(add_bias, k, 0)
+            on_tile(floor_second, k - 2, {-2: lambda: quantize_trans(0)})
+            on_unit(empty_vector, k - 1, 1)
+            on_unit(turn_x, k + 1, 0)
+            on_tile(empty_v, k - 1)
+            on_unit(find_max, k, 0)
+            on_unit(widen, k + 1, 2)
 
-            widen_scalar(s + 4)
-            empty_x(s + 2)
-            for_tile(s, 4, empty_v)
-            if paired(s - 1):
-                if units[s - 1][1] == 2:
-                    exponent(s - 2)
-                    exponent(s - 1)
-            else:
-                exponent(s - 1)
-            for_tile(s, 6, floor_first)
+            on_unit(quantize_and_emit, k - 1, 1)
+            on_unit(widen, k, 1)
+            on_unit(add_bias, k, 2)
+            on_tile(multiply, k - 2, {-2: scale_gain, -1: lambda: interleave_trans(1)})
+            on_unit(turn_x, k + 1, 2)
+            on_unit(empty_scalar, k + 1, 0)
+            on_unit(exponent, k, 0)
+            on_unit(empty_vector, k + 1, 0)
+            on_unit(find_max, k, 2)
 
-            if VECTOR_BLOCKS[s + 4] > 0:
-                widen_vector(s + 4)
-            for_tile(s, 2, invert_sums)
-            add_bias(s)
-            for_tile(s, 6, floor_second)
-            for_tile(s, 7, multiply)
-            for_tile(s, 3, message_second)
-            for_tile(s, 2, message_first)
-            if not (paired(s) and units[s][1] == 0):
-                find_max(s)
-            for_tile(s, 7, weigh)
+            if k == 1:
+                quantize_trans(1)
+            on_tile(quantize_and_pass_on, k - 1)
+            on_unit(add_bias, k - 1, 1)
+            on_unit(exponent, k, 2)
+            on_unit(empty_vector, k + 1, 2)
+            on_tile(weigh, k - 2)
+            on_unit(turn_x, k, 1)
+            on_unit(widen, k + 2, 0)
 
-        tail = [
-            (turn_x, 22), (empty_x, 21), (add_bias, 19), (turn_v, 5), (quantize_x, 20), (widen_scalar, 23),
-            (emit, 20), (multiply, 4), (empty_v, 5), (exponent, 17), (find_max, 19), (turn_x, 23), (quantize_x, 21),
-            (add_bias, 20), (pass_on, 5), (emit, 21), (exponent, 18), (empty_x, 23), (invert_sums, 6),
-            (message_first, 6), (message_second, 6), (exponent, 19), (empty_x, 22), (turn_v, 6), (quantize_x, 23),
-            (add_bias, 21), (quantize_x, 22), (find_max, 21), (emit, 23), (add_bias, 23), (emit, 22), (add_bias, 22),
-            (floor_second_scalar, 5), (empty_v, 6), (floor_first, 5), (open_total, 1), (exponent, 21), (exponent, 20),
-            (find_max, 23), (find_max, 22), (weigh, 4), (multiply, 5), (invert_sums, 7), (exponent, 23),
-            (quantize_v, 6), (open_total, 0), (exponent, 22), (pass_on, 6), (take_log, 0), (weigh, 5),
-            (message_first, 7), (floor_first, 6), (take_log, 2), (message_second, 7), (turn_v, 7), (floor_second, 6),
-            (close_total, 0), (invert_weight, 5), (take_log, 1), (multiply, 6), (finish, 2), (empty_v, 7),
-            (quantize_v, 7), (weigh, 6), (take_log, 5), (take_log, 4), (finish, 5), (pass_on, 7), (floor_first, 7),
-            (floor_second, 7), (close_total, 1), (finish_total, 0), (invert_weight, 6), (finish_total, 1),
-            (multiply, 7), (finish, 4), (take_log, 6), (weigh, 7), (finish, 6), (take_log, 3), (invert_weight, 7),
-            (finish, 3), (take_log, 7), (finish, 7),
-        ]
-        for step, index in tail:
-            step(index)
+        last = LAST_TILE
+        first_end, second_end, middle = unit_of[last, 0], unit_of[last, 2], unit_of[last, 1]
+        middle_1, middle_2 = unit_of[last - 1, 1], unit_of[last - 2, 1]
+        empty_scalar(second_end)
+        quantize_and_emit(first_end)
+        invert_sums(last - 1)
+        find_max(middle_2)
+        widen(middle)
+        message_first(last - 1)
+        quantize_and_emit(second_end)
+        empty_scalar(middle_1)
+        turn_x(middle)
+        add_bias(first_end)
+        message_second(last - 1)
+        turn_v(last - 1)
+        floor_first(last - 2)
+        exponent(middle_2)
+        find_max(first_end)
+        quantize_and_emit(middle_1)
+        add_bias(second_end)
+        exponent(first_end)
+        empty_v(last - 1)
+        floor_second(last - 2)
+        find_max(second_end)
+        empty_scalar(middle)
+        quantize_and_pass_on(last - 1)
+        add_bias(middle_1)
+        exponent(second_end)
+        quantize_and_emit(middle)
+        find_max(middle_1)
+        invert_sums(last)
+        floor_first(last - 1)
+        multiply(last - 2)
+        message_first(last)
+        exponent(middle_1)
+        add_bias(middle)
+        message_second(last)
+        turn_v(last)
+        find_max(middle)
+        invert_weights(0, last - 2)
+        floor_second(last - 1)
+        exponent(middle)
+        empty_v(last)
+        weigh(last - 2)
+        quantize_and_pass_on(last)
+        take_log(0)
+        multiply(last - 1)
+        invert_weights(last - 2, last - 1)
+        weigh(last - 1)
+        floor_second(last)
+        floor_first(last)
+        finish(0)
+        invert_weights(last - 1, last)
+        take_log(1)
+        multiply(last)
+        take_log(2)
+        finish(1)
+        weigh(last)
+        take_log(3)
+        finish(2)
+        invert_weights(last, TILES)
+        for i in range(4, TILES):
+            take_log(i)
+            finish(i - 1)
+        finish(last)

@@ -29,8 +29,11 @@ HALF = T // 2
 FLOOR_SHIFT = 14.4
 FLOOR_VALUE = 1.6
 
+TURN_BANK = {0: 0, 2: 1, 1: 2}
+SCORE_BANK = {0: 3, 2: 4, 1: 5}
+MESSAGE_BANKS = (6, 7)
 VECTOR_EMPTIES = 1
-VECTOR_HALVES = (2, 4)
+VECTOR_HALVES = (1, 2, 3, 4, 5)
 
 
 def tile_chunkflooredmessagemiddlescore_kernel(tc, x_bytes, x_scale, we_words, we_scales, be, ends, gain, trans, out):
@@ -42,7 +45,7 @@ def tile_chunkflooredmessagemiddlescore_kernel(tc, x_bytes, x_scale, we_words, w
     with ExitStack() as ctx:
         keep = ctx.enter_context(tc.tile_pool(name="keep", bufs=1))
         work = ctx.enter_context(tc.tile_pool(name="work", bufs=4))
-        psum = ctx.enter_context(tc.psum_pool(name="psum", bufs=2))
+        psum = ctx.enter_context(tc.psum_pool(name="psum", bufs=1))
         ctx.enter_context(tc.manual_schedule())
 
         rows = keep.tile([P, T], BF16, name="rows")
@@ -98,14 +101,19 @@ def tile_chunkflooredmessagemiddlescore_kernel(tc, x_bytes, x_scale, we_words, w
         nc.gpsimd.memset(pick[32:33, 0:2], -1.0)
         nc.gpsimd.memset(pick[64:65, 4:6], -1.0)
         make_identity(nc, ident[:])
+        neg_ident = keep.tile([P, P], F32, name="neg_ident")
+        nc.gpsimd.tensor_scalar(out=neg_ident[:], in0=ident[:], scalar1=-1.0, scalar2=0.0, op0=ALU.mult, op1=ALU.add)
 
         for q in range(QUADS):
             nc.vector.tensor_copy(out=xs[32 * q:32 * q + 32, :], in_=xs_all[32 * q:32 * q + 32, :, q])
 
+        def bank_tile(bank, shape):
+            return psum.tile(shape, F32, name="bank%d" % bank, tag="bank%d" % bank)
+
         neg_bias = {}
 
         def spread_bias(l):
-            acc = psum.tile([P, T], F32, name="sum_ps", tag="sum_ps", bufs=5)
+            acc = bank_tile(MESSAGE_BANKS[l // 2], [P, T])
             nc.tensor.matmul(acc[:], lhsT=pick[:, 2 * l:2 * l + 1].to_broadcast([P, P]), rhs=rows[:], start=True, stop=True)
             neg_bias[l] = keep.tile([P, T], F32, name="neg_bias%d" % l)
             nc.vector.tensor_copy(out=neg_bias[l][:], in_=acc[:])
@@ -135,7 +143,9 @@ def tile_chunkflooredmessagemiddlescore_kernel(tc, x_bytes, x_scale, we_words, w
         sums = [keep.tile([P, PAIRS], F32, name="sums%d" % i) for i in range(TILES)]
         inverse = [keep.tile([P, PAIRS], F32, name="inv%d" % i) for i in range(TILES)]
         weight = keep.tile([P, TILES], F32, name="weight")
-        inv_weight = keep.tile([P, TILES], F32, name="inv_weight")
+        log_weight = keep.tile([P, TILES], F32, name="log_weight")
+        mid_neg_max = keep.tile([P, TILES], F32, name="mid_neg_max")
+        shift = keep.tile([P, TILES], F32, name="shift")
 
         def widen(s):
             x_wide[s] = work.tile([P, D], BF16, name="xw", tag="xw")
@@ -147,8 +157,8 @@ def tile_chunkflooredmessagemiddlescore_kernel(tc, x_bytes, x_scale, we_words, w
                 for u in range(2):
                     nc.tensor.transpose(bank[:, g, u, :], words[:, PASS_WORDS * g + u:PASS_WORDS * (g + 1):2], ident[:])
 
-        def turn_x(s):
-            x_turned[s] = psum.tile([P, PASSES, 2, P], F32, name="xt", tag="xt", bufs=3)
+        def turn_x(s, bank=None):
+            x_turned[s] = bank_tile(TURN_BANK[units[s][1]] if bank is None else bank, [P, PASSES, 2, P])
             turn(x_turned[s], x_wide[s][:])
 
         def vector_passes(s):
@@ -157,7 +167,7 @@ def tile_chunkflooredmessagemiddlescore_kernel(tc, x_bytes, x_scale, we_words, w
         def scaled_passes(s, passes):
             i, l = units[s]
             if s not in grouped:
-                grouped[s] = work.tile([P, PASSES, P, 4], BF16, name="xg", tag="xg", align_bytes=64)
+                grouped[s] = work.tile([P, PASSES, P, 4], BF16, name="xg", tag="xg", bufs=5, align_bytes=64)
             found = []
             for g in passes:
                 src = x_turned[s][:, g].rearrange("p u r -> p (u r)").bitcast(BF16).rearrange("p (u r e) -> p r u e", u=2, e=2)
@@ -182,8 +192,8 @@ def tile_chunkflooredmessagemiddlescore_kernel(tc, x_bytes, x_scale, we_words, w
                 in_=grouped[s][:].rearrange("p g r t -> p (g r t)"),
             )
 
-        def emit(s):
-            e_ps[s] = psum.tile([P, T], F32, name="sum_ps", tag="sum_ps", bufs=5)
+        def emit(s, bank=None):
+            e_ps[s] = bank_tile(SCORE_BANK[units[s][1]] if bank is None else bank, [P, T])
             for g in range(PASSES):
                 cols = slice(g * P, (g + 1) * P)
                 nc.tensor.matmul_mx(
@@ -205,22 +215,29 @@ def tile_chunkflooredmessagemiddlescore_kernel(tc, x_bytes, x_scale, we_words, w
                 nc.vector.tensor_tensor(out=neg_n[s][:], in0=neg_bias[l][:], in1=e_ps[s][:], op=ALU.subtract)
 
         def find_max(s):
-            neg_max[s] = keep.tile([P, 1], F32, name="neg_max%d" % s)
-            nc.vector.tensor_reduce(out=neg_max[s][:], in_=neg_n[s][:], axis=AX.X, op=ALU.min)
+            i, l = units[s]
+            if l == 1:
+                neg_max[s] = mid_neg_max[:, i:i + 1]
+            else:
+                column = keep.tile([P, 1], F32, name="neg_max%d" % s)
+                neg_max[s] = column[:]
+            nc.vector.tensor_reduce(out=neg_max[s], in_=neg_n[s][:], axis=AX.X, op=ALU.min)
 
         def exponent(s):
             i, l = units[s]
             if l == 1:
                 expo[s] = work.tile([P, T], F32, name="ex_mid", tag="ex_mid", bufs=4)
-                nc.scalar.activation(out=expo[s][:], in_=neg_n[s][:], func=ACT.Exp, bias=neg_max[s][:], scale=-1.0)
+                nc.scalar.activation(out=expo[s][:], in_=neg_n[s][:], func=ACT.Exp, bias=neg_max[s], scale=-1.0)
             else:
                 expo[s] = work.tile([P, T], F32, name="ex", tag="ex", bufs=8)
                 nc.scalar.activation(
-                    out=expo[s][:], in_=neg_n[s][:], func=ACT.Exp, bias=neg_max[s][:], scale=-1.0,
+                    out=expo[s][:], in_=neg_n[s][:], func=ACT.Exp, bias=neg_max[s], scale=-1.0,
                     accum_out=sums[i][:, l // 2:l // 2 + 1],
                 )
 
         v, v_turned, v_grouped, v_codes, v_scales, m_ps, cut0, floored1, product, log_a = {}, {}, {}, {}, {}, {}, {}, {}, {}, {}
+
+        floored0 = {}
 
         def invert_sums(i):
             nc.vector.reciprocal(out=inverse[i][:], in_=sums[i][:])
@@ -238,13 +255,17 @@ def tile_chunkflooredmessagemiddlescore_kernel(tc, x_bytes, x_scale, we_words, w
         def message_second(i):
             message(i, 1)
 
-        def turn_v(i):
-            v_turned[i] = psum.tile([P, PAIRS, 2, P], F32, name="xt", tag="xt", bufs=3)
+        def turn_v(i, bank=TURN_BANK[2]):
+            v_turned[i] = bank_tile(bank, [P, PAIRS, 2, P])
             turn(v_turned[i], v[i][:].rearrange("p a n -> p (a n)"))
 
         def empty_v(i):
             v_grouped[i] = work.tile([P, PAIRS, P, 2], F32, name="vg", tag="vg", bufs=2, align_bytes=64)
             nc.scalar.copy(out=v_grouped[i][:], in_=v_turned[i][:].rearrange("p g u r -> p g r u"))
+
+        def empty_v_vector(i):
+            v_grouped[i] = work.tile([P, PAIRS, P, 2], F32, name="vg", tag="vg", bufs=2, align_bytes=64)
+            nc.vector.tensor_copy(out=v_grouped[i][:], in_=v_turned[i][:].rearrange("p g u r -> p g r u"))
 
         def quantize_v(i):
             v_codes[i] = work.tile([P, PAIRS * P], U32, name="vq", tag="vq", bufs=2, align_bytes=64)
@@ -254,10 +275,10 @@ def tile_chunkflooredmessagemiddlescore_kernel(tc, x_bytes, x_scale, we_words, w
                 in_=v_grouped[i][:].rearrange("p g r u -> p (g r u)").bitcast(BF16),
             )
 
-        def pass_on(i):
+        def pass_on(i, banks):
             for p in range(PAIRS):
                 cols = slice(p * P, (p + 1) * P)
-                m_ps[i, p] = psum.tile([P, T], F32, name="sum_ps", tag="sum_ps", bufs=5)
+                m_ps[i, p] = bank_tile(banks[p], [P, T])
                 nc.tensor.matmul_mx(
                     out=m_ps[i, p][:], lhsT=v_codes[i][:, cols].bitcast(FP8X4), lhsT_scale=v_scales[i][:, cols],
                     rhs=trans_codes[:, p, :].bitcast(FP8X4), rhs_scale=trans_scales[:, p, :], start=True, stop=True,
@@ -279,6 +300,14 @@ def tile_chunkflooredmessagemiddlescore_kernel(tc, x_bytes, x_scale, we_words, w
                 out=product[i][:], in0=cut0[i][:], scalar=FLOOR_VALUE, in1=floored1[i][:], op0=ALU.add, op1=ALU.mult,
             )
 
+        def lift_first(i):
+            floored0[i] = grouped[unit_of[i + 2, 2]][:].rearrange("p g r t -> p (g r t)").bitcast(F32)
+            nc.gpsimd.tensor_scalar(out=floored0[i], in0=cut0[i][:], scalar1=1.0, scalar2=FLOOR_VALUE, op0=ALU.mult, op1=ALU.add)
+
+        def multiply_gpsimd(i):
+            product[i] = keep.tile([P, T], F32, name="prod%d" % i)
+            nc.gpsimd.tensor_tensor(out=product[i][:], in0=floored0[i], in1=floored1[i][:], op=ALU.mult)
+
         def weigh(i):
             terms = work.tile([P, T], F32, name="weighted", tag="weighted", bufs=1)
             nc.vector.scalar_tensor_tensor(
@@ -286,8 +315,11 @@ def tile_chunkflooredmessagemiddlescore_kernel(tc, x_bytes, x_scale, we_words, w
                 accum_out=weight[:, i:i + 1],
             )
 
-        def invert_weights(first, end):
-            nc.vector.reciprocal(out=inv_weight[:, first:end], in_=weight[:, first:end])
+        def log_weights(first, end):
+            nc.scalar.activation(out=log_weight[:, first:end], in_=weight[:, first:end], func=ACT.Ln)
+
+        def make_shifts(first, end):
+            nc.vector.tensor_tensor(out=shift[:, first:end], in0=mid_neg_max[:, first:end], in1=log_weight[:, first:end], op=ALU.subtract)
 
         def pieces(i):
             return [slice(0, HALF), slice(HALF, T)] if i == LAST_TILE else [slice(0, T)]
@@ -295,16 +327,30 @@ def tile_chunkflooredmessagemiddlescore_kernel(tc, x_bytes, x_scale, we_words, w
         def take_log(i):
             for h, cols in enumerate(pieces(i)):
                 log_a[i, h] = work.tile([P, cols.stop - cols.start], F32, name="logp", tag="logp", bufs=TILES + 1)
-                nc.scalar.activation(out=log_a[i, h][:], in_=product[i][:, cols], func=ACT.Ln, scale=inv_weight[:, i:i + 1])
+                nc.scalar.activation(out=log_a[i, h][:], in_=product[i][:, cols], func=ACT.Ln)
 
         def finish(i):
             s = unit_of[i, 1]
             for h, cols in enumerate(pieces(i)):
                 res = work.tile([P, cols.stop - cols.start], F32, name="res", tag="res", bufs=TILES + 1)
                 nc.vector.scalar_tensor_tensor(
-                    out=res[:], in0=log_a[i, h][:], scalar=neg_max[s][:], in1=neg_n[s][:, cols], op0=ALU.add, op1=ALU.subtract,
+                    out=res[:], in0=log_a[i, h][:], scalar=shift[:, i:i + 1], in1=neg_n[s][:, cols], op0=ALU.add, op1=ALU.subtract,
                 )
                 nc.sync.dma_start(out=out[i * P:(i + 1) * P, cols], in_=res[:])
+
+        total = {}
+
+        def open_total(i, bank):
+            total[i] = bank_tile(bank, [P, T])
+            nc.tensor.matmul(total[i][:], lhsT=neg_ident[:], rhs=neg_n[unit_of[i, 1]][:], start=True, stop=False)
+
+        def close_total(i):
+            nc.tensor.matmul(total[i][:], lhsT=ident[:], rhs=log_a[i, 0][:], start=False, stop=True)
+
+        def finish_total(i):
+            res = work.tile([P, T], F32, name="res", tag="res", bufs=TILES + 1)
+            nc.scalar.activation(out=res[:], in_=total[i][:], func=ACT.Identity, bias=shift[:, i:i + 1], scale=1.0)
+            nc.sync.dma_start(out=out[i * P:(i + 1) * P, :], in_=res[:])
 
         def on_unit(step, i, l):
             if 0 <= i < TILES:
@@ -316,119 +362,137 @@ def tile_chunkflooredmessagemiddlescore_kernel(tc, x_bytes, x_scale, we_words, w
             elif i < 0 and otherwise is not None and i in otherwise:
                 otherwise[i]()
 
-        def quantize_and_emit(s):
+        def quantize_and_emit(s, bank=None):
             quantize_x(s)
-            emit(s)
+            emit(s, bank)
 
-        def quantize_and_pass_on(i):
+        def quantize_and_pass_on(i, banks=MESSAGE_BANKS):
             quantize_v(i)
-            pass_on(i)
+            pass_on(i, banks)
 
         spread_bias(0)
         spread_bias(2)
         for k in range(-2, LAST_TILE):
             on_unit(empty_scalar, k, 2)
             on_unit(quantize_and_emit, k, 0)
+            on_tile(weigh, k - 3)
             on_tile(invert_sums, k - 1)
-            on_unit(find_max, k - 2, 1)
+            on_unit(add_bias, k - 2, 1)
             on_tile(floor_first, k - 2)
+            on_unit(turn_x, k + 1, 0)
             on_tile(message_first, k - 1, {-1: lambda: interleave_trans(0)})
             on_tile(message_second, k - 1)
-            on_unit(exponent, k - 2, 1)
+            on_unit(empty_scalar, k - 1, 1)
             on_tile(turn_v, k - 1)
 
             on_unit(quantize_and_emit, k, 2)
-            on_unit(empty_scalar, k - 1, 1)
-            on_unit(add_bias, k, 0)
-            on_tile(floor_second, k - 2, {-2: lambda: quantize_trans(0)})
-            on_unit(empty_vector, k - 1, 1)
-            on_unit(turn_x, k + 1, 0)
-            on_tile(empty_v, k - 1)
-            on_unit(find_max, k, 0)
+            on_tile(lift_first, k - 2)
             on_unit(widen, k + 1, 2)
+            on_unit(add_bias, k, 0)
+            on_unit(empty_vector, k - 1, 1)
+            on_unit(find_max, k - 2, 1)
+            if k == 0:
+                quantize_trans(0)
+            on_unit(widen, k, 1)
+            on_tile(empty_v, k - 1)
+            on_unit(turn_x, k + 1, 2)
 
             on_unit(quantize_and_emit, k - 1, 1)
-            on_unit(widen, k, 1)
+            on_tile(floor_second, k - 2, {-2: scale_gain, -1: lambda: interleave_trans(1)})
+            on_tile(multiply_gpsimd, k - 2)
+            on_unit(exponent, k - 2, 1)
+            on_unit(turn_x, k, 1)
             on_unit(add_bias, k, 2)
-            on_tile(multiply, k - 2, {-2: scale_gain, -1: lambda: interleave_trans(1)})
-            on_unit(turn_x, k + 1, 2)
             on_unit(empty_scalar, k + 1, 0)
-            on_unit(exponent, k, 0)
+            on_unit(find_max, k, 0)
             on_unit(empty_vector, k + 1, 0)
             on_unit(find_max, k, 2)
+            on_unit(widen, k + 2, 0)
 
             if k == 1:
                 quantize_trans(1)
             on_tile(quantize_and_pass_on, k - 1)
-            on_unit(add_bias, k - 1, 1)
+            on_unit(exponent, k, 0)
             on_unit(exponent, k, 2)
             on_unit(empty_vector, k + 1, 2)
-            on_tile(weigh, k - 2)
-            on_unit(turn_x, k, 1)
-            on_unit(widen, k + 2, 0)
 
         last = LAST_TILE
         first_end, second_end, middle = unit_of[last, 0], unit_of[last, 2], unit_of[last, 1]
         middle_1, middle_2 = unit_of[last - 1, 1], unit_of[last - 2, 1]
+        widen(middle)
         empty_scalar(second_end)
         quantize_and_emit(first_end)
+        turn_x(middle, TURN_BANK[0])
         invert_sums(last - 1)
+        add_bias(middle_2)
+        weigh(last - 3)
         find_max(middle_2)
-        widen(middle)
         message_first(last - 1)
         quantize_and_emit(second_end)
         empty_scalar(middle_1)
-        turn_x(middle)
         add_bias(first_end)
         message_second(last - 1)
         turn_v(last - 1)
-        floor_first(last - 2)
-        exponent(middle_2)
+        empty_scalar(middle)
         find_max(first_end)
         quantize_and_emit(middle_1)
         add_bias(second_end)
-        exponent(first_end)
+        quantize_and_emit(middle, SCORE_BANK[0])
+        open_total(1, TURN_BANK[0])
         empty_v(last - 1)
-        floor_second(last - 2)
+        exponent(first_end)
         find_max(second_end)
-        empty_scalar(middle)
-        quantize_and_pass_on(last - 1)
+        exponent(middle_2)
         add_bias(middle_1)
+        quantize_and_pass_on(last - 1, (SCORE_BANK[2], SCORE_BANK[1]))
+        open_total(2, TURN_BANK[2])
         exponent(second_end)
-        quantize_and_emit(middle)
+        add_bias(middle)
+        floor_first(last - 2)
         find_max(middle_1)
         invert_sums(last)
-        floor_first(last - 1)
-        multiply(last - 2)
-        message_first(last)
-        exponent(middle_1)
-        add_bias(middle)
-        message_second(last)
-        turn_v(last)
         find_max(middle)
-        invert_weights(0, last - 2)
-        floor_second(last - 1)
+        exponent(middle_1)
         exponent(middle)
-        empty_v(last)
-        weigh(last - 2)
-        quantize_and_pass_on(last)
+        message_first(last)
+        message_second(last)
+        turn_v(last, TURN_BANK[1])
+        open_total(3, SCORE_BANK[0])
+        floor_first(last - 1)
+        floor_second(last - 2)
+        floor_second(last - 1)
+        log_weights(0, last - 2)
         take_log(0)
-        multiply(last - 1)
-        invert_weights(last - 2, last - 1)
-        weigh(last - 1)
-        floor_second(last)
-        floor_first(last)
-        finish(0)
-        invert_weights(last - 1, last)
+        empty_v_vector(last)
+        multiply(last - 2)
+        quantize_and_pass_on(last)
         take_log(1)
-        multiply(last)
+        close_total(1)
+        make_shifts(0, last - 2)
+        multiply(last - 1)
         take_log(2)
-        finish(1)
-        weigh(last)
+        close_total(2)
+        finish(0)
+        floor_first(last)
+        floor_second(last)
+        weigh(last - 2)
         take_log(3)
-        finish(2)
-        invert_weights(last, TILES)
-        for i in range(4, TILES):
-            take_log(i)
-            finish(i - 1)
+        close_total(3)
+        take_log(4)
+        multiply(last)
+        finish_total(1)
+        finish(4)
+        weigh(last - 1)
+        take_log(5)
+        finish_total(2)
+        weigh(last)
+        log_weights(last - 2, last)
+        take_log(6)
+        make_shifts(last - 2, last)
+        log_weights(last, TILES)
+        finish_total(3)
+        take_log(last)
+        finish(5)
+        make_shifts(last, TILES)
+        finish(6)
         finish(last)

@@ -29,17 +29,26 @@ HALF = T // 2
 FLOOR_SHIFT = 14.4
 FLOOR_VALUE = 1.6
 
-TURN_BANK = {0: 0, 2: 1, 1: 2}
-SCORE_BANK = {0: 3, 2: 4, 1: 5}
+TENSOR_FINISHES = 2
+FINISH_BANKS = (0, 2, 5)
+MIDDLE_LAG = 2
+WEIGH_LAG = 4
+TURN_BANK = (0, 1, 2)
+SCORE_BANK = (3, 4, 5)
 MESSAGE_BANKS = (6, 7)
-VECTOR_EMPTIES = 1
-VECTOR_HALVES = (1, 2, 3, 4, 5)
+VECTOR_EMPTIES = 3
+VECTOR_SHARE = 144
+SHARE_END = 7
 
 
 def tile_chunkflooredmessagemiddlescore_kernel(tc, x_bytes, x_scale, we_words, we_scales, be, ends, gain, trans, out):
     nc = tc.nc
 
-    units = [(i, l) for i in range(TILES) for l in (0, 2, 1)]
+    rounds = [[(i, 0), (i, 2)] + ([(i - MIDDLE_LAG, 1)] if i >= MIDDLE_LAG else []) for i in range(TILES)]
+    rounds.append([(TILES - 2, 1), None, (TILES - 1, 1)])
+    units = [u for found in rounds for u in found if u is not None]
+    round_of = {u: k for k, found in enumerate(rounds) for u in found}
+    place_of = {u: j for found in rounds for j, u in enumerate(found)}
     unit_of = {u: s for s, u in enumerate(units)}
 
     with ExitStack() as ctx:
@@ -81,20 +90,21 @@ def tile_chunkflooredmessagemiddlescore_kernel(tc, x_bytes, x_scale, we_words, w
         load_x(0, slice(2, 3))
         load_x(1, slice(0, 3, 2))
         nc.sync.dma_start(out=we_w[:].bitcast(I32), in_=we_words.rearrange("g p n -> p g n").bitcast(I32))
-        load_trans(0)
+        load_x(2, slice(0, 3, 2))
         for q in range(4):
             nc.sync.dma_start(
                 out=we_s[32 * q:32 * q + 4, :, :].bitcast(I32),
                 in_=we_scales[:, 4 * q:4 * q + 4, :].rearrange("g r n -> r g n").bitcast(I32),
             )
-        load_x(0, slice(1, 2))
-        nc.sync.dma_start(out=gain_raw[:], in_=gain.rearrange("a n -> (a n)").partition_broadcast(P))
         load_trans(1)
-        load_x(2, slice(0, 3))
+        load_trans(0)
+        nc.sync.dma_start(out=gain_raw[:], in_=gain.rearrange("a n -> (a n)").partition_broadcast(P))
+        load_x(0, slice(1, 2))
         nc.sync.dma_start(out=be_wide[:], in_=be.partition_broadcast(P))
-        load_x(1, slice(1, 2))
-        for i in range(3, TILES):
-            load_x(i, slice(0, 3))
+        for i in range(3, TILES + MIDDLE_LAG):
+            if i < TILES:
+                load_x(i, slice(0, 3, 2))
+            load_x(i - MIDDLE_LAG, slice(1, 2))
 
         nc.gpsimd.memset(pick[:], 0.0)
         nc.gpsimd.memset(pick[0:1, :], -1.0)
@@ -125,18 +135,32 @@ def tile_chunkflooredmessagemiddlescore_kernel(tc, x_bytes, x_scale, we_words, w
         trans_codes = keep.tile([P, PAIRS, T], U32, name="tr_codes", align_bytes=64)
         trans_scales = keep.tile([P, PAIRS, T], U8, name="tr_scales", align_bytes=64)
 
-        def interleave_trans(p):
-            trans_grouped[p] = keep.tile([P, T, 4], BF16, name="tr_grouped%d" % p, align_bytes=64)
-            nc.vector.tensor_copy(
-                out=trans_grouped[p][:].rearrange("p (c i) t -> p c t i", i=4),
+        def interleave_scalar(p):
+            whole = keep.tile([P, T, 4], BF16, name="tr_grouped%d" % p, align_bytes=64)
+            trans_grouped[p] = [whole[:]]
+            nc.scalar.copy(
+                out=whole[:].rearrange("p (c i) t -> p c t i", i=4),
                 in_=trans_raw[p][:].rearrange("p t (c i) -> p c t i", i=4),
             )
 
+        def interleave_gpsimd(p, spent):
+            trans_grouped[p] = []
+            for h, s in enumerate(spent):
+                half = grouped[s][:].rearrange("p g r t -> p (g r) t")
+                trans_grouped[p].append(half)
+                nc.gpsimd.tensor_scalar(
+                    out=half, in0=trans_raw[p][:, :, h * HALF:(h + 1) * HALF].rearrange("p t n -> p n t"),
+                    scalar1=1.0, scalar2=0.0, op0=ALU.mult, op1=ALU.add,
+                )
+
         def quantize_trans(p):
-            nc.vector.quantize_mx(
-                out=trans_codes[:, p, :].bitcast(FP8X4), scales=trans_scales[:, p, :],
-                in_=trans_grouped[p][:].rearrange("p n t -> p (n t)"),
-            )
+            width = T // len(trans_grouped[p])
+            for h, part in enumerate(trans_grouped[p]):
+                cols = slice(h * width, (h + 1) * width)
+                nc.vector.quantize_mx(
+                    out=trans_codes[:, p, cols].bitcast(FP8X4), scales=trans_scales[:, p, cols],
+                    in_=part.rearrange("p n t -> p (n t)"),
+                )
 
         x_wide, x_turned, grouped, x_codes, x_scales, e_ps = {}, {}, {}, {}, {}, {}
         neg_n, neg_max, expo = {}, {}, {}
@@ -148,7 +172,7 @@ def tile_chunkflooredmessagemiddlescore_kernel(tc, x_bytes, x_scale, we_words, w
         shift = keep.tile([P, TILES], F32, name="shift")
 
         def widen(s):
-            x_wide[s] = work.tile([P, D], BF16, name="xw", tag="xw")
+            x_wide[s] = work.tile([P, D], BF16, name="xw", tag="xw", bufs=6)
             nc.scalar.copy(out=x_wide[s][:], in_=x_raw[s].bitcast(FP8))
 
         def turn(bank, values):
@@ -158,30 +182,34 @@ def tile_chunkflooredmessagemiddlescore_kernel(tc, x_bytes, x_scale, we_words, w
                     nc.tensor.transpose(bank[:, g, u, :], words[:, PASS_WORDS * g + u:PASS_WORDS * (g + 1):2], ident[:])
 
         def turn_x(s, bank=None):
-            x_turned[s] = bank_tile(TURN_BANK[units[s][1]] if bank is None else bank, [P, PASSES, 2, P])
+            x_turned[s] = bank_tile(TURN_BANK[place_of[units[s]]] if bank is None else bank, [P, PASSES, 2, P])
             turn(x_turned[s], x_wide[s][:])
 
-        def vector_passes(s):
-            return PASSES if s < VECTOR_EMPTIES else (1 if units[s][1] == 1 and units[s][0] in VECTOR_HALVES else 0)
+        def vector_share(s):
+            if s < VECTOR_EMPTIES:
+                return PASSES * P
+            return VECTOR_SHARE if place_of[units[s]] == 2 and 2 <= round_of[units[s]] < SHARE_END else 0
 
-        def scaled_passes(s, passes):
+        def scaled_parts(s, first, end):
             i, l = units[s]
             if s not in grouped:
-                grouped[s] = work.tile([P, PASSES, P, 4], BF16, name="xg", tag="xg", bufs=5, align_bytes=64)
+                grouped[s] = work.tile([P, PASSES, P, 4], BF16, name="xg", tag="xg", bufs=7, align_bytes=64)
             found = []
-            for g in passes:
-                src = x_turned[s][:, g].rearrange("p u r -> p (u r)").bitcast(BF16).rearrange("p (u r e) -> p r u e", u=2, e=2)
-                dst = grouped[s][:, g].rearrange("p r (u e) -> p r u e", u=2)
-                c = (l * TILES + i) * PASSES + g
-                found.append((src, dst, xs[:, c:c + 1]))
+            for g in range(PASSES):
+                lo, hi = max(first - g * P, 0), min(end - g * P, P)
+                if lo < hi:
+                    src = x_turned[s][:, g].rearrange("p u r -> p (u r)").bitcast(BF16).rearrange("p (u r e) -> p r u e", u=2, e=2)
+                    dst = grouped[s][:, g].rearrange("p r (u e) -> p r u e", u=2)
+                    c = (l * TILES + i) * PASSES + g
+                    found.append((src[:, lo:hi], dst[:, lo:hi], xs[:, c:c + 1]))
             return found
 
         def empty_vector(s):
-            for src, dst, scale in scaled_passes(s, range(PASSES - vector_passes(s), PASSES)):
+            for src, dst, scale in scaled_parts(s, PASSES * P - vector_share(s), PASSES * P):
                 nc.vector.tensor_scalar(out=dst, in0=src, scalar1=scale, scalar2=None, op0=ALU.mult)
 
         def empty_scalar(s):
-            for src, dst, scale in scaled_passes(s, range(PASSES - vector_passes(s))):
+            for src, dst, scale in scaled_parts(s, 0, PASSES * P - vector_share(s)):
                 nc.scalar.activation(out=dst, in_=src, func=ACT.Copy, scale=scale)
 
         def quantize_x(s):
@@ -192,8 +220,8 @@ def tile_chunkflooredmessagemiddlescore_kernel(tc, x_bytes, x_scale, we_words, w
                 in_=grouped[s][:].rearrange("p g r t -> p (g r t)"),
             )
 
-        def emit(s, bank=None):
-            e_ps[s] = bank_tile(SCORE_BANK[units[s][1]] if bank is None else bank, [P, T])
+        def emit(s, bank):
+            e_ps[s] = bank_tile(SCORE_BANK[place_of[units[s]]] if bank is None else bank, [P, T])
             for g in range(PASSES):
                 cols = slice(g * P, (g + 1) * P)
                 nc.tensor.matmul_mx(
@@ -237,7 +265,7 @@ def tile_chunkflooredmessagemiddlescore_kernel(tc, x_bytes, x_scale, we_words, w
 
         v, v_turned, v_grouped, v_codes, v_scales, m_ps, cut0, floored1, product, log_a = {}, {}, {}, {}, {}, {}, {}, {}, {}, {}
 
-        floored0 = {}
+        floored0, cut1 = {}, {}
 
         def invert_sums(i):
             nc.vector.reciprocal(out=inverse[i][:], in_=sums[i][:])
@@ -255,7 +283,7 @@ def tile_chunkflooredmessagemiddlescore_kernel(tc, x_bytes, x_scale, we_words, w
         def message_second(i):
             message(i, 1)
 
-        def turn_v(i, bank=TURN_BANK[2]):
+        def turn_v(i, bank=TURN_BANK[1]):
             v_turned[i] = bank_tile(bank, [P, PAIRS, 2, P])
             turn(v_turned[i], v[i][:].rearrange("p a n -> p (a n)"))
 
@@ -275,10 +303,10 @@ def tile_chunkflooredmessagemiddlescore_kernel(tc, x_bytes, x_scale, we_words, w
                 in_=v_grouped[i][:].rearrange("p g r u -> p (g r u)").bitcast(BF16),
             )
 
-        def pass_on(i, banks):
+        def pass_on(i):
             for p in range(PAIRS):
                 cols = slice(p * P, (p + 1) * P)
-                m_ps[i, p] = bank_tile(banks[p], [P, T])
+                m_ps[i, p] = bank_tile(MESSAGE_BANKS[p], [P, T])
                 nc.tensor.matmul_mx(
                     out=m_ps[i, p][:], lhsT=v_codes[i][:, cols].bitcast(FP8X4), lhsT_scale=v_scales[i][:, cols],
                     rhs=trans_codes[:, p, :].bitcast(FP8X4), rhs_scale=trans_scales[:, p, :], start=True, stop=True,
@@ -294,6 +322,14 @@ def tile_chunkflooredmessagemiddlescore_kernel(tc, x_bytes, x_scale, we_words, w
                 out=floored1[i][:], in0=m_ps[i, 1][:], scalar1=-FLOOR_SHIFT, scalar2=16.0, op0=ALU.max, op1=ALU.add,
             )
 
+        def cut_second(i):
+            cut1[i] = work.tile([P, T], F32, name="cut", tag="cut", bufs=1)
+            nc.scalar.activation(out=cut1[i][:], in_=m_ps[i, 1][:], func=ACT.Relu, bias=FLOOR_SHIFT, scale=1.0)
+
+        def lift_second(i):
+            floored1[i] = work.tile([P, T], F32, name="fl1", tag="fl1", bufs=2)
+            nc.scalar.activation(out=floored1[i][:], in_=cut1[i][:], func=ACT.Identity, bias=FLOOR_VALUE, scale=1.0)
+
         def multiply(i):
             product[i] = keep.tile([P, T], F32, name="prod%d" % i)
             nc.vector.scalar_tensor_tensor(
@@ -301,7 +337,7 @@ def tile_chunkflooredmessagemiddlescore_kernel(tc, x_bytes, x_scale, we_words, w
             )
 
         def lift_first(i):
-            floored0[i] = grouped[unit_of[i + 2, 2]][:].rearrange("p g r t -> p (g r t)").bitcast(F32)
+            floored0[i] = grouped[unit_of[rounds[i + 2][1]]][:].rearrange("p g r t -> p (g r t)").bitcast(F32)
             nc.gpsimd.tensor_scalar(out=floored0[i], in0=cut0[i][:], scalar1=1.0, scalar2=FLOOR_VALUE, op0=ALU.mult, op1=ALU.add)
 
         def multiply_gpsimd(i):
@@ -352,147 +388,202 @@ def tile_chunkflooredmessagemiddlescore_kernel(tc, x_bytes, x_scale, we_words, w
             nc.scalar.activation(out=res[:], in_=total[i][:], func=ACT.Identity, bias=shift[:, i:i + 1], scale=1.0)
             nc.sync.dma_start(out=out[i * P:(i + 1) * P, :], in_=res[:])
 
-        def on_unit(step, i, l):
-            if 0 <= i < TILES:
-                step(unit_of[i, l])
+        def on_unit(step, k, place):
+            if 0 <= k < len(rounds) and place < len(rounds[k]):
+                step(unit_of[rounds[k][place]])
 
         def on_tile(step, i, otherwise=None):
             if 0 <= i < TILES:
                 step(i)
-            elif i < 0 and otherwise is not None and i in otherwise:
+            elif otherwise is not None and i in otherwise:
                 otherwise[i]()
 
         def quantize_and_emit(s, bank=None):
             quantize_x(s)
             emit(s, bank)
 
-        def quantize_and_pass_on(i, banks=MESSAGE_BANKS):
+        def quantize_and_pass_on(i):
             quantize_v(i)
-            pass_on(i, banks)
+            pass_on(i)
 
+        a0, b0, a1, b1 = unit_of[0, 0], unit_of[0, 2], unit_of[1, 0], unit_of[1, 2]
         spread_bias(0)
         spread_bias(2)
-        for k in range(-2, LAST_TILE):
-            on_unit(empty_scalar, k, 2)
+        for s, bank in ((a0, 0), (b0, 1), (a1, 2)):
+            widen(s)
+            turn_x(s, bank)
+        empty_vector(a0)
+        widen(b1)
+        turn_x(b1, 0)
+        empty_vector(b0)
+        on_unit(widen, 2, 0)
+        on_unit(widen, 2, 1)
+        quantize_and_emit(a0)
+        quantize_and_emit(b0)
+        empty_scalar(a1)
+        empty_vector(a1)
+        empty_scalar(b1)
+        quantize_and_emit(a1, SCORE_BANK[2])
+        add_bias(a0)
+        quantize_and_emit(b1, SCORE_BANK[0])
+        interleave_gpsimd(0, (b1, a1))
+        on_unit(turn_x, 2, 0)
+        add_bias(b0)
+        on_unit(turn_x, 2, 1)
+        interleave_scalar(1)
+        find_max(a0)
+        find_max(b0)
+        exponent(a0)
+        exponent(b0)
+        add_bias(a1)
+        add_bias(b1)
+        on_unit(empty_scalar, 2, 0)
+        find_max(a1)
+        scale_gain()
+        invert_sums(0)
+        find_max(b1)
+        message_first(0)
+        message_second(0)
+        turn_v(0, TURN_BANK[2])
+        exponent(a1)
+        exponent(b1)
+        quantize_trans(1)
+        on_unit(widen, 2, 2)
+        on_unit(widen, 3, 0)
+        quantize_trans(0)
+        empty_v(0)
+        on_unit(turn_x, 2, 2)
+        quantize_and_pass_on(0)
+
+        for k in range(2, LAST_TILE):
+            on_unit(empty_scalar, k, 1)
             on_unit(quantize_and_emit, k, 0)
-            on_tile(weigh, k - 3)
             on_tile(invert_sums, k - 1)
-            on_unit(add_bias, k - 2, 1)
-            on_tile(floor_first, k - 2)
+            on_tile(weigh, k - WEIGH_LAG)
             on_unit(turn_x, k + 1, 0)
-            on_tile(message_first, k - 1, {-1: lambda: interleave_trans(0)})
+            on_tile(message_first, k - 1)
             on_tile(message_second, k - 1)
-            on_unit(empty_scalar, k - 1, 1)
+            on_unit(empty_scalar, k, 2)
+            on_tile(floor_first, k - 2)
+
+            on_unit(quantize_and_emit, k, 1)
             on_tile(turn_v, k - 1)
+            on_tile(lift_first, k - 2)
+            on_unit(widen, k + 1, 1)
+            on_unit(add_bias, k, 0)
+            on_unit(empty_vector, k, 2)
+            on_unit(find_max, k, 0)
+            on_unit(widen, k + 1, 2)
+            on_unit(empty_scalar, k + 1, 0)
 
             on_unit(quantize_and_emit, k, 2)
-            on_tile(lift_first, k - 2)
-            on_unit(widen, k + 1, 2)
-            on_unit(add_bias, k, 0)
-            on_unit(empty_vector, k - 1, 1)
-            on_unit(find_max, k - 2, 1)
-            if k == 0:
-                quantize_trans(0)
-            on_unit(widen, k, 1)
-            on_tile(empty_v, k - 1)
-            on_unit(turn_x, k + 1, 2)
-
-            on_unit(quantize_and_emit, k - 1, 1)
-            on_tile(floor_second, k - 2, {-2: scale_gain, -1: lambda: interleave_trans(1)})
-            on_tile(multiply_gpsimd, k - 2)
-            on_unit(exponent, k - 2, 1)
-            on_unit(turn_x, k, 1)
-            on_unit(add_bias, k, 2)
-            on_unit(empty_scalar, k + 1, 0)
-            on_unit(find_max, k, 0)
-            on_unit(empty_vector, k + 1, 0)
-            on_unit(find_max, k, 2)
-            on_unit(widen, k + 2, 0)
-
-            if k == 1:
-                quantize_trans(1)
-            on_tile(quantize_and_pass_on, k - 1)
             on_unit(exponent, k, 0)
-            on_unit(exponent, k, 2)
-            on_unit(empty_vector, k + 1, 2)
+            on_tile(empty_v, k - 1)
+            on_unit(turn_x, k + 1, 1)
+            on_unit(turn_x, k + 1, 2)
+            on_unit(add_bias, k, 1)
+            on_tile(floor_second, k - 2)
+            on_tile(multiply_gpsimd, k - 2)
+            on_unit(empty_vector, k + 1, 0)
+            on_unit(find_max, k, 1)
+            on_unit(widen, k + 2, 0)
+            on_unit(find_max, k - 1, 2)
+            on_unit(exponent, k, 1)
+            on_unit(add_bias, k, 2)
+            on_unit(exponent, k - 1, 2)
+
+            on_tile(quantize_and_pass_on, k - 1)
+            on_unit(empty_vector, k + 1, 1)
 
         last = LAST_TILE
-        first_end, second_end, middle = unit_of[last, 0], unit_of[last, 2], unit_of[last, 1]
-        middle_1, middle_2 = unit_of[last - 1, 1], unit_of[last - 2, 1]
-        widen(middle)
+        first_end, second_end = unit_of[last, 0], unit_of[last, 2]
+        middle = {i: unit_of[i, 1] for i in range(TILES)}
         empty_scalar(second_end)
         quantize_and_emit(first_end)
-        turn_x(middle, TURN_BANK[0])
         invert_sums(last - 1)
-        add_bias(middle_2)
-        weigh(last - 3)
-        find_max(middle_2)
+        weigh(last - WEIGH_LAG)
+        turn_x(middle[last - 1])
         message_first(last - 1)
-        quantize_and_emit(second_end)
-        empty_scalar(middle_1)
-        add_bias(first_end)
         message_second(last - 1)
-        turn_v(last - 1)
-        empty_scalar(middle)
-        find_max(first_end)
-        quantize_and_emit(middle_1)
-        add_bias(second_end)
-        quantize_and_emit(middle, SCORE_BANK[0])
-        open_total(1, TURN_BANK[0])
-        empty_v(last - 1)
-        exponent(first_end)
-        find_max(second_end)
-        exponent(middle_2)
-        add_bias(middle_1)
-        quantize_and_pass_on(last - 1, (SCORE_BANK[2], SCORE_BANK[1]))
-        open_total(2, TURN_BANK[2])
-        exponent(second_end)
-        add_bias(middle)
+        empty_scalar(middle[last - 2])
         floor_first(last - 2)
-        find_max(middle_1)
-        invert_sums(last)
-        find_max(middle)
-        exponent(middle_1)
-        exponent(middle)
-        message_first(last)
-        message_second(last)
-        turn_v(last, TURN_BANK[1])
-        open_total(3, SCORE_BANK[0])
-        floor_first(last - 1)
+
+        quantize_and_emit(second_end)
+        turn_v(last - 1)
+        lift_first(last - 2)
+        widen(middle[last])
+        turn_x(middle[last])
+        add_bias(first_end)
+        find_max(middle[last - 3])
+        find_max(first_end)
+        empty_scalar(middle[last - 1])
+
+        quantize_and_emit(middle[last - 2])
+        exponent(first_end)
+        empty_v(last - 1)
+        add_bias(second_end)
+        quantize_and_emit(middle[last - 1])
         floor_second(last - 2)
-        floor_second(last - 1)
-        log_weights(0, last - 2)
-        take_log(0)
+        multiply_gpsimd(last - 2)
+        empty_scalar(middle[last])
+        find_max(second_end)
+        add_bias(middle[last - 2])
+        exponent(second_end)
+        add_bias(middle[last - 1])
+        exponent(middle[last - 3])
+
+        quantize_and_emit(middle[last], SCORE_BANK[1])
+        quantize_and_pass_on(last - 1)
+        invert_sums(last)
+        find_max(middle[last - 2])
+        find_max(middle[last - 1])
+        exponent(middle[last - 2])
+        floor_first(last - 1)
+        cut_second(last - 1)
+        message_first(last)
+        exponent(middle[last - 1])
+        add_bias(middle[last])
+        lift_second(last - 1)
+        message_second(last)
+        for i in range(TENSOR_FINISHES):
+            if i == 1:
+                turn_v(last)
+            open_total(1 + 2 * i, FINISH_BANKS[i])
+        find_max(middle[last])
+        exponent(middle[last])
+
+        done = TILES - WEIGH_LAG
+        log_weights(0, done)
+        weigh(done)
+        multiply(last - 1)
         empty_v_vector(last)
-        multiply(last - 2)
+        weigh(last - 2)
         quantize_and_pass_on(last)
+        take_log(0)
+        weigh(last - 1)
+        make_shifts(0, done)
         take_log(1)
         close_total(1)
-        make_shifts(0, last - 2)
-        multiply(last - 1)
-        take_log(2)
-        close_total(2)
         finish(0)
+        take_log(2)
         floor_first(last)
         floor_second(last)
-        weigh(last - 2)
+        log_weights(done, last)
+        take_log(4)
+        finish(2)
+        make_shifts(done, last)
         take_log(3)
         close_total(3)
-        take_log(4)
         multiply(last)
-        finish_total(1)
         finish(4)
-        weigh(last - 1)
         take_log(5)
-        finish_total(2)
+        finish_total(1)
         weigh(last)
-        log_weights(last - 2, last)
         take_log(6)
-        make_shifts(last - 2, last)
-        log_weights(last, TILES)
-        finish_total(3)
-        take_log(last)
         finish(5)
-        make_shifts(last, TILES)
+        log_weights(last, TILES)
+        take_log(last)
         finish(6)
+        make_shifts(last, TILES)
+        finish_total(3)
         finish(last)

@@ -29,16 +29,14 @@ HALF = T // 2
 FLOOR_SHIFT = 14.4
 FLOOR_VALUE = 1.6
 
-TENSOR_FINISHES = 2
-FINISH_BANKS = (0, 2, 5)
 MIDDLE_LAG = 2
 WEIGH_LAG = 4
 TURN_BANK = (0, 1, 2)
 SCORE_BANK = (3, 4, 5)
 MESSAGE_BANKS = (6, 7)
 VECTOR_EMPTIES = 3
-VECTOR_SHARE = 144
-SHARE_END = 7
+WARM = (512, 256, 0, 512, 256)
+VECTOR_SHARE = 160
 
 
 def tile_chunkflooredmessagemiddlescore_kernel(tc, x_bytes, x_scale, we_words, we_scales, be, ends, gain, trans, out):
@@ -67,7 +65,9 @@ def tile_chunkflooredmessagemiddlescore_kernel(tc, x_bytes, x_scale, we_words, w
         xs_all = keep.tile([P, L * TILES * PASSES, QUADS], F32, name="xs_all")
         xs = keep.tile([P, L * TILES * PASSES], F32, name="xs")
         ident = keep.tile([P, P], F32, name="ident")
+        zeros = keep.tile([P, T], F32, name="zeros")
         nc.vector.memset(rows[:].bitcast(I32), 0)
+        nc.vector.memset(zeros[:], 0.0)
         nc.vector.memset(we_s[:].rearrange("p g n -> p (g n)").bitcast(I32), 0)
 
         x_raw, trans_raw = {}, {}
@@ -120,6 +120,10 @@ def tile_chunkflooredmessagemiddlescore_kernel(tc, x_bytes, x_scale, we_words, w
         def bank_tile(bank, shape):
             return psum.tile(shape, F32, name="bank%d" % bank, tag="bank%d" % bank)
 
+        def warm_up(bank, columns):
+            if columns:
+                nc.tensor.matmul(bank_tile(bank, [P, columns])[:], lhsT=zeros[:, 0:P], rhs=zeros[:, 0:columns], start=True, stop=True)
+
         neg_bias = {}
 
         def spread_bias(l):
@@ -135,32 +139,35 @@ def tile_chunkflooredmessagemiddlescore_kernel(tc, x_bytes, x_scale, we_words, w
         trans_codes = keep.tile([P, PAIRS, T], U32, name="tr_codes", align_bytes=64)
         trans_scales = keep.tile([P, PAIRS, T], U8, name="tr_scales", align_bytes=64)
 
-        def interleave_scalar(p):
-            whole = keep.tile([P, T, 4], BF16, name="tr_grouped%d" % p, align_bytes=64)
-            trans_grouped[p] = [whole[:]]
-            nc.scalar.copy(
-                out=whole[:].rearrange("p (c i) t -> p c t i", i=4),
-                in_=trans_raw[p][:].rearrange("p t (c i) -> p c t i", i=4),
+        def interleave_views(p, h):
+            half = keep.tile([P, HALF, 4], BF16, name="tr_grouped%d_%d" % (p, h), align_bytes=64)
+            trans_grouped[p, h] = half[:]
+            return (
+                half[:].rearrange("p (c i) t -> p c t i", i=4),
+                trans_raw[p][:, :, h * HALF:(h + 1) * HALF].rearrange("p t (c i) -> p c t i", i=4),
             )
 
-        def interleave_gpsimd(p, spent):
-            trans_grouped[p] = []
-            for h, s in enumerate(spent):
-                half = grouped[s][:].rearrange("p g r t -> p (g r) t")
-                trans_grouped[p].append(half)
-                nc.gpsimd.tensor_scalar(
-                    out=half, in0=trans_raw[p][:, :, h * HALF:(h + 1) * HALF].rearrange("p t n -> p n t"),
-                    scalar1=1.0, scalar2=0.0, op0=ALU.mult, op1=ALU.add,
-                )
+        def interleave_scalar(p, h):
+            dst, src = interleave_views(p, h)
+            nc.scalar.copy(out=dst, in_=src)
 
-        def quantize_trans(p):
-            width = T // len(trans_grouped[p])
-            for h, part in enumerate(trans_grouped[p]):
-                cols = slice(h * width, (h + 1) * width)
-                nc.vector.quantize_mx(
-                    out=trans_codes[:, p, cols].bitcast(FP8X4), scales=trans_scales[:, p, cols],
-                    in_=part.rearrange("p n t -> p (n t)"),
-                )
+        def interleave_vector(p, h):
+            dst, src = interleave_views(p, h)
+            nc.vector.tensor_copy(out=dst, in_=src)
+
+        def interleave_gpsimd(p, h, spent):
+            trans_grouped[p, h] = grouped[spent][:].rearrange("p g r t -> p (g r) t")
+            nc.gpsimd.tensor_scalar(
+                out=trans_grouped[p, h], in0=trans_raw[p][:, :, h * HALF:(h + 1) * HALF].rearrange("p t n -> p n t"),
+                scalar1=1.0, scalar2=0.0, op0=ALU.mult, op1=ALU.add,
+            )
+
+        def quantize_trans(p, h):
+            cols = slice(h * HALF, (h + 1) * HALF)
+            nc.vector.quantize_mx(
+                out=trans_codes[:, p, cols].bitcast(FP8X4), scales=trans_scales[:, p, cols],
+                in_=trans_grouped[p, h].rearrange("p n t -> p (n t)"),
+            )
 
         x_wide, x_turned, grouped, x_codes, x_scales, e_ps = {}, {}, {}, {}, {}, {}
         neg_n, neg_max, expo = {}, {}, {}
@@ -188,7 +195,7 @@ def tile_chunkflooredmessagemiddlescore_kernel(tc, x_bytes, x_scale, we_words, w
         def vector_share(s):
             if s < VECTOR_EMPTIES:
                 return PASSES * P
-            return VECTOR_SHARE if place_of[units[s]] == 2 and 2 <= round_of[units[s]] < SHARE_END else 0
+            return VECTOR_SHARE if place_of[units[s]] == 2 and round_of[units[s]] < LAST_TILE else 0
 
         def scaled_parts(s, first, end):
             i, l = units[s]
@@ -270,6 +277,12 @@ def tile_chunkflooredmessagemiddlescore_kernel(tc, x_bytes, x_scale, we_words, w
         def invert_sums(i):
             nc.vector.reciprocal(out=inverse[i][:], in_=sums[i][:])
 
+        def invert_first(i):
+            nc.vector.reciprocal(out=inverse[i][:, 0:1], in_=sums[i][:, 0:1])
+
+        def invert_second(i):
+            nc.vector.reciprocal(out=inverse[i][:, 1:2], in_=sums[i][:, 1:2])
+
         def message(i, p):
             nc.vector.scalar_tensor_tensor(
                 out=v[i][:, p, :], in0=expo[unit_of[i, 2 * p]][:], scalar=inverse[i][:, p:p + 1],
@@ -291,10 +304,6 @@ def tile_chunkflooredmessagemiddlescore_kernel(tc, x_bytes, x_scale, we_words, w
             v_grouped[i] = work.tile([P, PAIRS, P, 2], F32, name="vg", tag="vg", bufs=2, align_bytes=64)
             nc.scalar.copy(out=v_grouped[i][:], in_=v_turned[i][:].rearrange("p g u r -> p g r u"))
 
-        def empty_v_vector(i):
-            v_grouped[i] = work.tile([P, PAIRS, P, 2], F32, name="vg", tag="vg", bufs=2, align_bytes=64)
-            nc.vector.tensor_copy(out=v_grouped[i][:], in_=v_turned[i][:].rearrange("p g u r -> p g r u"))
-
         def quantize_v(i):
             v_codes[i] = work.tile([P, PAIRS * P], U32, name="vq", tag="vq", bufs=2, align_bytes=64)
             v_scales[i] = work.tile([P, PAIRS * P], U8, name="vqs", tag="vqs", bufs=2, align_bytes=64)
@@ -303,10 +312,10 @@ def tile_chunkflooredmessagemiddlescore_kernel(tc, x_bytes, x_scale, we_words, w
                 in_=v_grouped[i][:].rearrange("p g r u -> p (g r u)").bitcast(BF16),
             )
 
-        def pass_on(i):
+        def pass_on(i, banks):
             for p in range(PAIRS):
                 cols = slice(p * P, (p + 1) * P)
-                m_ps[i, p] = bank_tile(MESSAGE_BANKS[p], [P, T])
+                m_ps[i, p] = bank_tile(banks[p], [P, T])
                 nc.tensor.matmul_mx(
                     out=m_ps[i, p][:], lhsT=v_codes[i][:, cols].bitcast(FP8X4), lhsT_scale=v_scales[i][:, cols],
                     rhs=trans_codes[:, p, :].bitcast(FP8X4), rhs_scale=trans_scales[:, p, :], start=True, stop=True,
@@ -402,19 +411,23 @@ def tile_chunkflooredmessagemiddlescore_kernel(tc, x_bytes, x_scale, we_words, w
             quantize_x(s)
             emit(s, bank)
 
-        def quantize_and_pass_on(i):
+        def quantize_and_pass_on(i, banks=MESSAGE_BANKS):
             quantize_v(i)
-            pass_on(i)
+            pass_on(i, banks)
 
         a0, b0, a1, b1 = unit_of[0, 0], unit_of[0, 2], unit_of[1, 0], unit_of[1, 2]
+        warm_up(SCORE_BANK[0], WARM[0])
         spread_bias(0)
         spread_bias(2)
         for s, bank in ((a0, 0), (b0, 1), (a1, 2)):
             widen(s)
             turn_x(s, bank)
+            if s == b0:
+                warm_up(SCORE_BANK[1], WARM[1])
         empty_vector(a0)
         widen(b1)
         turn_x(b1, 0)
+        warm_up(SCORE_BANK[2], WARM[2])
         empty_vector(b0)
         on_unit(widen, 2, 0)
         on_unit(widen, 2, 1)
@@ -426,11 +439,12 @@ def tile_chunkflooredmessagemiddlescore_kernel(tc, x_bytes, x_scale, we_words, w
         quantize_and_emit(a1, SCORE_BANK[2])
         add_bias(a0)
         quantize_and_emit(b1, SCORE_BANK[0])
-        interleave_gpsimd(0, (b1, a1))
+        interleave_gpsimd(0, 0, b1)
+        interleave_gpsimd(0, 1, a1)
         on_unit(turn_x, 2, 0)
         add_bias(b0)
         on_unit(turn_x, 2, 1)
-        interleave_scalar(1)
+        interleave_scalar(1, 0)
         find_max(a0)
         find_max(b0)
         exponent(a0)
@@ -442,148 +456,150 @@ def tile_chunkflooredmessagemiddlescore_kernel(tc, x_bytes, x_scale, we_words, w
         scale_gain()
         invert_sums(0)
         find_max(b1)
+        warm_up(SCORE_BANK[0], WARM[3])
         message_first(0)
         message_second(0)
         turn_v(0, TURN_BANK[2])
+        warm_up(SCORE_BANK[1], WARM[4])
         exponent(a1)
         exponent(b1)
-        quantize_trans(1)
+        interleave_vector(1, 1)
+        for p in range(PAIRS):
+            for h in range(2):
+                quantize_trans(p, h)
         on_unit(widen, 2, 2)
         on_unit(widen, 3, 0)
-        quantize_trans(0)
         empty_v(0)
         on_unit(turn_x, 2, 2)
         quantize_and_pass_on(0)
 
         for k in range(2, LAST_TILE):
             on_unit(empty_scalar, k, 1)
-            on_unit(quantize_and_emit, k, 0)
-            on_tile(invert_sums, k - 1)
+            on_tile(invert_first, k - 1)
             on_tile(weigh, k - WEIGH_LAG)
-            on_unit(turn_x, k + 1, 0)
+            on_unit(quantize_and_emit, k, 0)
+            on_tile(invert_second, k - 1)
             on_tile(message_first, k - 1)
             on_tile(message_second, k - 1)
             on_unit(empty_scalar, k, 2)
             on_tile(floor_first, k - 2)
+            on_tile(turn_v, k - 1)
+            on_unit(turn_x, k + 1, 0)
 
             on_unit(quantize_and_emit, k, 1)
-            on_tile(turn_v, k - 1)
             on_tile(lift_first, k - 2)
-            on_unit(widen, k + 1, 1)
+            on_unit(widen, k + 1, 2)
             on_unit(add_bias, k, 0)
             on_unit(empty_vector, k, 2)
+            on_unit(turn_x, k + 1, 2)
             on_unit(find_max, k, 0)
-            on_unit(widen, k + 1, 2)
+            on_unit(widen, k + 1, 1)
+            on_tile(empty_v, k - 1)
             on_unit(empty_scalar, k + 1, 0)
+            on_tile(floor_second, k - 2)
 
             on_unit(quantize_and_emit, k, 2)
-            on_unit(exponent, k, 0)
-            on_tile(empty_v, k - 1)
-            on_unit(turn_x, k + 1, 1)
-            on_unit(turn_x, k + 1, 2)
-            on_unit(add_bias, k, 1)
-            on_tile(floor_second, k - 2)
             on_tile(multiply_gpsimd, k - 2)
-            on_unit(empty_vector, k + 1, 0)
+            on_unit(turn_x, k + 1, 1)
+            on_unit(exponent, k, 0)
+            on_unit(add_bias, k, 1)
+            on_unit(find_max, k - 1, 2)
             on_unit(find_max, k, 1)
             on_unit(widen, k + 2, 0)
-            on_unit(find_max, k - 1, 2)
-            on_unit(exponent, k, 1)
-            on_unit(add_bias, k, 2)
             on_unit(exponent, k - 1, 2)
+            on_unit(exponent, k, 1)
 
             on_tile(quantize_and_pass_on, k - 1)
-            on_unit(empty_vector, k + 1, 1)
+            on_unit(add_bias, k, 2)
 
         last = LAST_TILE
         first_end, second_end = unit_of[last, 0], unit_of[last, 2]
         middle = {i: unit_of[i, 1] for i in range(TILES)}
+        widen(middle[last])
         empty_scalar(second_end)
         quantize_and_emit(first_end)
-        invert_sums(last - 1)
+        invert_first(last - 1)
         weigh(last - WEIGH_LAG)
+        invert_second(last - 1)
         turn_x(middle[last - 1])
+        floor_first(last - 2)
         message_first(last - 1)
         message_second(last - 1)
         empty_scalar(middle[last - 2])
-        floor_first(last - 2)
 
         quantize_and_emit(second_end)
         turn_v(last - 1)
-        lift_first(last - 2)
-        widen(middle[last])
         turn_x(middle[last])
+        lift_first(last - 2)
         add_bias(first_end)
         find_max(middle[last - 3])
         find_max(first_end)
         empty_scalar(middle[last - 1])
 
         quantize_and_emit(middle[last - 2])
-        exponent(first_end)
         empty_v(last - 1)
+        empty_scalar(middle[last])
         add_bias(second_end)
         quantize_and_emit(middle[last - 1])
+        quantize_and_pass_on(last - 1, TURN_BANK[0:2])
+        exponent(first_end)
+        find_max(second_end)
+        quantize_and_emit(middle[last], SCORE_BANK[1])
         floor_second(last - 2)
         multiply_gpsimd(last - 2)
-        empty_scalar(middle[last])
-        find_max(second_end)
-        add_bias(middle[last - 2])
         exponent(second_end)
-        add_bias(middle[last - 1])
         exponent(middle[last - 3])
-
-        quantize_and_emit(middle[last], SCORE_BANK[1])
-        quantize_and_pass_on(last - 1)
-        invert_sums(last)
-        find_max(middle[last - 2])
-        find_max(middle[last - 1])
-        exponent(middle[last - 2])
         floor_first(last - 1)
         cut_second(last - 1)
-        message_first(last)
-        exponent(middle[last - 1])
+        add_bias(middle[last - 2])
+        add_bias(middle[last - 1])
+        find_max(middle[last - 2])
         add_bias(middle[last])
-        lift_second(last - 1)
-        message_second(last)
-        for i in range(TENSOR_FINISHES):
-            if i == 1:
-                turn_v(last)
-            open_total(1 + 2 * i, FINISH_BANKS[i])
+        open_total(4, SCORE_BANK[1])
+        find_max(middle[last - 1])
         find_max(middle[last])
+        exponent(middle[last - 2])
+        lift_second(last - 1)
+        exponent(middle[last - 1])
         exponent(middle[last])
 
         done = TILES - WEIGH_LAG
-        log_weights(0, done)
-        weigh(done)
+        invert_sums(last)
         multiply(last - 1)
-        empty_v_vector(last)
-        weigh(last - 2)
-        quantize_and_pass_on(last)
+        message_first(last)
+        message_second(last)
+        turn_v(last)
+        open_total(2, TURN_BANK[2])
+        log_weights(0, done)
         take_log(0)
-        weigh(last - 1)
+        weigh(done)
+        weigh(last - 2)
         make_shifts(0, done)
-        take_log(1)
-        close_total(1)
+        empty_v(last)
         finish(0)
+        quantize_and_pass_on(last)
+        take_log(1)
         take_log(2)
+        close_total(2)
+        finish(1)
+        weigh(last - 1)
+        take_log(3)
         floor_first(last)
         floor_second(last)
         log_weights(done, last)
         take_log(4)
-        finish(2)
+        close_total(4)
+        finish(3)
         make_shifts(done, last)
-        take_log(3)
-        close_total(3)
         multiply(last)
-        finish(4)
         take_log(5)
-        finish_total(1)
+        finish_total(2)
+        finish(5)
         weigh(last)
         take_log(6)
-        finish(5)
-        log_weights(last, TILES)
         take_log(last)
+        log_weights(last, TILES)
         finish(6)
         make_shifts(last, TILES)
-        finish_total(3)
+        finish_total(4)
         finish(last)

@@ -36,7 +36,7 @@ SCORE_BANK = (3, 4, 5)
 MESSAGE_BANKS = (6, 7)
 VECTOR_EMPTIES = 3
 WARM = (512, 256, 0, 512, 256)
-VECTOR_SHARE = 160
+VECTOR_SHARE = 64
 
 
 def tile_chunkflooredmessagemiddlescore_kernel(tc, x_bytes, x_scale, we_words, we_scales, be, ends, gain, trans, out):
@@ -170,7 +170,7 @@ def tile_chunkflooredmessagemiddlescore_kernel(tc, x_bytes, x_scale, we_words, w
             )
 
         x_wide, x_turned, grouped, x_codes, x_scales, e_ps = {}, {}, {}, {}, {}, {}
-        neg_n, neg_max, expo = {}, {}, {}
+        neg_n, neg_max, expo, room = {}, {}, {}, {}
         sums = [keep.tile([P, PAIRS], F32, name="sums%d" % i) for i in range(TILES)]
         inverse = [keep.tile([P, PAIRS], F32, name="inv%d" % i) for i in range(TILES)]
         weight = keep.tile([P, TILES], F32, name="weight")
@@ -193,14 +193,19 @@ def tile_chunkflooredmessagemiddlescore_kernel(tc, x_bytes, x_scale, we_words, w
             turn(x_turned[s], x_wide[s][:])
 
         def vector_share(s):
-            if s < VECTOR_EMPTIES:
+            k, place = round_of[units[s]], place_of[units[s]]
+            if s < VECTOR_EMPTIES or (place == 2 and k < TILES) or (place == 1 and 2 <= k < WEIGH_LAG):
                 return PASSES * P
-            return VECTOR_SHARE if place_of[units[s]] == 2 and round_of[units[s]] < LAST_TILE else 0
+            return VECTOR_SHARE if place == 1 and 2 <= k < LAST_TILE else 0
 
         def scaled_parts(s, first, end):
             i, l = units[s]
             if s not in grouped:
-                grouped[s] = work.tile([P, PASSES, P, 4], BF16, name="xg", tag="xg", bufs=7, align_bytes=64)
+                if place_of[units[s]] == 2 and round_of[units[s]] != LAST_TILE:
+                    room[s] = keep.tile([P, PASSES, P, 4], BF16, name="xg%d" % s, align_bytes=64)
+                else:
+                    room[s] = work.tile([P, PAIRS * PASSES, P, 4], BF16, name="xg", tag="xg", bufs=5, align_bytes=64)
+                grouped[s] = room[s][:, 0:PASSES]
             found = []
             for g in range(PASSES):
                 lo, hi = max(first - g * P, 0), min(end - g * P, P)
@@ -272,16 +277,12 @@ def tile_chunkflooredmessagemiddlescore_kernel(tc, x_bytes, x_scale, we_words, w
 
         v, v_turned, v_grouped, v_codes, v_scales, m_ps, cut0, floored1, product, log_a = {}, {}, {}, {}, {}, {}, {}, {}, {}, {}
 
-        floored0, cut1 = {}, {}
+        cut1 = {}
+
+        cuts, lifted = {}, {}
 
         def invert_sums(i):
             nc.vector.reciprocal(out=inverse[i][:], in_=sums[i][:])
-
-        def invert_first(i):
-            nc.vector.reciprocal(out=inverse[i][:, 0:1], in_=sums[i][:, 0:1])
-
-        def invert_second(i):
-            nc.vector.reciprocal(out=inverse[i][:, 1:2], in_=sums[i][:, 1:2])
 
         def message(i, p):
             nc.vector.scalar_tensor_tensor(
@@ -345,18 +346,25 @@ def tile_chunkflooredmessagemiddlescore_kernel(tc, x_bytes, x_scale, we_words, w
                 out=product[i][:], in0=cut0[i][:], scalar=FLOOR_VALUE, in1=floored1[i][:], op0=ALU.add, op1=ALU.mult,
             )
 
-        def lift_first(i):
-            floored0[i] = grouped[unit_of[rounds[i + 2][1]]][:].rearrange("p g r t -> p (g r t)").bitcast(F32)
-            nc.gpsimd.tensor_scalar(out=floored0[i], in0=cut0[i][:], scalar1=1.0, scalar2=FLOOR_VALUE, op0=ALU.mult, op1=ALU.add)
+        def cut_both(i):
+            cuts[i] = work.tile([P, PAIRS, T], F32, name="cuts", tag="cuts", bufs=1)
+            for p in range(PAIRS):
+                nc.scalar.activation(out=cuts[i][:, p, :], in_=m_ps[i, p][:], func=ACT.Relu, bias=FLOOR_SHIFT, scale=1.0)
 
-        def multiply_gpsimd(i):
-            product[i] = keep.tile([P, T], F32, name="prod%d" % i)
-            nc.gpsimd.tensor_tensor(out=product[i][:], in0=floored0[i], in1=floored1[i][:], op=ALU.mult)
+        def lift_both(i):
+            lifted[i] = room[unit_of[rounds[i + 2][1]]][:].rearrange("p g r t -> p (g r t)").bitcast(F32)
+            nc.gpsimd.tensor_scalar(
+                out=lifted[i], in0=cuts[i][:].rearrange("p a n -> p (a n)"), scalar1=1.0, scalar2=FLOOR_VALUE, op0=ALU.mult, op1=ALU.add,
+            )
+
+        def multiply_lifted(i, spent=None):
+            product[i] = room[unit_of[rounds[i + 2][2]] if spent is None else spent][:].rearrange("p g r t -> p (g r t)").bitcast(F32)
+            nc.gpsimd.tensor_tensor(out=product[i], in0=lifted[i][:, 0:T], in1=lifted[i][:, T:2 * T], op=ALU.mult)
 
         def weigh(i):
             terms = work.tile([P, T], F32, name="weighted", tag="weighted", bufs=1)
             nc.vector.scalar_tensor_tensor(
-                out=terms[:], in0=expo[unit_of[i, 1]][:], scalar=1.0 / T, in1=product[i][:], op0=ALU.mult, op1=ALU.mult,
+                out=terms[:], in0=expo[unit_of[i, 1]][:], scalar=1.0 / T, in1=product[i][:, :], op0=ALU.mult, op1=ALU.mult,
                 accum_out=weight[:, i:i + 1],
             )
 
@@ -475,37 +483,38 @@ def tile_chunkflooredmessagemiddlescore_kernel(tc, x_bytes, x_scale, we_words, w
 
         for k in range(2, LAST_TILE):
             on_unit(empty_scalar, k, 1)
-            on_tile(invert_first, k - 1)
+            if k < WEIGH_LAG:
+                on_unit(empty_vector, k, 1)
             on_tile(weigh, k - WEIGH_LAG)
+            on_tile(invert_sums, k - 1)
             on_unit(quantize_and_emit, k, 0)
-            on_tile(invert_second, k - 1)
-            on_tile(message_first, k - 1)
-            on_tile(message_second, k - 1)
-            on_unit(empty_scalar, k, 2)
-            on_tile(floor_first, k - 2)
-            on_tile(turn_v, k - 1)
             on_unit(turn_x, k + 1, 0)
+            on_tile(cut_both, k - 2)
+            on_tile(message_first, k - 1)
+            if k >= WEIGH_LAG:
+                on_unit(empty_vector, k, 1)
+            on_tile(message_second, k - 1)
 
             on_unit(quantize_and_emit, k, 1)
-            on_tile(lift_first, k - 2)
+            on_tile(turn_v, k - 1)
+            on_tile(lift_both, k - 2)
             on_unit(widen, k + 1, 2)
+            on_unit(widen, k + 1, 1)
             on_unit(add_bias, k, 0)
             on_unit(empty_vector, k, 2)
             on_unit(turn_x, k + 1, 2)
             on_unit(find_max, k, 0)
-            on_unit(widen, k + 1, 1)
-            on_tile(empty_v, k - 1)
             on_unit(empty_scalar, k + 1, 0)
-            on_tile(floor_second, k - 2)
 
             on_unit(quantize_and_emit, k, 2)
-            on_tile(multiply_gpsimd, k - 2)
+            on_tile(multiply_lifted, k - 2)
+            on_unit(widen, k + 2, 0)
+            on_tile(empty_v, k - 1)
             on_unit(turn_x, k + 1, 1)
             on_unit(exponent, k, 0)
             on_unit(add_bias, k, 1)
             on_unit(find_max, k - 1, 2)
             on_unit(find_max, k, 1)
-            on_unit(widen, k + 2, 0)
             on_unit(exponent, k - 1, 2)
             on_unit(exponent, k, 1)
 
@@ -515,24 +524,22 @@ def tile_chunkflooredmessagemiddlescore_kernel(tc, x_bytes, x_scale, we_words, w
         last = LAST_TILE
         first_end, second_end = unit_of[last, 0], unit_of[last, 2]
         middle = {i: unit_of[i, 1] for i in range(TILES)}
-        widen(middle[last])
         empty_scalar(second_end)
-        quantize_and_emit(first_end)
-        invert_first(last - 1)
         weigh(last - WEIGH_LAG)
-        invert_second(last - 1)
+        invert_sums(last - 1)
+        quantize_and_emit(first_end)
         turn_x(middle[last - 1])
-        floor_first(last - 2)
+        cut_both(last - 2)
+        widen(middle[last])
         message_first(last - 1)
         message_second(last - 1)
-        empty_scalar(middle[last - 2])
 
         quantize_and_emit(second_end)
         turn_v(last - 1)
-        turn_x(middle[last])
-        lift_first(last - 2)
+        lift_both(last - 2)
         add_bias(first_end)
-        find_max(middle[last - 3])
+        empty_vector(middle[last - 2])
+        turn_x(middle[last])
         find_max(first_end)
         empty_scalar(middle[last - 1])
 
@@ -545,21 +552,21 @@ def tile_chunkflooredmessagemiddlescore_kernel(tc, x_bytes, x_scale, we_words, w
         exponent(first_end)
         find_max(second_end)
         quantize_and_emit(middle[last], SCORE_BANK[1])
-        floor_second(last - 2)
-        multiply_gpsimd(last - 2)
+        multiply_lifted(last - 2, middle[last])
         exponent(second_end)
-        exponent(middle[last - 3])
         floor_first(last - 1)
         cut_second(last - 1)
         add_bias(middle[last - 2])
+        find_max(middle[last - 3])
         add_bias(middle[last - 1])
+        exponent(middle[last - 3])
         find_max(middle[last - 2])
         add_bias(middle[last])
         open_total(4, SCORE_BANK[1])
         find_max(middle[last - 1])
         find_max(middle[last])
-        exponent(middle[last - 2])
         lift_second(last - 1)
+        exponent(middle[last - 2])
         exponent(middle[last - 1])
         exponent(middle[last])
 

@@ -30,24 +30,28 @@ FLOOR_SHIFT = 14.4
 FLOOR_VALUE = 1.6
 
 MIDDLE_LAG = 2
+FIRST_ROUND = 2
+FLOOR_LAG = 2
 WEIGH_LAG = 4
+
 TURN_BANK = (0, 1, 2)
 SCORE_BANK = (3, 4, 5)
 MESSAGE_BANKS = (6, 7)
-VECTOR_EMPTIES = 3
-WARM = (512, 256, 0, 512, 256)
+
+VECTOR_FIRST = 3
 VECTOR_SHARE = 64
+
+FIRST_TENSOR_TILE, SECOND_TENSOR_TILE = 2, 4
 
 
 def tile_chunkflooredmessagemiddlescore_kernel(tc, x_bytes, x_scale, we_words, we_scales, be, ends, gain, trans, out):
     nc = tc.nc
 
     rounds = [[(i, 0), (i, 2)] + ([(i - MIDDLE_LAG, 1)] if i >= MIDDLE_LAG else []) for i in range(TILES)]
-    rounds.append([(TILES - 2, 1), None, (TILES - 1, 1)])
-    units = [u for found in rounds for u in found if u is not None]
-    round_of = {u: k for k, found in enumerate(rounds) for u in found}
-    place_of = {u: j for found in rounds for j, u in enumerate(found)}
-    unit_of = {u: s for s, u in enumerate(units)}
+    rounds.append([(LAST_TILE - 1, 1), None, (LAST_TILE, 1)])
+    units = [unit for members in rounds for unit in members if unit is not None]
+    round_of = {unit: k for k, members in enumerate(rounds) for unit in members}
+    place_of = {unit: place for members in rounds for place, unit in enumerate(members)}
 
     with ExitStack() as ctx:
         keep = ctx.enter_context(tc.tile_pool(name="keep", bufs=1))
@@ -57,7 +61,7 @@ def tile_chunkflooredmessagemiddlescore_kernel(tc, x_bytes, x_scale, we_words, w
 
         rows = keep.tile([P, T], BF16, name="rows")
         be_wide = keep.tile([P, T], BF16, name="be_wide")
-        pick = keep.tile([P, 2 * L], BF16, name="pick")
+        pick = keep.tile([P, 2 * PAIRS], BF16, name="pick")
         gain_raw = keep.tile([P, PAIRS * T], BF16, name="gain_raw")
         gain_wide = keep.tile([P, PAIRS * T], BF16, name="gain_wide")
         we_s = keep.tile([P, PASSES, T], U8, name="we_s", align_bytes=64)
@@ -73,25 +77,26 @@ def tile_chunkflooredmessagemiddlescore_kernel(tc, x_bytes, x_scale, we_words, w
         x_raw, trans_raw = {}, {}
 
         def load_x(i, positions):
-            found = list(range(L))[positions]
-            raw = keep.tile([P, len(found), D], U8, name="xbytes%d_%d" % (i, found[0]))
+            named = list(range(L))[positions]
+            raw = keep.tile([P, len(named), D], U8, name="xbytes%d_%d" % (i, named[0]))
             nc.sync.dma_start(out=raw[:], in_=x_bytes[positions, i * P:(i + 1) * P, :].rearrange("l r k -> r l k"))
-            for j, l in enumerate(found):
-                x_raw[unit_of[i, l]] = raw[:, j, :]
+            for j, l in enumerate(named):
+                x_raw[i, l] = raw[:, j, :]
 
         def load_trans(p):
             trans_raw[p] = keep.tile([P, 4, T], BF16, name="tr_raw%d" % p)
             nc.sync.dma_start(out=trans_raw[p][:], in_=trans[p].rearrange("(p j) n -> p j n", j=4))
 
+        first, middle, second, both_ends = slice(0, 1), slice(1, 2), slice(2, 3), slice(0, 3, 2)
         nc.scalar.dma_start(out=xs_all[:].rearrange("p c q -> p (c q)"), in_=x_scale.rearrange("l i j -> (l i j)").partition_broadcast(P))
-        load_x(0, slice(0, 1))
+        load_x(0, first)
         nc.sync.dma_start(out=rows[0:1, :], in_=be.rearrange("(o n) -> o n", o=1))
         nc.sync.dma_start(out=rows[32:65:32, :], in_=ends)
-        load_x(0, slice(2, 3))
-        load_x(1, slice(0, 3, 2))
+        load_x(0, second)
+        load_x(1, both_ends)
         nc.sync.dma_start(out=we_w[:].bitcast(I32), in_=we_words.rearrange("g p n -> p g n").bitcast(I32))
-        load_x(2, slice(0, 3, 2))
-        for q in range(4):
+        load_x(2, both_ends)
+        for q in range(QUADS):
             nc.sync.dma_start(
                 out=we_s[32 * q:32 * q + 4, :, :].bitcast(I32),
                 in_=we_scales[:, 4 * q:4 * q + 4, :].rearrange("g r n -> r g n").bitcast(I32),
@@ -99,17 +104,17 @@ def tile_chunkflooredmessagemiddlescore_kernel(tc, x_bytes, x_scale, we_words, w
         load_trans(1)
         load_trans(0)
         nc.sync.dma_start(out=gain_raw[:], in_=gain.rearrange("a n -> (a n)").partition_broadcast(P))
-        load_x(0, slice(1, 2))
+        load_x(0, middle)
         nc.sync.dma_start(out=be_wide[:], in_=be.partition_broadcast(P))
         for i in range(3, TILES + MIDDLE_LAG):
             if i < TILES:
-                load_x(i, slice(0, 3, 2))
-            load_x(i - MIDDLE_LAG, slice(1, 2))
+                load_x(i, both_ends)
+            load_x(i - MIDDLE_LAG, middle)
 
         nc.gpsimd.memset(pick[:], 0.0)
         nc.gpsimd.memset(pick[0:1, :], -1.0)
         nc.gpsimd.memset(pick[32:33, 0:2], -1.0)
-        nc.gpsimd.memset(pick[64:65, 4:6], -1.0)
+        nc.gpsimd.memset(pick[64:65, 2:4], -1.0)
         make_identity(nc, ident[:])
         neg_ident = keep.tile([P, P], F32, name="neg_ident")
         nc.gpsimd.tensor_scalar(out=neg_ident[:], in0=ident[:], scalar1=-1.0, scalar2=0.0, op0=ALU.mult, op1=ALU.add)
@@ -121,14 +126,13 @@ def tile_chunkflooredmessagemiddlescore_kernel(tc, x_bytes, x_scale, we_words, w
             return psum.tile(shape, F32, name="bank%d" % bank, tag="bank%d" % bank)
 
         def warm_up(bank, columns):
-            if columns:
-                nc.tensor.matmul(bank_tile(bank, [P, columns])[:], lhsT=zeros[:, 0:P], rhs=zeros[:, 0:columns], start=True, stop=True)
+            nc.tensor.matmul(bank_tile(bank, [P, columns])[:], lhsT=zeros[:, 0:P], rhs=zeros[:, 0:columns], start=True, stop=True)
 
         neg_bias = {}
 
         def spread_bias(l):
             acc = bank_tile(MESSAGE_BANKS[l // 2], [P, T])
-            nc.tensor.matmul(acc[:], lhsT=pick[:, 2 * l:2 * l + 1].to_broadcast([P, P]), rhs=rows[:], start=True, stop=True)
+            nc.tensor.matmul(acc[:], lhsT=pick[:, l:l + 1].to_broadcast([P, P]), rhs=rows[:], start=True, stop=True)
             neg_bias[l] = keep.tile([P, T], F32, name="neg_bias%d" % l)
             nc.vector.tensor_copy(out=neg_bias[l][:], in_=acc[:])
 
@@ -139,38 +143,37 @@ def tile_chunkflooredmessagemiddlescore_kernel(tc, x_bytes, x_scale, we_words, w
         trans_codes = keep.tile([P, PAIRS, T], U32, name="tr_codes", align_bytes=64)
         trans_scales = keep.tile([P, PAIRS, T], U8, name="tr_scales", align_bytes=64)
 
-        def interleave_views(p, h):
-            half = keep.tile([P, HALF, 4], BF16, name="tr_grouped%d_%d" % (p, h), align_bytes=64)
-            trans_grouped[p, h] = half[:]
+        def group_views(cols):
             return (
-                half[:].rearrange("p (c i) t -> p c t i", i=4),
-                trans_raw[p][:, :, h * HALF:(h + 1) * HALF].rearrange("p t (c i) -> p c t i", i=4),
+                trans_grouped[1][:, cols, :].rearrange("p (c i) t -> p c t i", i=4),
+                trans_raw[1][:, :, cols].rearrange("p t (c i) -> p c t i", i=4),
             )
 
-        def interleave_scalar(p, h):
-            dst, src = interleave_views(p, h)
+        def group_second_left():
+            whole = keep.tile([P, T, 4], BF16, name="tr_grouped1", align_bytes=64)
+            trans_grouped[1] = whole[:]
+            dst, src = group_views(slice(0, HALF))
             nc.scalar.copy(out=dst, in_=src)
 
-        def interleave_vector(p, h):
-            dst, src = interleave_views(p, h)
+        def group_second_right():
+            dst, src = group_views(slice(HALF, T))
             nc.vector.tensor_copy(out=dst, in_=src)
 
-        def interleave_gpsimd(p, h, spent):
-            trans_grouped[p, h] = grouped[spent][:].rearrange("p g r t -> p (g r) t")
+        def group_first(spent):
+            trans_grouped[0] = x_room[spent][:].rearrange("p g r t -> p (g r) t")
             nc.gpsimd.tensor_scalar(
-                out=trans_grouped[p, h], in0=trans_raw[p][:, :, h * HALF:(h + 1) * HALF].rearrange("p t n -> p n t"),
+                out=trans_grouped[0], in0=trans_raw[0][:].rearrange("p t n -> p n t"),
                 scalar1=1.0, scalar2=0.0, op0=ALU.mult, op1=ALU.add,
             )
 
-        def quantize_trans(p, h):
-            cols = slice(h * HALF, (h + 1) * HALF)
+        def quantize_trans(p):
             nc.vector.quantize_mx(
-                out=trans_codes[:, p, cols].bitcast(FP8X4), scales=trans_scales[:, p, cols],
-                in_=trans_grouped[p, h].rearrange("p n t -> p (n t)"),
+                out=trans_codes[:, p, :].bitcast(FP8X4), scales=trans_scales[:, p, :],
+                in_=trans_grouped[p].rearrange("p n t -> p (n t)"),
             )
 
-        x_wide, x_turned, grouped, x_codes, x_scales, e_ps = {}, {}, {}, {}, {}, {}
-        neg_n, neg_max, expo, room = {}, {}, {}, {}
+        x_wide, x_turned, x_room, x_grouped, e_ps = {}, {}, {}, {}, {}
+        neg_n, neg_max, expo, end_expo = {}, {}, {}, {}
         sums = [keep.tile([P, PAIRS], F32, name="sums%d" % i) for i in range(TILES)]
         inverse = [keep.tile([P, PAIRS], F32, name="inv%d" % i) for i in range(TILES)]
         weight = keep.tile([P, TILES], F32, name="weight")
@@ -178,9 +181,9 @@ def tile_chunkflooredmessagemiddlescore_kernel(tc, x_bytes, x_scale, we_words, w
         mid_neg_max = keep.tile([P, TILES], F32, name="mid_neg_max")
         shift = keep.tile([P, TILES], F32, name="shift")
 
-        def widen(s):
-            x_wide[s] = work.tile([P, D], BF16, name="xw", tag="xw", bufs=6)
-            nc.scalar.copy(out=x_wide[s][:], in_=x_raw[s].bitcast(FP8))
+        def widen(unit):
+            x_wide[unit] = work.tile([P, D], BF16, name="xw", tag="xw", bufs=6)
+            nc.scalar.copy(out=x_wide[unit][:], in_=x_raw[unit].bitcast(FP8))
 
         def turn(bank, values):
             words = values.bitcast(F32)
@@ -188,114 +191,111 @@ def tile_chunkflooredmessagemiddlescore_kernel(tc, x_bytes, x_scale, we_words, w
                 for u in range(2):
                     nc.tensor.transpose(bank[:, g, u, :], words[:, PASS_WORDS * g + u:PASS_WORDS * (g + 1):2], ident[:])
 
-        def turn_x(s, bank=None):
-            x_turned[s] = bank_tile(TURN_BANK[place_of[units[s]]] if bank is None else bank, [P, PASSES, 2, P])
-            turn(x_turned[s], x_wide[s][:])
+        def turn_x(unit, bank=None):
+            x_turned[unit] = bank_tile(TURN_BANK[place_of[unit]] if bank is None else bank, [P, PASSES, 2, P])
+            turn(x_turned[unit], x_wide[unit][:])
 
-        def vector_share(s):
-            k, place = round_of[units[s]], place_of[units[s]]
-            if s < VECTOR_EMPTIES or (place == 2 and k < TILES) or (place == 1 and 2 <= k < WEIGH_LAG):
+        def vector_share(unit):
+            k, place = round_of[unit], place_of[unit]
+            if units.index(unit) < VECTOR_FIRST or (place == 2 and k < TILES) or (place == 1 and FIRST_ROUND <= k < WEIGH_LAG):
                 return PASSES * P
-            return VECTOR_SHARE if place == 1 and 2 <= k < LAST_TILE else 0
+            if (k, place) == (FIRST_ROUND + 1, 0):
+                return P
+            return VECTOR_SHARE if place == 1 and FIRST_ROUND <= k < LAST_TILE else 0
 
-        def scaled_parts(s, first, end):
-            i, l = units[s]
-            if s not in grouped:
-                if place_of[units[s]] == 2 and round_of[units[s]] != LAST_TILE:
-                    room[s] = keep.tile([P, PASSES, P, 4], BF16, name="xg%d" % s, align_bytes=64)
-                else:
-                    room[s] = work.tile([P, PAIRS * PASSES, P, 4], BF16, name="xg", tag="xg", bufs=5, align_bytes=64)
-                grouped[s] = room[s][:, 0:PASSES]
-            found = []
+        def make_room(unit):
+            name = "xg%d" % units.index(unit)
+            if unit == (1, 2):
+                x_room[unit] = keep.tile([P, 2 * PASSES, P, 4], BF16, name=name, align_bytes=64)
+            elif place_of[unit] == 2 and round_of[unit] != LAST_TILE:
+                x_room[unit] = keep.tile([P, PASSES, P, 4], BF16, name=name, align_bytes=64)
+            else:
+                x_room[unit] = work.tile([P, PASSES, P, 4], BF16, name="xg", tag="xg", bufs=6, align_bytes=64)
+            x_grouped[unit] = x_room[unit][:, 0:PASSES]
+
+        def scaled_parts(unit, begin, end):
+            i, l = unit
+            if unit not in x_room:
+                make_room(unit)
+            parts = []
             for g in range(PASSES):
-                lo, hi = max(first - g * P, 0), min(end - g * P, P)
+                lo, hi = max(begin - g * P, 0), min(end - g * P, P)
                 if lo < hi:
-                    src = x_turned[s][:, g].rearrange("p u r -> p (u r)").bitcast(BF16).rearrange("p (u r e) -> p r u e", u=2, e=2)
-                    dst = grouped[s][:, g].rearrange("p r (u e) -> p r u e", u=2)
-                    c = (l * TILES + i) * PASSES + g
-                    found.append((src[:, lo:hi], dst[:, lo:hi], xs[:, c:c + 1]))
-            return found
+                    src = x_turned[unit][:, g].rearrange("p u r -> p (u r)").bitcast(BF16).rearrange("p (u r e) -> p r u e", u=2, e=2)
+                    dst = x_grouped[unit][:, g].rearrange("p r (u e) -> p r u e", u=2)
+                    column = (l * TILES + i) * PASSES + g
+                    parts.append((src[:, lo:hi], dst[:, lo:hi], xs[:, column:column + 1]))
+            return parts
 
-        def empty_vector(s):
-            for src, dst, scale in scaled_parts(s, PASSES * P - vector_share(s), PASSES * P):
+        def empty_vector(unit):
+            for src, dst, scale in scaled_parts(unit, PASSES * P - vector_share(unit), PASSES * P):
                 nc.vector.tensor_scalar(out=dst, in0=src, scalar1=scale, scalar2=None, op0=ALU.mult)
 
-        def empty_scalar(s):
-            for src, dst, scale in scaled_parts(s, 0, PASSES * P - vector_share(s)):
+        def empty_scalar(unit):
+            for src, dst, scale in scaled_parts(unit, 0, PASSES * P - vector_share(unit)):
                 nc.scalar.activation(out=dst, in_=src, func=ACT.Copy, scale=scale)
 
-        def quantize_x(s):
-            x_codes[s] = work.tile([P, PASSES * P], U32, name="xq", tag="xq", align_bytes=64)
-            x_scales[s] = work.tile([P, PASSES * P], U8, name="xqs", tag="xqs", align_bytes=64)
+        def score(unit, bank=None):
+            codes = work.tile([P, PASSES * P], U32, name="xq", tag="xq", align_bytes=64)
+            scales = work.tile([P, PASSES * P], U8, name="xqs", tag="xqs", align_bytes=64)
             nc.vector.quantize_mx(
-                out=x_codes[s][:].bitcast(FP8X4), scales=x_scales[s][:],
-                in_=grouped[s][:].rearrange("p g r t -> p (g r t)"),
+                out=codes[:].bitcast(FP8X4), scales=scales[:], in_=x_grouped[unit].rearrange("p g r t -> p (g r t)"),
             )
-
-        def emit(s, bank):
-            e_ps[s] = bank_tile(SCORE_BANK[place_of[units[s]]] if bank is None else bank, [P, T])
+            e_ps[unit] = bank_tile(SCORE_BANK[place_of[unit]] if bank is None else bank, [P, T])
             for g in range(PASSES):
                 cols = slice(g * P, (g + 1) * P)
                 nc.tensor.matmul_mx(
-                    out=e_ps[s][:], lhsT=x_codes[s][:, cols].bitcast(FP8X4), lhsT_scale=x_scales[s][:, cols],
+                    out=e_ps[unit][:], lhsT=codes[:, cols].bitcast(FP8X4), lhsT_scale=scales[:, cols],
                     rhs=we_w[:, g, :].bitcast(FP4X4), rhs_scale=we_s[:, g, :], start=(g == 0), stop=(g == PASSES - 1),
                 )
 
-        def add_bias(s):
-            i, l = units[s]
+        def add_bias(unit):
+            i, l = unit
             if l == 1:
-                neg_n[s] = keep.tile([P, T], F32, name="neg_mid%d" % i)
-            else:
-                neg_n[s] = work.tile([P, T], F32, name="neg_end", tag="neg_end")
-            if l == 1:
+                neg_n[unit] = keep.tile([P, T], F32, name="neg_mid%d" % i)
                 nc.vector.scalar_tensor_tensor(
-                    out=neg_n[s][:], in0=e_ps[s][:], scalar=-1.0, in1=be_wide[:], op0=ALU.mult, op1=ALU.subtract,
+                    out=neg_n[unit][:], in0=e_ps[unit][:], scalar=-1.0, in1=be_wide[:], op0=ALU.mult, op1=ALU.subtract,
                 )
             else:
-                nc.vector.tensor_tensor(out=neg_n[s][:], in0=neg_bias[l][:], in1=e_ps[s][:], op=ALU.subtract)
+                neg_n[unit] = work.tile([P, T], F32, name="neg_end", tag="neg_end")
+                nc.vector.tensor_tensor(out=neg_n[unit][:], in0=neg_bias[l][:], in1=e_ps[unit][:], op=ALU.subtract)
 
-        def find_max(s):
-            i, l = units[s]
+        def find_max(unit):
+            i, l = unit
             if l == 1:
-                neg_max[s] = mid_neg_max[:, i:i + 1]
+                neg_max[unit] = mid_neg_max[:, i:i + 1]
             else:
-                column = keep.tile([P, 1], F32, name="neg_max%d" % s)
-                neg_max[s] = column[:]
-            nc.vector.tensor_reduce(out=neg_max[s], in_=neg_n[s][:], axis=AX.X, op=ALU.min)
+                column = keep.tile([P, 1], F32, name="neg_max%d" % units.index(unit))
+                neg_max[unit] = column[:]
+            nc.vector.tensor_reduce(out=neg_max[unit], in_=neg_n[unit][:], axis=AX.X, op=ALU.min)
 
-        def exponent(s):
-            i, l = units[s]
+        def exponent(unit):
+            i, l = unit
             if l == 1:
-                expo[s] = work.tile([P, T], F32, name="ex_mid", tag="ex_mid", bufs=4)
-                nc.scalar.activation(out=expo[s][:], in_=neg_n[s][:], func=ACT.Exp, bias=neg_max[s], scale=-1.0)
+                expo[unit] = work.tile([P, T], F32, name="ex_mid", tag="ex_mid")
+                nc.scalar.activation(out=expo[unit][:], in_=neg_n[unit][:], func=ACT.Exp, bias=neg_max[unit], scale=-1.0)
             else:
-                expo[s] = work.tile([P, T], F32, name="ex", tag="ex", bufs=8)
+                if i not in end_expo:
+                    end_expo[i] = work.tile([P, PAIRS, T], F32, name="ex", tag="ex")
+                expo[unit] = end_expo[i][:, l // 2, :]
                 nc.scalar.activation(
-                    out=expo[s][:], in_=neg_n[s][:], func=ACT.Exp, bias=neg_max[s], scale=-1.0,
+                    out=expo[unit], in_=neg_n[unit][:], func=ACT.Exp, bias=neg_max[unit], scale=-1.0,
                     accum_out=sums[i][:, l // 2:l // 2 + 1],
                 )
 
-        v, v_turned, v_grouped, v_codes, v_scales, m_ps, cut0, floored1, product, log_a = {}, {}, {}, {}, {}, {}, {}, {}, {}, {}
-
-        cut1 = {}
-
-        cuts, lifted = {}, {}
+        v, v_turned, v_grouped, m_ps = {}, {}, {}, {}
+        cuts, lifted, cut0, cut1, floored1, product, log_a, total = {}, {}, {}, {}, {}, {}, {}, {}
 
         def invert_sums(i):
             nc.vector.reciprocal(out=inverse[i][:], in_=sums[i][:])
 
         def message(i, p):
+            if p == 0:
+                v[i] = work.tile([P, PAIRS, T], BF16, name="v", tag="v", bufs=2)
             nc.vector.scalar_tensor_tensor(
-                out=v[i][:, p, :], in0=expo[unit_of[i, 2 * p]][:], scalar=inverse[i][:, p:p + 1],
+                out=v[i][:, p, :], in0=expo[i, 2 * p], scalar=inverse[i][:, p:p + 1],
                 in1=gain_wide[:, p * T:(p + 1) * T], op0=ALU.mult, op1=ALU.mult,
             )
-
-        def message_first(i):
-            v[i] = work.tile([P, PAIRS, T], BF16, name="v", tag="v", bufs=2)
-            message(i, 0)
-
-        def message_second(i):
-            message(i, 1)
 
         def turn_v(i, bank=TURN_BANK[1]):
             v_turned[i] = bank_tile(bank, [P, PAIRS, 2, P])
@@ -305,32 +305,39 @@ def tile_chunkflooredmessagemiddlescore_kernel(tc, x_bytes, x_scale, we_words, w
             v_grouped[i] = work.tile([P, PAIRS, P, 2], F32, name="vg", tag="vg", bufs=2, align_bytes=64)
             nc.scalar.copy(out=v_grouped[i][:], in_=v_turned[i][:].rearrange("p g u r -> p g r u"))
 
-        def quantize_v(i):
-            v_codes[i] = work.tile([P, PAIRS * P], U32, name="vq", tag="vq", bufs=2, align_bytes=64)
-            v_scales[i] = work.tile([P, PAIRS * P], U8, name="vqs", tag="vqs", bufs=2, align_bytes=64)
+        def pass_on(i, banks=MESSAGE_BANKS):
+            codes = work.tile([P, PAIRS * P], U32, name="vq", tag="vq", bufs=2, align_bytes=64)
+            scales = work.tile([P, PAIRS * P], U8, name="vqs", tag="vqs", bufs=2, align_bytes=64)
             nc.vector.quantize_mx(
-                out=v_codes[i][:].bitcast(FP8X4), scales=v_scales[i][:],
+                out=codes[:].bitcast(FP8X4), scales=scales[:],
                 in_=v_grouped[i][:].rearrange("p g r u -> p (g r u)").bitcast(BF16),
             )
-
-        def pass_on(i, banks):
             for p in range(PAIRS):
                 cols = slice(p * P, (p + 1) * P)
                 m_ps[i, p] = bank_tile(banks[p], [P, T])
                 nc.tensor.matmul_mx(
-                    out=m_ps[i, p][:], lhsT=v_codes[i][:, cols].bitcast(FP8X4), lhsT_scale=v_scales[i][:, cols],
+                    out=m_ps[i, p][:], lhsT=codes[:, cols].bitcast(FP8X4), lhsT_scale=scales[:, cols],
                     rhs=trans_codes[:, p, :].bitcast(FP8X4), rhs_scale=trans_scales[:, p, :], start=True, stop=True,
                 )
 
-        def floor_first(i):
+        def cut_both(i):
+            cuts[i] = work.tile([P, PAIRS, T], F32, name="cuts", tag="cuts", bufs=1)
+            for p in range(PAIRS):
+                nc.scalar.activation(out=cuts[i][:, p, :], in_=m_ps[i, p][:], func=ACT.Relu, bias=FLOOR_SHIFT, scale=1.0)
+
+        def lift_both(i):
+            lifted[i] = end_expo[i + 1][:].rearrange("p a n -> p (a n)")
+            nc.gpsimd.tensor_scalar(
+                out=lifted[i], in0=cuts[i][:].rearrange("p a n -> p (a n)"), scalar1=1.0, scalar2=FLOOR_VALUE, op0=ALU.mult, op1=ALU.add,
+            )
+
+        def multiply_lifted(i, spent):
+            product[i] = x_room[spent][:].rearrange("p g r t -> p (g r t)").bitcast(F32)
+            nc.gpsimd.tensor_tensor(out=product[i], in0=lifted[i][:, 0:T], in1=lifted[i][:, T:2 * T], op=ALU.mult)
+
+        def cut_first(i):
             cut0[i] = work.tile([P, T], F32, name="fl0", tag="fl0", bufs=2)
             nc.scalar.activation(out=cut0[i][:], in_=m_ps[i, 0][:], func=ACT.Relu, bias=FLOOR_SHIFT, scale=1.0)
-
-        def floor_second(i):
-            floored1[i] = work.tile([P, T], F32, name="fl1", tag="fl1", bufs=2)
-            nc.vector.tensor_scalar(
-                out=floored1[i][:], in0=m_ps[i, 1][:], scalar1=-FLOOR_SHIFT, scalar2=16.0, op0=ALU.max, op1=ALU.add,
-            )
 
         def cut_second(i):
             cut1[i] = work.tile([P, T], F32, name="cut", tag="cut", bufs=1)
@@ -340,39 +347,31 @@ def tile_chunkflooredmessagemiddlescore_kernel(tc, x_bytes, x_scale, we_words, w
             floored1[i] = work.tile([P, T], F32, name="fl1", tag="fl1", bufs=2)
             nc.scalar.activation(out=floored1[i][:], in_=cut1[i][:], func=ACT.Identity, bias=FLOOR_VALUE, scale=1.0)
 
+        def floor_second(i):
+            floored1[i] = work.tile([P, T], F32, name="fl1", tag="fl1", bufs=2)
+            nc.vector.tensor_scalar(
+                out=floored1[i][:], in0=m_ps[i, 1][:], scalar1=-FLOOR_SHIFT, scalar2=16.0, op0=ALU.max, op1=ALU.add,
+            )
+
         def multiply(i):
-            product[i] = keep.tile([P, T], F32, name="prod%d" % i)
+            whole = keep.tile([P, T], F32, name="prod%d" % i)
+            product[i] = whole[:]
             nc.vector.scalar_tensor_tensor(
-                out=product[i][:], in0=cut0[i][:], scalar=FLOOR_VALUE, in1=floored1[i][:], op0=ALU.add, op1=ALU.mult,
+                out=product[i], in0=cut0[i][:], scalar=FLOOR_VALUE, in1=floored1[i][:], op0=ALU.add, op1=ALU.mult,
             )
-
-        def cut_both(i):
-            cuts[i] = work.tile([P, PAIRS, T], F32, name="cuts", tag="cuts", bufs=1)
-            for p in range(PAIRS):
-                nc.scalar.activation(out=cuts[i][:, p, :], in_=m_ps[i, p][:], func=ACT.Relu, bias=FLOOR_SHIFT, scale=1.0)
-
-        def lift_both(i):
-            lifted[i] = room[unit_of[rounds[i + 2][1]]][:].rearrange("p g r t -> p (g r t)").bitcast(F32)
-            nc.gpsimd.tensor_scalar(
-                out=lifted[i], in0=cuts[i][:].rearrange("p a n -> p (a n)"), scalar1=1.0, scalar2=FLOOR_VALUE, op0=ALU.mult, op1=ALU.add,
-            )
-
-        def multiply_lifted(i, spent=None):
-            product[i] = room[unit_of[rounds[i + 2][2]] if spent is None else spent][:].rearrange("p g r t -> p (g r t)").bitcast(F32)
-            nc.gpsimd.tensor_tensor(out=product[i], in0=lifted[i][:, 0:T], in1=lifted[i][:, T:2 * T], op=ALU.mult)
 
         def weigh(i):
             terms = work.tile([P, T], F32, name="weighted", tag="weighted", bufs=1)
             nc.vector.scalar_tensor_tensor(
-                out=terms[:], in0=expo[unit_of[i, 1]][:], scalar=1.0 / T, in1=product[i][:, :], op0=ALU.mult, op1=ALU.mult,
+                out=terms[:], in0=expo[i, 1][:], scalar=1.0 / T, in1=product[i], op0=ALU.mult, op1=ALU.mult,
                 accum_out=weight[:, i:i + 1],
             )
 
-        def log_weights(first, end):
-            nc.scalar.activation(out=log_weight[:, first:end], in_=weight[:, first:end], func=ACT.Ln)
+        def log_weights(begin, end):
+            nc.scalar.activation(out=log_weight[:, begin:end], in_=weight[:, begin:end], func=ACT.Ln)
 
-        def make_shifts(first, end):
-            nc.vector.tensor_tensor(out=shift[:, first:end], in0=mid_neg_max[:, first:end], in1=log_weight[:, first:end], op=ALU.subtract)
+        def make_shifts(begin, end):
+            nc.vector.tensor_tensor(out=shift[:, begin:end], in0=mid_neg_max[:, begin:end], in1=log_weight[:, begin:end], op=ALU.subtract)
 
         def pieces(i):
             return [slice(0, HALF), slice(HALF, T)] if i == LAST_TILE else [slice(0, T)]
@@ -383,19 +382,16 @@ def tile_chunkflooredmessagemiddlescore_kernel(tc, x_bytes, x_scale, we_words, w
                 nc.scalar.activation(out=log_a[i, h][:], in_=product[i][:, cols], func=ACT.Ln)
 
         def finish(i):
-            s = unit_of[i, 1]
             for h, cols in enumerate(pieces(i)):
                 res = work.tile([P, cols.stop - cols.start], F32, name="res", tag="res", bufs=TILES + 1)
                 nc.vector.scalar_tensor_tensor(
-                    out=res[:], in0=log_a[i, h][:], scalar=shift[:, i:i + 1], in1=neg_n[s][:, cols], op0=ALU.add, op1=ALU.subtract,
+                    out=res[:], in0=log_a[i, h][:], scalar=shift[:, i:i + 1], in1=neg_n[i, 1][:, cols], op0=ALU.add, op1=ALU.subtract,
                 )
                 nc.sync.dma_start(out=out[i * P:(i + 1) * P, cols], in_=res[:])
 
-        total = {}
-
         def open_total(i, bank):
             total[i] = bank_tile(bank, [P, T])
-            nc.tensor.matmul(total[i][:], lhsT=neg_ident[:], rhs=neg_n[unit_of[i, 1]][:], start=True, stop=False)
+            nc.tensor.matmul(total[i][:], lhsT=neg_ident[:], rhs=neg_n[i, 1][:], start=True, stop=False)
 
         def close_total(i):
             nc.tensor.matmul(total[i][:], lhsT=ident[:], rhs=log_a[i, 0][:], start=False, stop=True)
@@ -405,208 +401,190 @@ def tile_chunkflooredmessagemiddlescore_kernel(tc, x_bytes, x_scale, we_words, w
             nc.scalar.activation(out=res[:], in_=total[i][:], func=ACT.Identity, bias=shift[:, i:i + 1], scale=1.0)
             nc.sync.dma_start(out=out[i * P:(i + 1) * P, :], in_=res[:])
 
-        def on_unit(step, k, place):
-            if 0 <= k < len(rounds) and place < len(rounds[k]):
-                step(unit_of[rounds[k][place]])
-
-        def on_tile(step, i, otherwise=None):
-            if 0 <= i < TILES:
-                step(i)
-            elif otherwise is not None and i in otherwise:
-                otherwise[i]()
-
-        def quantize_and_emit(s, bank=None):
-            quantize_x(s)
-            emit(s, bank)
-
-        def quantize_and_pass_on(i, banks=MESSAGE_BANKS):
-            quantize_v(i)
-            pass_on(i, banks)
-
-        a0, b0, a1, b1 = unit_of[0, 0], unit_of[0, 2], unit_of[1, 0], unit_of[1, 2]
-        warm_up(SCORE_BANK[0], WARM[0])
+        warm_up(SCORE_BANK[0], T)
         spread_bias(0)
         spread_bias(2)
-        for s, bank in ((a0, 0), (b0, 1), (a1, 2)):
-            widen(s)
-            turn_x(s, bank)
-            if s == b0:
-                warm_up(SCORE_BANK[1], WARM[1])
-        empty_vector(a0)
-        widen(b1)
-        turn_x(b1, 0)
-        warm_up(SCORE_BANK[2], WARM[2])
-        empty_vector(b0)
-        on_unit(widen, 2, 0)
-        on_unit(widen, 2, 1)
-        quantize_and_emit(a0)
-        quantize_and_emit(b0)
-        empty_scalar(a1)
-        empty_vector(a1)
-        empty_scalar(b1)
-        quantize_and_emit(a1, SCORE_BANK[2])
-        add_bias(a0)
-        quantize_and_emit(b1, SCORE_BANK[0])
-        interleave_gpsimd(0, 0, b1)
-        interleave_gpsimd(0, 1, a1)
-        on_unit(turn_x, 2, 0)
-        add_bias(b0)
-        on_unit(turn_x, 2, 1)
-        interleave_scalar(1, 0)
-        find_max(a0)
-        find_max(b0)
-        exponent(a0)
-        exponent(b0)
-        add_bias(a1)
-        add_bias(b1)
-        on_unit(empty_scalar, 2, 0)
-        find_max(a1)
+        widen((0, 0))
+        turn_x((0, 0))
+        widen((0, 2))
+        turn_x((0, 2))
+        warm_up(SCORE_BANK[1], HALF)
+        widen((1, 0))
+        turn_x((1, 0), TURN_BANK[2])
+        empty_vector((0, 0))
+        widen((1, 2))
+        turn_x((1, 2), TURN_BANK[0])
+        empty_vector((0, 2))
+        widen((2, 0))
+        widen((2, 2))
+        score((0, 0))
+        score((0, 2))
+        empty_vector((1, 0))
+        empty_scalar((1, 2))
+        score((1, 0), SCORE_BANK[2])
+        add_bias((0, 0))
+        score((1, 2), SCORE_BANK[0])
+        group_first((1, 2))
+        turn_x((2, 0))
+        add_bias((0, 2))
+        turn_x((2, 2))
+        group_second_left()
+        find_max((0, 0))
+        find_max((0, 2))
+        exponent((0, 0))
+        exponent((0, 2))
+        add_bias((1, 0))
+        add_bias((1, 2))
+        empty_scalar((2, 0))
+        find_max((1, 0))
         scale_gain()
         invert_sums(0)
-        find_max(b1)
-        warm_up(SCORE_BANK[0], WARM[3])
-        message_first(0)
-        message_second(0)
+        find_max((1, 2))
+        warm_up(SCORE_BANK[0], T)
+        message(0, 0)
+        message(0, 1)
         turn_v(0, TURN_BANK[2])
-        warm_up(SCORE_BANK[1], WARM[4])
-        exponent(a1)
-        exponent(b1)
-        interleave_vector(1, 1)
+        warm_up(SCORE_BANK[1], HALF)
+        exponent((1, 0))
+        exponent((1, 2))
+        group_second_right()
         for p in range(PAIRS):
-            for h in range(2):
-                quantize_trans(p, h)
-        on_unit(widen, 2, 2)
-        on_unit(widen, 3, 0)
+            quantize_trans(p)
+        widen((0, 1))
+        widen((3, 0))
         empty_v(0)
-        on_unit(turn_x, 2, 2)
-        quantize_and_pass_on(0)
+        turn_x((0, 1))
+        pass_on(0)
 
-        for k in range(2, LAST_TILE):
-            on_unit(empty_scalar, k, 1)
+        for k in range(FIRST_ROUND, LAST_TILE):
+            here, ahead = rounds[k], rounds[k + 1]
+            empty_scalar(here[1])
             if k < WEIGH_LAG:
-                on_unit(empty_vector, k, 1)
-            on_tile(weigh, k - WEIGH_LAG)
-            on_tile(invert_sums, k - 1)
-            on_unit(quantize_and_emit, k, 0)
-            on_unit(turn_x, k + 1, 0)
-            on_tile(cut_both, k - 2)
-            on_tile(message_first, k - 1)
+                empty_vector(here[1])
+            else:
+                weigh(k - WEIGH_LAG)
+            invert_sums(k - 1)
+            score(here[0])
+            turn_x(ahead[0])
+            cut_both(k - FLOOR_LAG)
+            message(k - 1, 0)
             if k >= WEIGH_LAG:
-                on_unit(empty_vector, k, 1)
-            on_tile(message_second, k - 1)
+                empty_vector(here[1])
+            message(k - 1, 1)
 
-            on_unit(quantize_and_emit, k, 1)
-            on_tile(turn_v, k - 1)
-            on_tile(lift_both, k - 2)
-            on_unit(widen, k + 1, 2)
-            on_unit(widen, k + 1, 1)
-            on_unit(add_bias, k, 0)
-            on_unit(empty_vector, k, 2)
-            on_unit(turn_x, k + 1, 2)
-            on_unit(find_max, k, 0)
-            on_unit(empty_scalar, k + 1, 0)
+            score(here[1])
+            turn_v(k - 1)
+            lift_both(k - FLOOR_LAG)
+            widen(ahead[2])
+            widen(ahead[1])
+            add_bias(here[0])
+            empty_vector(here[2])
+            turn_x(ahead[2])
+            find_max(here[0])
+            empty_scalar(ahead[0])
 
-            on_unit(quantize_and_emit, k, 2)
-            on_tile(multiply_lifted, k - 2)
-            on_unit(widen, k + 2, 0)
-            on_tile(empty_v, k - 1)
-            on_unit(turn_x, k + 1, 1)
-            on_unit(exponent, k, 0)
-            on_unit(add_bias, k, 1)
-            on_unit(find_max, k - 1, 2)
-            on_unit(find_max, k, 1)
-            on_unit(exponent, k - 1, 2)
-            on_unit(exponent, k, 1)
+            score(here[2])
+            multiply_lifted(k - FLOOR_LAG, here[2])
+            widen(rounds[k + 2][0])
+            empty_v(k - 1)
+            turn_x(ahead[1])
+            exponent(here[0])
+            add_bias(here[1])
+            if k == FIRST_ROUND:
+                empty_vector(ahead[0])
+            else:
+                find_max(rounds[k - 1][2])
+            find_max(here[1])
+            if k > FIRST_ROUND:
+                exponent(rounds[k - 1][2])
+            exponent(here[1])
 
-            on_tile(quantize_and_pass_on, k - 1)
-            on_unit(add_bias, k, 2)
+            pass_on(k - 1)
+            add_bias(here[2])
 
         last = LAST_TILE
-        first_end, second_end = unit_of[last, 0], unit_of[last, 2]
-        middle = {i: unit_of[i, 1] for i in range(TILES)}
-        empty_scalar(second_end)
+        empty_scalar((last, 2))
         weigh(last - WEIGH_LAG)
         invert_sums(last - 1)
-        quantize_and_emit(first_end)
-        turn_x(middle[last - 1])
-        cut_both(last - 2)
-        widen(middle[last])
-        message_first(last - 1)
-        message_second(last - 1)
+        score((last, 0))
+        turn_x((last - 1, 1))
+        cut_both(last - FLOOR_LAG)
+        widen((last, 1))
+        message(last - 1, 0)
+        message(last - 1, 1)
 
-        quantize_and_emit(second_end)
+        score((last, 2))
         turn_v(last - 1)
-        lift_both(last - 2)
-        add_bias(first_end)
-        empty_vector(middle[last - 2])
-        turn_x(middle[last])
-        find_max(first_end)
-        empty_scalar(middle[last - 1])
+        lift_both(last - FLOOR_LAG)
+        add_bias((last, 0))
+        empty_vector((last - 2, 1))
+        turn_x((last, 1))
+        find_max((last, 0))
+        empty_scalar((last - 1, 1))
 
-        quantize_and_emit(middle[last - 2])
+        score((last - 2, 1))
         empty_v(last - 1)
-        empty_scalar(middle[last])
-        add_bias(second_end)
-        quantize_and_emit(middle[last - 1])
-        quantize_and_pass_on(last - 1, TURN_BANK[0:2])
-        exponent(first_end)
-        find_max(second_end)
-        quantize_and_emit(middle[last], SCORE_BANK[1])
-        multiply_lifted(last - 2, middle[last])
-        exponent(second_end)
-        floor_first(last - 1)
+        empty_scalar((last, 1))
+        add_bias((last, 2))
+        score((last - 1, 1))
+        pass_on(last - 1, TURN_BANK[0:2])
+        exponent((last, 0))
+        find_max((last, 2))
+        score((last, 1), SCORE_BANK[1])
+        multiply_lifted(last - FLOOR_LAG, (last, 1))
+        exponent((last, 2))
+        cut_first(last - 1)
         cut_second(last - 1)
-        add_bias(middle[last - 2])
-        find_max(middle[last - 3])
-        add_bias(middle[last - 1])
-        exponent(middle[last - 3])
-        find_max(middle[last - 2])
-        add_bias(middle[last])
-        open_total(4, SCORE_BANK[1])
-        find_max(middle[last - 1])
-        find_max(middle[last])
+        add_bias((last - 2, 1))
+        find_max((last - 3, 1))
+        add_bias((last - 1, 1))
+        exponent((last - 3, 1))
+        find_max((last - 2, 1))
+        add_bias((last, 1))
+        open_total(SECOND_TENSOR_TILE, SCORE_BANK[1])
+        find_max((last - 1, 1))
+        find_max((last, 1))
         lift_second(last - 1)
-        exponent(middle[last - 2])
-        exponent(middle[last - 1])
-        exponent(middle[last])
+        for i in range(last - 2, TILES):
+            exponent((i, 1))
 
-        done = TILES - WEIGH_LAG
+        weighed = TILES - WEIGH_LAG
         invert_sums(last)
         multiply(last - 1)
-        message_first(last)
-        message_second(last)
+        message(last, 0)
+        message(last, 1)
         turn_v(last)
-        open_total(2, TURN_BANK[2])
-        log_weights(0, done)
+        open_total(FIRST_TENSOR_TILE, TURN_BANK[2])
+        log_weights(0, weighed)
         take_log(0)
-        weigh(done)
+        weigh(weighed)
         weigh(last - 2)
-        make_shifts(0, done)
+        make_shifts(0, weighed)
         empty_v(last)
         finish(0)
-        quantize_and_pass_on(last)
+        pass_on(last)
         take_log(1)
-        take_log(2)
-        close_total(2)
+        take_log(FIRST_TENSOR_TILE)
+        close_total(FIRST_TENSOR_TILE)
         finish(1)
         weigh(last - 1)
-        take_log(3)
-        floor_first(last)
+        take_log(FIRST_TENSOR_TILE + 1)
+        cut_first(last)
         floor_second(last)
-        log_weights(done, last)
-        take_log(4)
-        close_total(4)
-        finish(3)
-        make_shifts(done, last)
+        log_weights(weighed, last)
+        take_log(SECOND_TENSOR_TILE)
+        close_total(SECOND_TENSOR_TILE)
+        finish(FIRST_TENSOR_TILE + 1)
+        make_shifts(weighed, last)
         multiply(last)
-        take_log(5)
-        finish_total(2)
-        finish(5)
+        take_log(last - 2)
+        finish_total(FIRST_TENSOR_TILE)
+        finish(last - 2)
         weigh(last)
-        take_log(6)
+        take_log(last - 1)
         take_log(last)
         log_weights(last, TILES)
-        finish(6)
+        finish(last - 1)
         make_shifts(last, TILES)
-        finish_total(4)
+        finish_total(SECOND_TENSOR_TILE)
         finish(last)

@@ -69,9 +69,7 @@ def tile_chunkflooredmessagemiddlescore_kernel(tc, x_bytes, x_scale, we_words, w
         xs_all = keep.tile([P, L * TILES * PASSES, QUADS], F32, name="xs_all")
         xs = keep.tile([P, L * TILES * PASSES], F32, name="xs")
         ident = keep.tile([P, P], F32, name="ident")
-        zeros = keep.tile([P, T], F32, name="zeros")
         nc.vector.memset(rows[:].bitcast(I32), 0)
-        nc.vector.memset(zeros[:], 0.0)
         nc.vector.memset(we_s[:].rearrange("p g n -> p (g n)").bitcast(I32), 0)
 
         x_raw, trans_raw = {}, {}
@@ -124,9 +122,6 @@ def tile_chunkflooredmessagemiddlescore_kernel(tc, x_bytes, x_scale, we_words, w
 
         def bank_tile(bank, shape):
             return psum.tile(shape, F32, name="bank%d" % bank, tag="bank%d" % bank)
-
-        def warm_up(bank, columns):
-            nc.tensor.matmul(bank_tile(bank, [P, columns])[:], lhsT=zeros[:, 0:P], rhs=zeros[:, 0:columns], start=True, stop=True)
 
         neg_bias = {}
 
@@ -401,14 +396,12 @@ def tile_chunkflooredmessagemiddlescore_kernel(tc, x_bytes, x_scale, we_words, w
             nc.scalar.activation(out=res[:], in_=total[i][:], func=ACT.Identity, bias=shift[:, i:i + 1], scale=1.0)
             nc.sync.dma_start(out=out[i * P:(i + 1) * P, :], in_=res[:])
 
-        warm_up(SCORE_BANK[0], T)
         spread_bias(0)
         spread_bias(2)
         widen((0, 0))
         turn_x((0, 0))
         widen((0, 2))
         turn_x((0, 2))
-        warm_up(SCORE_BANK[1], HALF)
         widen((1, 0))
         turn_x((1, 0), TURN_BANK[2])
         empty_vector((0, 0))
@@ -440,11 +433,9 @@ def tile_chunkflooredmessagemiddlescore_kernel(tc, x_bytes, x_scale, we_words, w
         scale_gain()
         invert_sums(0)
         find_max((1, 2))
-        warm_up(SCORE_BANK[0], T)
         message(0, 0)
         message(0, 1)
         turn_v(0, TURN_BANK[2])
-        warm_up(SCORE_BANK[1], HALF)
         exponent((1, 0))
         exponent((1, 2))
         group_second_right()

@@ -29,28 +29,25 @@ HALF = T // 2
 FLOOR_SHIFT = 14.4
 FLOOR_VALUE = 1.6
 
-MIDDLE_LAG = 2
-FIRST_ROUND = 2
+WIDEN_AHEAD = 2
 FLOOR_LAG = 2
-WEIGH_LAG = 4
+WEIGH_LAG = 3
 
 TURN_BANK = (0, 1, 2)
 SCORE_BANK = (3, 4, 5)
 MESSAGE_BANKS = (6, 7)
 
-VECTOR_FIRST = 3
+VECTOR_FIRST = 4
 VECTOR_SHARE = 64
 
-FIRST_TENSOR_TILE, SECOND_TENSOR_TILE = 2, 4
+FIRST_TENSOR_TILE, SECOND_TENSOR_TILE = 1, 3
 
 
 def tile_chunkflooredmessagemiddlescore_kernel(tc, x_bytes, x_scale, we_words, we_scales, be, ends, gain, trans, out):
     nc = tc.nc
 
-    rounds = [[(i, 0), (i, 2)] + ([(i - MIDDLE_LAG, 1)] if i >= MIDDLE_LAG else []) for i in range(TILES)]
-    rounds.append([(LAST_TILE - 1, 1), None, (LAST_TILE, 1)])
-    units = [unit for members in rounds for unit in members if unit is not None]
-    round_of = {unit: k for k, members in enumerate(rounds) for unit in members}
+    rounds = [[(i, 0), (i, 2), (i, 1)] for i in range(TILES)]
+    units = [unit for members in rounds for unit in members]
     place_of = {unit: place for members in rounds for place, unit in enumerate(members)}
 
     with ExitStack() as ctx:
@@ -63,7 +60,8 @@ def tile_chunkflooredmessagemiddlescore_kernel(tc, x_bytes, x_scale, we_words, w
         be_wide = keep.tile([P, T], BF16, name="be_wide")
         pick = keep.tile([P, 2 * PAIRS], BF16, name="pick")
         gain_raw = keep.tile([P, PAIRS * T], BF16, name="gain_raw")
-        gain_wide = keep.tile([P, PAIRS * T], BF16, name="gain_wide")
+        gain_room = keep.tile([P, PASSES, P, 4], BF16, name="gain_wide", align_bytes=64)
+        gain_wide = gain_room[:].rearrange("p g r t -> p (g r t)")
         we_s = keep.tile([P, PASSES, T], U8, name="we_s", align_bytes=64)
         we_w = keep.tile([P, PASSES, 2 * T], U8, name="we_w", align_bytes=64)
         xs_all = keep.tile([P, L * TILES * PASSES, QUADS], F32, name="xs_all")
@@ -85,29 +83,26 @@ def tile_chunkflooredmessagemiddlescore_kernel(tc, x_bytes, x_scale, we_words, w
             trans_raw[p] = keep.tile([P, 4, T], BF16, name="tr_raw%d" % p)
             nc.sync.dma_start(out=trans_raw[p][:], in_=trans[p].rearrange("(p j) n -> p j n", j=4))
 
-        first, middle, second, both_ends = slice(0, 1), slice(1, 2), slice(2, 3), slice(0, 3, 2)
+        first, rest, every = slice(0, 1), slice(1, 3), slice(0, 3)
         nc.scalar.dma_start(out=xs_all[:].rearrange("p c q -> p (c q)"), in_=x_scale.rearrange("l i j -> (l i j)").partition_broadcast(P))
         load_x(0, first)
         nc.sync.dma_start(out=rows[0:1, :], in_=be.rearrange("(o n) -> o n", o=1))
         nc.sync.dma_start(out=rows[32:65:32, :], in_=ends)
-        load_x(0, second)
-        load_x(1, both_ends)
+        load_x(0, rest)
         nc.sync.dma_start(out=we_w[:].bitcast(I32), in_=we_words.rearrange("g p n -> p g n").bitcast(I32))
-        load_x(2, both_ends)
+        load_x(1, every)
+        load_x(2, every)
         for q in range(QUADS):
             nc.sync.dma_start(
                 out=we_s[32 * q:32 * q + 4, :, :].bitcast(I32),
                 in_=we_scales[:, 4 * q:4 * q + 4, :].rearrange("g r n -> r g n").bitcast(I32),
             )
         load_trans(1)
-        load_trans(0)
         nc.sync.dma_start(out=gain_raw[:], in_=gain.rearrange("a n -> (a n)").partition_broadcast(P))
-        load_x(0, middle)
         nc.sync.dma_start(out=be_wide[:], in_=be.partition_broadcast(P))
-        for i in range(3, TILES + MIDDLE_LAG):
-            if i < TILES:
-                load_x(i, both_ends)
-            load_x(i - MIDDLE_LAG, middle)
+        load_trans(0)
+        for i in range(3, TILES):
+            load_x(i, every)
 
         nc.gpsimd.memset(pick[:], 0.0)
         nc.gpsimd.memset(pick[0:1, :], -1.0)
@@ -132,42 +127,38 @@ def tile_chunkflooredmessagemiddlescore_kernel(tc, x_bytes, x_scale, we_words, w
             nc.vector.tensor_copy(out=neg_bias[l][:], in_=acc[:])
 
         def scale_gain():
-            nc.vector.tensor_scalar(out=gain_wide[:], in0=gain_raw[:], scalar1=float(T), scalar2=None, op0=ALU.mult)
+            nc.gpsimd.tensor_scalar(out=gain_wide, in0=gain_raw[:], scalar1=float(T), scalar2=0.0, op0=ALU.mult, op1=ALU.add)
 
         trans_grouped = {}
         trans_codes = keep.tile([P, PAIRS, T], U32, name="tr_codes", align_bytes=64)
         trans_scales = keep.tile([P, PAIRS, T], U8, name="tr_scales", align_bytes=64)
 
-        def group_views(cols):
-            return (
-                trans_grouped[1][:, cols, :].rearrange("p (c i) t -> p c t i", i=4),
-                trans_raw[1][:, :, cols].rearrange("p t (c i) -> p c t i", i=4),
-            )
-
-        def group_second_left():
+        def group_second():
             whole = keep.tile([P, T, 4], BF16, name="tr_grouped1", align_bytes=64)
             trans_grouped[1] = whole[:]
-            dst, src = group_views(slice(0, HALF))
-            nc.scalar.copy(out=dst, in_=src)
+            nc.scalar.copy(
+                out=trans_grouped[1].rearrange("p (c i) t -> p c t i", i=4),
+                in_=trans_raw[1][:].rearrange("p t (c i) -> p c t i", i=4),
+            )
 
-        def group_second_right():
-            dst, src = group_views(slice(HALF, T))
-            nc.vector.tensor_copy(out=dst, in_=src)
+        first_grouped = keep.tile([P, 2, PASSES, P, 4], BF16, name="tr_grouped0", align_bytes=64)
+        trans_grouped[0] = first_grouped[:].rearrange("p h g r t -> p (h g r) t")
 
-        def group_first(spent):
-            trans_grouped[0] = x_room[spent][:].rearrange("p g r t -> p (g r) t")
+        def group_first(h):
+            cols = slice(h * HALF, (h + 1) * HALF)
             nc.gpsimd.tensor_scalar(
-                out=trans_grouped[0], in0=trans_raw[0][:].rearrange("p t n -> p n t"),
+                out=trans_grouped[0][:, cols, :], in0=trans_raw[0][:, :, cols].rearrange("p t n -> p n t"),
                 scalar1=1.0, scalar2=0.0, op0=ALU.mult, op1=ALU.add,
             )
 
-        def quantize_trans(p):
+        def quantize_trans(p, h):
+            cols = slice(h * HALF, (h + 1) * HALF)
             nc.vector.quantize_mx(
-                out=trans_codes[:, p, :].bitcast(FP8X4), scales=trans_scales[:, p, :],
-                in_=trans_grouped[p].rearrange("p n t -> p (n t)"),
+                out=trans_codes[:, p, cols].bitcast(FP8X4), scales=trans_scales[:, p, cols],
+                in_=trans_grouped[p][:, cols, :].rearrange("p n t -> p (n t)"),
             )
 
-        x_wide, x_turned, x_room, x_grouped, e_ps = {}, {}, {}, {}, {}
+        x_wide, x_turned, x_grouped, e_ps = {}, {}, {}, {}
         neg_n, neg_max, expo, end_expo = {}, {}, {}, {}
         sums = [keep.tile([P, PAIRS], F32, name="sums%d" % i) for i in range(TILES)]
         inverse = [keep.tile([P, PAIRS], F32, name="inv%d" % i) for i in range(TILES)]
@@ -177,40 +168,48 @@ def tile_chunkflooredmessagemiddlescore_kernel(tc, x_bytes, x_scale, we_words, w
         shift = keep.tile([P, TILES], F32, name="shift")
 
         def widen(unit):
-            x_wide[unit] = work.tile([P, D], BF16, name="xw", tag="xw", bufs=6)
+            x_wide[unit] = work.tile([P, D], BF16, name="xw", tag="xw", bufs=8)
             nc.scalar.copy(out=x_wide[unit][:], in_=x_raw[unit].bitcast(FP8))
 
-        def turn(bank, values):
+        def turn(bank, values, halves):
             words = values.bitcast(F32)
-            for g in range(2):
+            for g in halves:
                 for u in range(2):
                     nc.tensor.transpose(bank[:, g, u, :], words[:, PASS_WORDS * g + u:PASS_WORDS * (g + 1):2], ident[:])
 
         def turn_x(unit, bank=None):
             x_turned[unit] = bank_tile(TURN_BANK[place_of[unit]] if bank is None else bank, [P, PASSES, 2, P])
-            turn(x_turned[unit], x_wide[unit][:])
+            turn(x_turned[unit], x_wide[unit][:], range(PASSES))
+
+        def light(k):
+            return k < FLOOR_LAG or k + WIDEN_AHEAD >= TILES
 
         def vector_share(unit):
-            k, place = round_of[unit], place_of[unit]
-            if units.index(unit) < VECTOR_FIRST or (place == 2 and k < TILES) or (place == 1 and FIRST_ROUND <= k < WEIGH_LAG):
+            k, place = unit[0], place_of[unit]
+            if units.index(unit) < VECTOR_FIRST:
                 return PASSES * P
-            if (k, place) == (FIRST_ROUND + 1, 0):
-                return P
-            return VECTOR_SHARE if place == 1 and FIRST_ROUND <= k < LAST_TILE else 0
+            if place == 0:
+                return P if light(k - 1) else 0
+            if light(k):
+                return 0
+            return PASSES * P if place == 2 else VECTOR_SHARE
 
         def make_room(unit):
-            name = "xg%d" % units.index(unit)
-            if unit == (1, 2):
-                x_room[unit] = keep.tile([P, 2 * PASSES, P, 4], BF16, name=name, align_bytes=64)
-            elif place_of[unit] == 2 and round_of[unit] != LAST_TILE:
-                x_room[unit] = keep.tile([P, PASSES, P, 4], BF16, name=name, align_bytes=64)
+            k, place = unit[0], place_of[unit]
+            if unit == (0, 1):
+                x_grouped[unit] = gain_room[:]
+            elif k == 1 and place > 0:
+                x_grouped[unit] = first_grouped[:, place - 1]
+            elif place == 2 and k >= FLOOR_LAG:
+                room = keep.tile([P, PASSES, P, 4], BF16, name="xg%d" % k, align_bytes=64)
+                x_grouped[unit] = room[:]
             else:
-                x_room[unit] = work.tile([P, PASSES, P, 4], BF16, name="xg", tag="xg", bufs=6, align_bytes=64)
-            x_grouped[unit] = x_room[unit][:, 0:PASSES]
+                room = work.tile([P, PASSES, P, 4], BF16, name="xg", tag="xg", bufs=6, align_bytes=64)
+                x_grouped[unit] = room[:]
 
         def scaled_parts(unit, begin, end):
             i, l = unit
-            if unit not in x_room:
+            if unit not in x_grouped:
                 make_room(unit)
             parts = []
             for g in range(PASSES):
@@ -279,7 +278,7 @@ def tile_chunkflooredmessagemiddlescore_kernel(tc, x_bytes, x_scale, we_words, w
                 )
 
         v, v_turned, v_grouped, m_ps = {}, {}, {}, {}
-        cuts, lifted, cut0, cut1, floored1, product, log_a, total = {}, {}, {}, {}, {}, {}, {}, {}
+        cuts, lifted, cut0, floored, product, log_a, total = {}, {}, {}, {}, {}, {}, {}
 
         def invert_sums(i):
             nc.vector.reciprocal(out=inverse[i][:], in_=sums[i][:])
@@ -292,9 +291,10 @@ def tile_chunkflooredmessagemiddlescore_kernel(tc, x_bytes, x_scale, we_words, w
                 in1=gain_wide[:, p * T:(p + 1) * T], op0=ALU.mult, op1=ALU.mult,
             )
 
-        def turn_v(i, bank=TURN_BANK[1]):
-            v_turned[i] = bank_tile(bank, [P, PAIRS, 2, P])
-            turn(v_turned[i], v[i][:].rearrange("p a n -> p (a n)"))
+        def turn_v(i, pairs=range(PAIRS)):
+            if i not in v_turned:
+                v_turned[i] = bank_tile(TURN_BANK[1], [P, PAIRS, 2, P])
+            turn(v_turned[i], v[i][:].rearrange("p a n -> p (a n)"), pairs)
 
         def empty_v(i):
             v_grouped[i] = work.tile([P, PAIRS, P, 2], F32, name="vg", tag="vg", bufs=2, align_bytes=64)
@@ -327,32 +327,29 @@ def tile_chunkflooredmessagemiddlescore_kernel(tc, x_bytes, x_scale, we_words, w
             )
 
         def multiply_lifted(i, spent):
-            product[i] = x_room[spent][:].rearrange("p g r t -> p (g r t)").bitcast(F32)
+            product[i] = x_grouped[spent].rearrange("p g r t -> p (g r t)").bitcast(F32)
             nc.gpsimd.tensor_tensor(out=product[i], in0=lifted[i][:, 0:T], in1=lifted[i][:, T:2 * T], op=ALU.mult)
 
         def cut_first(i):
-            cut0[i] = work.tile([P, T], F32, name="fl0", tag="fl0", bufs=2)
+            cut0[i] = work.tile([P, T], F32, name="cut0", tag="cut0", bufs=1)
             nc.scalar.activation(out=cut0[i][:], in_=m_ps[i, 0][:], func=ACT.Relu, bias=FLOOR_SHIFT, scale=1.0)
 
-        def cut_second(i):
-            cut1[i] = work.tile([P, T], F32, name="cut", tag="cut", bufs=1)
-            nc.scalar.activation(out=cut1[i][:], in_=m_ps[i, 1][:], func=ACT.Relu, bias=FLOOR_SHIFT, scale=1.0)
-
-        def lift_second(i):
-            floored1[i] = work.tile([P, T], F32, name="fl1", tag="fl1", bufs=2)
-            nc.scalar.activation(out=floored1[i][:], in_=cut1[i][:], func=ACT.Identity, bias=FLOOR_VALUE, scale=1.0)
-
-        def floor_second(i):
-            floored1[i] = work.tile([P, T], F32, name="fl1", tag="fl1", bufs=2)
+        def floor(i, p):
+            floored[i, p] = work.tile([P, T], F32, name="floored", tag="floored", bufs=3)
             nc.vector.tensor_scalar(
-                out=floored1[i][:], in0=m_ps[i, 1][:], scalar1=-FLOOR_SHIFT, scalar2=16.0, op0=ALU.max, op1=ALU.add,
+                out=floored[i, p][:], in0=m_ps[i, p][:], scalar1=-FLOOR_SHIFT, scalar2=16.0, op0=ALU.max, op1=ALU.add,
             )
 
-        def multiply(i):
+        def multiply_floored(i):
+            whole = keep.tile([P, T], F32, name="prod%d" % i)
+            product[i] = whole[:]
+            nc.vector.tensor_tensor(out=product[i], in0=floored[i, 0][:], in1=floored[i, 1][:], op=ALU.mult)
+
+        def multiply_cut(i):
             whole = keep.tile([P, T], F32, name="prod%d" % i)
             product[i] = whole[:]
             nc.vector.scalar_tensor_tensor(
-                out=product[i], in0=cut0[i][:], scalar=FLOOR_VALUE, in1=floored1[i][:], op0=ALU.add, op1=ALU.mult,
+                out=product[i], in0=cut0[i][:], scalar=FLOOR_VALUE, in1=floored[i, 1][:], op0=ALU.add, op1=ALU.mult,
             )
 
         def weigh(i):
@@ -384,9 +381,11 @@ def tile_chunkflooredmessagemiddlescore_kernel(tc, x_bytes, x_scale, we_words, w
                 )
                 nc.sync.dma_start(out=out[i * P:(i + 1) * P, cols], in_=res[:])
 
-        def open_total(i, bank):
-            total[i] = bank_tile(bank, [P, T])
-            nc.tensor.matmul(total[i][:], lhsT=neg_ident[:], rhs=neg_n[i, 1][:], start=True, stop=False)
+        def open_total(i, h, bank=None):
+            if h == 0:
+                total[i] = bank_tile(bank, [P, T])
+            cols = slice(h * HALF, (h + 1) * HALF)
+            nc.tensor.matmul(total[i][:, cols], lhsT=neg_ident[:], rhs=neg_n[i, 1][:, cols], start=(h == 0), stop=False)
 
         def close_total(i):
             nc.tensor.matmul(total[i][:], lhsT=ident[:], rhs=log_a[i, 0][:], start=False, stop=True)
@@ -398,184 +397,166 @@ def tile_chunkflooredmessagemiddlescore_kernel(tc, x_bytes, x_scale, we_words, w
 
         spread_bias(0)
         spread_bias(2)
-        widen((0, 0))
-        turn_x((0, 0))
-        widen((0, 2))
-        turn_x((0, 2))
-        widen((1, 0))
-        turn_x((1, 0), TURN_BANK[2])
+        for unit in rounds[0]:
+            widen(unit)
+            turn_x(unit)
         empty_vector((0, 0))
-        widen((1, 2))
-        turn_x((1, 2), TURN_BANK[0])
+        widen((1, 0))
+        turn_x((1, 0))
         empty_vector((0, 2))
-        widen((2, 0))
-        widen((2, 2))
+        widen((1, 2))
         score((0, 0))
+        empty_vector((0, 1))
+        widen((1, 1))
         score((0, 2))
+        turn_x((1, 2))
+        turn_x((1, 1))
         empty_vector((1, 0))
-        empty_scalar((1, 2))
-        score((1, 0), SCORE_BANK[2])
+        for unit in rounds[2]:
+            widen(unit)
+        group_second()
         add_bias((0, 0))
-        score((1, 2), SCORE_BANK[0])
-        group_first((1, 2))
-        turn_x((2, 0))
-        add_bias((0, 2))
-        turn_x((2, 2))
-        group_second_left()
-        find_max((0, 0))
-        find_max((0, 2))
-        exponent((0, 0))
-        exponent((0, 2))
-        add_bias((1, 0))
-        add_bias((1, 2))
-        empty_scalar((2, 0))
-        find_max((1, 0))
+        score((0, 1))
         scale_gain()
-        invert_sums(0)
-        find_max((1, 2))
-        message(0, 0)
-        message(0, 1)
-        turn_v(0, TURN_BANK[2])
-        exponent((1, 0))
-        exponent((1, 2))
-        group_second_right()
-        for p in range(PAIRS):
-            quantize_trans(p)
-        widen((0, 1))
-        widen((3, 0))
-        empty_v(0)
-        turn_x((0, 1))
-        pass_on(0)
+        add_bias((0, 2))
+        find_max((0, 0))
+        exponent((0, 0))
+        find_max((0, 2))
+        exponent((0, 2))
+        add_bias((0, 1))
 
-        for k in range(FIRST_ROUND, LAST_TILE):
+        for k in range(1, LAST_TILE):
             here, ahead = rounds[k], rounds[k + 1]
+            fresh = rounds[k + WIDEN_AHEAD] if k + WIDEN_AHEAD < TILES else []
             empty_scalar(here[1])
-            if k < WEIGH_LAG:
-                empty_vector(here[1])
-            else:
-                weigh(k - WEIGH_LAG)
-            invert_sums(k - 1)
-            score(here[0])
-            turn_x(ahead[0])
-            cut_both(k - FLOOR_LAG)
-            message(k - 1, 0)
             if k >= WEIGH_LAG:
-                empty_vector(here[1])
+                weigh(k - WEIGH_LAG)
+            if k < FLOOR_LAG:
+                score(here[0])
+                quantize_trans(1, 0)
+                invert_sums(k - 1)
+                quantize_trans(1, 1)
+            else:
+                invert_sums(k - 1)
+                score(here[0])
+            turn_x(ahead[0])
+            if k >= FLOOR_LAG:
+                cut_both(k - FLOOR_LAG)
+            message(k - 1, 0)
+            empty_vector(here[1])
             message(k - 1, 1)
 
             score(here[1])
             turn_v(k - 1)
-            lift_both(k - FLOOR_LAG)
-            widen(ahead[2])
-            widen(ahead[1])
+            if k >= FLOOR_LAG:
+                lift_both(k - FLOOR_LAG)
+            else:
+                group_first(0)
+            empty_scalar(here[2])
+            for unit in fresh[:2]:
+                widen(unit)
             add_bias(here[0])
-            empty_vector(here[2])
+            if light(k):
+                find_max(rounds[k - 1][2])
+            else:
+                empty_vector(here[2])
             turn_x(ahead[2])
             find_max(here[0])
             empty_scalar(ahead[0])
 
             score(here[2])
-            multiply_lifted(k - FLOOR_LAG, here[2])
-            widen(rounds[k + 2][0])
+            if k >= FLOOR_LAG:
+                multiply_lifted(k - FLOOR_LAG, here[2])
+            else:
+                group_first(1)
+            for unit in fresh[2:]:
+                widen(unit)
             empty_v(k - 1)
             turn_x(ahead[1])
             exponent(here[0])
             add_bias(here[1])
-            if k == FIRST_ROUND:
+            if light(k):
                 empty_vector(ahead[0])
             else:
                 find_max(rounds[k - 1][2])
             find_max(here[1])
-            if k > FIRST_ROUND:
-                exponent(rounds[k - 1][2])
+            exponent(rounds[k - 1][2])
             exponent(here[1])
 
+            if k < FLOOR_LAG:
+                quantize_trans(0, 0)
+                quantize_trans(0, 1)
             pass_on(k - 1)
             add_bias(here[2])
 
         last = LAST_TILE
         empty_scalar((last, 2))
-        weigh(last - WEIGH_LAG)
-        invert_sums(last - 1)
-        score((last, 0))
-        turn_x((last - 1, 1))
-        cut_both(last - FLOOR_LAG)
-        widen((last, 1))
-        message(last - 1, 0)
-        message(last - 1, 1)
-
-        score((last, 2))
-        turn_v(last - 1)
-        lift_both(last - FLOOR_LAG)
-        add_bias((last, 0))
-        empty_vector((last - 2, 1))
-        turn_x((last, 1))
-        find_max((last, 0))
-        empty_scalar((last - 1, 1))
-
-        score((last - 2, 1))
-        empty_v(last - 1)
         empty_scalar((last, 1))
-        add_bias((last, 2))
-        score((last - 1, 1))
-        pass_on(last - 1, TURN_BANK[0:2])
-        exponent((last, 0))
-        find_max((last, 2))
-        score((last, 1), SCORE_BANK[1])
-        multiply_lifted(last - FLOOR_LAG, (last, 1))
-        exponent((last, 2))
-        cut_first(last - 1)
-        cut_second(last - 1)
-        add_bias((last - 2, 1))
-        find_max((last - 3, 1))
-        add_bias((last - 1, 1))
-        exponent((last - 3, 1))
-        find_max((last - 2, 1))
-        add_bias((last, 1))
-        open_total(SECOND_TENSOR_TILE, SCORE_BANK[1])
+        score((last, 0))
         find_max((last - 1, 1))
+        invert_sums(last - 1)
+        weigh(last - WEIGH_LAG)
+        score((last, 2))
+        message(last - 1, 0)
+        add_bias((last, 0))
+        message(last - 1, 1)
+        cut_both(last - 2)
+        turn_v(last - 1)
+        score((last, 1))
+        open_total(FIRST_TENSOR_TILE, 0, TURN_BANK[0])
+        open_total(FIRST_TENSOR_TILE, 1)
+        lift_both(last - 2)
+        multiply_lifted(last - 2, (last, 1))
+        exponent((last - 1, 1))
+        empty_v(last - 1)
+        add_bias((last, 2))
+        find_max((last, 0))
+        add_bias((last, 1))
+        find_max((last, 2))
         find_max((last, 1))
-        lift_second(last - 1)
-        for i in range(last - 2, TILES):
-            exponent((i, 1))
+        for unit in rounds[last]:
+            exponent(unit)
 
-        weighed = TILES - WEIGH_LAG
+        pass_on(last - 1)
         invert_sums(last)
-        multiply(last - 1)
-        message(last, 0)
-        message(last, 1)
-        turn_v(last)
-        open_total(FIRST_TENSOR_TILE, TURN_BANK[2])
-        log_weights(0, weighed)
-        take_log(0)
-        weigh(weighed)
         weigh(last - 2)
-        make_shifts(0, weighed)
+        message(last, 0)
+        turn_v(last, [0])
+        open_total(SECOND_TENSOR_TILE, 0, TURN_BANK[2])
+        message(last, 1)
+        turn_v(last, [1])
+        open_total(SECOND_TENSOR_TILE, 1)
+        log_weights(0, last - 1)
+        take_log(0)
+        floor(last - 1, 0)
+        floor(last - 1, 1)
+        make_shifts(0, last - 1)
         empty_v(last)
-        finish(0)
-        pass_on(last)
-        take_log(1)
+        multiply_floored(last - 1)
+        pass_on(last, SCORE_BANK[0:2])
         take_log(FIRST_TENSOR_TILE)
         close_total(FIRST_TENSOR_TILE)
-        finish(1)
+        finish(0)
         weigh(last - 1)
         take_log(FIRST_TENSOR_TILE + 1)
-        cut_first(last)
-        floor_second(last)
-        log_weights(weighed, last)
         take_log(SECOND_TENSOR_TILE)
         close_total(SECOND_TENSOR_TILE)
+        cut_first(last)
+        floor(last, 1)
         finish(FIRST_TENSOR_TILE + 1)
-        make_shifts(weighed, last)
-        multiply(last)
-        take_log(last - 2)
+        multiply_cut(last)
+        log_weights(last - 1, last)
+        take_log(SECOND_TENSOR_TILE + 1)
         finish_total(FIRST_TENSOR_TILE)
-        finish(last - 2)
+        make_shifts(last - 1, last)
+        finish(SECOND_TENSOR_TILE + 1)
         weigh(last)
-        take_log(last - 1)
-        take_log(last)
-        log_weights(last, TILES)
-        finish(last - 1)
-        make_shifts(last, TILES)
+        take_log(last - 2)
         finish_total(SECOND_TENSOR_TILE)
+        finish(last - 2)
+        take_log(last - 1)
+        log_weights(last, TILES)
+        take_log(last)
+        make_shifts(last, TILES)
+        finish(last - 1)
         finish(last)

@@ -25,6 +25,7 @@ PASSES = D // 512
 QUADS = 4
 PASS_WORDS = 256
 HALF = T // 2
+SCALE_ROWS, SCALE_SETS = 16, 3
 
 FLOOR_SHIFT = 14.4
 FLOOR_VALUE = 1.6
@@ -64,11 +65,14 @@ def tile_chunkflooredmessagemiddlescore_kernel(tc, x_bytes, x_scale, we_words, w
         gain_wide = gain_room[:].rearrange("p g r t -> p (g r t)")
         we_s = keep.tile([P, PASSES, T], U8, name="we_s", align_bytes=64)
         we_w = keep.tile([P, PASSES, 2 * T], U8, name="we_w", align_bytes=64)
-        xs_all = keep.tile([P, L * TILES * PASSES, QUADS], F32, name="xs_all")
+        xs_rows = keep.tile([SCALE_ROWS, SCALE_SETS, QUADS], F32, name="xs_rows")
+        xs_wide = keep.tile([P, SCALE_SETS, P], F32, name="xs_wide")
         xs = keep.tile([P, L * TILES * PASSES], F32, name="xs")
         ident = keep.tile([P, P], F32, name="ident")
         nc.vector.memset(rows[:].bitcast(I32), 0)
         nc.vector.memset(we_s[:].rearrange("p g n -> p (g n)").bitcast(I32), 0)
+
+        nc.vector.memset(xs_wide[:].rearrange("p s m -> p (s m)"), 0.0)
 
         x_raw, trans_raw = {}, {}
 
@@ -84,20 +88,23 @@ def tile_chunkflooredmessagemiddlescore_kernel(tc, x_bytes, x_scale, we_words, w
             nc.sync.dma_start(out=trans_raw[p][:], in_=trans[p].rearrange("(p j) n -> p j n", j=4))
 
         first, rest, every = slice(0, 1), slice(1, 3), slice(0, 3)
-        nc.scalar.dma_start(out=xs_all[:].rearrange("p c q -> p (c q)"), in_=x_scale.rearrange("l i j -> (l i j)").partition_broadcast(P))
         load_x(0, first)
+        nc.sync.dma_start(
+            out=xs_rows[:].rearrange("r s q -> r (s q)"),
+            in_=x_scale.rearrange("l i j -> (l i j)").rearrange("(r c) -> r c", r=SCALE_ROWS),
+        )
         nc.sync.dma_start(out=rows[0:1, :], in_=be.rearrange("(o n) -> o n", o=1))
         nc.sync.dma_start(out=rows[32:65:32, :], in_=ends)
         load_x(0, rest)
         nc.sync.dma_start(out=we_w[:].bitcast(I32), in_=we_words.rearrange("g p n -> p g n").bitcast(I32))
-        load_x(1, every)
-        load_x(2, every)
         for q in range(QUADS):
             nc.sync.dma_start(
                 out=we_s[32 * q:32 * q + 4, :, :].bitcast(I32),
                 in_=we_scales[:, 4 * q:4 * q + 4, :].rearrange("g r n -> r g n").bitcast(I32),
             )
+        load_x(1, every)
         load_trans(1)
+        load_x(2, every)
         nc.sync.dma_start(out=gain_raw[:], in_=gain.rearrange("a n -> (a n)").partition_broadcast(P))
         nc.sync.dma_start(out=be_wide[:], in_=be.partition_broadcast(P))
         load_trans(0)
@@ -112,19 +119,37 @@ def tile_chunkflooredmessagemiddlescore_kernel(tc, x_bytes, x_scale, we_words, w
         neg_ident = keep.tile([P, P], F32, name="neg_ident")
         nc.gpsimd.tensor_scalar(out=neg_ident[:], in0=ident[:], scalar1=-1.0, scalar2=0.0, op0=ALU.mult, op1=ALU.add)
 
-        for q in range(QUADS):
-            nc.vector.tensor_copy(out=xs[32 * q:32 * q + 32, :], in_=xs_all[32 * q:32 * q + 32, :, q])
-
         def bank_tile(bank, shape):
             return psum.tile(shape, F32, name="bank%d" % bank, tag="bank%d" % bank)
 
-        neg_bias = {}
+        def spread_scales():
+            nc.vector.tensor_copy(
+                out=xs_wide[0:SCALE_ROWS].rearrange("r s (q m) -> r (s q) m", q=QUADS),
+                in_=xs_rows[:].rearrange("r s q -> r (s q)").unsqueeze(2).to_broadcast([SCALE_ROWS, SCALE_SETS * QUADS, 32]),
+            )
+
+        scales_ps = {}
+
+        def turn_scales():
+            scales_ps[0] = bank_tile(SCORE_BANK[2], [P, SCALE_SETS, P])
+            for s in range(SCALE_SETS):
+                nc.tensor.transpose(scales_ps[0][:, s, :], xs_wide[:, s, :], ident[:])
+
+        def keep_scales():
+            acc = scales_ps[0]
+            nc.vector.tensor_copy(
+                out=xs[:].rearrange("p (r s) -> p r s", s=SCALE_SETS), in_=acc[:, :, 0:SCALE_ROWS].rearrange("p s r -> p r s"),
+            )
+
+        neg_bias, bias_ps = {}, {}
 
         def spread_bias(l):
-            acc = bank_tile(MESSAGE_BANKS[l // 2], [P, T])
-            nc.tensor.matmul(acc[:], lhsT=pick[:, l:l + 1].to_broadcast([P, P]), rhs=rows[:], start=True, stop=True)
+            bias_ps[l] = bank_tile(MESSAGE_BANKS[l // 2], [P, T])
+            nc.tensor.matmul(bias_ps[l][:], lhsT=pick[:, l:l + 1].to_broadcast([P, P]), rhs=rows[:], start=True, stop=True)
+
+        def keep_bias(l):
             neg_bias[l] = keep.tile([P, T], F32, name="neg_bias%d" % l)
-            nc.vector.tensor_copy(out=neg_bias[l][:], in_=acc[:])
+            nc.vector.tensor_copy(out=neg_bias[l][:], in_=bias_ps[l][:])
 
         def scale_gain():
             nc.gpsimd.tensor_scalar(out=gain_wide, in0=gain_raw[:], scalar1=float(T), scalar2=0.0, op0=ALU.mult, op1=ALU.add)
@@ -229,12 +254,22 @@ def tile_chunkflooredmessagemiddlescore_kernel(tc, x_bytes, x_scale, we_words, w
             for src, dst, scale in scaled_parts(unit, 0, PASSES * P - vector_share(unit)):
                 nc.scalar.activation(out=dst, in_=src, func=ACT.Copy, scale=scale)
 
-        def score(unit, bank=None):
+        x_codes = {}
+
+        def quantize_x(unit):
             codes = work.tile([P, PASSES * P], U32, name="xq", tag="xq", align_bytes=64)
             scales = work.tile([P, PASSES * P], U8, name="xqs", tag="xqs", align_bytes=64)
+            x_codes[unit] = codes, scales
             nc.vector.quantize_mx(
                 out=codes[:].bitcast(FP8X4), scales=scales[:], in_=x_grouped[unit].rearrange("p g r t -> p (g r t)"),
             )
+
+        def score(unit, bank=None):
+            quantize_x(unit)
+            multiply_x(unit, bank)
+
+        def multiply_x(unit, bank=None):
+            codes, scales = x_codes[unit]
             e_ps[unit] = bank_tile(SCORE_BANK[place_of[unit]] if bank is None else bank, [P, T])
             for g in range(PASSES):
                 cols = slice(g * P, (g + 1) * P)
@@ -395,34 +430,39 @@ def tile_chunkflooredmessagemiddlescore_kernel(tc, x_bytes, x_scale, we_words, w
             nc.scalar.activation(out=res[:], in_=total[i][:], func=ACT.Identity, bias=shift[:, i:i + 1], scale=1.0)
             nc.sync.dma_start(out=out[i * P:(i + 1) * P, :], in_=res[:])
 
+        spread_scales()
         spread_bias(0)
         spread_bias(2)
+        turn_scales()
+        keep_bias(0)
+        keep_scales()
+        keep_bias(2)
         for unit in rounds[0]:
             widen(unit)
             turn_x(unit)
         empty_vector((0, 0))
-        widen((1, 0))
+        for unit in rounds[1]:
+            widen(unit)
         turn_x((1, 0))
         empty_vector((0, 2))
-        widen((1, 2))
         score((0, 0))
         empty_vector((0, 1))
-        widen((1, 1))
         score((0, 2))
         turn_x((1, 2))
-        turn_x((1, 1))
         empty_vector((1, 0))
-        for unit in rounds[2]:
-            widen(unit)
-        group_second()
-        add_bias((0, 0))
         score((0, 1))
         scale_gain()
+        turn_x((1, 1))
+        add_bias((0, 0))
         add_bias((0, 2))
         find_max((0, 0))
-        exponent((0, 0))
         find_max((0, 2))
+        group_second()
+        for unit in rounds[2][:2]:
+            widen(unit)
+        exponent((0, 0))
         exponent((0, 2))
+        widen(rounds[2][2])
         add_bias((0, 1))
 
         for k in range(1, LAST_TILE):

@@ -30,26 +30,14 @@ SCALE_ROWS, SCALE_SETS = 16, 3
 FLOOR_SHIFT = 14.4
 FLOOR_VALUE = 1.6
 
-WIDEN_AHEAD = 2
-FLOOR_LAG = 2
-WEIGH_LAG = 3
+TRANS_HOSTS = [(0, 1), (1, 0)]
+LIGHT_ROUNDS = (2,)
 
-TURN_BANK = (0, 1, 2)
-SCORE_BANK = (3, 4, 5)
-MESSAGE_BANKS = (6, 7)
-
-VECTOR_FIRST = 4
-VECTOR_SHARE = 64
-
-FIRST_TENSOR_TILE, SECOND_TENSOR_TILE = 1, 3
+BANKS = 7
 
 
 def tile_chunkflooredmessagemiddlescore_kernel(tc, x_bytes, x_scale, we_words, we_scales, be, ends, gain, trans, out):
     nc = tc.nc
-
-    rounds = [[(i, 0), (i, 2), (i, 1)] for i in range(TILES)]
-    units = [unit for members in rounds for unit in members]
-    place_of = {unit: place for members in rounds for place, unit in enumerate(members)}
 
     with ExitStack() as ctx:
         keep = ctx.enter_context(tc.tile_pool(name="keep", bufs=1))
@@ -57,22 +45,23 @@ def tile_chunkflooredmessagemiddlescore_kernel(tc, x_bytes, x_scale, we_words, w
         psum = ctx.enter_context(tc.psum_pool(name="psum", bufs=1))
         ctx.enter_context(tc.manual_schedule())
 
-        rows = keep.tile([P, T], BF16, name="rows")
-        be_wide = keep.tile([P, T], BF16, name="be_wide")
-        pick = keep.tile([P, 2 * PAIRS], BF16, name="pick")
-        gain_raw = keep.tile([P, PAIRS * T], BF16, name="gain_raw")
-        gain_room = keep.tile([P, PASSES, P, 4], BF16, name="gain_wide", align_bytes=64)
-        gain_wide = gain_room[:].rearrange("p g r t -> p (g r t)")
+        rows = keep.tile([P, 2, T], BF16, name="rows")
+        pick = keep.tile([P, L + PAIRS, 2], BF16, name="pick")
         we_s = keep.tile([P, PASSES, T], U8, name="we_s", align_bytes=64)
         we_w = keep.tile([P, PASSES, 2 * T], U8, name="we_w", align_bytes=64)
         xs_rows = keep.tile([SCALE_ROWS, SCALE_SETS, QUADS], F32, name="xs_rows")
         xs_wide = keep.tile([P, SCALE_SETS, P], F32, name="xs_wide")
         xs = keep.tile([P, L * TILES * PASSES], F32, name="xs")
         ident = keep.tile([P, P], F32, name="ident")
-        nc.vector.memset(rows[:].bitcast(I32), 0)
+        nc.vector.memset(rows[:].rearrange("p a n -> p (a n)").bitcast(I32), 0)
+        nc.vector.memset(pick[:].rearrange("p c e -> p (c e)").bitcast(I32), 0)
         nc.vector.memset(we_s[:].rearrange("p g n -> p (g n)").bitcast(I32), 0)
-
         nc.vector.memset(xs_wide[:].rearrange("p s m -> p (s m)"), 0.0)
+        nc.vector.memset(pick[0:1, 0:L, :].rearrange("p c e -> p (c e)"), -1.0)
+        for p in range(PAIRS):
+            nc.vector.memset(pick[32 + 32 * p:33 + 32 * p, 2 * p, :], -1.0)
+            nc.vector.memset(pick[32 + 32 * p:33 + 32 * p, L + p, :], float(T))
+        make_identity(nc, ident[:])
 
         x_raw, trans_raw = {}, {}
 
@@ -93,107 +82,95 @@ def tile_chunkflooredmessagemiddlescore_kernel(tc, x_bytes, x_scale, we_words, w
             out=xs_rows[:].rearrange("r s q -> r (s q)"),
             in_=x_scale.rearrange("l i j -> (l i j)").rearrange("(r c) -> r c", r=SCALE_ROWS),
         )
-        nc.sync.dma_start(out=rows[0:1, :], in_=be.rearrange("(o n) -> o n", o=1))
-        nc.sync.dma_start(out=rows[32:65:32, :], in_=ends)
+        nc.sync.dma_start(out=rows[0:1, 0, :], in_=be.rearrange("(o n) -> o n", o=1))
+        nc.sync.dma_start(out=rows[32:65:32, 0, :], in_=ends)
         load_x(0, rest)
+        load_x(1, every)
         nc.sync.dma_start(out=we_w[:].bitcast(I32), in_=we_words.rearrange("g p n -> p g n").bitcast(I32))
         for q in range(QUADS):
             nc.sync.dma_start(
                 out=we_s[32 * q:32 * q + 4, :, :].bitcast(I32),
                 in_=we_scales[:, 4 * q:4 * q + 4, :].rearrange("g r n -> r g n").bitcast(I32),
             )
-        load_x(1, every)
         load_trans(1)
+        nc.sync.dma_start(out=rows[32:65:32, 1, :], in_=gain)
         load_x(2, every)
-        nc.sync.dma_start(out=gain_raw[:], in_=gain.rearrange("a n -> (a n)").partition_broadcast(P))
-        nc.sync.dma_start(out=be_wide[:], in_=be.partition_broadcast(P))
         load_trans(0)
         for i in range(3, TILES):
             load_x(i, every)
 
-        nc.gpsimd.memset(pick[:], 0.0)
-        nc.gpsimd.memset(pick[0:1, :], -1.0)
-        nc.gpsimd.memset(pick[32:33, 0:2], -1.0)
-        nc.gpsimd.memset(pick[64:65, 2:4], -1.0)
-        make_identity(nc, ident[:])
-        neg_ident = keep.tile([P, P], F32, name="neg_ident")
-        nc.gpsimd.tensor_scalar(out=neg_ident[:], in0=ident[:], scalar1=-1.0, scalar2=0.0, op0=ALU.mult, op1=ALU.add)
+        def next_bank(shape):
+            return psum.tile(shape, F32, name="bank", tag="bank", bufs=BANKS)
 
-        def bank_tile(bank, shape):
-            return psum.tile(shape, F32, name="bank%d" % bank, tag="bank%d" % bank)
+        scales_ps = next_bank([P, SCALE_SETS, P])
 
-        def spread_scales():
+        def repeat_scales():
             nc.vector.tensor_copy(
                 out=xs_wide[0:SCALE_ROWS].rearrange("r s (q m) -> r (s q) m", q=QUADS),
                 in_=xs_rows[:].rearrange("r s q -> r (s q)").unsqueeze(2).to_broadcast([SCALE_ROWS, SCALE_SETS * QUADS, 32]),
             )
 
-        scales_ps = {}
-
         def turn_scales():
-            scales_ps[0] = bank_tile(SCORE_BANK[2], [P, SCALE_SETS, P])
             for s in range(SCALE_SETS):
-                nc.tensor.transpose(scales_ps[0][:, s, :], xs_wide[:, s, :], ident[:])
+                nc.tensor.transpose(scales_ps[:, s, :], xs_wide[:, s, :], ident[:])
 
         def keep_scales():
-            acc = scales_ps[0]
             nc.vector.tensor_copy(
-                out=xs[:].rearrange("p (r s) -> p r s", s=SCALE_SETS), in_=acc[:, :, 0:SCALE_ROWS].rearrange("p s r -> p r s"),
+                out=xs[:].rearrange("p (r s) -> p r s", s=SCALE_SETS), in_=scales_ps[:, :, 0:SCALE_ROWS].rearrange("p s r -> p r s"),
             )
 
         neg_bias, bias_ps = {}, {}
 
         def spread_bias(l):
-            bias_ps[l] = bank_tile(MESSAGE_BANKS[l // 2], [P, T])
-            nc.tensor.matmul(bias_ps[l][:], lhsT=pick[:, l:l + 1].to_broadcast([P, P]), rhs=rows[:], start=True, stop=True)
+            bias_ps[l] = next_bank([P, T])
+            nc.tensor.matmul(bias_ps[l][:], lhsT=pick[:, l, 0:1].to_broadcast([P, P]), rhs=rows[:, 0, :], start=True, stop=True)
 
-        def keep_bias(l):
+        def keep_bias(l, copy):
             neg_bias[l] = keep.tile([P, T], F32, name="neg_bias%d" % l)
-            nc.vector.tensor_copy(out=neg_bias[l][:], in_=bias_ps[l][:])
+            copy(out=neg_bias[l][:], in_=bias_ps[l][:])
 
-        def scale_gain():
-            nc.gpsimd.tensor_scalar(out=gain_wide, in0=gain_raw[:], scalar1=float(T), scalar2=0.0, op0=ALU.mult, op1=ALU.add)
+        gain_ps = psum.tile([P, PAIRS, T], BF16, name="gain_ps", tag="gain_ps")
 
-        trans_grouped = {}
+        def spread_gain(p):
+            nc.tensor.matmul(gain_ps[:, p, :], lhsT=pick[:, L + p, 0:1].to_broadcast([P, P]), rhs=rows[:, 1, :], start=True, stop=True)
+
+        trans_room = keep.tile([P, 2 * PAIRS, PASSES, P, 4], BF16, name="tr_grouped", align_bytes=64)
+        trans_grouped = trans_room[:].rearrange("p (a h) g r t -> p a (h g r) t", a=PAIRS)
         trans_codes = keep.tile([P, PAIRS, T], U32, name="tr_codes", align_bytes=64)
         trans_scales = keep.tile([P, PAIRS, T], U8, name="tr_scales", align_bytes=64)
 
-        def group_second():
-            whole = keep.tile([P, T, 4], BF16, name="tr_grouped1", align_bytes=64)
-            trans_grouped[1] = whole[:]
-            nc.scalar.copy(
-                out=trans_grouped[1].rearrange("p (c i) t -> p c t i", i=4),
-                in_=trans_raw[1][:].rearrange("p t (c i) -> p c t i", i=4),
-            )
-
-        first_grouped = keep.tile([P, 2, PASSES, P, 4], BF16, name="tr_grouped0", align_bytes=64)
-        trans_grouped[0] = first_grouped[:].rearrange("p h g r t -> p (h g r) t")
-
-        def group_first(h):
+        def group_trans(quarter):
+            p, h = divmod(quarter, 2)
             cols = slice(h * HALF, (h + 1) * HALF)
             nc.gpsimd.tensor_scalar(
-                out=trans_grouped[0][:, cols, :], in0=trans_raw[0][:, :, cols].rearrange("p t n -> p n t"),
+                out=trans_grouped[:, p, cols, :], in0=trans_raw[p][:, :, cols].rearrange("p t n -> p n t"),
                 scalar1=1.0, scalar2=0.0, op0=ALU.mult, op1=ALU.add,
             )
 
-        def quantize_trans(p, h):
+        def group_second():
+            nc.scalar.copy(
+                out=trans_grouped[:, 1].rearrange("p (c i) t -> p c t i", i=4),
+                in_=trans_raw[1][:].rearrange("p t (c i) -> p c t i", i=4),
+            )
+
+        def quantize_trans(quarter):
+            p, h = divmod(quarter, 2)
             cols = slice(h * HALF, (h + 1) * HALF)
             nc.vector.quantize_mx(
                 out=trans_codes[:, p, cols].bitcast(FP8X4), scales=trans_scales[:, p, cols],
-                in_=trans_grouped[p][:, cols, :].rearrange("p n t -> p (n t)"),
+                in_=trans_grouped[:, p, cols, :].rearrange("p n t -> p (n t)"),
             )
 
-        x_wide, x_turned, x_grouped, e_ps = {}, {}, {}, {}
-        neg_n, neg_max, expo, end_expo = {}, {}, {}, {}
+        x_wide, x_turned, x_grouped, x_room, x_codes, e_ps = {}, {}, {}, {}, {}, {}
+        neg_n, neg_max, expo = {}, {}, {}
         sums = [keep.tile([P, PAIRS], F32, name="sums%d" % i) for i in range(TILES)]
         inverse = [keep.tile([P, PAIRS], F32, name="inv%d" % i) for i in range(TILES)]
         weight = keep.tile([P, TILES], F32, name="weight")
-        log_weight = keep.tile([P, TILES], F32, name="log_weight")
+        inv_weight = keep.tile([P, TILES], F32, name="inv_weight")
         mid_neg_max = keep.tile([P, TILES], F32, name="mid_neg_max")
-        shift = keep.tile([P, TILES], F32, name="shift")
 
         def widen(unit):
-            x_wide[unit] = work.tile([P, D], BF16, name="xw", tag="xw", bufs=8)
+            x_wide[unit] = work.tile([P, D], BF16, name="xw", tag="xw", bufs=6)
             nc.scalar.copy(out=x_wide[unit][:], in_=x_raw[unit].bitcast(FP8))
 
         def turn(bank, values, halves):
@@ -202,59 +179,44 @@ def tile_chunkflooredmessagemiddlescore_kernel(tc, x_bytes, x_scale, we_words, w
                 for u in range(2):
                     nc.tensor.transpose(bank[:, g, u, :], words[:, PASS_WORDS * g + u:PASS_WORDS * (g + 1):2], ident[:])
 
-        def turn_x(unit, bank=None):
-            x_turned[unit] = bank_tile(TURN_BANK[place_of[unit]] if bank is None else bank, [P, PASSES, 2, P])
+        def turn_x(unit):
+            x_turned[unit] = next_bank([P, PASSES, 2, P])
             turn(x_turned[unit], x_wide[unit][:], range(PASSES))
 
-        def light(k):
-            return k < FLOOR_LAG or k + WIDEN_AHEAD >= TILES
-
-        def vector_share(unit):
-            k, place = unit[0], place_of[unit]
-            if units.index(unit) < VECTOR_FIRST:
-                return PASSES * P
-            if place == 0:
-                return P if light(k - 1) else 0
-            if light(k):
-                return 0
-            return PASSES * P if place == 2 else VECTOR_SHARE
-
         def make_room(unit):
-            k, place = unit[0], place_of[unit]
-            if unit == (0, 1):
-                x_grouped[unit] = gain_room[:]
-            elif k == 1 and place > 0:
-                x_grouped[unit] = first_grouped[:, place - 1]
-            elif place == 2 and k >= FLOOR_LAG:
-                room = keep.tile([P, PASSES, P, 4], BF16, name="xg%d" % k, align_bytes=64)
-                x_grouped[unit] = room[:]
+            i, l = unit
+            if unit in TRANS_HOSTS:
+                x_grouped[unit] = trans_room[:, TRANS_HOSTS.index(unit)]
+                return
+            if unit == (LAST_TILE, 2):
+                room = keep.tile([P, 2, PASSES, P, 4], BF16, name="xg_last", align_bytes=64)
+            elif l == 0:
+                room = keep.tile([P, 1, PASSES, P, 4], BF16, name="xg%d_%d" % unit, align_bytes=64)
+            elif l == 1:
+                room = work.tile([P, 2, PASSES, P, 4], BF16, name="xg_mid", tag="xg_mid", bufs=2, align_bytes=64)
             else:
-                room = work.tile([P, PASSES, P, 4], BF16, name="xg", tag="xg", bufs=6, align_bytes=64)
-                x_grouped[unit] = room[:]
+                room = work.tile([P, 1, PASSES, P, 4], BF16, name="xg_end", tag="xg_end", bufs=3, align_bytes=64)
+            x_grouped[unit] = room[:, 0]
+            x_room[unit] = room[:].rearrange("p a g r t -> p (a g r t)").bitcast(F32)
 
-        def scaled_parts(unit, begin, end):
+        def scaled_part(unit, g):
             i, l = unit
             if unit not in x_grouped:
                 make_room(unit)
-            parts = []
-            for g in range(PASSES):
-                lo, hi = max(begin - g * P, 0), min(end - g * P, P)
-                if lo < hi:
-                    src = x_turned[unit][:, g].rearrange("p u r -> p (u r)").bitcast(BF16).rearrange("p (u r e) -> p r u e", u=2, e=2)
-                    dst = x_grouped[unit][:, g].rearrange("p r (u e) -> p r u e", u=2)
-                    column = (l * TILES + i) * PASSES + g
-                    parts.append((src[:, lo:hi], dst[:, lo:hi], xs[:, column:column + 1]))
-            return parts
+            src = x_turned[unit][:, g].rearrange("p u r -> p (u r)").bitcast(BF16).rearrange("p (u r e) -> p r u e", u=2, e=2)
+            dst = x_grouped[unit][:, g].rearrange("p r (u e) -> p r u e", u=2)
+            column = (l * TILES + i) * PASSES + g
+            return src, dst, xs[:, column:column + 1]
 
-        def empty_vector(unit):
-            for src, dst, scale in scaled_parts(unit, PASSES * P - vector_share(unit), PASSES * P):
+        def empty_vector(unit, passes=range(PASSES)):
+            for g in passes:
+                src, dst, scale = scaled_part(unit, g)
                 nc.vector.tensor_scalar(out=dst, in0=src, scalar1=scale, scalar2=None, op0=ALU.mult)
 
-        def empty_scalar(unit):
-            for src, dst, scale in scaled_parts(unit, 0, PASSES * P - vector_share(unit)):
+        def empty_scalar(unit, passes=range(PASSES)):
+            for g in passes:
+                src, dst, scale = scaled_part(unit, g)
                 nc.scalar.activation(out=dst, in_=src, func=ACT.Copy, scale=scale)
-
-        x_codes = {}
 
         def quantize_x(unit):
             codes = work.tile([P, PASSES * P], U32, name="xq", tag="xq", align_bytes=64)
@@ -264,13 +226,9 @@ def tile_chunkflooredmessagemiddlescore_kernel(tc, x_bytes, x_scale, we_words, w
                 out=codes[:].bitcast(FP8X4), scales=scales[:], in_=x_grouped[unit].rearrange("p g r t -> p (g r t)"),
             )
 
-        def score(unit, bank=None):
-            quantize_x(unit)
-            multiply_x(unit, bank)
-
-        def multiply_x(unit, bank=None):
+        def multiply_x(unit):
             codes, scales = x_codes[unit]
-            e_ps[unit] = bank_tile(SCORE_BANK[place_of[unit]] if bank is None else bank, [P, T])
+            e_ps[unit] = next_bank([P, T])
             for g in range(PASSES):
                 cols = slice(g * P, (g + 1) * P)
                 nc.tensor.matmul_mx(
@@ -278,23 +236,24 @@ def tile_chunkflooredmessagemiddlescore_kernel(tc, x_bytes, x_scale, we_words, w
                     rhs=we_w[:, g, :].bitcast(FP4X4), rhs_scale=we_s[:, g, :], start=(g == 0), stop=(g == PASSES - 1),
                 )
 
+        def score(unit):
+            quantize_x(unit)
+            multiply_x(unit)
+
         def add_bias(unit):
             i, l = unit
             if l == 1:
                 neg_n[unit] = keep.tile([P, T], F32, name="neg_mid%d" % i)
-                nc.vector.scalar_tensor_tensor(
-                    out=neg_n[unit][:], in0=e_ps[unit][:], scalar=-1.0, in1=be_wide[:], op0=ALU.mult, op1=ALU.subtract,
-                )
             else:
                 neg_n[unit] = work.tile([P, T], F32, name="neg_end", tag="neg_end")
-                nc.vector.tensor_tensor(out=neg_n[unit][:], in0=neg_bias[l][:], in1=e_ps[unit][:], op=ALU.subtract)
+            nc.vector.tensor_tensor(out=neg_n[unit][:], in0=neg_bias[l][:], in1=e_ps[unit][:], op=ALU.subtract)
 
         def find_max(unit):
             i, l = unit
             if l == 1:
                 neg_max[unit] = mid_neg_max[:, i:i + 1]
             else:
-                column = keep.tile([P, 1], F32, name="neg_max%d" % units.index(unit))
+                column = keep.tile([P, 1], F32, name="neg_max%d_%d" % unit)
                 neg_max[unit] = column[:]
             nc.vector.tensor_reduce(out=neg_max[unit], in_=neg_n[unit][:], axis=AX.X, op=ALU.min)
 
@@ -304,70 +263,83 @@ def tile_chunkflooredmessagemiddlescore_kernel(tc, x_bytes, x_scale, we_words, w
                 expo[unit] = work.tile([P, T], F32, name="ex_mid", tag="ex_mid")
                 nc.scalar.activation(out=expo[unit][:], in_=neg_n[unit][:], func=ACT.Exp, bias=neg_max[unit], scale=-1.0)
             else:
-                if i not in end_expo:
-                    end_expo[i] = work.tile([P, PAIRS, T], F32, name="ex", tag="ex")
-                expo[unit] = end_expo[i][:, l // 2, :]
+                expo[unit] = work.tile([P, T], F32, name="ex_end", tag="ex_end")
                 nc.scalar.activation(
-                    out=expo[unit], in_=neg_n[unit][:], func=ACT.Exp, bias=neg_max[unit], scale=-1.0,
+                    out=expo[unit][:], in_=neg_n[unit][:], func=ACT.Exp, bias=neg_max[unit], scale=-1.0,
                     accum_out=sums[i][:, l // 2:l // 2 + 1],
                 )
 
-        v, v_turned, v_grouped, m_ps = {}, {}, {}, {}
-        cuts, lifted, cut0, floored, product, log_a, total = {}, {}, {}, {}, {}, {}, {}
+        v, v_turned, v_grouped, v_codes, m_ps = {}, {}, {}, {}, {}
+        cuts, lifted, floored, product, terms, log_a, total = {}, {}, {}, {}, {}, {}, {}
 
-        def invert_sums(i):
-            nc.vector.reciprocal(out=inverse[i][:], in_=sums[i][:])
+        def invert_sums(i, pairs=slice(0, PAIRS)):
+            nc.vector.reciprocal(out=inverse[i][:, pairs], in_=sums[i][:, pairs])
 
         def message(i, p):
             if p == 0:
                 v[i] = work.tile([P, PAIRS, T], BF16, name="v", tag="v", bufs=2)
             nc.vector.scalar_tensor_tensor(
-                out=v[i][:, p, :], in0=expo[i, 2 * p], scalar=inverse[i][:, p:p + 1],
-                in1=gain_wide[:, p * T:(p + 1) * T], op0=ALU.mult, op1=ALU.mult,
+                out=v[i][:, p, :], in0=expo[i, 2 * p][:], scalar=inverse[i][:, p:p + 1],
+                in1=gain_ps[:, p, :], op0=ALU.mult, op1=ALU.mult,
             )
 
         def turn_v(i, pairs=range(PAIRS)):
             if i not in v_turned:
-                v_turned[i] = bank_tile(TURN_BANK[1], [P, PAIRS, 2, P])
+                v_turned[i] = next_bank([P, PAIRS, 2, P])
             turn(v_turned[i], v[i][:].rearrange("p a n -> p (a n)"), pairs)
 
-        def empty_v(i):
-            v_grouped[i] = work.tile([P, PAIRS, P, 2], F32, name="vg", tag="vg", bufs=2, align_bytes=64)
-            nc.scalar.copy(out=v_grouped[i][:], in_=v_turned[i][:].rearrange("p g u r -> p g r u"))
+        def empty_v(i, copy=nc.scalar.copy):
+            v_grouped[i] = work.tile([P, PAIRS, P, 2], F32, name="vg", tag="vg", bufs=3, align_bytes=64)
+            copy(out=v_grouped[i][:], in_=v_turned[i][:].rearrange("p g u r -> p g r u"))
 
-        def pass_on(i, banks=MESSAGE_BANKS):
+        def quantize_v(i):
             codes = work.tile([P, PAIRS * P], U32, name="vq", tag="vq", bufs=2, align_bytes=64)
             scales = work.tile([P, PAIRS * P], U8, name="vqs", tag="vqs", bufs=2, align_bytes=64)
+            v_codes[i] = codes, scales
             nc.vector.quantize_mx(
                 out=codes[:].bitcast(FP8X4), scales=scales[:],
                 in_=v_grouped[i][:].rearrange("p g r u -> p (g r u)").bitcast(BF16),
             )
+
+        def multiply_v(i):
+            codes, scales = v_codes[i]
             for p in range(PAIRS):
                 cols = slice(p * P, (p + 1) * P)
-                m_ps[i, p] = bank_tile(banks[p], [P, T])
+                m_ps[i, p] = next_bank([P, T])
                 nc.tensor.matmul_mx(
                     out=m_ps[i, p][:], lhsT=codes[:, cols].bitcast(FP8X4), lhsT_scale=scales[:, cols],
                     rhs=trans_codes[:, p, :].bitcast(FP8X4), rhs_scale=trans_scales[:, p, :], start=True, stop=True,
                 )
 
-        def cut_both(i):
-            cuts[i] = work.tile([P, PAIRS, T], F32, name="cuts", tag="cuts", bufs=1)
-            for p in range(PAIRS):
-                nc.scalar.activation(out=cuts[i][:, p, :], in_=m_ps[i, p][:], func=ACT.Relu, bias=FLOOR_SHIFT, scale=1.0)
+        def pass_on(i):
+            quantize_v(i)
+            multiply_v(i)
 
-        def lift_both(i):
-            lifted[i] = end_expo[i + 1][:].rearrange("p a n -> p (a n)")
+        def cut(i, p):
+            if i not in cuts:
+                cuts[i] = work.tile([P, PAIRS, T], F32, name="cuts", tag="cuts", bufs=2)
+            nc.scalar.activation(out=cuts[i][:, p, :], in_=m_ps[i, p][:], func=ACT.Relu, bias=FLOOR_SHIFT, scale=1.0)
+
+        def fresh_room(name, width):
+            room = keep.tile([P, width], F32, name=name)
+            return room[:]
+
+        def lift_both(i, room):
+            lifted[i] = room
             nc.gpsimd.tensor_scalar(
                 out=lifted[i], in0=cuts[i][:].rearrange("p a n -> p (a n)"), scalar1=1.0, scalar2=FLOOR_VALUE, op0=ALU.mult, op1=ALU.add,
             )
 
-        def multiply_lifted(i, spent):
-            product[i] = x_grouped[spent].rearrange("p g r t -> p (g r t)").bitcast(F32)
+        def multiply_lifted(i, room):
+            product[i] = room
             nc.gpsimd.tensor_tensor(out=product[i], in0=lifted[i][:, 0:T], in1=lifted[i][:, T:2 * T], op=ALU.mult)
 
-        def cut_first(i):
-            cut0[i] = work.tile([P, T], F32, name="cut0", tag="cut0", bufs=1)
-            nc.scalar.activation(out=cut0[i][:], in_=m_ps[i, 0][:], func=ACT.Relu, bias=FLOOR_SHIFT, scale=1.0)
+        def make_terms(i, room):
+            terms[i] = room
+            nc.gpsimd.tensor_tensor(out=terms[i], in0=expo[i, 1][:], in1=product[i], op=ALU.mult)
+
+        def sum_terms(i):
+            nc.scalar.activation(out=terms[i], in_=terms[i], func=ACT.Identity, scale=1.0 / T, accum_out=weight[:, i:i + 1])
 
         def floor(i, p):
             floored[i, p] = work.tile([P, T], F32, name="floored", tag="floored", bufs=3)
@@ -376,227 +348,255 @@ def tile_chunkflooredmessagemiddlescore_kernel(tc, x_bytes, x_scale, we_words, w
             )
 
         def multiply_floored(i):
-            whole = keep.tile([P, T], F32, name="prod%d" % i)
-            product[i] = whole[:]
+            product[i] = fresh_room("prod%d" % i, T)
             nc.vector.tensor_tensor(out=product[i], in0=floored[i, 0][:], in1=floored[i, 1][:], op=ALU.mult)
 
         def multiply_cut(i):
-            whole = keep.tile([P, T], F32, name="prod%d" % i)
-            product[i] = whole[:]
+            product[i] = fresh_room("prod%d" % i, T)
             nc.vector.scalar_tensor_tensor(
-                out=product[i], in0=cut0[i][:], scalar=FLOOR_VALUE, in1=floored[i, 1][:], op0=ALU.add, op1=ALU.mult,
+                out=product[i], in0=cuts[i][:, 0, :], scalar=FLOOR_VALUE, in1=floored[i, 1][:], op0=ALU.add, op1=ALU.mult,
             )
 
         def weigh(i):
-            terms = work.tile([P, T], F32, name="weighted", tag="weighted", bufs=1)
+            spent = work.tile([P, T], F32, name="weighted", tag="weighted", bufs=2)
             nc.vector.scalar_tensor_tensor(
-                out=terms[:], in0=expo[i, 1][:], scalar=1.0 / T, in1=product[i], op0=ALU.mult, op1=ALU.mult,
+                out=spent[:], in0=expo[i, 1][:], scalar=1.0 / T, in1=product[i], op0=ALU.mult, op1=ALU.mult,
                 accum_out=weight[:, i:i + 1],
             )
 
-        def log_weights(begin, end):
-            nc.scalar.activation(out=log_weight[:, begin:end], in_=weight[:, begin:end], func=ACT.Ln)
-
-        def make_shifts(begin, end):
-            nc.vector.tensor_tensor(out=shift[:, begin:end], in0=mid_neg_max[:, begin:end], in1=log_weight[:, begin:end], op=ALU.subtract)
+        def invert_weights(begin, end):
+            nc.vector.reciprocal(out=inv_weight[:, begin:end], in_=weight[:, begin:end])
 
         def pieces(i):
             return [slice(0, HALF), slice(HALF, T)] if i == LAST_TILE else [slice(0, T)]
 
         def take_log(i):
             for h, cols in enumerate(pieces(i)):
-                log_a[i, h] = work.tile([P, cols.stop - cols.start], F32, name="logp", tag="logp", bufs=TILES + 1)
-                nc.scalar.activation(out=log_a[i, h][:], in_=product[i][:, cols], func=ACT.Ln)
+                log_a[i, h] = work.tile([P, cols.stop - cols.start], F32, name="logp", tag="logp", bufs=5)
+                nc.scalar.activation(out=log_a[i, h][:], in_=product[i][:, cols], func=ACT.Ln, scale=inv_weight[:, i:i + 1])
 
         def finish(i):
             for h, cols in enumerate(pieces(i)):
                 res = work.tile([P, cols.stop - cols.start], F32, name="res", tag="res", bufs=TILES + 1)
                 nc.vector.scalar_tensor_tensor(
-                    out=res[:], in0=log_a[i, h][:], scalar=shift[:, i:i + 1], in1=neg_n[i, 1][:, cols], op0=ALU.add, op1=ALU.subtract,
+                    out=res[:], in0=log_a[i, h][:], scalar=mid_neg_max[:, i:i + 1], in1=neg_n[i, 1][:, cols], op0=ALU.add, op1=ALU.subtract,
                 )
                 nc.sync.dma_start(out=out[i * P:(i + 1) * P, cols], in_=res[:])
 
-        def open_total(i, h, bank=None):
-            if h == 0:
-                total[i] = bank_tile(bank, [P, T])
-            cols = slice(h * HALF, (h + 1) * HALF)
-            nc.tensor.matmul(total[i][:, cols], lhsT=neg_ident[:], rhs=neg_n[i, 1][:, cols], start=(h == 0), stop=False)
+        neg_ident = keep.tile([P, P], F32, name="neg_ident")
+
+        def negate_identity():
+            nc.gpsimd.tensor_scalar(out=neg_ident[:], in0=ident[:], scalar1=-1.0, scalar2=0.0, op0=ALU.mult, op1=ALU.add)
+
+        def open_total(i):
+            total[i] = next_bank([P, T])
+            nc.tensor.matmul(total[i][:], lhsT=neg_ident[:], rhs=neg_n[i, 1][:], start=True, stop=False)
 
         def close_total(i):
             nc.tensor.matmul(total[i][:], lhsT=ident[:], rhs=log_a[i, 0][:], start=False, stop=True)
 
         def finish_total(i):
             res = work.tile([P, T], F32, name="res", tag="res", bufs=TILES + 1)
-            nc.scalar.activation(out=res[:], in_=total[i][:], func=ACT.Identity, bias=shift[:, i:i + 1], scale=1.0)
+            nc.scalar.activation(out=res[:], in_=total[i][:], func=ACT.Identity, bias=mid_neg_max[:, i:i + 1], scale=1.0)
             nc.sync.dma_start(out=out[i * P:(i + 1) * P, :], in_=res[:])
 
-        spread_scales()
+        negate_identity()
+        repeat_scales()
         spread_bias(0)
         spread_bias(2)
         turn_scales()
-        keep_bias(0)
+        keep_bias(0, nc.vector.tensor_copy)
         keep_scales()
-        keep_bias(2)
-        for unit in rounds[0]:
+        keep_bias(2, nc.vector.tensor_copy)
+        for unit in [(0, 0), (0, 2), (0, 1), (1, 0)]:
             widen(unit)
             turn_x(unit)
         empty_vector((0, 0))
-        for unit in rounds[1]:
-            widen(unit)
-        turn_x((1, 0))
+        widen((1, 2))
+        widen((1, 1))
+        group_second()
         empty_vector((0, 2))
+        spread_bias(1)
         score((0, 0))
         empty_vector((0, 1))
         score((0, 2))
         turn_x((1, 2))
+        keep_bias(1, nc.scalar.copy)
         empty_vector((1, 0))
         score((0, 1))
-        scale_gain()
+        group_trans(0)
         turn_x((1, 1))
+        empty_scalar((1, 2))
+        widen((2, 0))
         add_bias((0, 0))
         add_bias((0, 2))
         find_max((0, 0))
-        find_max((0, 2))
-        group_second()
-        for unit in rounds[2][:2]:
-            widen(unit)
         exponent((0, 0))
+        score((1, 0))
+        group_trans(1)
+        spread_gain(0)
+        spread_gain(1)
+        turn_x((2, 0))
+        find_max((0, 2))
         exponent((0, 2))
-        widen(rounds[2][2])
+
+        widen((2, 2))
         add_bias((0, 1))
+        empty_vector((1, 1))
+        quantize_trans(2)
+        score((1, 2))
+        quantize_trans(3)
+        turn_x((2, 2))
+        empty_scalar((2, 0))
+        widen((2, 1))
+        invert_sums(0)
+        add_bias((1, 0))
+        message(0, 0)
+        message(0, 1)
+        turn_v(0)
+        score((1, 1))
+        turn_x((2, 1))
+        find_max((1, 0))
+        widen((3, 0))
+        empty_v(0)
+        exponent((1, 0))
+        add_bias((1, 2))
+        find_max((0, 1))
+        find_max((1, 2))
+        exponent((0, 1))
+        exponent((1, 2))
+        quantize_trans(0)
+        quantize_trans(1)
+        pass_on(0)
 
-        for k in range(1, LAST_TILE):
-            here, ahead = rounds[k], rounds[k + 1]
-            fresh = rounds[k + WIDEN_AHEAD] if k + WIDEN_AHEAD < TILES else []
-            empty_scalar(here[1])
-            if k >= WEIGH_LAG:
-                weigh(k - WEIGH_LAG)
-            if k < FLOOR_LAG:
-                score(here[0])
-                quantize_trans(1, 0)
-                invert_sums(k - 1)
-                quantize_trans(1, 1)
-            else:
-                invert_sums(k - 1)
-                score(here[0])
-            turn_x(ahead[0])
-            if k >= FLOOR_LAG:
-                cut_both(k - FLOOR_LAG)
+        for k in range(2, LAST_TILE):
+            quantize_x((k, 0))
+            if k >= 3:
+                multiply_lifted(k - 3, x_room[k, 0])
+            empty_scalar((k, 1))
+            multiply_x((k, 0))
+            add_bias((k - 1, 1))
+            invert_sums(k - 1)
+            empty_vector((k, 2))
             message(k - 1, 0)
-            empty_vector(here[1])
+            if k >= 3:
+                exponent((k - 2, 1))
+            cut(k - 2, 0)
+            cut(k - 2, 1)
+
+            quantize_x((k, 2))
+            if k >= 3:
+                make_terms(k - 3, x_room[k, 2])
+            multiply_x((k, 2))
+            turn_x((k + 1, 0))
+            add_bias((k, 0))
             message(k - 1, 1)
-
-            score(here[1])
             turn_v(k - 1)
-            if k >= FLOOR_LAG:
-                lift_both(k - FLOOR_LAG)
-            else:
-                group_first(0)
-            empty_scalar(here[2])
-            for unit in fresh[:2]:
-                widen(unit)
-            add_bias(here[0])
-            if light(k):
-                find_max(rounds[k - 1][2])
-            else:
-                empty_vector(here[2])
-            turn_x(ahead[2])
-            find_max(here[0])
-            empty_scalar(ahead[0])
+            find_max((k, 0))
+            widen((k + 1, 2))
+            widen((k + 1, 1))
+            if k + 2 < TILES:
+                widen((k + 2, 0))
 
-            score(here[2])
-            if k >= FLOOR_LAG:
-                multiply_lifted(k - FLOOR_LAG, here[2])
+            quantize_x((k, 1))
+            lift_both(k - 2, x_room[k, 1])
+            multiply_x((k, 1))
+            turn_x((k + 1, 2))
+            turn_x((k + 1, 1))
+            add_bias((k, 2))
+            if k in LIGHT_ROUNDS:
+                find_max((k - 1, 1))
+                find_max((k, 2))
+                empty_scalar((k + 1, 0), [0])
+                empty_v(k - 1)
+                empty_scalar((k + 1, 0), [1])
+                exponent((k, 0))
+                exponent((k, 2))
+                if k >= 3:
+                    sum_terms(k - 3)
+                pass_on(k - 1)
             else:
-                group_first(1)
-            for unit in fresh[2:]:
-                widen(unit)
-            empty_v(k - 1)
-            turn_x(ahead[1])
-            exponent(here[0])
-            add_bias(here[1])
-            if light(k):
-                empty_vector(ahead[0])
-            else:
-                find_max(rounds[k - 1][2])
-            find_max(here[1])
-            exponent(rounds[k - 1][2])
-            exponent(here[1])
-
-            if k < FLOOR_LAG:
-                quantize_trans(0, 0)
-                quantize_trans(0, 1)
-            pass_on(k - 1)
-            add_bias(here[2])
+                empty_vector((k + 1, 0))
+                find_max((k, 2))
+                empty_v(k - 1)
+                exponent((k, 0))
+                sum_terms(k - 3)
+                exponent((k, 2))
+                pass_on(k - 1)
+                find_max((k - 1, 1))
 
         last = LAST_TILE
+        quantize_x((last, 0))
+        multiply_lifted(last - 3, x_room[last, 0])
+        multiply_x((last, 0))
         empty_scalar((last, 2))
+        cut(last - 2, 0)
+        cut(last - 2, 1)
         empty_scalar((last, 1))
-        score((last, 0))
-        find_max((last - 1, 1))
+        add_bias((last - 1, 1))
         invert_sums(last - 1)
-        weigh(last - WEIGH_LAG)
-        score((last, 2))
-        message(last - 1, 0)
+        find_max((last - 1, 1))
         add_bias((last, 0))
-        message(last - 1, 1)
-        cut_both(last - 2)
-        turn_v(last - 1)
-        score((last, 1))
-        open_total(FIRST_TENSOR_TILE, 0, TURN_BANK[0])
-        open_total(FIRST_TENSOR_TILE, 1)
-        lift_both(last - 2)
-        multiply_lifted(last - 2, (last, 1))
-        exponent((last - 1, 1))
-        empty_v(last - 1)
-        add_bias((last, 2))
+        quantize_x((last, 2))
+        lift_both(last - 2, x_room[last, 2])
+        multiply_x((last, 2))
+        open_total(0)
+        exponent((last - 2, 1))
+        message(last - 1, 0)
         find_max((last, 0))
-        add_bias((last, 1))
+        add_bias((last, 2))
+        quantize_x((last, 1))
+        multiply_lifted(last - 2, x_room[last, 1][:, 0:T])
+        multiply_x((last, 1))
+        exponent((last - 1, 1))
+        exponent((last, 0))
+        message(last - 1, 1)
+        turn_v(last - 1)
+        open_total(2)
         find_max((last, 2))
-        find_max((last, 1))
-        for unit in rounds[last]:
-            exponent(unit)
-
-        pass_on(last - 1)
+        exponent((last, 2))
+        add_bias((last, 1))
+        empty_v(last - 1)
+        weigh(last - 3)
         invert_sums(last)
-        weigh(last - 2)
+        find_max((last, 1))
+        exponent((last, 1))
         message(last, 0)
         turn_v(last, [0])
-        open_total(SECOND_TENSOR_TILE, 0, TURN_BANK[2])
+        invert_weights(0, last - 2)
         message(last, 1)
         turn_v(last, [1])
-        open_total(SECOND_TENSOR_TILE, 1)
-        log_weights(0, last - 1)
-        take_log(0)
+        pass_on(last - 1)
+        open_total(4)
+        weigh(last - 2)
+        empty_v(last, nc.vector.tensor_copy)
         floor(last - 1, 0)
+        invert_weights(last - 2, last - 1)
+        pass_on(last)
         floor(last - 1, 1)
-        make_shifts(0, last - 1)
-        empty_v(last)
-        multiply_floored(last - 1)
-        pass_on(last, SCORE_BANK[0:2])
-        take_log(FIRST_TENSOR_TILE)
-        close_total(FIRST_TENSOR_TILE)
-        finish(0)
-        weigh(last - 1)
-        take_log(FIRST_TENSOR_TILE + 1)
-        take_log(SECOND_TENSOR_TILE)
-        close_total(SECOND_TENSOR_TILE)
-        cut_first(last)
+        take_log(0)
+        close_total(0)
+        take_log(1)
+        take_log(2)
+        close_total(2)
+        finish(1)
         floor(last, 1)
-        finish(FIRST_TENSOR_TILE + 1)
+        cut(last, 0)
+        multiply_floored(last - 1)
+        take_log(3)
+        take_log(4)
+        close_total(4)
+        finish_total(0)
         multiply_cut(last)
-        log_weights(last - 1, last)
-        take_log(SECOND_TENSOR_TILE + 1)
-        finish_total(FIRST_TENSOR_TILE)
-        make_shifts(last - 1, last)
-        finish(SECOND_TENSOR_TILE + 1)
+        weigh(last - 1)
+        take_log(5)
+        finish_total(2)
         weigh(last)
-        take_log(last - 2)
-        finish_total(SECOND_TENSOR_TILE)
-        finish(last - 2)
-        take_log(last - 1)
-        log_weights(last, TILES)
-        take_log(last)
-        make_shifts(last, TILES)
-        finish(last - 1)
-        finish(last)
+        finish(3)
+        invert_weights(last - 1, TILES)
+        finish_total(4)
+        finish(5)
+        take_log(6)
+        take_log(7)
+        finish(6)
+        finish(7)

@@ -31,7 +31,6 @@ FLOOR_SHIFT = 14.4
 FLOOR_VALUE = 1.6
 
 TRANS_HOSTS = [(0, 1), (1, 0)]
-LIGHT_ROUNDS = (2,)
 
 BANKS = 7
 
@@ -188,16 +187,12 @@ def tile_chunkflooredmessagemiddlescore_kernel(tc, x_bytes, x_scale, we_words, w
             if unit in TRANS_HOSTS:
                 x_grouped[unit] = trans_room[:, TRANS_HOSTS.index(unit)]
                 return
-            if unit == (LAST_TILE, 2):
-                room = keep.tile([P, 2, PASSES, P, 4], BF16, name="xg_last", align_bytes=64)
-            elif l == 0:
-                room = keep.tile([P, 1, PASSES, P, 4], BF16, name="xg%d_%d" % unit, align_bytes=64)
-            elif l == 1:
-                room = work.tile([P, 2, PASSES, P, 4], BF16, name="xg_mid", tag="xg_mid", bufs=2, align_bytes=64)
+            if l == 2 and i >= 3 or unit == (LAST_TILE, 1):
+                room = keep.tile([P, PASSES, P, 4], BF16, name="xg%d_%d" % unit, align_bytes=64)
             else:
-                room = work.tile([P, 1, PASSES, P, 4], BF16, name="xg_end", tag="xg_end", bufs=3, align_bytes=64)
-            x_grouped[unit] = room[:, 0]
-            x_room[unit] = room[:].rearrange("p a g r t -> p (a g r t)").bitcast(F32)
+                room = work.tile([P, PASSES, P, 4], BF16, name="xg", tag="xg", align_bytes=64)
+            x_grouped[unit] = room[:]
+            x_room[unit] = room[:].rearrange("p g r t -> p (g r t)").bitcast(F32)
 
         def scaled_part(unit, g):
             i, l = unit
@@ -292,6 +287,9 @@ def tile_chunkflooredmessagemiddlescore_kernel(tc, x_bytes, x_scale, we_words, w
             v_grouped[i] = work.tile([P, PAIRS, P, 2], F32, name="vg", tag="vg", bufs=3, align_bytes=64)
             copy(out=v_grouped[i][:], in_=v_turned[i][:].rearrange("p g u r -> p g r u"))
 
+        def v_room(i):
+            return v_grouped[i][:].rearrange("p g r u -> p (g r u)")
+
         def quantize_v(i):
             codes = work.tile([P, PAIRS * P], U32, name="vq", tag="vq", bufs=2, align_bytes=64)
             scales = work.tile([P, PAIRS * P], U8, name="vqs", tag="vqs", bufs=2, align_bytes=64)
@@ -317,17 +315,17 @@ def tile_chunkflooredmessagemiddlescore_kernel(tc, x_bytes, x_scale, we_words, w
 
         def cut(i, p):
             if i not in cuts:
-                cuts[i] = work.tile([P, PAIRS, T], F32, name="cuts", tag="cuts", bufs=2)
+                cuts[i] = work.tile([P, PAIRS, T], F32, name="cuts", tag="cuts", bufs=3)
             nc.scalar.activation(out=cuts[i][:, p, :], in_=m_ps[i, p][:], func=ACT.Relu, bias=FLOOR_SHIFT, scale=1.0)
 
         def fresh_room(name, width):
             room = keep.tile([P, width], F32, name=name)
             return room[:]
 
-        def lift_both(i, room):
-            lifted[i] = room
+        def lift_both(i):
+            lifted[i] = cuts[i][:].rearrange("p a n -> p (a n)")
             nc.gpsimd.tensor_scalar(
-                out=lifted[i], in0=cuts[i][:].rearrange("p a n -> p (a n)"), scalar1=1.0, scalar2=FLOOR_VALUE, op0=ALU.mult, op1=ALU.add,
+                out=lifted[i], in0=lifted[i], scalar1=1.0, scalar2=FLOOR_VALUE, op0=ALU.mult, op1=ALU.add,
             )
 
         def multiply_lifted(i, room):
@@ -346,6 +344,10 @@ def tile_chunkflooredmessagemiddlescore_kernel(tc, x_bytes, x_scale, we_words, w
             nc.vector.tensor_scalar(
                 out=floored[i, p][:], in0=m_ps[i, p][:], scalar1=-FLOOR_SHIFT, scalar2=16.0, op0=ALU.max, op1=ALU.add,
             )
+
+        def lift_second(i):
+            floored[i, 1] = work.tile([P, T], F32, name="floored", tag="floored", bufs=3)
+            nc.vector.tensor_scalar(out=floored[i, 1][:], in0=cuts[i][:, 1, :], scalar1=FLOOR_VALUE, scalar2=None, op0=ALU.add)
 
         def multiply_floored(i):
             product[i] = fresh_room("prod%d" % i, T)
@@ -468,135 +470,116 @@ def tile_chunkflooredmessagemiddlescore_kernel(tc, x_bytes, x_scale, we_words, w
         quantize_trans(0)
         quantize_trans(1)
         pass_on(0)
+        empty_vector((2, 2))
 
         for k in range(2, LAST_TILE):
-            quantize_x((k, 0))
+            score((k, 0))
+            score((k, 2))
             if k >= 3:
-                multiply_lifted(k - 3, x_room[k, 0])
-            empty_scalar((k, 1))
-            multiply_x((k, 0))
-            add_bias((k - 1, 1))
-            invert_sums(k - 1)
-            empty_vector((k, 2))
-            message(k - 1, 0)
-            if k >= 3:
-                exponent((k - 2, 1))
+                multiply_lifted(k - 3, x_room[k, 2])
+            widen((k + 1, 2))
             cut(k - 2, 0)
             cut(k - 2, 1)
-
-            quantize_x((k, 2))
-            if k >= 3:
-                make_terms(k - 3, x_room[k, 2])
-            multiply_x((k, 2))
-            turn_x((k + 1, 0))
-            add_bias((k, 0))
+            lift_both(k - 2)
+            empty_scalar((k, 1))
+            invert_sums(k - 1)
+            add_bias((k - 1, 1))
+            message(k - 1, 0)
             message(k - 1, 1)
             turn_v(k - 1)
+            turn_x((k + 1, 0))
+            turn_x((k + 1, 2))
+            add_bias((k, 0))
+            find_max((k - 1, 1))
+            add_bias((k, 2))
             find_max((k, 0))
-            widen((k + 1, 2))
+            if k >= 4:
+                sum_terms(k - 4)
             widen((k + 1, 1))
+            empty_v(k - 1)
+            exponent((k - 1, 1))
+            exponent((k, 0))
+
+            score((k, 1))
+            pass_on(k - 1)
+            if k >= 3:
+                make_terms(k - 3, v_room(k - 1))
+            turn_x((k + 1, 1))
+            find_max((k, 2))
             if k + 2 < TILES:
                 widen((k + 2, 0))
-
-            quantize_x((k, 1))
-            lift_both(k - 2, x_room[k, 1])
-            multiply_x((k, 1))
-            turn_x((k + 1, 2))
-            turn_x((k + 1, 1))
-            add_bias((k, 2))
-            if k in LIGHT_ROUNDS:
-                find_max((k - 1, 1))
-                find_max((k, 2))
-                empty_scalar((k + 1, 0), [0])
-                empty_v(k - 1)
-                empty_scalar((k + 1, 0), [1])
-                exponent((k, 0))
-                exponent((k, 2))
-                if k >= 3:
-                    sum_terms(k - 3)
-                pass_on(k - 1)
-            else:
-                empty_vector((k + 1, 0))
-                find_max((k, 2))
-                empty_v(k - 1)
-                exponent((k, 0))
-                sum_terms(k - 3)
-                exponent((k, 2))
-                pass_on(k - 1)
-                find_max((k - 1, 1))
+            exponent((k, 2))
+            empty_vector((k + 1, 0))
+            empty_vector((k + 1, 2))
 
         last = LAST_TILE
-        quantize_x((last, 0))
-        multiply_lifted(last - 3, x_room[last, 0])
-        multiply_x((last, 0))
-        empty_scalar((last, 2))
+        score((last, 0))
+        score((last, 2))
+        multiply_lifted(last - 3, x_room[last, 2])
         cut(last - 2, 0)
         cut(last - 2, 1)
+        lift_both(last - 2)
         empty_scalar((last, 1))
-        add_bias((last - 1, 1))
         invert_sums(last - 1)
-        find_max((last - 1, 1))
-        add_bias((last, 0))
-        quantize_x((last, 2))
-        lift_both(last - 2, x_room[last, 2])
-        multiply_x((last, 2))
-        open_total(0)
-        exponent((last - 2, 1))
+        add_bias((last - 1, 1))
         message(last - 1, 0)
-        find_max((last, 0))
-        add_bias((last, 2))
-        quantize_x((last, 1))
-        multiply_lifted(last - 2, x_room[last, 1][:, 0:T])
-        multiply_x((last, 1))
-        exponent((last - 1, 1))
-        exponent((last, 0))
         message(last - 1, 1)
         turn_v(last - 1)
-        open_total(2)
+        open_total(0)
+        add_bias((last, 0))
+        add_bias((last, 2))
+        find_max((last, 0))
         find_max((last, 2))
-        exponent((last, 2))
-        add_bias((last, 1))
+        sum_terms(last - 4)
         empty_v(last - 1)
-        weigh(last - 3)
+        exponent((last, 0))
+        exponent((last, 2))
+        score((last, 1))
+        pass_on(last - 1)
+        multiply_lifted(last - 2, v_room(last - 1))
+        find_max((last - 1, 1))
+        exponent((last - 1, 1))
         invert_sums(last)
-        find_max((last, 1))
-        exponent((last, 1))
+        invert_weights(0, last - 3)
+        add_bias((last, 1))
         message(last, 0)
         turn_v(last, [0])
-        invert_weights(0, last - 2)
+        find_max((last, 1))
         message(last, 1)
         turn_v(last, [1])
-        pass_on(last - 1)
-        open_total(4)
-        weigh(last - 2)
+        open_total(2)
+        cut(last - 1, 0)
+        cut(last - 1, 1)
+        exponent((last, 1))
+        weigh(last - 3)
         empty_v(last, nc.vector.tensor_copy)
-        floor(last - 1, 0)
-        invert_weights(last - 2, last - 1)
+        lift_second(last - 1)
         pass_on(last)
-        floor(last - 1, 1)
+        multiply_cut(last - 1)
+        weigh(last - 2)
+        floor(last, 1)
+        invert_weights(last - 3, last - 1)
         take_log(0)
         close_total(0)
         take_log(1)
+        cut(last, 0)
         take_log(2)
         close_total(2)
         finish(1)
-        floor(last, 1)
-        cut(last, 0)
-        multiply_floored(last - 1)
-        take_log(3)
-        take_log(4)
-        close_total(4)
-        finish_total(0)
         multiply_cut(last)
         weigh(last - 1)
+        take_log(3)
+        finish_total(0)
+        take_log(4)
+        finish(3)
+        weigh(last)
+        invert_weights(last - 1, last)
         take_log(5)
         finish_total(2)
-        weigh(last)
-        finish(3)
-        invert_weights(last - 1, TILES)
-        finish_total(4)
-        finish(5)
+        finish(4)
+        invert_weights(last, TILES)
         take_log(6)
+        finish(5)
         take_log(7)
         finish(6)
         finish(7)

@@ -168,9 +168,9 @@ def tile_chunkflooredmessagemiddlescore_kernel(tc, x_bytes, x_scale, we_words, w
         inv_weight = keep.tile([P, TILES], F32, name="inv_weight")
         mid_neg_max = keep.tile([P, TILES], F32, name="mid_neg_max")
 
-        def widen(unit):
+        def widen(unit, copy=nc.scalar.copy):
             x_wide[unit] = work.tile([P, D], BF16, name="xw", tag="xw", bufs=6)
-            nc.scalar.copy(out=x_wide[unit][:], in_=x_raw[unit].bitcast(FP8))
+            copy(out=x_wide[unit][:], in_=x_raw[unit].bitcast(FP8))
 
         def turn(bank, values, halves):
             words = values.bitcast(F32)
@@ -187,10 +187,10 @@ def tile_chunkflooredmessagemiddlescore_kernel(tc, x_bytes, x_scale, we_words, w
             if unit in TRANS_HOSTS:
                 x_grouped[unit] = trans_room[:, TRANS_HOSTS.index(unit)]
                 return
-            if l == 2 and i >= 3 or unit == (LAST_TILE, 1):
+            if l == 0 and i >= 3:
                 room = keep.tile([P, PASSES, P, 4], BF16, name="xg%d_%d" % unit, align_bytes=64)
             else:
-                room = work.tile([P, PASSES, P, 4], BF16, name="xg", tag="xg", align_bytes=64)
+                room = work.tile([P, PASSES, P, 4], BF16, name="xg", tag="xg", bufs=5, align_bytes=64)
             x_grouped[unit] = room[:]
             x_room[unit] = room[:].rearrange("p g r t -> p (g r t)").bitcast(F32)
 
@@ -402,7 +402,6 @@ def tile_chunkflooredmessagemiddlescore_kernel(tc, x_bytes, x_scale, we_words, w
             nc.scalar.activation(out=res[:], in_=total[i][:], func=ACT.Identity, bias=mid_neg_max[:, i:i + 1], scale=1.0)
             nc.sync.dma_start(out=out[i * P:(i + 1) * P, :], in_=res[:])
 
-        negate_identity()
         repeat_scales()
         spread_bias(0)
         spread_bias(2)
@@ -445,6 +444,7 @@ def tile_chunkflooredmessagemiddlescore_kernel(tc, x_bytes, x_scale, we_words, w
         widen((2, 2))
         add_bias((0, 1))
         empty_vector((1, 1))
+        add_bias((1, 0))
         quantize_trans(2)
         score((1, 2))
         quantize_trans(3)
@@ -452,16 +452,15 @@ def tile_chunkflooredmessagemiddlescore_kernel(tc, x_bytes, x_scale, we_words, w
         empty_scalar((2, 0))
         widen((2, 1))
         invert_sums(0)
-        add_bias((1, 0))
+        find_max((1, 0))
         message(0, 0)
         message(0, 1)
         turn_v(0)
         score((1, 1))
         turn_x((2, 1))
-        find_max((1, 0))
         widen((3, 0))
-        empty_v(0)
         exponent((1, 0))
+        empty_v(0)
         add_bias((1, 2))
         find_max((0, 1))
         find_max((1, 2))
@@ -476,11 +475,13 @@ def tile_chunkflooredmessagemiddlescore_kernel(tc, x_bytes, x_scale, we_words, w
             score((k, 0))
             score((k, 2))
             if k >= 3:
-                multiply_lifted(k - 3, x_room[k, 2])
+                multiply_lifted(k - 3, x_room[k, 0])
             widen((k + 1, 2))
             cut(k - 2, 0)
             cut(k - 2, 1)
             lift_both(k - 2)
+            if k == 2:
+                negate_identity()
             empty_scalar((k, 1))
             invert_sums(k - 1)
             add_bias((k - 1, 1))
@@ -489,19 +490,22 @@ def tile_chunkflooredmessagemiddlescore_kernel(tc, x_bytes, x_scale, we_words, w
             turn_v(k - 1)
             turn_x((k + 1, 0))
             turn_x((k + 1, 2))
-            add_bias((k, 0))
             find_max((k - 1, 1))
+            add_bias((k, 0))
             add_bias((k, 2))
             find_max((k, 0))
             if k >= 4:
                 sum_terms(k - 4)
-            widen((k + 1, 1))
-            empty_v(k - 1)
+                empty_v(k - 1)
+                widen((k + 1, 1))
+            else:
+                widen((k + 1, 1))
+                empty_v(k - 1)
             exponent((k - 1, 1))
             exponent((k, 0))
 
-            score((k, 1))
             pass_on(k - 1)
+            score((k, 1))
             if k >= 3:
                 make_terms(k - 3, v_room(k - 1))
             turn_x((k + 1, 1))
@@ -515,7 +519,7 @@ def tile_chunkflooredmessagemiddlescore_kernel(tc, x_bytes, x_scale, we_words, w
         last = LAST_TILE
         score((last, 0))
         score((last, 2))
-        multiply_lifted(last - 3, x_room[last, 2])
+        multiply_lifted(last - 3, x_room[last, 0])
         cut(last - 2, 0)
         cut(last - 2, 1)
         lift_both(last - 2)

@@ -30,9 +30,17 @@ SCALE_ROWS, SCALE_SETS = 16, 3
 FLOOR_SHIFT = 14.4
 FLOOR_VALUE = 1.6
 
-TRANS_HOSTS = [(0, 1), (1, 0)]
+TRANS_HOSTS = {(0, 1): 0, (1, 2): 2, (1, 1): 3}
 
-BANKS = 7
+BANK_OF = {
+    ("e", 0): "bank0", ("bias", 0): "bank0",
+    ("turned", 0): "bank1", ("total", 1): "bank1",
+    "v": "bank2", ("m", 0): "bank2", "scales": "bank2", ("bias", 1): "bank2",
+    ("e", 2): "bank3", ("m", 1): "bank3", ("bias", 2): "bank3",
+    ("turned", 2): "bank4", ("total", 3): "bank4",
+    ("e", 1): "bank5",
+    ("turned", 1): "bank6", ("total", 0): "bank6",
+}
 
 
 def tile_chunkflooredmessagemiddlescore_kernel(tc, x_bytes, x_scale, we_words, we_scales, be, ends, gain, trans, out):
@@ -85,23 +93,24 @@ def tile_chunkflooredmessagemiddlescore_kernel(tc, x_bytes, x_scale, we_words, w
         nc.sync.dma_start(out=rows[32:65:32, 0, :], in_=ends)
         load_x(0, rest)
         load_x(1, every)
+        nc.sync.dma_start(out=rows[32:65:32, 1, :], in_=gain)
         nc.sync.dma_start(out=we_w[:].bitcast(I32), in_=we_words.rearrange("g p n -> p g n").bitcast(I32))
         for q in range(QUADS):
             nc.sync.dma_start(
                 out=we_s[32 * q:32 * q + 4, :, :].bitcast(I32),
                 in_=we_scales[:, 4 * q:4 * q + 4, :].rearrange("g r n -> r g n").bitcast(I32),
             )
-        load_trans(1)
-        nc.sync.dma_start(out=rows[32:65:32, 1, :], in_=gain)
         load_x(2, every)
         load_trans(0)
+        load_trans(1)
         for i in range(3, TILES):
             load_x(i, every)
 
-        def next_bank(shape):
-            return psum.tile(shape, F32, name="bank", tag="bank", bufs=BANKS)
+        def next_bank(role, shape):
+            tag = BANK_OF[role]
+            return psum.tile(shape, F32, name=tag, tag=tag)
 
-        scales_ps = next_bank([P, SCALE_SETS, P])
+        scales_ps = next_bank("scales", [P, SCALE_SETS, P])
 
         def repeat_scales():
             nc.vector.tensor_copy(
@@ -121,7 +130,7 @@ def tile_chunkflooredmessagemiddlescore_kernel(tc, x_bytes, x_scale, we_words, w
         neg_bias, bias_ps = {}, {}
 
         def spread_bias(l):
-            bias_ps[l] = next_bank([P, T])
+            bias_ps[l] = next_bank(("bias", l), [P, T])
             nc.tensor.matmul(bias_ps[l][:], lhsT=pick[:, l, 0:1].to_broadcast([P, P]), rhs=rows[:, 0, :], start=True, stop=True)
 
         def keep_bias(l, copy):
@@ -146,10 +155,12 @@ def tile_chunkflooredmessagemiddlescore_kernel(tc, x_bytes, x_scale, we_words, w
                 scalar1=1.0, scalar2=0.0, op0=ALU.mult, op1=ALU.add,
             )
 
-        def group_second():
+        def group_scalar(quarter):
+            p, h = divmod(quarter, 2)
+            cols = slice(h * HALF, (h + 1) * HALF)
             nc.scalar.copy(
-                out=trans_grouped[:, 1].rearrange("p (c i) t -> p c t i", i=4),
-                in_=trans_raw[1][:].rearrange("p t (c i) -> p c t i", i=4),
+                out=trans_grouped[:, p, cols, :].rearrange("p (c i) t -> p c t i", i=4),
+                in_=trans_raw[p][:, :, cols].rearrange("p t (c i) -> p c t i", i=4),
             )
 
         def quantize_trans(quarter):
@@ -169,7 +180,7 @@ def tile_chunkflooredmessagemiddlescore_kernel(tc, x_bytes, x_scale, we_words, w
         mid_neg_max = keep.tile([P, TILES], F32, name="mid_neg_max")
 
         def widen(unit, copy=nc.scalar.copy):
-            x_wide[unit] = work.tile([P, D], BF16, name="xw", tag="xw", bufs=6)
+            x_wide[unit] = work.tile([P, D], BF16, name="xw", tag="xw", bufs=7)
             copy(out=x_wide[unit][:], in_=x_raw[unit].bitcast(FP8))
 
         def turn(bank, values, halves):
@@ -179,13 +190,13 @@ def tile_chunkflooredmessagemiddlescore_kernel(tc, x_bytes, x_scale, we_words, w
                     nc.tensor.transpose(bank[:, g, u, :], words[:, PASS_WORDS * g + u:PASS_WORDS * (g + 1):2], ident[:])
 
         def turn_x(unit):
-            x_turned[unit] = next_bank([P, PASSES, 2, P])
+            x_turned[unit] = next_bank(("turned", unit[1]), [P, PASSES, 2, P])
             turn(x_turned[unit], x_wide[unit][:], range(PASSES))
 
         def make_room(unit):
             i, l = unit
             if unit in TRANS_HOSTS:
-                x_grouped[unit] = trans_room[:, TRANS_HOSTS.index(unit)]
+                x_grouped[unit] = trans_room[:, TRANS_HOSTS[unit]]
                 return
             if l == 0 and i >= 3:
                 room = keep.tile([P, PASSES, P, 4], BF16, name="xg%d_%d" % unit, align_bytes=64)
@@ -223,7 +234,7 @@ def tile_chunkflooredmessagemiddlescore_kernel(tc, x_bytes, x_scale, we_words, w
 
         def multiply_x(unit):
             codes, scales = x_codes[unit]
-            e_ps[unit] = next_bank([P, T])
+            e_ps[unit] = next_bank(("e", unit[1]), [P, T])
             for g in range(PASSES):
                 cols = slice(g * P, (g + 1) * P)
                 nc.tensor.matmul_mx(
@@ -255,7 +266,7 @@ def tile_chunkflooredmessagemiddlescore_kernel(tc, x_bytes, x_scale, we_words, w
         def exponent(unit):
             i, l = unit
             if l == 1:
-                expo[unit] = work.tile([P, T], F32, name="ex_mid", tag="ex_mid")
+                expo[unit] = work.tile([P, T], F32, name="ex_mid", tag="ex_mid", bufs=5)
                 nc.scalar.activation(out=expo[unit][:], in_=neg_n[unit][:], func=ACT.Exp, bias=neg_max[unit], scale=-1.0)
             else:
                 expo[unit] = work.tile([P, T], F32, name="ex_end", tag="ex_end")
@@ -280,7 +291,7 @@ def tile_chunkflooredmessagemiddlescore_kernel(tc, x_bytes, x_scale, we_words, w
 
         def turn_v(i, pairs=range(PAIRS)):
             if i not in v_turned:
-                v_turned[i] = next_bank([P, PAIRS, 2, P])
+                v_turned[i] = next_bank("v", [P, PAIRS, 2, P])
             turn(v_turned[i], v[i][:].rearrange("p a n -> p (a n)"), pairs)
 
         def empty_v(i, copy=nc.scalar.copy):
@@ -303,7 +314,7 @@ def tile_chunkflooredmessagemiddlescore_kernel(tc, x_bytes, x_scale, we_words, w
             codes, scales = v_codes[i]
             for p in range(PAIRS):
                 cols = slice(p * P, (p + 1) * P)
-                m_ps[i, p] = next_bank([P, T])
+                m_ps[i, p] = next_bank(("m", p), [P, T])
                 nc.tensor.matmul_mx(
                     out=m_ps[i, p][:], lhsT=codes[:, cols].bitcast(FP8X4), lhsT_scale=scales[:, cols],
                     rhs=trans_codes[:, p, :].bitcast(FP8X4), rhs_scale=trans_scales[:, p, :], start=True, stop=True,
@@ -388,10 +399,10 @@ def tile_chunkflooredmessagemiddlescore_kernel(tc, x_bytes, x_scale, we_words, w
         neg_ident = keep.tile([P, P], F32, name="neg_ident")
 
         def negate_identity():
-            nc.gpsimd.tensor_scalar(out=neg_ident[:], in0=ident[:], scalar1=-1.0, scalar2=0.0, op0=ALU.mult, op1=ALU.add)
+            nc.scalar.activation(out=neg_ident[:], in_=ident[:], func=ACT.Copy, scale=-1.0)
 
         def open_total(i):
-            total[i] = next_bank([P, T])
+            total[i] = next_bank(("total", i), [P, T])
             nc.tensor.matmul(total[i][:], lhsT=neg_ident[:], rhs=neg_n[i, 1][:], start=True, stop=False)
 
         def close_total(i):
@@ -402,188 +413,206 @@ def tile_chunkflooredmessagemiddlescore_kernel(tc, x_bytes, x_scale, we_words, w
             nc.scalar.activation(out=res[:], in_=total[i][:], func=ACT.Identity, bias=mid_neg_max[:, i:i + 1], scale=1.0)
             nc.sync.dma_start(out=out[i * P:(i + 1) * P, :], in_=res[:])
 
+        negate_identity()
         repeat_scales()
         spread_bias(0)
         spread_bias(2)
         turn_scales()
         keep_bias(0, nc.vector.tensor_copy)
         keep_scales()
-        keep_bias(2, nc.vector.tensor_copy)
-        for unit in [(0, 0), (0, 2), (0, 1), (1, 0)]:
+        widen((0, 0))
+        turn_x((0, 0))
+        spread_gain(0)
+        spread_gain(1)
+        for unit in [(0, 2), (0, 1)]:
             widen(unit)
             turn_x(unit)
+        for unit in [(1, 0), (1, 2), (1, 1)]:
+            widen(unit)
         empty_vector((0, 0))
-        widen((1, 2))
-        widen((1, 1))
-        group_second()
-        empty_vector((0, 2))
-        spread_bias(1)
+        keep_bias(2, nc.vector.tensor_copy)
         score((0, 0))
+        for unit in [(2, 0), (2, 2), (2, 1)]:
+            widen(unit)
+        turn_x((1, 0))
+        empty_vector((0, 2))
         empty_vector((0, 1))
         score((0, 2))
         turn_x((1, 2))
-        keep_bias(1, nc.scalar.copy)
-        empty_vector((1, 0))
+        spread_bias(1)
+        add_bias((0, 0))
+        group_scalar(1)
         score((0, 1))
         group_trans(0)
         turn_x((1, 1))
+        empty_vector((1, 0))
+        turn_x((2, 0))
         empty_scalar((1, 2))
-        widen((2, 0))
-        add_bias((0, 0))
+        keep_bias(1, nc.scalar.copy)
         add_bias((0, 2))
         find_max((0, 0))
         exponent((0, 0))
-        score((1, 0))
-        group_trans(1)
-        spread_gain(0)
-        spread_gain(1)
-        turn_x((2, 0))
         find_max((0, 2))
         exponent((0, 2))
-
-        widen((2, 2))
-        add_bias((0, 1))
-        empty_vector((1, 1))
-        add_bias((1, 0))
-        quantize_trans(2)
+        score((1, 0))
+        quantize_trans(1)
+        quantize_trans(0)
         score((1, 2))
-        quantize_trans(3)
+        group_trans(2)
         turn_x((2, 2))
-        empty_scalar((2, 0))
-        widen((2, 1))
+        empty_scalar((1, 1))
+        turn_x((2, 1))
+        add_bias((0, 1))
         invert_sums(0)
-        find_max((1, 0))
+        add_bias((1, 0))
+        empty_scalar((2, 0))
         message(0, 0)
         message(0, 1)
         turn_v(0)
         score((1, 1))
-        turn_x((2, 1))
-        widen((3, 0))
-        exponent((1, 0))
-        empty_v(0)
+        group_trans(3)
+        empty_scalar((2, 1))
         add_bias((1, 2))
-        find_max((0, 1))
+        empty_v(0)
+        widen((3, 1))
+        turn_x((3, 1))
+        find_max((1, 0))
+        exponent((1, 0))
         find_max((1, 2))
-        exponent((0, 1))
         exponent((1, 2))
-        quantize_trans(0)
-        quantize_trans(1)
+        find_max((0, 1))
+        exponent((0, 1))
+        quantize_trans(2)
+        quantize_trans(3)
         pass_on(0)
+        quantize_x((2, 1))
+        widen((3, 0))
+        widen((3, 2))
+        add_bias((1, 1))
+        multiply_x((2, 1))
         empty_vector((2, 2))
+        find_max((1, 1))
+        exponent((1, 1))
 
         for k in range(2, LAST_TILE):
+            later = k + 2 < TILES
             score((k, 0))
-            score((k, 2))
+            quantize_x((k, 2))
             if k >= 3:
                 multiply_lifted(k - 3, x_room[k, 0])
-            widen((k + 1, 2))
+                widen((k + 1, 2))
             cut(k - 2, 0)
             cut(k - 2, 1)
             lift_both(k - 2)
-            if k == 2:
-                negate_identity()
-            empty_scalar((k, 1))
+            empty_scalar((k + 1, 1))
             invert_sums(k - 1)
-            add_bias((k - 1, 1))
+            add_bias((k, 1))
+            turn_x((k + 1, 0))
             message(k - 1, 0)
             message(k - 1, 1)
             turn_v(k - 1)
-            turn_x((k + 1, 0))
+            multiply_x((k, 2))
             turn_x((k + 1, 2))
-            find_max((k - 1, 1))
             add_bias((k, 0))
-            add_bias((k, 2))
+            find_max((k, 1))
             find_max((k, 0))
+            add_bias((k, 2))
             if k >= 4:
                 sum_terms(k - 4)
                 empty_v(k - 1)
-                widen((k + 1, 1))
+                if later:
+                    widen((k + 2, 1))
+                    exponent((k, 1))
+                else:
+                    empty_scalar((k + 1, 0))
             else:
-                widen((k + 1, 1))
+                widen((k + 2, 1))
                 empty_v(k - 1)
-            exponent((k - 1, 1))
+                exponent((k, 1))
+                empty_scalar((k + 1, 0), [1])
             exponent((k, 0))
 
             pass_on(k - 1)
-            score((k, 1))
+            score((k + 1, 1))
             if k >= 3:
                 make_terms(k - 3, v_room(k - 1))
-            turn_x((k + 1, 1))
+            if later:
+                turn_x((k + 2, 1))
             find_max((k, 2))
-            if k + 2 < TILES:
+            if later:
                 widen((k + 2, 0))
             exponent((k, 2))
-            empty_vector((k + 1, 0))
+            if k < 4:
+                empty_vector((k + 1, 0), [0])
+            elif later:
+                empty_vector((k + 1, 0))
             empty_vector((k + 1, 2))
 
-        last = LAST_TILE
-        score((last, 0))
-        score((last, 2))
-        multiply_lifted(last - 3, x_room[last, 0])
-        cut(last - 2, 0)
-        cut(last - 2, 1)
-        lift_both(last - 2)
-        empty_scalar((last, 1))
-        invert_sums(last - 1)
-        add_bias((last - 1, 1))
-        message(last - 1, 0)
-        message(last - 1, 1)
-        turn_v(last - 1)
+        add_bias((7, 1))
+        invert_sums(6)
+        cut(5, 0)
+        cut(5, 1)
+        score((7, 0))
+        score((7, 2))
+        multiply_lifted(4, x_room[7, 0])
+        lift_both(5)
+        exponent((6, 1))
+        message(6, 0)
+        message(6, 1)
+        turn_v(6)
         open_total(0)
-        add_bias((last, 0))
-        add_bias((last, 2))
-        find_max((last, 0))
-        find_max((last, 2))
-        sum_terms(last - 4)
-        empty_v(last - 1)
-        exponent((last, 0))
-        exponent((last, 2))
-        score((last, 1))
-        pass_on(last - 1)
-        multiply_lifted(last - 2, v_room(last - 1))
-        find_max((last - 1, 1))
-        exponent((last - 1, 1))
-        invert_sums(last)
-        invert_weights(0, last - 3)
-        add_bias((last, 1))
-        message(last, 0)
-        turn_v(last, [0])
-        find_max((last, 1))
-        message(last, 1)
-        turn_v(last, [1])
-        open_total(2)
-        cut(last - 1, 0)
-        cut(last - 1, 1)
-        exponent((last, 1))
-        weigh(last - 3)
-        empty_v(last, nc.vector.tensor_copy)
-        lift_second(last - 1)
-        pass_on(last)
-        multiply_cut(last - 1)
-        weigh(last - 2)
-        floor(last, 1)
-        invert_weights(last - 3, last - 1)
+        add_bias((7, 0))
+        add_bias((7, 2))
+        find_max((7, 0))
+        find_max((7, 2))
+        sum_terms(3)
+        empty_v(6)
+        exponent((7, 0))
+        exponent((7, 2))
+        pass_on(6)
+        make_terms(4, v_room(6))
+        multiply_lifted(5, fresh_room("prod5", T))
+        open_total(1)
+        find_max((7, 1))
+        exponent((7, 1))
+        invert_weights(0, 4)
+        invert_sums(7)
+        floor(6, 0)
+        message(7, 0)
+        turn_v(7, [0])
+        message(7, 1)
+        turn_v(7, [1])
+        open_total(3)
         take_log(0)
         close_total(0)
+        floor(6, 1)
         take_log(1)
-        cut(last, 0)
+        empty_v(7, nc.vector.tensor_copy)
+        multiply_floored(6)
+        pass_on(7)
+        close_total(1)
         take_log(2)
-        close_total(2)
-        finish(1)
-        multiply_cut(last)
-        weigh(last - 1)
         take_log(3)
+        close_total(3)
+        sum_terms(4)
+        weigh(5)
+        finish(2)
         finish_total(0)
+        cut(7, 0)
+        floor(7, 1)
+        invert_weights(4, 6)
+        weigh(6)
         take_log(4)
-        finish(3)
-        weigh(last)
-        invert_weights(last - 1, last)
-        take_log(5)
-        finish_total(2)
+        multiply_cut(7)
+        invert_weights(6, 7)
+        finish_total(1)
         finish(4)
-        invert_weights(last, TILES)
-        take_log(6)
+        take_log(5)
+        weigh(7)
+        finish_total(3)
         finish(5)
-        take_log(7)
+        invert_weights(7, 8)
+        take_log(6)
         finish(6)
+        take_log(7)
         finish(7)

@@ -25,6 +25,7 @@ PASSES = D // 512
 QUADS = 4
 PASS_WORDS = 256
 HALF = T // 2
+WARM_UPS = 4
 SCALE_ROWS, SCALE_SETS = 16, 3
 
 FLOOR_SHIFT = 14.4
@@ -60,6 +61,11 @@ def tile_chunkflooredmessagemiddlescore_kernel(tc, x_bytes, x_scale, we_words, w
         xs_wide = keep.tile([P, SCALE_SETS, P], F32, name="xs_wide")
         xs = keep.tile([P, L * TILES * PASSES], F32, name="xs")
         ident = keep.tile([P, P], F32, name="ident")
+        idle = keep.tile([P, T], BF16, name="idle")
+        nc.vector.memset(idle[:].bitcast(I32), 0)
+        warm_ps = psum.tile([P, T], F32, name="bank5", tag="bank5")
+        for w in range(WARM_UPS):
+            nc.tensor.matmul(warm_ps[:], lhsT=idle[:, 0:P], rhs=idle[:], start=True, stop=True)
         nc.vector.memset(rows[:].rearrange("p a n -> p (a n)").bitcast(I32), 0)
         nc.vector.memset(pick[:].rearrange("p c e -> p (c e)").bitcast(I32), 0)
         nc.vector.memset(we_s[:].rearrange("p g n -> p (g n)").bitcast(I32), 0)
@@ -70,12 +76,13 @@ def tile_chunkflooredmessagemiddlescore_kernel(tc, x_bytes, x_scale, we_words, w
             nc.vector.memset(pick[32 + 32 * p:33 + 32 * p, L + p, :], float(T))
         make_identity(nc, ident[:])
 
-        x_raw, trans_raw = {}, {}
+        x_raw, x_tile, trans_raw = {}, {}, {}
 
         def load_x(i, positions):
             named = list(range(L))[positions]
             raw = keep.tile([P, len(named), D], U8, name="xbytes%d_%d" % (i, named[0]))
             nc.sync.dma_start(out=raw[:], in_=x_bytes[positions, i * P:(i + 1) * P, :].rearrange("l r k -> r l k"))
+            x_tile[i] = raw[:].rearrange("p l k -> p (l k)")
             for j, l in enumerate(named):
                 x_raw[i, l] = raw[:, j, :]
 
@@ -89,17 +96,18 @@ def tile_chunkflooredmessagemiddlescore_kernel(tc, x_bytes, x_scale, we_words, w
             out=xs_rows[:].rearrange("r s q -> r (s q)"),
             in_=x_scale.rearrange("l i j -> (l i j)").rearrange("(r c) -> r c", r=SCALE_ROWS),
         )
+        load_x(0, rest)
         nc.sync.dma_start(out=rows[0:1, 0, :], in_=be.rearrange("(o n) -> o n", o=1))
         nc.sync.dma_start(out=rows[32:65:32, 0, :], in_=ends)
-        load_x(0, rest)
-        load_x(1, every)
-        nc.sync.dma_start(out=rows[32:65:32, 1, :], in_=gain)
+        load_x(1, first)
+        load_x(1, rest)
         nc.sync.dma_start(out=we_w[:].bitcast(I32), in_=we_words.rearrange("g p n -> p g n").bitcast(I32))
         for q in range(QUADS):
             nc.sync.dma_start(
                 out=we_s[32 * q:32 * q + 4, :, :].bitcast(I32),
                 in_=we_scales[:, 4 * q:4 * q + 4, :].rearrange("g r n -> r g n").bitcast(I32),
             )
+        nc.sync.dma_start(out=rows[32:65:32, 1, :], in_=gain)
         load_x(2, every)
         load_trans(0)
         load_trans(1)
@@ -180,8 +188,14 @@ def tile_chunkflooredmessagemiddlescore_kernel(tc, x_bytes, x_scale, we_words, w
         mid_neg_max = keep.tile([P, TILES], F32, name="mid_neg_max")
 
         def widen(unit, copy=nc.scalar.copy):
-            x_wide[unit] = work.tile([P, D], BF16, name="xw", tag="xw", bufs=7)
-            copy(out=x_wide[unit][:], in_=x_raw[unit].bitcast(FP8))
+            wide = work.tile([P, D], BF16, name="xw", tag="xw", bufs=6)
+            x_wide[unit] = wide[:]
+            copy(out=wide[:], in_=x_raw[unit].bitcast(FP8))
+
+        def widen_two(i):
+            wide = work.tile([P, 2 * D], BF16, name="xw2", tag="xw2", bufs=2)
+            x_wide[i, 0], x_wide[i, 1] = wide[:, 0:D], wide[:, D:2 * D]
+            nc.scalar.copy(out=wide[:], in_=x_tile[i][:, 0:2 * D].bitcast(FP8))
 
         def turn(bank, values, halves):
             words = values.bitcast(F32)
@@ -191,7 +205,7 @@ def tile_chunkflooredmessagemiddlescore_kernel(tc, x_bytes, x_scale, we_words, w
 
         def turn_x(unit):
             x_turned[unit] = next_bank(("turned", unit[1]), [P, PASSES, 2, P])
-            turn(x_turned[unit], x_wide[unit][:], range(PASSES))
+            turn(x_turned[unit], x_wide[unit], range(PASSES))
 
         def make_room(unit):
             i, l = unit
@@ -415,29 +429,28 @@ def tile_chunkflooredmessagemiddlescore_kernel(tc, x_bytes, x_scale, we_words, w
 
         negate_identity()
         repeat_scales()
-        spread_bias(0)
-        spread_bias(2)
         turn_scales()
-        keep_bias(0, nc.vector.tensor_copy)
-        keep_scales()
         widen((0, 0))
         turn_x((0, 0))
-        spread_gain(0)
-        spread_gain(1)
-        for unit in [(0, 2), (0, 1)]:
-            widen(unit)
-            turn_x(unit)
+        widen((0, 2), nc.vector.tensor_copy)
+        turn_x((0, 2))
+        keep_scales()
+        widen((0, 1), nc.vector.tensor_copy)
+        spread_bias(0)
+        spread_bias(2)
+        turn_x((0, 1))
         for unit in [(1, 0), (1, 2), (1, 1)]:
             widen(unit)
+        keep_bias(0, nc.scalar.copy)
+        keep_bias(2, nc.scalar.copy)
         empty_vector((0, 0))
-        keep_bias(2, nc.vector.tensor_copy)
+        empty_vector((0, 2))
         score((0, 0))
+        score((0, 2))
         for unit in [(2, 0), (2, 2), (2, 1)]:
             widen(unit)
         turn_x((1, 0))
-        empty_vector((0, 2))
         empty_vector((0, 1))
-        score((0, 2))
         turn_x((1, 2))
         spread_bias(1)
         add_bias((0, 0))
@@ -445,11 +458,13 @@ def tile_chunkflooredmessagemiddlescore_kernel(tc, x_bytes, x_scale, we_words, w
         score((0, 1))
         group_trans(0)
         turn_x((1, 1))
+        spread_gain(0)
+        spread_gain(1)
+        add_bias((0, 2))
         empty_vector((1, 0))
         turn_x((2, 0))
-        empty_scalar((1, 2))
+        empty_vector((1, 2))
         keep_bias(1, nc.scalar.copy)
-        add_bias((0, 2))
         find_max((0, 0))
         exponent((0, 0))
         find_max((0, 2))
@@ -466,6 +481,7 @@ def tile_chunkflooredmessagemiddlescore_kernel(tc, x_bytes, x_scale, we_words, w
         invert_sums(0)
         add_bias((1, 0))
         empty_scalar((2, 0))
+        empty_scalar((2, 2), [1])
         message(0, 0)
         message(0, 1)
         turn_v(0)
@@ -490,7 +506,7 @@ def tile_chunkflooredmessagemiddlescore_kernel(tc, x_bytes, x_scale, we_words, w
         widen((3, 2))
         add_bias((1, 1))
         multiply_x((2, 1))
-        empty_vector((2, 2))
+        empty_vector((2, 2), [0])
         find_max((1, 1))
         exponent((1, 1))
 
@@ -521,26 +537,28 @@ def tile_chunkflooredmessagemiddlescore_kernel(tc, x_bytes, x_scale, we_words, w
                 sum_terms(k - 4)
                 empty_v(k - 1)
                 if later:
-                    widen((k + 2, 1))
+                    widen_two(k + 2)
                     exponent((k, 1))
                 else:
                     empty_scalar((k + 1, 0))
             else:
-                widen((k + 2, 1))
                 empty_v(k - 1)
-                exponent((k, 1))
                 empty_scalar((k + 1, 0), [1])
+                widen_two(k + 2)
+                exponent((k, 1))
             exponent((k, 0))
 
-            pass_on(k - 1)
-            score((k + 1, 1))
+            if later:
+                pass_on(k - 1)
+                score((k + 1, 1))
+            else:
+                score((k + 1, 1))
+                pass_on(k - 1)
             if k >= 3:
                 make_terms(k - 3, v_room(k - 1))
             if later:
                 turn_x((k + 2, 1))
             find_max((k, 2))
-            if later:
-                widen((k + 2, 0))
             exponent((k, 2))
             if k < 4:
                 empty_vector((k + 1, 0), [0])

@@ -34,12 +34,12 @@ FLOOR_VALUE = 1.6
 TRANS_HOSTS = {(0, 1): 0, (1, 2): 2, (1, 1): 3}
 
 BANK_OF = {
-    ("e", 0): "bank0", ("bias", 0): "bank0",
+    ("e", 0): "bank0",
     ("turned", 0): "bank1", ("total", 1): "bank1",
-    "v": "bank2", ("m", 0): "bank2", "scales": "bank2", ("bias", 1): "bank2",
-    ("e", 2): "bank3", ("m", 1): "bank3", ("bias", 2): "bank3",
+    "v": "bank2", ("m", 0): "bank2", "scales": "bank2", ("bias", 1): "bank2", ("bias", 2): "bank2",
+    ("e", 2): "bank3", ("m", 1): "bank3",
     ("turned", 2): "bank4", ("total", 3): "bank4",
-    ("e", 1): "bank5",
+    ("e", 1): "bank5", ("bias", 0): "bank5",
     ("turned", 1): "bank6", ("total", 0): "bank6",
 }
 
@@ -67,8 +67,8 @@ def tile_chunkflooredmessagemiddlescore_kernel(tc, x_bytes, x_scale, we_words, w
         for w in range(WARM_UPS):
             nc.tensor.matmul(warm_ps[:], lhsT=idle[:, 0:P], rhs=idle[:], start=True, stop=True)
         nc.vector.memset(rows[:].rearrange("p a n -> p (a n)").bitcast(I32), 0)
-        nc.vector.memset(pick[:].rearrange("p c e -> p (c e)").bitcast(I32), 0)
         nc.vector.memset(we_s[:].rearrange("p g n -> p (g n)").bitcast(I32), 0)
+        nc.vector.memset(pick[:].rearrange("p c e -> p (c e)").bitcast(I32), 0)
         nc.vector.memset(xs_wide[:].rearrange("p s m -> p (s m)"), 0.0)
         nc.vector.memset(pick[0:1, 0:L, :].rearrange("p c e -> p (c e)"), -1.0)
         for p in range(PAIRS):
@@ -76,13 +76,12 @@ def tile_chunkflooredmessagemiddlescore_kernel(tc, x_bytes, x_scale, we_words, w
             nc.vector.memset(pick[32 + 32 * p:33 + 32 * p, L + p, :], float(T))
         make_identity(nc, ident[:])
 
-        x_raw, x_tile, trans_raw = {}, {}, {}
+        x_raw, trans_raw = {}, {}
 
         def load_x(i, positions):
             named = list(range(L))[positions]
             raw = keep.tile([P, len(named), D], U8, name="xbytes%d_%d" % (i, named[0]))
             nc.sync.dma_start(out=raw[:], in_=x_bytes[positions, i * P:(i + 1) * P, :].rearrange("l r k -> r l k"))
-            x_tile[i] = raw[:].rearrange("p l k -> p (l k)")
             for j, l in enumerate(named):
                 x_raw[i, l] = raw[:, j, :]
 
@@ -99,14 +98,13 @@ def tile_chunkflooredmessagemiddlescore_kernel(tc, x_bytes, x_scale, we_words, w
         load_x(0, rest)
         nc.sync.dma_start(out=rows[0:1, 0, :], in_=be.rearrange("(o n) -> o n", o=1))
         nc.sync.dma_start(out=rows[32:65:32, 0, :], in_=ends)
-        load_x(1, first)
-        load_x(1, rest)
-        nc.sync.dma_start(out=we_w[:].bitcast(I32), in_=we_words.rearrange("g p n -> p g n").bitcast(I32))
         for q in range(QUADS):
             nc.sync.dma_start(
                 out=we_s[32 * q:32 * q + 4, :, :].bitcast(I32),
                 in_=we_scales[:, 4 * q:4 * q + 4, :].rearrange("g r n -> r g n").bitcast(I32),
             )
+        load_x(1, every)
+        nc.sync.dma_start(out=we_w[:].bitcast(I32), in_=we_words.rearrange("g p n -> p g n").bitcast(I32))
         nc.sync.dma_start(out=rows[32:65:32, 1, :], in_=gain)
         load_x(2, every)
         load_trans(0)
@@ -188,14 +186,8 @@ def tile_chunkflooredmessagemiddlescore_kernel(tc, x_bytes, x_scale, we_words, w
         mid_neg_max = keep.tile([P, TILES], F32, name="mid_neg_max")
 
         def widen(unit, copy=nc.scalar.copy):
-            wide = work.tile([P, D], BF16, name="xw", tag="xw", bufs=6)
-            x_wide[unit] = wide[:]
-            copy(out=wide[:], in_=x_raw[unit].bitcast(FP8))
-
-        def widen_two(i):
-            wide = work.tile([P, 2 * D], BF16, name="xw2", tag="xw2", bufs=2)
-            x_wide[i, 0], x_wide[i, 1] = wide[:, 0:D], wide[:, D:2 * D]
-            nc.scalar.copy(out=wide[:], in_=x_tile[i][:, 0:2 * D].bitcast(FP8))
+            x_wide[unit] = work.tile([P, D], BF16, name="xw", tag="xw", bufs=7)
+            copy(out=x_wide[unit][:], in_=x_raw[unit].bitcast(FP8))
 
         def turn(bank, values, halves):
             words = values.bitcast(F32)
@@ -205,7 +197,7 @@ def tile_chunkflooredmessagemiddlescore_kernel(tc, x_bytes, x_scale, we_words, w
 
         def turn_x(unit):
             x_turned[unit] = next_bank(("turned", unit[1]), [P, PASSES, 2, P])
-            turn(x_turned[unit], x_wide[unit], range(PASSES))
+            turn(x_turned[unit], x_wide[unit][:], range(PASSES))
 
         def make_room(unit):
             i, l = unit
@@ -430,27 +422,26 @@ def tile_chunkflooredmessagemiddlescore_kernel(tc, x_bytes, x_scale, we_words, w
         negate_identity()
         repeat_scales()
         turn_scales()
+        keep_scales()
         widen((0, 0))
         turn_x((0, 0))
-        widen((0, 2), nc.vector.tensor_copy)
-        turn_x((0, 2))
-        keep_scales()
-        widen((0, 1), nc.vector.tensor_copy)
         spread_bias(0)
         spread_bias(2)
-        turn_x((0, 1))
+        for unit in [(0, 2), (0, 1)]:
+            widen(unit)
+            turn_x(unit)
+        keep_bias(2, nc.scalar.copy)
         for unit in [(1, 0), (1, 2), (1, 1)]:
             widen(unit)
-        keep_bias(0, nc.scalar.copy)
-        keep_bias(2, nc.scalar.copy)
         empty_vector((0, 0))
-        empty_vector((0, 2))
+        keep_bias(0, nc.vector.tensor_copy)
         score((0, 0))
+        empty_vector((0, 2))
+        empty_vector((0, 1))
         score((0, 2))
         for unit in [(2, 0), (2, 2), (2, 1)]:
             widen(unit)
         turn_x((1, 0))
-        empty_vector((0, 1))
         turn_x((1, 2))
         spread_bias(1)
         add_bias((0, 0))
@@ -460,12 +451,12 @@ def tile_chunkflooredmessagemiddlescore_kernel(tc, x_bytes, x_scale, we_words, w
         turn_x((1, 1))
         spread_gain(0)
         spread_gain(1)
+        find_max((0, 0))
         add_bias((0, 2))
         empty_vector((1, 0))
         turn_x((2, 0))
         empty_vector((1, 2))
         keep_bias(1, nc.scalar.copy)
-        find_max((0, 0))
         exponent((0, 0))
         find_max((0, 2))
         exponent((0, 2))
@@ -537,15 +528,15 @@ def tile_chunkflooredmessagemiddlescore_kernel(tc, x_bytes, x_scale, we_words, w
                 sum_terms(k - 4)
                 empty_v(k - 1)
                 if later:
-                    widen_two(k + 2)
+                    widen((k + 2, 1))
                     exponent((k, 1))
                 else:
                     empty_scalar((k + 1, 0))
             else:
+                widen((k + 2, 1))
                 empty_v(k - 1)
-                empty_scalar((k + 1, 0), [1])
-                widen_two(k + 2)
                 exponent((k, 1))
+                empty_scalar((k + 1, 0), [1])
             exponent((k, 0))
 
             if later:
@@ -559,6 +550,8 @@ def tile_chunkflooredmessagemiddlescore_kernel(tc, x_bytes, x_scale, we_words, w
             if later:
                 turn_x((k + 2, 1))
             find_max((k, 2))
+            if later:
+                widen((k + 2, 0))
             exponent((k, 2))
             if k < 4:
                 empty_vector((k + 1, 0), [0])

@@ -25,7 +25,6 @@ PASSES = D // 512
 QUADS = 4
 PASS_WORDS = 256
 HALF = T // 2
-WARM_UPS = 4
 SCALE_ROWS, SCALE_SETS = 16, 3
 
 FLOOR_SHIFT = 14.4
@@ -61,11 +60,6 @@ def tile_chunkflooredmessagemiddlescore_kernel(tc, x_bytes, x_scale, we_words, w
         xs_wide = keep.tile([P, SCALE_SETS, P], F32, name="xs_wide")
         xs = keep.tile([P, L * TILES * PASSES], F32, name="xs")
         ident = keep.tile([P, P], F32, name="ident")
-        idle = keep.tile([P, T], BF16, name="idle")
-        nc.vector.memset(idle[:].bitcast(I32), 0)
-        warm_ps = psum.tile([P, T], F32, name="bank5", tag="bank5")
-        for w in range(WARM_UPS):
-            nc.tensor.matmul(warm_ps[:], lhsT=idle[:, 0:P], rhs=idle[:], start=True, stop=True)
         nc.vector.memset(rows[:].rearrange("p a n -> p (a n)").bitcast(I32), 0)
         nc.vector.memset(we_s[:].rearrange("p g n -> p (g n)").bitcast(I32), 0)
         nc.vector.memset(pick[:].rearrange("p c e -> p (c e)").bitcast(I32), 0)

from contextlib import ExitStack

import concourse.mybir as mybir
from concourse.masks import make_identity

L, PAIRS, B, D, T = 3, 2, 1024, 1024, 512
FLOPS = 2 * L * B * D * T + 2 * PAIRS * B * T * T

F32 = mybir.dt.float32
BF16 = mybir.dt.bfloat16
I32 = mybir.dt.int32
U32 = mybir.dt.uint32
U8 = mybir.dt.uint8
FP8 = mybir.dt.float8_e4m3fn
FP8X4 = mybir.dt.float8_e4m3fn_x4
FP4X4 = mybir.dt.float4_e2m1fn_x4
ACT = mybir.ActivationFunctionType
ALU = mybir.AluOpType
AX = mybir.AxisListType

P = 128
TILES = B // P
LAST_TILE = TILES - 1
PASSES = D // 512
QUADS = 4
PASS_WORDS = 256
HALF = T // 2
SCALE_ROWS, SCALE_SETS = 16, 3

FLOOR_SHIFT = 14.4
FLOOR_VALUE = 1.6

TRANS_HOSTS = {(0, 1): 0, (1, 2): 2, (1, 1): 3}

BANK_OF = {
    ("e", 0): "bank0",
    ("turned", 0): "bank1", ("total", 1): "bank1",
    "v": "bank2", ("m", 0): "bank2", "scales": "bank2", ("bias", 1): "bank2", ("bias", 2): "bank2",
    ("e", 2): "bank3", ("m", 1): "bank3",
    ("turned", 2): "bank4", ("total", 3): "bank4",
    ("e", 1): "bank5", ("bias", 0): "bank5",
    ("turned", 1): "bank6", ("total", 0): "bank6",
}


def tile_chunkflooredmessagemiddlescore_kernel(tc, x_bytes, x_scale, we_words, we_scales, be, ends, gain, trans, out):
    nc = tc.nc

    with ExitStack() as ctx:
        keep = ctx.enter_context(tc.tile_pool(name="keep", bufs=1))
        work = ctx.enter_context(tc.tile_pool(name="work", bufs=4))
        psum = ctx.enter_context(tc.psum_pool(name="psum", bufs=1))
        ctx.enter_context(tc.manual_schedule())

        rows = keep.tile([P, 2, T], BF16, name="rows")
        pick = keep.tile([P, L + PAIRS, 2], BF16, name="pick")
        we_s = keep.tile([P, PASSES, T], U8, name="we_s", align_bytes=64)
        we_w = keep.tile([P, PASSES, 2 * T], U8, name="we_w", align_bytes=64)
        xs_rows = keep.tile([SCALE_ROWS, SCALE_SETS, QUADS], F32, name="xs_rows")
        xs_wide = keep.tile([P, SCALE_SETS, P], F32, name="xs_wide")
        xs = keep.tile([P, L * TILES * PASSES], F32, name="xs")
        ident = keep.tile([P, P], F32, name="ident")
        nc.vector.memset(rows[:].rearrange("p a n -> p (a n)").bitcast(I32), 0)
        nc.vector.memset(we_s[:].rearrange("p g n -> p (g n)").bitcast(I32), 0)
        nc.vector.memset(pick[:].rearrange("p c e -> p (c e)").bitcast(I32), 0)
        nc.vector.memset(xs_wide[:].rearrange("p s m -> p (s m)"), 0.0)
        nc.vector.memset(pick[0:1, 0:L, :].rearrange("p c e -> p (c e)"), -1.0)
        for p in range(PAIRS):
            nc.vector.memset(pick[32 + 32 * p:33 + 32 * p, 2 * p, :], -1.0)
            nc.vector.memset(pick[32 + 32 * p:33 + 32 * p, L + p, :], float(T))
        make_identity(nc, ident[:])

        x_raw, trans_raw = {}, {}

        def load_x(i, positions):
            named = list(range(L))[positions]
            raw = keep.tile([P, len(named), D], U8, name="xbytes%d_%d" % (i, named[0]))
            nc.sync.dma_start(out=raw[:], in_=x_bytes[positions, i * P:(i + 1) * P, :].rearrange("l r k -> r l k"))
            for j, l in enumerate(named):
                x_raw[i, l] = raw[:, j, :]

        def load_trans(p):
            trans_raw[p] = keep.tile([P, 4, T], BF16, name="tr_raw%d" % p)
            nc.sync.dma_start(out=trans_raw[p][:], in_=trans[p].rearrange("(p j) n -> p j n", j=4))

        first, rest, every = slice(0, 1), slice(1, 3), slice(0, 3)
        load_x(0, first)
        nc.sync.dma_start(
            out=xs_rows[:].rearrange("r s q -> r (s q)"),
            in_=x_scale.rearrange("l i j -> (l i j)").rearrange("(r c) -> r c", r=SCALE_ROWS),
        )
        load_x(0, rest)
        nc.sync.dma_start(out=rows[0:1, 0, :], in_=be.rearrange("(o n) -> o n", o=1))
        nc.sync.dma_start(out=rows[32:65:32, 0, :], in_=ends)
        for q in range(QUADS):
            nc.sync.dma_start(
                out=we_s[32 * q:32 * q + 4, :, :].bitcast(I32),
                in_=we_scales[:, 4 * q:4 * q + 4, :].rearrange("g r n -> r g n").bitcast(I32),
            )
        load_x(1, every)
        nc.sync.dma_start(out=we_w[:].bitcast(I32), in_=we_words.rearrange("g p n -> p g n").bitcast(I32))
        nc.sync.dma_start(out=rows[32:65:32, 1, :], in_=gain)
        load_x(2, every)
        load_trans(0)
        load_trans(1)
        for i in range(3, TILES):
            load_x(i, every)

        def next_bank(role, shape):
            tag = BANK_OF[role]
            return psum.tile(shape, F32, name=tag, tag=tag)

        scales_ps = next_bank("scales", [P, SCALE_SETS, P])

        def repeat_scales():
            nc.vector.tensor_copy(
                out=xs_wide[0:SCALE_ROWS].rearrange("r s (q m) -> r (s q) m", q=QUADS),
                in_=xs_rows[:].rearrange("r s q -> r (s q)").unsqueeze(2).to_broadcast([SCALE_ROWS, SCALE_SETS * QUADS, 32]),
            )

        def turn_scales():
            for s in range(SCALE_SETS):
                nc.tensor.transpose(scales_ps[:, s, :], xs_wide[:, s, :], ident[:])

        def keep_scales():
            nc.vector.tensor_copy(
                out=xs[:].rearrange("p (r s) -> p r s", s=SCALE_SETS), in_=scales_ps[:, :, 0:SCALE_ROWS].rearrange("p s r -> p r s"),
            )

        neg_bias, bias_ps = {}, {}

        def spread_bias(l):
            bias_ps[l] = next_bank(("bias", l), [P, T])
            nc.tensor.matmul(bias_ps[l][:], lhsT=pick[:, l, 0:1].to_broadcast([P, P]), rhs=rows[:, 0, :], start=True, stop=True)

        def keep_bias(l, copy):
            neg_bias[l] = keep.tile([P, T], F32, name="neg_bias%d" % l)
            copy(out=neg_bias[l][:], in_=bias_ps[l][:])

        gain_ps = psum.tile([P, PAIRS, T], BF16, name="gain_ps", tag="gain_ps")

        def spread_gain(p):
            nc.tensor.matmul(gain_ps[:, p, :], lhsT=pick[:, L + p, 0:1].to_broadcast([P, P]), rhs=rows[:, 1, :], start=True, stop=True)

        trans_room = keep.tile([P, 2 * PAIRS, PASSES, P, 4], BF16, name="tr_grouped", align_bytes=64)
        trans_grouped = trans_room[:].rearrange("p (a h) g r t -> p a (h g r) t", a=PAIRS)
        trans_codes = keep.tile([P, PAIRS, T], U32, name="tr_codes", align_bytes=64)
        trans_scales = keep.tile([P, PAIRS, T], U8, name="tr_scales", align_bytes=64)

        def group_trans(quarter):
            p, h = divmod(quarter, 2)
            cols = slice(h * HALF, (h + 1) * HALF)
            nc.gpsimd.tensor_scalar(
                out=trans_grouped[:, p, cols, :], in0=trans_raw[p][:, :, cols].rearrange("p t n -> p n t"),
                scalar1=1.0, scalar2=0.0, op0=ALU.mult, op1=ALU.add,
            )

        def group_scalar(quarter):
            p, h = divmod(quarter, 2)
            cols = slice(h * HALF, (h + 1) * HALF)
            nc.scalar.copy(
                out=trans_grouped[:, p, cols, :].rearrange("p (c i) t -> p c t i", i=4),
                in_=trans_raw[p][:, :, cols].rearrange("p t (c i) -> p c t i", i=4),
            )

        def quantize_trans(quarter):
            p, h = divmod(quarter, 2)
            cols = slice(h * HALF, (h + 1) * HALF)
            nc.vector.quantize_mx(
                out=trans_codes[:, p, cols].bitcast(FP8X4), scales=trans_scales[:, p, cols],
                in_=trans_grouped[:, p, cols, :].rearrange("p n t -> p (n t)"),
            )

        x_wide, x_turned, x_grouped, x_room, x_codes, e_ps = {}, {}, {}, {}, {}, {}
        neg_n, neg_max, expo = {}, {}, {}
        sums = [keep.tile([P, PAIRS], F32, name="sums%d" % i) for i in range(TILES)]
        inverse = [keep.tile([P, PAIRS], F32, name="inv%d" % i) for i in range(TILES)]
        weight = keep.tile([P, TILES], F32, name="weight")
        inv_weight = keep.tile([P, TILES], F32, name="inv_weight")
        mid_neg_max = keep.tile([P, TILES], F32, name="mid_neg_max")

        def widen(unit, copy=nc.scalar.copy):
            x_wide[unit] = work.tile([P, D], BF16, name="xw", tag="xw", bufs=7)
            copy(out=x_wide[unit][:], in_=x_raw[unit].bitcast(FP8))

        def turn(bank, values, halves):
            words = values.bitcast(F32)
            for g in halves:
                for u in range(2):
                    nc.tensor.transpose(bank[:, g, u, :], words[:, PASS_WORDS * g + u:PASS_WORDS * (g + 1):2], ident[:])

        def turn_x(unit):
            x_turned[unit] = next_bank(("turned", unit[1]), [P, PASSES, 2, P])
            turn(x_turned[unit], x_wide[unit][:], range(PASSES))

        def make_room(unit):
            i, l = unit
            if unit in TRANS_HOSTS:
                x_grouped[unit] = trans_room[:, TRANS_HOSTS[unit]]
                return
            if l == 0 and i >= 3:
                room = keep.tile([P, PASSES, P, 4], BF16, name="xg%d_%d" % unit, align_bytes=64)
            else:
                room = work.tile([P, PASSES, P, 4], BF16, name="xg", tag="xg", bufs=5, align_bytes=64)
            x_grouped[unit] = room[:]
            x_room[unit] = room[:].rearrange("p g r t -> p (g r t)").bitcast(F32)

        def scaled_part(unit, g):
            i, l = unit
            if unit not in x_grouped:
                make_room(unit)
            src = x_turned[unit][:, g].rearrange("p u r -> p (u r)").bitcast(BF16).rearrange("p (u r e) -> p r u e", u=2, e=2)
            dst = x_grouped[unit][:, g].rearrange("p r (u e) -> p r u e", u=2)
            column = (l * TILES + i) * PASSES + g
            return src, dst, xs[:, column:column + 1]

        def empty_vector(unit, passes=range(PASSES)):
            for g in passes:
                src, dst, scale = scaled_part(unit, g)
                nc.vector.tensor_scalar(out=dst, in0=src, scalar1=scale, scalar2=None, op0=ALU.mult)

        def empty_scalar(unit, passes=range(PASSES)):
            for g in passes:
                src, dst, scale = scaled_part(unit, g)
                nc.scalar.activation(out=dst, in_=src, func=ACT.Copy, scale=scale)

        def quantize_x(unit):
            codes = work.tile([P, PASSES * P], U32, name="xq", tag="xq", align_bytes=64)
            scales = work.tile([P, PASSES * P], U8, name="xqs", tag="xqs", align_bytes=64)
            x_codes[unit] = codes, scales
            nc.vector.quantize_mx(
                out=codes[:].bitcast(FP8X4), scales=scales[:], in_=x_grouped[unit].rearrange("p g r t -> p (g r t)"),
            )

        def multiply_x(unit):
            codes, scales = x_codes[unit]
            e_ps[unit] = next_bank(("e", unit[1]), [P, T])
            for g in range(PASSES):
                cols = slice(g * P, (g + 1) * P)
                nc.tensor.matmul_mx(
                    out=e_ps[unit][:], lhsT=codes[:, cols].bitcast(FP8X4), lhsT_scale=scales[:, cols],
                    rhs=we_w[:, g, :].bitcast(FP4X4), rhs_scale=we_s[:, g, :], start=(g == 0), stop=(g == PASSES - 1),
                )

        def score(unit):
            quantize_x(unit)
            multiply_x(unit)

        def add_bias(unit):
            i, l = unit
            if l == 1:
                neg_n[unit] = keep.tile([P, T], F32, name="neg_mid%d" % i)
            else:
                neg_n[unit] = work.tile([P, T], F32, name="neg_end", tag="neg_end")
            nc.vector.tensor_tensor(out=neg_n[unit][:], in0=neg_bias[l][:], in1=e_ps[unit][:], op=ALU.subtract)

        def find_max(unit):
            i, l = unit
            if l == 1:
                neg_max[unit] = mid_neg_max[:, i:i + 1]
            else:
                column = keep.tile([P, 1], F32, name="neg_max%d_%d" % unit)
                neg_max[unit] = column[:]
            nc.vector.tensor_reduce(out=neg_max[unit], in_=neg_n[unit][:], axis=AX.X, op=ALU.min)

        def exponent(unit):
            i, l = unit
            if l == 1:
                expo[unit] = work.tile([P, T], F32, name="ex_mid", tag="ex_mid", bufs=5)
                nc.scalar.activation(out=expo[unit][:], in_=neg_n[unit][:], func=ACT.Exp, bias=neg_max[unit], scale=-1.0)
            else:
                expo[unit] = work.tile([P, T], F32, name="ex_end", tag="ex_end")
                nc.scalar.activation(
                    out=expo[unit][:], in_=neg_n[unit][:], func=ACT.Exp, bias=neg_max[unit], scale=-1.0,
                    accum_out=sums[i][:, l // 2:l // 2 + 1],
                )

        v, v_turned, v_grouped, v_codes, m_ps = {}, {}, {}, {}, {}
        cuts, lifted, floored, product, terms, log_a, total = {}, {}, {}, {}, {}, {}, {}

        def invert_sums(i, pairs=slice(0, PAIRS)):
            nc.vector.reciprocal(out=inverse[i][:, pairs], in_=sums[i][:, pairs])

        def message(i, p):
            if p == 0:
                v[i] = work.tile([P, PAIRS, T], BF16, name="v", tag="v", bufs=2)
            nc.vector.scalar_tensor_tensor(
                out=v[i][:, p, :], in0=expo[i, 2 * p][:], scalar=inverse[i][:, p:p + 1],
                in1=gain_ps[:, p, :], op0=ALU.mult, op1=ALU.mult,
            )

        def turn_v(i, pairs=range(PAIRS)):
            if i not in v_turned:
                v_turned[i] = next_bank("v", [P, PAIRS, 2, P])
            turn(v_turned[i], v[i][:].rearrange("p a n -> p (a n)"), pairs)

        def empty_v(i, copy=nc.scalar.copy):
            v_grouped[i] = work.tile([P, PAIRS, P, 2], F32, name="vg", tag="vg", bufs=3, align_bytes=64)
            copy(out=v_grouped[i][:], in_=v_turned[i][:].rearrange("p g u r -> p g r u"))

        def v_room(i):
            return v_grouped[i][:].rearrange("p g r u -> p (g r u)")

        def quantize_v(i):
            codes = work.tile([P, PAIRS * P], U32, name="vq", tag="vq", bufs=2, align_bytes=64)
            scales = work.tile([P, PAIRS * P], U8, name="vqs", tag="vqs", bufs=2, align_bytes=64)
            v_codes[i] = codes, scales
            nc.vector.quantize_mx(
                out=codes[:].bitcast(FP8X4), scales=scales[:],
                in_=v_grouped[i][:].rearrange("p g r u -> p (g r u)").bitcast(BF16),
            )

        def multiply_v(i):
            codes, scales = v_codes[i]
            for p in range(PAIRS):
                cols = slice(p * P, (p + 1) * P)
                m_ps[i, p] = next_bank(("m", p), [P, T])
                nc.tensor.matmul_mx(
                    out=m_ps[i, p][:], lhsT=codes[:, cols].bitcast(FP8X4), lhsT_scale=scales[:, cols],
                    rhs=trans_codes[:, p, :].bitcast(FP8X4), rhs_scale=trans_scales[:, p, :], start=True, stop=True,
                )

        def pass_on(i):
            quantize_v(i)
            multiply_v(i)

        def cut(i, p):
            if i not in cuts:
                cuts[i] = work.tile([P, PAIRS, T], F32, name="cuts", tag="cuts", bufs=3)
            nc.scalar.activation(out=cuts[i][:, p, :], in_=m_ps[i, p][:], func=ACT.Relu, bias=FLOOR_SHIFT, scale=1.0)

        def fresh_room(name, width):
            room = keep.tile([P, width], F32, name=name)
            return room[:]

        def lift_both(i):
            lifted[i] = cuts[i][:].rearrange("p a n -> p (a n)")
            nc.gpsimd.tensor_scalar(
                out=lifted[i], in0=lifted[i], scalar1=1.0, scalar2=FLOOR_VALUE, op0=ALU.mult, op1=ALU.add,
            )

        def multiply_lifted(i, room):
            product[i] = room
            nc.gpsimd.tensor_tensor(out=product[i], in0=lifted[i][:, 0:T], in1=lifted[i][:, T:2 * T], op=ALU.mult)

        def make_terms(i, room):
            terms[i] = room
            nc.gpsimd.tensor_tensor(out=terms[i], in0=expo[i, 1][:], in1=product[i], op=ALU.mult)

        def sum_terms(i):
            nc.scalar.activation(out=terms[i], in_=terms[i], func=ACT.Identity, scale=1.0 / T, accum_out=weight[:, i:i + 1])

        def floor(i, p):
            floored[i, p] = work.tile([P, T], F32, name="floored", tag="floored", bufs=3)
            nc.vector.tensor_scalar(
                out=floored[i, p][:], in0=m_ps[i, p][:], scalar1=-FLOOR_SHIFT, scalar2=16.0, op0=ALU.max, op1=ALU.add,
            )

        def lift_second(i):
            floored[i, 1] = work.tile([P, T], F32, name="floored", tag="floored", bufs=3)
            nc.vector.tensor_scalar(out=floored[i, 1][:], in0=cuts[i][:, 1, :], scalar1=FLOOR_VALUE, scalar2=None, op0=ALU.add)

        def multiply_floored(i):
            product[i] = fresh_room("prod%d" % i, T)
            nc.vector.tensor_tensor(out=product[i], in0=floored[i, 0][:], in1=floored[i, 1][:], op=ALU.mult)

        def multiply_cut(i):
            product[i] = fresh_room("prod%d" % i, T)
            nc.vector.scalar_tensor_tensor(
                out=product[i], in0=cuts[i][:, 0, :], scalar=FLOOR_VALUE, in1=floored[i, 1][:], op0=ALU.add, op1=ALU.mult,
            )

        def weigh(i):
            spent = work.tile([P, T], F32, name="weighted", tag="weighted", bufs=2)
            nc.vector.scalar_tensor_tensor(
                out=spent[:], in0=expo[i, 1][:], scalar=1.0 / T, in1=product[i], op0=ALU.mult, op1=ALU.mult,
                accum_out=weight[:, i:i + 1],
            )

        def invert_weights(begin, end):
            nc.vector.reciprocal(out=inv_weight[:, begin:end], in_=weight[:, begin:end])

        def pieces(i):
            return [slice(0, HALF), slice(HALF, T)] if i == LAST_TILE else [slice(0, T)]

        def take_log(i):
            for h, cols in enumerate(pieces(i)):
                log_a[i, h] = work.tile([P, cols.stop - cols.start], F32, name="logp", tag="logp", bufs=5)
                nc.scalar.activation(out=log_a[i, h][:], in_=product[i][:, cols], func=ACT.Ln, scale=inv_weight[:, i:i + 1])

        def finish(i):
            for h, cols in enumerate(pieces(i)):
                res = work.tile([P, cols.stop - cols.start], F32, name="res", tag="res", bufs=TILES + 1)
                nc.vector.scalar_tensor_tensor(
                    out=res[:], in0=log_a[i, h][:], scalar=mid_neg_max[:, i:i + 1], in1=neg_n[i, 1][:, cols], op0=ALU.add, op1=ALU.subtract,
                )
                nc.sync.dma_start(out=out[i * P:(i + 1) * P, cols], in_=res[:])

        neg_ident = keep.tile([P, P], F32, name="neg_ident")

        def negate_identity():
            nc.scalar.activation(out=neg_ident[:], in_=ident[:], func=ACT.Copy, scale=-1.0)

        def open_total(i):
            total[i] = next_bank(("total", i), [P, T])
            nc.tensor.matmul(total[i][:], lhsT=neg_ident[:], rhs=neg_n[i, 1][:], start=True, stop=False)

        def close_total(i):
            nc.tensor.matmul(total[i][:], lhsT=ident[:], rhs=log_a[i, 0][:], start=False, stop=True)

        def finish_total(i):
            res = work.tile([P, T], F32, name="res", tag="res", bufs=TILES + 1)
            nc.scalar.activation(out=res[:], in_=total[i][:], func=ACT.Identity, bias=mid_neg_max[:, i:i + 1], scale=1.0)
            nc.sync.dma_start(out=out[i * P:(i + 1) * P, :], in_=res[:])

        negate_identity()
        repeat_scales()
        turn_scales()
        keep_scales()
        widen((0, 0))
        turn_x((0, 0))
        spread_bias(0)
        spread_bias(2)
        for unit in [(0, 2), (0, 1)]:
            widen(unit)
            turn_x(unit)
        keep_bias(2, nc.scalar.copy)
        for unit in [(1, 0), (1, 2), (1, 1)]:
            widen(unit)
        empty_vector((0, 0))
        keep_bias(0, nc.vector.tensor_copy)
        score((0, 0))
        empty_vector((0, 2))
        empty_vector((0, 1))
        score((0, 2))
        for unit in [(2, 0), (2, 2), (2, 1)]:
            widen(unit)
        turn_x((1, 0))
        turn_x((1, 2))
        spread_bias(1)
        add_bias((0, 0))
        group_scalar(1)
        score((0, 1))
        group_trans(0)
        turn_x((1, 1))
        spread_gain(0)
        spread_gain(1)
        find_max((0, 0))
        add_bias((0, 2))
        empty_vector((1, 0))
        turn_x((2, 0))
        empty_vector((1, 2))
        keep_bias(1, nc.scalar.copy)
        exponent((0, 0))
        find_max((0, 2))
        exponent((0, 2))
        score((1, 0))
        quantize_trans(1)
        quantize_trans(0)
        score((1, 2))
        group_trans(2)
        turn_x((2, 2))
        empty_scalar((1, 1))
        turn_x((2, 1))
        add_bias((0, 1))
        invert_sums(0)
        add_bias((1, 0))
        empty_scalar((2, 0))
        empty_scalar((2, 2), [1])
        message(0, 0)
        message(0, 1)
        turn_v(0)
        score((1, 1))
        group_trans(3)
        empty_scalar((2, 1))
        add_bias((1, 2))
        empty_v(0)
        widen((3, 1))
        turn_x((3, 1))
        find_max((1, 0))
        exponent((1, 0))
        find_max((1, 2))
        exponent((1, 2))
        find_max((0, 1))
        exponent((0, 1))
        quantize_trans(2)
        quantize_trans(3)
        pass_on(0)
        quantize_x((2, 1))
        widen((3, 0))
        widen((3, 2))
        add_bias((1, 1))
        multiply_x((2, 1))
        empty_vector((2, 2), [0])
        find_max((1, 1))
        exponent((1, 1))

        for k in range(2, LAST_TILE):
            later = k + 2 < TILES
            score((k, 0))
            quantize_x((k, 2))
            if k >= 3:
                multiply_lifted(k - 3, x_room[k, 0])
                widen((k + 1, 2))
            cut(k - 2, 0)
            cut(k - 2, 1)
            lift_both(k - 2)
            empty_scalar((k + 1, 1))
            invert_sums(k - 1)
            add_bias((k, 1))
            turn_x((k + 1, 0))
            message(k - 1, 0)
            message(k - 1, 1)
            turn_v(k - 1)
            multiply_x((k, 2))
            turn_x((k + 1, 2))
            add_bias((k, 0))
            find_max((k, 1))
            find_max((k, 0))
            add_bias((k, 2))
            if k >= 4:
                sum_terms(k - 4)
                empty_v(k - 1)
                if later:
                    widen((k + 2, 1))
                    exponent((k, 1))
                else:
                    empty_scalar((k + 1, 0))
            else:
                widen((k + 2, 1))
                empty_v(k - 1)
                exponent((k, 1))
                empty_scalar((k + 1, 0), [1])
            exponent((k, 0))

            if later:
                pass_on(k - 1)
                score((k + 1, 1))
            else:
                score((k + 1, 1))
                pass_on(k - 1)
            if k >= 3:
                make_terms(k - 3, v_room(k - 1))
            if later:
                turn_x((k + 2, 1))
            find_max((k, 2))
            if later:
                widen((k + 2, 0))
            exponent((k, 2))
            if k < 4:
                empty_vector((k + 1, 0), [0])
            elif later:
                empty_vector((k + 1, 0))
            empty_vector((k + 1, 2))

        add_bias((7, 1))
        invert_sums(6)
        cut(5, 0)
        cut(5, 1)
        score((7, 0))
        score((7, 2))
        multiply_lifted(4, x_room[7, 0])
        lift_both(5)
        exponent((6, 1))
        message(6, 0)
        message(6, 1)
        turn_v(6)
        open_total(0)
        add_bias((7, 0))
        add_bias((7, 2))
        find_max((7, 0))
        find_max((7, 2))
        sum_terms(3)
        empty_v(6)
        exponent((7, 0))
        exponent((7, 2))
        pass_on(6)
        make_terms(4, v_room(6))
        multiply_lifted(5, fresh_room("prod5", T))
        open_total(1)
        find_max((7, 1))
        exponent((7, 1))
        invert_weights(0, 4)
        invert_sums(7)
        floor(6, 0)
        message(7, 0)
        turn_v(7, [0])
        message(7, 1)
        turn_v(7, [1])
        open_total(3)
        take_log(0)
        close_total(0)
        floor(6, 1)
        take_log(1)
        empty_v(7, nc.vector.tensor_copy)
        multiply_floored(6)
        pass_on(7)
        close_total(1)
        take_log(2)
        take_log(3)
        close_total(3)
        sum_terms(4)
        weigh(5)
        finish(2)
        finish_total(0)
        cut(7, 0)
        floor(7, 1)
        invert_weights(4, 6)
        weigh(6)
        take_log(4)
        multiply_cut(7)
        invert_weights(6, 7)
        finish_total(1)
        finish(4)
        take_log(5)
        weigh(7)
        finish_total(3)
        finish(5)
        invert_weights(7, 8)
        take_log(6)
        finish(6)
        take_log(7)
        finish(7)
